import numpy as np, ml_dtypes
CORES = [3,7,11,15,131,135,139,143]
N = 8
BF = ml_dtypes.bfloat16
W, L, S, T, HS, AS = 2048, 256, 8, 2, 1, 3
def parts(rng):
    D = rng.integers(0, W, (N, 8, 16, W)); one = rng.integers(0, W, (N, 8, 1, W))
    D = np.where((rng.random((N, 8, 1, W)) < 0.5) & (rng.random(D.shape) < 0.5), one, D)
    D = np.where(rng.random(D.shape) < 0.25, S * rng.integers(0, L, D.shape) + rng.integers(0, T, D.shape), D)
    X = rng.integers(0, 256, (N, 8, 16, W)); th = rng.integers(1000, 1800, (N, 8, 16))
    n = np.array([1, 1, 2, 2, 4, 4, 16, 16])[np.argsort(rng.random((N, 8)), axis=1)]
    j = (np.arange(16)[None, None, :] % n[:, :, None])[..., None]
    ti = np.take_along_axis(np.argsort(rng.random((N, 8, 16, 16)), axis=-1)[..., :3], j, 2)
    sg = np.take_along_axis(2 * rng.integers(0, 2, (N, 8, 16, 3)) - 1, j, 2)
    return D, X, th, ti, sg
def pack(D, X, th, ti, sg):
    return {"dg": np.ascontiguousarray(D.reshape(N, 128, W)).astype(np.int32), "xv": np.ascontiguousarray(X.reshape(N, 128, W)).astype(np.float32).astype(BF),
            "th": np.ascontiguousarray(th.reshape(N, 128, 1)).astype(np.int32), "ti": np.ascontiguousarray(ti.reshape(N, 128, 3)).astype(np.int32), "sg": np.ascontiguousarray(sg.reshape(N, 128, 3)).astype(np.int32)}
def setup_inputs(rng):
    return pack(*parts(rng))
def setup_inputs_corners(rng):
    D, X, th, ti, sg = parts(rng); c = np.arange(W)[None, :]; base = int(rng.integers(0, N)); o = rng.permutation(8)
    th = rng.choice(np.array([0, 1, 1365, 4080, 4081, 4081]), th.shape)
    for q in range(N):
        for g in range(8):
            m = int(o[g])
            if m == 0: D[q, g] = c
            if m == 1: D[q, g] = rng.choice(np.array([0, W - 1]), (16, W))
            if m == 2: D[q, g] = (c + 1 + np.arange(16)[:, None]) % W; th[q, g] = 4081
            if m == 3: D[q, g] = S * rng.integers(0, L, (16, W)) + rng.integers(0, T, (16, W))
            if m == 4: D[q, g] = rng.integers(0, W, (1, W)); th[q, g] = 4081
            if m == 5: D[q, g] = (c - 1) % W; th[q, g] = 0
            if m == 6: D[q, g] = rng.integers(0, W // 2, (16, W)) + (W // 2) * int(rng.integers(0, 2)); th[q, g] = 4081
            if m == 7: th[q, g] = 4080
    k = rng.random((N, 8, 1, W)); X = np.where(k < 0.1, 0, np.where(k < 0.2, 255, X))
    for q in (base % N, (base + 1) % N):
        for t in range(T): X[q, :, :, t::S] = 255
    a = (base + 2) % N; b = (base + 3) % N
    sg[a, :, :, 0] = -sg[a, :, :, 1]; sg[b] = sg[b][:, :, :1]
    return pack(D, X, th, ti, sg)
def setup_inputs_ties(rng):
    D, X, th, ti, sg = parts(rng)
    pr = rng.integers(0, 256, (8, 16, 24))
    pr[..., 12:] = np.minimum(pr[..., :12] + (np.arange(16)[None, :, None] == rng.integers(0, 16, (8, 1, 12))), 255)
    X = np.take_along_axis(np.broadcast_to(pr, (N, 8, 16, 24)), rng.integers(0, 24, (N, 8, 1, W)), 3)
    dd = np.add.reduce(np.abs(pr[:, :, :, None] - pr[:, :, None, :]), axis=1)
    th = dd[np.arange(8)[None, :, None], rng.integers(0, 24, (N, 8, 16)), rng.integers(0, 24, (N, 8, 16))] + rng.integers(0, 2, (N, 8, 16))
    return pack(D, X, th, ti, sg)
def setup_inputs_spread(rng):
    D, X, th, ti, sg = parts(rng)
    X = np.minimum((np.exp2(8 * rng.random((N, 8, 1, W))) * rng.random(X.shape)).astype(np.int64), 255)
    e = rng.choice(np.array([1, 2, 4]), (N, 8, 16, 1)); u = rng.random(D.shape)
    D = np.minimum((W * np.where(e == 1, u, np.where(e == 2, u * u, u * u * u * u))).astype(np.int64), W - 1)
    D = np.where(rng.random((N, 8, 16, 1)) < 0.5, D, W - 1 - D)
    th = np.minimum(np.exp2(12 * rng.random(th.shape)).astype(np.int64), 4081)
    return pack(D, X, th, ti, sg)
def setup_inputs_ends(rng):
    D, X, th, ti, sg = parts(rng)
    k = rng.random((N, 8, 1, W)); D = np.where(k < 0.4, (W - 1) * rng.integers(0, 2, k.shape), np.where(k < 0.75, (W - 1) * rng.integers(0, 2, D.shape), D))
    k = rng.random((N, 8, 1, W)); X = 255 * np.where(k < 0.3, rng.integers(0, 2, k.shape), rng.integers(0, 2, X.shape))
    th = 4081 * rng.integers(0, 2, th.shape); th[:, 0, 0] = 0; th[:, 7, 15] = 4081
    low = np.zeros((N, 8, 16, 1), np.int64); mid = rng.integers(1, 15, (N, 8, 16, 1))
    low[:, 4] = 1; mid[:, 4] = rng.integers(2, 15, (N, 16, 1))
    mid[:, 7] = 1 + np.arange(16).reshape(16, 1) % 14
    ti = np.concatenate([low, np.full((N, 8, 16, 1), 15), mid], axis=-1)
    ti = np.take_along_axis(ti, np.argsort(rng.random(ti.shape), axis=-1), 3)
    for q in (N - 2, N - 1, 0):
        c = (W - 1) * rng.integers(0, 2, (8, 1, L)); z = 255 * rng.integers(0, 2, (8, 1, L))
        c[..., 0] = 0; c[..., 1] = W - 1; c[..., L - 1] = W - 1; z[..., 0] = 0; z[..., 1] = 0; z[..., L - 1] = 0
        far = ((c == 0) == (z == 255)) & (rng.random((8, 1, L)) < 0.5); far[..., 0] = False; far[..., L - 1] = False
        off = (rng.integers(0, 16, (8, 16, L)) >> (3 * rng.integers(0, 2, (8, 1, L)))) * far
        x = np.abs(z - off)
        if q == N - 2:
            u = rng.permutation(8 * (L - 2))[:19 + 2 * int(rng.integers(0, 50))]; a = u // (L - 2); i = 1 + u % (L - 2)
            h = 255 * rng.integers(0, 2, (len(u), 16)); h[:, :2] = 0; h[:, 15] = 255
            c[a, 0, i] = W - 1; x[a, :, i] = h
        D[q, :, :, 0::S] = c; X[q, :, :, 0::S] = x
    for q in (N - 2, N - 1, 0, 1):
        D[q, :, :, 0] = 0; D[q, :, :, W - 1] = W - 1; X[q, :, :, 0] = 0; X[q, :, :, W - 1] = 255
    for q in (N - 1, 0):
        sg[q] = sg[q][:, :, :1]; sg[q, :, 0] = 1; sg[q, :, 15] = -1
    sg[1, :, :, 0] = -sg[1, :, :, 1]
    return pack(D, X, th, ti, sg)
def check_inputs(d):
    bad = []
    for k, lo, hi in (("dg", 0, W - 1), ("xv", 0, 255), ("th", 0, 4081), ("ti", 0, 15), ("sg", -1, 1)):
        a = np.asarray(d[k]).astype(np.float64)
        if not (np.min(a) >= lo and np.max(a) <= hi): bad.append("range of " + k)
    a = np.asarray(d["xv"]).astype(np.float64)
    if not np.all(a == np.floor(a)): bad.append("whole numbers in xv")
    a = np.asarray(d["ti"])
    if np.any(a[..., 0] == a[..., 1]) or np.any(a[..., 0] == a[..., 2]) or np.any(a[..., 1] == a[..., 2]): bad.append("different rows in a triple of ti")
    if np.any(np.asarray(d["sg"]) == 0): bad.append("no zero in sg")
    return bad
def reference(dg, xv, th, ti, sg):
    D = dg.astype(np.int64).reshape(N, 8, 16, W); X = xv.astype(np.float32).astype(np.int32).reshape(N, 8, 16, W); H = th.astype(np.int64).reshape(N, 8, 16, 1)
    G = np.zeros((N, 8, 16, 16), np.int64); np.put_along_axis(G, ti.astype(np.int64).reshape(N, 8, 16, 3), sg.astype(np.int64).reshape(N, 8, 16, 3), 3)
    def dist(q, E, x):
        y = np.take_along_axis(X[q], E.reshape(8, 1, 16 * L), 2).reshape(8, 16, 16, L)
        return np.add.reduce(np.abs(y - x[:, :, None, :]), axis=1).astype(np.int64)
    for t in range(T):
        v = S * np.arange(L) + t; new = np.array(D); last = []
        for r in range(N):
            s = (r + 1 + t) % N; x = X[r][:, :, v]; E = D[r][:, :, v]; go = np.ones((8, 16, L), bool)
            for step in range(HS + AS):
                q = r if step < HS else s
                n = np.take_along_axis(D[q], E, 2)
                go = go & (dist(q, n, x) < H[q]); E = np.where(go, n, E)
            d = dist(s, E, x); b = np.where(np.take_along_axis(X[s], E, 2) > x, 1, -1)
            cyc = np.abs(np.matmul(G[s], b)) == 3
            charged = np.matmul(np.abs(G[s]).transpose(0, 2, 1), cyc.astype(np.int64)) > 0
            A = int(np.count_nonzero(np.any(cyc, axis=1)))
            keep = np.argmin(np.where(charged, d, 2 ** 20), axis=1)
            gone = charged & (np.arange(16)[None, :, None] != keep[:, None, :])
            new[r][:, :, v] = np.where(gone, (37 * E + d + A) & (W - 1), D[r][:, :, v]); last.append(E)
        D = new
    yd = np.concatenate([D[:, :, :, t::S] for t in range(T)], axis=3)
    return {"yd": yd.reshape(N, 128, T * L).astype(np.float32), "ye": np.stack(last).reshape(N, 128, L).astype(np.float32)}

@@ -1,0 +1,669 @@
+from concourse.bass import DstId, RemoteDMATransfer
+from concourse.mybir import dt, AluOpType, AxisListType, ActivationFunctionType
+
+W, L, S, N = 2048, 256, 8, 8
+NCH = 4
+LC = L // NCH
+CW = 16 * LC
+ALPHA = 60.0
+MID = 1023.5
+BIGP = 8192.0
+AL = AluOpType
+AF = ActivationFunctionType
+
+U_ = ["L0a", "L0b", "L0i", "LEa", "LEb", "LEi", "L1_0", "L1_1", "ndo", "ndi", "nd2"] + ["%s_%d" % (n, t) for n in ("L2", "L3", "L4", "LF") for t in (0, 1)]
+H_ = ["e0b", "d0i", "wd", "mh"] + ["%s_%d" % (n, t) for n in ("h1", "m1", "g1", "h2", "h3", "h4", "hF", "m2", "m3", "m4") for t in (0, 1)]
+F_ = ["d0f", "dS_0", "dS_1", "mq", "q", "ga", "yd0", "yd1", "yef", "ndf", "ndg"] + ["ln%d_%d" % (k, t) for k in (2, 3, 4) for t in (0, 1)]
+B_ = ["x0", "xi", "r1a", "r1b", "r1i", "any"] + ["%s_%d" % (n, t) for n in ("r2", "r3", "r4", "bs", "sq", "ch", "go") for t in (0, 1)]
+I_ = ["qi", "ni"]
+POOLS = {"PU": (U_, "uint16"), "PH": (H_, "float16"), "PF": (F_, "float32"), "PB": (B_, "bfloat16"), "PI": (I_, "int32")}
+SLOT = {}
+SCRATCH = {}
+for _p in POOLS:
+    _names, _dt = POOLS[_p]
+    SCRATCH[_p] = ("sbuf", [128, 256 * len(_names)], _dt)
+    for _k, _n in enumerate(_names):
+        SLOT[_n] = (_p, 256 * _k)
+SCRATCH.update({
+    "dgs": ("sbuf", [128, W], "int32"), "dgf": ("sbuf", [128, W], "float32"), "xs": ("sbuf", [128, W], "bfloat16"),
+    "dcod": ("sbuf", [128, W], "bfloat16"), "xs2": ("sbuf", [128, W], "bfloat16"), "code2": ("sbuf", [128, W], "bfloat16"),
+    "xr0": ("sbuf", [128, 16 * L], "bfloat16"), "xr1": ("sbuf", [128, 16 * L], "bfloat16"), "xrn": ("sbuf", [128, 16 * L], "bfloat16"),
+    "zb": ("sbuf", [128, 32 * L], "bfloat16"), "ab": ("sbuf", [128, 32 * L], "bfloat16"), "gb": ("sbuf", [128, 32 * L], "bfloat16"),
+    "gh": ("sbuf", [128, 16 * L], "float16"),
+    "selb": ("sbuf", [128, 2048], "bfloat16"), "seln": ("sbuf", [128, 2048], "bfloat16"), "edb": ("sbuf", [128, 2048], "bfloat16"), "edh": ("sbuf", [128, 2048], "float16"),
+    "onb": ("sbuf", [128, 256], "bfloat16"), "onf": ("sbuf", [128, 256], "float32"), "on16": ("sbuf", [128, 128], "float32"),
+    "idb": ("sbuf", [128, 128], "bfloat16"), "idh": ("sbuf", [128, 128], "float16"), "idn": ("sbuf", [128, 128], "float16"), "idq": ("sbuf", [128, 128], "float16"), "idm": ("sbuf", [128, 128], "float16"),
+    "id37": ("sbuf", [128, 128], "float16"), "idp": ("sbuf", [128, 128], "bfloat16"), "idnb": ("sbuf", [128, 128], "bfloat16"), "idf": ("sbuf", [128, 128], "float32"),
+    "blk0": ("sbuf", [128, 128], "bfloat16"), "blk": ("sbuf", [128, 128], "bfloat16"),
+    "dupf": ("sbuf", [128, 256], "float32"), "dupb": ("sbuf", [128, 256], "bfloat16"), "iop": ("sbuf", [128, 256], "float32"),
+    "prow": ("sbuf", [128, 256], "bfloat16"), "rst": ("sbuf", [128, 256], "float32"),
+    "pm": ("sbuf", [128, 512], "float32"), "eq": ("sbuf", [128, 256], "bfloat16"),
+    "iq": ("sbuf", [128, 128], "float32"), "thi": ("sbuf", [128, 4], "int32"), "tii": ("sbuf", [128, 4], "int32"), "sgi": ("sbuf", [128, 4], "int32"),
+    "tif": ("sbuf", [128, 4], "float32"), "sgf": ("sbuf", [128, 4], "float32"),
+    "gq": ("sbuf", [128, 512], "float32"), "gj": ("sbuf", [128, 128], "bfloat16"),
+    "pk": ("sbuf", [128, 256], "bfloat16"), "pk2": ("sbuf", [128, 256], "bfloat16"),
+    "pt": ("sbuf", [128, 8], "float32"), "pt2": ("sbuf", [128, 8], "float32"),
+    "asum": ("sbuf", [128, 8], "float32"), "acol": ("sbuf", [128, 8], "float32"),
+})
+for _k in range(8):
+    SCRATCH["bank%d" % _k] = ("psum", [128, 512], "float32")
+SEMAPHORES = ["cv", "cs", "cp", "cg", "lsem", "ltab", "rx", "rtab", "rpk", "rpt", "rnh", "rn2"] + ["re%d" % c for c in range(NCH)] + ["rr%d" % c for c in range(NCH)] + ["ld%d" % k for k in range(10)]
+
+CY = 0.83e-3 * 1.2
+RELU = {(1, 0), (1, 2), (2, 3), (3, 3)}
+SG1 = ((1, 2), (0, 1))
+RS = ()
+CHS = True
+EDV, XR0, XRN, XR1 = "ssvsssssssvsssvs", "ssv", "v", "vs"
+GC = 1.5
+HOP = 2.5
+
+
+def rank_program(g, core, T, topo):
+    rank = T.rank_of(core)
+    if rank is None:
+        return
+    cores = T.cores
+    ops, lastw, readers, tiles, own = [], {}, {}, [], {}
+    bankof = {}
+    cur = [0]
+    ENG = {"v": g.vector, "s": g.scalar, "p": g.tensor, "g": g, "y": g.sync}
+    CSEM = {"v": "cv", "s": "cs", "p": "cp", "g": "cg"}
+
+    def add(eng, dur, fn, r=(), w=(), ps=(), sem=None, inc=1, lat=0.0, extra=(), boost=0.0):
+        k = len(ops)
+        deps = set(extra)
+        keys_w = list(w) + [("ps", t) for t in ps]
+        for x in r:
+            if x in lastw:
+                deps.add(lastw[x])
+        for x in keys_w:
+            if x in lastw:
+                deps.add(lastw[x])
+            deps.update(readers.get(x, ()))
+        for x in r:
+            readers.setdefault(x, []).append(k)
+        for x in keys_w:
+            lastw[x] = k
+            readers[x] = []
+        deps.discard(k)
+        hard = set(extra)
+        for x in list(r) + list(w):
+            hard.update(own.get(("w", x), ()))
+        for x in w:
+            hard.update(own.get(("r", x), ()))
+            own.setdefault(("w", x), []).append(k)
+        for x in r:
+            own.setdefault(("r", x), []).append(k)
+        soft = set(d for d in deps if ops[d]["e"] == eng and d not in hard and ps)
+        ops.append({"e": eng, "d": dur, "f": fn, "deps": deps, "ps": list(ps), "sem": sem, "inc": inc, "lat": lat, "c": cur[0], "soft": soft, "n": keys_w[0] if keys_w else "-"})
+        for t in ps:
+            tiles[t].append(k)
+        return k
+
+    def tile():
+        tiles.append([])
+        return len(tiles) - 1
+
+    def ps(t):
+        return T["bank%d" % bankof[t]]
+
+    def rng(c):
+        if c is None:
+            return 0, L
+        if c < 0:
+            h = -1 - c
+            return 128 * h, 128 * h + 128
+        return LC * c, LC * c + LC
+
+    def A(name, c=None):
+        p, o = SLOT[name]
+        a, b = rng(c)
+        return T[p][:, o + a:o + b]
+
+    def K(name, c=None):
+        a, b = rng(c)
+        return [(name, k) for k in range(a // LC, b // LC)]
+
+    def nn(c):
+        a, b = rng(c)
+        return b - a
+
+    def vt(n, f):
+        return 0.04 + max(64, n * f) * CY
+
+    def vcopy(out, in_, n, f, r, w, p=()):
+        return add("v", vt(n, f), lambda: g.vector.tensor_copy(R(out), R(in_)), r, w, p)
+
+    def R(x):
+        return x[0]() if isinstance(x, tuple) else x
+
+    def vts(out, in0, s1, s2, o0, o1, n, f, r, w, p=()):
+        def em():
+            i0 = R(in0)
+            if o1 is None:
+                return g.vector.tensor_scalar(out, i0, s1, None, o0)
+            return g.vector.tensor_scalar(out, i0, s1, s2, o0, o1)
+        return add("v", vt(n, f), em, r, w, p)
+
+    def vtt(out, in0, in1, op, n, f, r, w, p=()):
+        return add("v", vt(n, f), lambda: g.vector.tensor_tensor(out, R(in0), R(in1), op), r, w, p)
+
+    def sact(out, in_, func, n, r, w, p=(), bias=0.0, scale=1.0, acc=None):
+        def em():
+            i0 = R(in_)
+            if acc is not None:
+                return g.scalar.activation(out, i0, func, bias=bias, scale=scale, accum_out=acc)
+            return g.scalar.activation(out, i0, func, bias=bias, scale=scale)
+        return add("s", 0.08 + n * CY, em, r, w, p)
+
+    def mm(lst, cyc, r, p):
+        def em():
+            out = None
+            for (a, b, lhs, rhs, st, sp) in lst:
+                out = g.tensor.matmul(ps(p)[:, a:b], lhs, rhs, st, sp)
+            return out
+        return add("p", 0.03 + cyc * 0.6e-3, em, r, (), (p,))
+
+    def load(eng, buf, src, sem, lat):
+        q = g.sync if eng == "y" else g.scalar
+        return add(eng, 0.1, lambda: q.dma_start(buf, src), (), [(sem, "ld")], (), sem, 16, lat)
+
+    load("y", T.dgs[:, 0:W // 2], T.dg[:, 0:W // 2], "ld1", 4.5)
+    load("y", T.dgs[:, W // 2:W], T.dg[:, W // 2:W], "ld8", 7.0)
+    load("y", T.xs[:, :], T.xv[:, :], "ld0", 9.0)
+    load("y", T.thi[:, 0:1], T.th[:, :], "ld4", 9.5)
+    load("y", T.tii[:, 0:3], T.ti[:, :], "ld2", 9.5)
+    load("y", T.sgi[:, 0:3], T.sg[:, :], "ld3", 9.5)
+    KX, KDG = ("ld0", "ld"), [("ld1", "ld"), ("ld8", "ld")]
+
+    add("v", vt(256, 0.5), lambda: g.vector.memset(T.onb[:, :], 1.0), (), ["onb"])
+    add("v", vt(256, 1), lambda: g.vector.memset(T.onf[:, :], 1.0), (), ["onf"])
+    add("v", vt(2048, 0.5), lambda: g.vector.memset(T.edb[:, :], 0.0), (), ["edb0"])
+    add("v", vt(2048, 0.5), lambda: g.vector.memset(T.selb[:, :], 0.0), (), ["selb0"])
+    add("g", 0.4, lambda: g.affine_select(T.idb[:, :], T.onb[:, 0:128], [[-1, 128]], AL.is_equal, 0.0, 0, 1), ["onb"], ["idb"])
+    add("g", 0.4, lambda: g.affine_select(T.blk0[:, :], T.onb[:, 0:128], [[-16, 8], [0, 16]], AL.is_ge, 0.0, 0, 1), ["onb"], ["blk0"])
+    add("g", 0.4, lambda: g.affine_select(T.blk[:, :], T.blk0[:, :], [[16, 8], [0, 16]], AL.is_ge, 0.0, 15, -1), ["blk0"], ["blk"])
+    add("g", 0.4, lambda: g.iota(T.iq[:, :], [[0, 8], [1, 16]], 0, 0, allow_small_or_imprecise_dtypes=True), (), ["iq"])
+    add("g", 0.6, lambda: g.affine_select(T.dupf[:, :], T.onf[:, :], [[-16, 8], [0, 2], [-1, 16]], AL.is_equal, 0.0, 0, 1), ["onf"], ["dupf"])
+    add("g", 0.6, lambda: g.iota(T.iop[:, :], [[0, 8], [0, 2], [1, 16]], 0, 0, allow_small_or_imprecise_dtypes=True), (), ["iop"])
+    for p in range(16):
+        def cp(p=p):
+            if EDV[p] == "v":
+                return g.vector.tensor_copy(T.edb[:, p * 128 + p:(p + 1) * 128:16], T.idb[:, p:128:16])
+            return g.scalar.activation(T.edb[:, p * 128 + p:(p + 1) * 128:16], T.idb[:, p:128:16], AF.Copy)
+        add(EDV[p], vt(8, 1), cp, ["idb", "edb0"], [("edb", p)])
+    KED = [("edb", p) for p in range(16)]
+    vcopy(T.edh[:, :], T.edb[:, :], 2048, 0.5, KED, ["edh"])
+    for p in range(16):
+        def cp2(p=p):
+            return g.scalar.activation(T.selb[:, p * 128 + p:(p + 1) * 128:16], T.blk[:, 0:128:16], AF.Copy)
+        add("s", 0.08 + 8 * CY, cp2, ["blk", "selb0"], [("selb", p)])
+    KSEL = [("selb", p) for p in range(16)]
+    if RELU:
+        vts(T.seln[:, :], T.selb[:, :], -1.0, None, AL.mult, None, 2048, 0.5, KSEL, ["seln"])
+    vcopy(T.idh[:, :], T.idb[:, :], 128, 0.5, ["idb"], ["idh"])
+    vts(T.idn[:, :], T.idb[:, :], -1.0, None, AL.mult, None, 128, 0.5, ["idb"], ["idn"])
+    vts(T.id37[:, :], T.idb[:, :], 37.0, None, AL.mult, None, 128, 0.5, ["idb"], ["id37"])
+    vts(T.idp[:, :], T.idb[:, :], BIGP / 2, None, AL.mult, None, 128, 0.5, ["idb"], ["idp"])
+    vts(T.idq[:, :], T.idb[:, :], 0.5, None, AL.mult, None, 128, 0.5, ["idb"], ["idq"])
+    vts(T.idm[:, :], T.idb[:, :], -0.5, None, AL.mult, None, 128, 0.5, ["idb"], ["idm"])
+
+    def xrep(buf, src, rk, engs):
+        keys = []
+        for p in range(16):
+            e = engs[p % len(engs)]
+            o = T[buf][:, p:16 * L:16]
+            key = (buf, p)
+            keys.append(key)
+            if e == "v":
+                vcopy(o, src, 256, 0.5, rk, [key])
+            else:
+                sact(o, src, AF.Copy, 256, rk, [key])
+        return keys
+
+    xr0k = xrep("xr0", T.xs[:, 0:W:S], [KX], XR0)
+    vcopy(A("x0"), T.xs[:, 0:W:S], 256, 0.5, [KX], K("x0"))
+    for h in (0, 1):
+        vcopy(A("L0a", -1 - h), T.dgs[:, h * W // 2:(h + 1) * W // 2:S], 128, 1, [KDG[h]], K("L0a", -1 - h))
+
+    vcopy(T.tif[:, 0:3], T.tii[:, 0:3], 3, 1, [("ld2", "ld")], ["tif"])
+    vcopy(T.sgf[:, 0:3], T.sgi[:, 0:3], 3, 1, [("ld3", "ld")], ["sgf"])
+    for j, (a, b) in enumerate(((-1.0, 0.5), (-1.0, 0.5 + BIGP / 2), (1.0, 0.0), (1.0, -BIGP / 2))):
+        vts(T.pt[:, j:j + 1], T.thi[:, 0:1], a, b, AL.mult, AL.add, 1, 1, [("ld4", "ld")], ["ptk"])
+    PTK = ["ptk"]
+
+    def dest(r):
+        return cores[r % N]
+
+    def send(dsts, names_in, names_out, sem, dur, rd, after=(), lsem="lsem"):
+        trs, tot = [], 0
+        pieces = len(names_in)
+        for k in range(pieces):
+            d = dsts[k]
+            rid, pid = topo.addr(d, core)
+            es = topo.engines(core, d)
+            n = 1
+            while 2 * n * pieces <= min(len(es), 8):
+                n *= 2
+            m = sum(1 << e for e in es[k * n:(k + 1) * n])
+            trs.append((DstId(rid=rid, pnc=pid), m, names_in[k], names_out[k], sem[k]))
+            tot += n
+        if lsem == "lsem":
+            cnt["l"] += tot
+
+        def em():
+            return g.remote_dma_fused([RemoteDMATransfer(dst_ids=[a], dma_engine_mask=m, remote_sem=T.sem[s_], src=i, dst=o)
+                                       for (a, m, i, o, s_) in trs], local_sem=T.sem[lsem])
+        return add("g", dur, em, rd, (), (), "-", 0, 0.0, after)
+
+    cnt = {"l": 0}
+
+    def recv(sem, val, lat, after, keys):
+        return add("n", 0.0, None, (), keys, (), sem, val, lat, [after])
+
+    s1 = dest(rank + 1)
+    k = send([s1, s1], [A("x0"), A("L0a")], [A("xi"), A("L0i")], ["rx", "rx"], 1.5, K("x0") + K("L0a"))
+    recv("rx", 8, HOP, k, K("xi") + K("L0i"))
+
+    par = {}
+
+    def bufpair(buf, c):
+        n = par.get((buf, c), 0)
+        par[(buf, c)] = n + 1
+        o = (n % 2) * 16 * L + c * CW
+        return o, (buf, n % 2, c)
+
+    GT_ = 0.06 + CW * GC * CY
+
+    def diag(src, key, ed, kd, p, off=0, o0=0):
+        mm([(off, off + LC, ed[:, q * 128:(q + 1) * 128], src[:, o0 + q:o0 + CW:16], q == 0, q == 15) for q in range(16)], CW, [key] + kd, p)
+
+    def view(X, kx, lst, kl, xr, kxr, c, st):
+        zo, zk = bufpair("zb", c)
+        add("v", GT_, lambda: g.vector.tensor_tensor(T.zb[:, zo:zo + CW], X[:, :].indirect(lst), xr[:, c * CW:(c + 1) * CW], AL.subtract),
+            [kx] + kl + kxr, [zk])
+        ao, ak = bufpair("ab", c)
+        if (st, c) in RELU:
+            vts(T.ab[:, ao:ao + CW], T.zb[:, zo:zo + CW], 0.0, 2.0, AL.max, AL.mult, CW, 0.5, [zk], [ak])
+        else:
+            sact(T.ab[:, ao:ao + CW], T.zb[:, zo:zo + CW], AF.Abs, CW, [zk], [ak])
+        return zo, zk, ao, ak
+
+    def dist(v4, st, c, p, off, pen=None):
+        zo, zk, ao, ak = v4
+        two = (st, c) in RELU
+        if two:
+            mm([(off, off + LC, T.seln[:, q * 128:(q + 1) * 128], T.zb[:, zo + q:zo + CW:16], q == 0, False) for q in range(16)], CW, [zk, "seln"], p)
+        mm([(off, off + LC, T.selb[:, q * 128:(q + 1) * 128], T.ab[:, ao + q:ao + CW:16], q == 0 and not two, q == 15 and pen is None) for q in range(16)],
+           CW, [ak] + KSEL, p)
+        if pen is not None:
+            mm([(off, off + LC, T.idp[:, :], pen[0], False, True)], LC, pen[1] + ["idp"], p)
+
+    def rest(k, c, rk, q, th, kth):
+        j = 1 if (k - 1) in RS else 0
+        if k in RS:
+            sact(A(rk, c), F(lambda: ps(q)[:, 0:LC]), AF.Sign, LC, [kth], K(rk, c), (q,), bias=th[:, j:j + 1])
+        else:
+            vts(A(rk, c), F(lambda: ps(q)[:, 0:LC]), th[:, 2 + j:3 + j], 2.0, AL.is_ge, AL.mult, LC, 1, [kth], K(rk, c), (q,))
+
+    def home(t, c, L0, L1, r1, xr, kxr, kdg):
+        p = tile()
+        if c in SG1[t]:
+            go, gk = bufpair("gb", c)
+            add("s", GT_, lambda: g.scalar.activation(T.gb[:, go:go + CW], T.dcod[:, :].indirect(A(L0, c)), AF.Copy), ["code"] + K(L0, c), [gk])
+            diag(T.gb, gk, T.edb, KED, p, 0, go)
+            lk = "ln2_%d" % t
+            sact(A(lk, c), F(lambda: ps(p)[:, 0:LC]), AF.Ln, LC, (), K(lk, c), (p,))
+            vts(A(L1, c), A(lk, c), ALPHA, MID + 0.25, AL.mult, AL.add, LC, 1, K(lk, c), K(L1, c))
+        else:
+            add("v", GT_, lambda: g.vector.tensor_copy(T.gh[:, c * CW:(c + 1) * CW], T.dgs[:, :].indirect(A(L0, c))), kdg + K(L0, c), [("gh", c)])
+            diag(T.gh, ("gh", c), T.edh, ["edh"], p, 0, c * CW)
+            vcopy(A(L1, c), F(lambda: ps(p)[:, 0:LC]), LC, 1, (), K(L1, c), (p,))
+        yield
+        q = tile()
+        dist(view(T.xs, KX, A(L1, c), K(L1, c), xr, kxr, c, 1), 1, c, q, 0)
+        rest(1, c, r1, q, T.pt, "ptk")
+        yield
+
+    def walk(t, c, L1, r1, e0, tb, xr, kxr):
+        X, kx, code, kc, th, kth = tb["X"], tb["kx"], tb["code"], tb["kc"], tb["th"], tb["kth"]
+        h1 = "h1_%d" % t
+        m1 = "m1_%d" % t
+        vcopy(A(h1, c), A(L1, c), LC, 0.5, K(L1, c), K(h1, c))
+        lst, hp, rp, ms = L1, h1, r1, [m1]
+        for k in (2, 3, 4):
+            Lk, hk, lk, rk, mk = ["%s%d_%d" % (n, k, t) for n in ("L", "h", "ln", "r", "m")]
+            go, gk = bufpair("gb", c)
+
+            def gat(go=go, lst=lst):
+                return g.scalar.activation(T.gb[:, go:go + CW], code[:, :].indirect(A(lst, c)), AF.Copy)
+            add("s", GT_, gat, [kc] + K(lst, c), [gk])
+            p = tile()
+            diag(T.gb, gk, T.edb, KED, p, 0, go)
+            sact(A(lk, c), F(lambda p=p: ps(p)[:, 0:LC]), AF.Ln, LC, (), K(lk, c), (p,))
+            vts(A(Lk, c), A(lk, c), ALPHA, MID + 0.25, AL.mult, AL.add, LC, 1, K(lk, c), K(Lk, c))
+            vcopy(A(hk, c), A(Lk, c), LC, 0.5, K(Lk, c), K(hk, c))
+            q = tile()
+            mm([(LC, 2 * LC, T.idh[:, :], A(hp, c), True, False), (LC, 2 * LC, T.idn[:, :], A(hk, c), False, True)], 2 * LC,
+               K(hp, c) + K(hk, c) + ["idh", "idn"], q)
+            if k == 2:
+                mm([(2 * LC, 3 * LC, T.idh[:, :], A(e0, c), True, False), (2 * LC, 3 * LC, T.idn[:, :], A(h1, c), False, True)], 2 * LC,
+                   K(e0, c) + K(h1, c) + ["idh", "idn"], q)
+                vtt(A(m1, c), A(r1, c), F(lambda q=q: ps(q)[:, 2 * LC:3 * LC]), AL.mult, LC, 1, K(r1, c), K(m1, c), (q,))
+            dist(view(X, kx, A(Lk, c), K(Lk, c), xr, kxr, c, k), k, c, q, 0, (A(rp, c), K(rp, c)))
+            rest(k, c, rk, q, th, kth)
+            vtt(A(mk, c), A(rk, c), F(lambda q=q: ps(q)[:, LC:2 * LC]), AL.mult, LC, 1, K(rk, c), K(mk, c), (q,))
+            lst, hp, rp = Lk, hk, rk
+            ms.append(mk)
+            yield
+        LF, hF = "LF_%d" % t, "hF_%d" % t
+        p = tile()
+        hs = [e0, h1] + ["h%d_%d" % (k, t) for k in (2, 3, 4)]
+        seq = [(T.idh, hp)] + [(T.idq, x) for x in ms]
+        for k in RS:
+            seq += [(T.idq, hs[k - 1]), (T.idm, hs[k])]
+        mm([(0, LC, w[:, :], A(x, c), i == 0, i == len(seq) - 1) for i, (w, x) in enumerate(seq)], len(seq) * LC,
+           sum([K(x, c) for w, x in seq], []) + ["idq", "idh", "idm"], p)
+        vcopy(A(LF, c), F(lambda: ps(p)[:, 0:LC]), LC, 1, (), K(LF, c), (p,))
+        zo, zk, ao, ak = v4 = view(X, kx, A(LF, c), K(LF, c), xr, kxr, c, 5)
+        vcopy(A(hF, c), A(LF, c), LC, 0.5, K(LF, c), K(hF, c))
+        p2 = tile()
+        diag(T.zb, zk, T.edb, KED, p2, LC, zo)
+        bs, sq, ch, dS = "bs_%d" % t, "sq_%d" % t, "ch_%d" % t, "dS_%d" % t
+        sact(A(bs, c), F(lambda: ps(p2)[:, LC:2 * LC]), AF.Sign, LC, (), K(bs, c), (p2,), bias=-0.5)
+        p3 = tile()
+        dist(v4, 5, c, p3, 0)
+        sact(A(dS, c), F(lambda: ps(p3)[:, 0:LC]), AF.Copy, LC, (), K(dS, c), (p3,))
+        p4 = tile()
+        mm([(0, LC, tb["GT"], A(bs, c), True, True)], LC, K(bs, c) + [tb["kgt"]], p4)
+        sact(A(sq, c), F(lambda: ps(p4)[:, 0:LC]), AF.Square, LC, (), K(sq, c), (p4,))
+        p5 = tile()
+        mm([(0, LC, tb["aG"], A(sq, c), True, True), (LC, 2 * LC, T.blk[:, :], A(sq, c), True, True)], 2 * LC, K(sq, c) + [tb["kag"], "blk"], p5)
+        if CHS:
+            sact(A(ch, c), F(lambda: ps(p5)[:, 0:LC]), AF.Sign, LC, [tb["knt"]], K(ch, c), (p5,), bias=tb["nt"][:, 4:5])
+        else:
+            vts(A(ch, c), F(lambda: ps(p5)[:, 0:LC]), tb["nt"][:, 5:6], None, AL.is_gt, None, LC, 1, [tb["knt"]], K(ch, c), (p5,))
+        sact(A("any", c), F(lambda: ps(p5)[:, LC:2 * LC]), AF.Sign, LC, (), K("any", c) + [("asum", t, c)], (p5,), bias=-16.0,
+             acc=T.asum[:, 4 * t + c:4 * t + c + 1])
+        yield
+
+    def keep(t, h, D0h):
+        c = -1 - h
+        dS, ch, hF, go = "dS_%d" % t, "ch_%d" % t, "hF_%d" % t, "go_%d" % t
+        p = tile()
+        mm([(0, 256, A(dS, c), T.dupf[:, :], True, False), (0, 256, T.onb[:, 0:128], T.prow[:, :], False, False)],
+           1024 + 256, K(dS, c) + ["dupf", "onb", "prow"], p)
+        mm([(0, 256, A(ch, c), T.dupb[:, :], False, True)], 256, K(ch, c) + ["dupb"], p)
+        add("v", vt(256, 1), lambda: g.vector.tensor_tensor_scan(T.pm[:, 256 * h:256 * h + 256], T.rst[:, :], ps(p)[:, 0:256], 0.0, AL.mult, AL.min),
+            ["rst"], [("pm", h)], (p,))
+        for x in range(8):
+            vtt(T.eq[:, 128 * h + 16 * x:128 * h + 16 * x + 16], T.pm[:, 256 * h + 32 * x + 16:256 * h + 32 * x + 32],
+                F(lambda x=x: ps(p)[:, 32 * x + 16:32 * x + 32]), AL.is_equal, 16, 1, [("pm", h)], [("eq", h, x)], (p,))
+        q = tile()
+        mm([(0, 128, T.id37[:, :], A(hF, c), True, False), (0, 128, T.idf[:, :], A(dS, c), False, True)],
+           640, K(hF, c) + K(dS, c) + ["id37", "idf"], q)
+        u = tile()
+        mm([(0, 128, T.idb[:, :], A(ch, c), True, False)], 128, K(ch, c) + ["idb"], u)
+        mm([(0, 128, T.eq[:, 128 * h:128 * h + 128], T.idnb[:, :], False, True)], 128, [("eq", h, x) for x in range(8)] + ["idnb"], u)
+        return q, u
+
+    def finish(t, out, D0f, D0h, wt):
+        p = tile()
+        mm([(0, 1, T.on16[:, :], T.asum[:, 4 * t + c:4 * t + c + 1], c == 0, c == NCH - 1) for c in range(NCH)], 4 * 4 * 64,
+           [("asum", t, c) for c in range(NCH)] + ["on16"], p)
+        vcopy(T.acol[:, t:t + 1], F(lambda: ps(p)[:, 0:1]), 1, 1, (), [("acol", t)], (p,))
+        for c in (-1, -2):
+            q, u = wt[-1 - c]
+            vts(A("qi", c), F(lambda q=q: ps(q)[:, 0:128]), T.acol[:, t:t + 1], None, AL.add, None, 128, 1, [("acol", t)], K("qi", c), (q,))
+            vts(A("ni", c), A("qi", c), W - 1, None, AL.bitwise_and, None, 128, 1, K("qi", c), K("ni", c))
+            vtt(A("wd", c), A("ni", c), A(D0f, c), AL.subtract, 128, 2, K("ni", c) + K(D0f, c), K("wd", c))
+            vtt(A("mh", c), A("wd", c), F(lambda u=u: ps(u)[:, 0:128]), AL.mult, 128, 1, K("wd", c), K("mh", c), (u,))
+            v = tile()
+            mm([(0, 128, T.idh[:, :], A(D0h, c), True, False), (0, 128, T.idh[:, :], A("mh", c), False, True)], 256, K(D0h, c) + K("mh", c) + ["idh"], v)
+            vcopy(A(out, c), F(lambda v=v: ps(v)[:, 0:128]), 128, 1, (), K(out, c), (v,))
+
+    def run(gens):
+        gens = list(enumerate(gens))
+        while gens:
+            nxt = []
+            for c, x in gens:
+                cur[0] = c
+                try:
+                    next(x)
+                    nxt.append((c, x))
+                except StopIteration:
+                    pass
+            gens = nxt
+        cur[0] = 0
+
+    for h in (0, 1):
+        a, b = h * W // 2, (h + 1) * W // 2
+        vcopy(T.dgf[:, a:b], T.dgs[:, a:b], W // 2, 1, [KDG[h]], [("dgf", h)])
+        sact(T.dcod[:, a:b], T.dgf[:, a:b], AF.Exp, W // 2, [("dgf", h)], ["code"], bias=-MID / ALPHA, scale=1.0 / ALPHA)
+
+    run(home(0, c, "L0a", "LEa", "r1a", T.xr0, xr0k, KDG) for c in range(NCH))
+    for c in range(NCH):
+        last = send([s1], [A("LEa", c)], [A("LEi", c)], ["re%d" % c], 1.0, K("LEa", c))
+        recv("re%d" % c, 8, HOP, last, K("LEi", c))
+    for c in range(NCH):
+        last = send([s1], [A("r1a", c)], [A("r1i", c)], ["rr%d" % c], 1.0, K("r1a", c))
+        recv("rr%d" % c, 8, HOP, last, K("r1i", c))
+
+    for k in range(3):
+        vts(T.gq[:, 128 * k:128 * k + 128], T.iq[:, :], T.tif[:, k:k + 1], T.sgf[:, k:k + 1], AL.is_equal, AL.mult, 128, 1, ["iq", "tif", "sgf"], [("gq", k)])
+    vtt(T.gq[:, 384:512], T.gq[:, 0:128], T.gq[:, 128:256], AL.add, 128, 2, [("gq", 0), ("gq", 1)], [("gq", 3)])
+    vtt(T.gq[:, 0:128], T.gq[:, 384:512], T.gq[:, 256:384], AL.add, 128, 2, [("gq", 3), ("gq", 2)], [("gq", 0)])
+    vtt(T.gj[:, :], T.gq[:, 0:128], T.blk[:, :], AL.mult, 128, 2, [("gq", 0), "blk"], ["gj"])
+    sact(T.pk[:, 128:256], T.gj[:, :], AF.Abs, 128, ["gj"], ["pkA"])
+    p0 = tile()
+    mm([(0, 128, T.gj[:, :], T.idb[:, :], True, True), (128, 129, T.pk[:, 128:256], T.onb[:, 0:1], True, True)], 192, ["gj", "idb", "pkA", "onb"], p0)
+    sact(T.pk[:, 0:128], F(lambda: ps(p0)[:, 0:128]), AF.Copy, 128, (), ["pkG"], (p0,))
+    vts(T.pt[:, 4:5], F(lambda: ps(p0)[:, 128:129]), -1.0, None, AL.mult, None, 1, 1, (), ["ptn"], (p0,))
+    vcopy(T.pt[:, 5:6], F(lambda: ps(p0)[:, 128:129]), 1, 1, (), ["ptn"], (p0,))
+    xrnk = xrep("xrn", A("xi"), K("xi"), XRN)
+    vcopy(A("d0i"), A("L0i"), L, 0.5, K("L0i"), K("d0i"))
+    vcopy(A("d0f"), A("L0i"), L, 1, K("L0i"), K("d0f"))
+
+    h2 = dest(rank - 2)
+    k = send([h2, h2], [T.xs[:, :], T.dcod[:, :]], [T.xs2[:, :], T.code2[:, :]], ["rtab", "rtab"], 1.0, [KX, "code"], (last,), "ltab")
+    add("n", 0.0, None, ["code"], (), (), "ltab", 8, 25.0, [k])
+    recv("rtab", 8, 25.0, k, ["xs2", "code2"])
+    k = send([h2], [T.pk[:, :]], [T.pk2[:, :]], ["rpk"], 1.0, ["pkA", "pkG"], (k,))
+    recv("rpk", 8, 25.0, k, ["pk2"])
+    k = send([h2], [T.pt[:, 0:6]], [T.pt2[:, 0:6]], ["rpt"], 1.0, PTK + ["ptn"], (k,))
+    recv("rpt", 8, 25.0, k, ["pt2"])
+
+    vcopy(T.idf[:, :], T.idb[:, :], 128, 1, ["idb"], ["idf"])
+    vts(T.dupb[:, :], T.dupf[:, :], -BIGP, None, AL.mult, None, 256, 1, ["dupf"], ["dupb"])
+    vts(T.prow[:, :], T.iop[:, :], 1.0 / 4096, 1.0 / 8192, AL.mult, AL.add, 256, 1, ["iop"], ["prow"])
+    add("v", vt(256, 1), lambda: g.vector.memset(T.rst[:, :], 1.0), (), ["rst"])
+    add("v", vt(8, 1), lambda: g.vector.memset(T.rst[:, 0:256:32], 0.0), (), ["rst"])
+    vts(T.idnb[:, :], T.idb[:, :], -1.0, None, AL.mult, None, 128, 0.5, ["idb"], ["idnb"])
+    add("v", vt(128, 1), lambda: g.vector.memset(T.on16[:, :], 1.0 / 16), (), ["on16"])
+
+    tb = {"X": T.xs, "kx": KX, "code": T.dcod, "kc": "code", "th": T.pt, "kth": "ptk", "nt": T.pt, "knt": "ptn",
+          "GT": T.pk[:, 0:128], "kgt": "pkG", "aG": T.pk[:, 128:256], "kag": "pkA"}
+    run(walk(0, c, "LEi", "r1i", "d0i", tb, T.xrn, xrnk) for c in range(NCH))
+    wt = [keep(0, h, "d0i") for h in (0, 1)]
+    finish(0, "ndo", "d0f", "d0i", wt)
+    d1, d2 = dest(rank - 1), dest(rank - 3)
+    k = send([d1], [A("ndo")], [A("ndi")], ["rnh"], 1.0, K("ndo"))
+    recv("rnh", 8, HOP, k, K("ndi"))
+    k = send([d2], [A("ndo")], [A("nd2")], ["rn2"], 1.0, K("ndo"), (k,))
+    recv("rn2", 8, HOP, k, K("nd2"))
+
+    vcopy(A("L0b"), T.dgs[:, 1:W:S], 256, 1, KDG, K("L0b"))
+    vcopy(A("e0b"), A("L0b"), 256, 0.5, K("L0b"), K("e0b"))
+    xr1k = xrep("xr1", T.xs[:, 1:W:S], [KX], XR1)
+    if SG1[1]:
+        vcopy(A("ndg"), A("ndi"), 256, 1, K("ndi"), K("ndg"))
+        sact(T.dcod[:, 0:W:S], A("ndg"), AF.Exp, 256, K("ndg"), ["code"], bias=-MID / ALPHA, scale=1.0 / ALPHA)
+    vcopy(T.dgs[:, 0:W:S], A("ndi"), 256, 1, K("ndi"), KDG)
+    run(home(1, c, "L0b", "LEb", "r1b", T.xr1, xr1k, KDG) for c in range(NCH))
+    vcopy(A("ndf"), A("nd2"), 256, 1, K("nd2"), K("ndf"))
+    sact(T.code2[:, 0:W:S], A("ndf"), AF.Exp, 256, K("ndf"), ["code2"], bias=-MID / ALPHA, scale=1.0 / ALPHA)
+    vcopy(A("yd0"), A("ndi"), 256, 1, K("ndi"), K("yd0"))
+    add("y", 0.1, lambda: g.sync.dma_start(T.yd[:, 0:L], A("yd0")), K("yd0"), (), (), "ld5", 16, 2.0)
+    vcopy(A("d0f"), A("L0b"), L, 1, K("L0b"), K("d0f"))
+    tb = {"X": T.xs2, "kx": "xs2", "code": T.code2, "kc": "code2", "th": T.pt2, "kth": "pt2", "nt": T.pt2, "knt": "pt2",
+          "GT": T.pk2[:, 0:128], "kgt": "pk2", "aG": T.pk2[:, 128:256], "kag": "pk2"}
+    run(walk(1, c, "LEb", "r1b", "e0b", tb, T.xr1, xr1k) for c in range(NCH))
+    vcopy(A("yef"), A("LF_1"), L, 1, K("LF_1"), K("yef"))
+    add("y", 0.1, lambda: g.sync.dma_start(T.ye[:, :], A("yef")), K("yef"), (), (), "ld6", 16, 2.0)
+    wt = [keep(1, h, "e0b") for h in (0, 1)]
+    finish(1, "yd1", "d0f", "e0b", wt)
+    add("y", 0.1, lambda: g.sync.dma_start(T.yd[:, L:2 * L], A("yd1")), K("yd1"), (), (), "ld7", 16, 2.0)
+
+    order = schedule(ops, tiles, bankof)
+    emit(g, T, ENG, CSEM, ops, order, cnt["l"])
+
+
+def F(fn):
+    return (fn,)
+
+
+PW = 0.01
+SKEW = 1.4
+BONUS = {}
+
+
+def kind(o):
+    n = o["n"]
+    return "%s%d %s" % (o["e"], o["c"], n[0] if isinstance(n, tuple) else n)
+
+
+SEML = 0.1
+
+
+def schedule(ops, tiles, bankof):
+    n = len(ops)
+    succ = [[] for _ in range(n)]
+    for k in range(n):
+        for d in ops[k]["deps"]:
+            succ[d].append(k)
+    bl = [0.0] * n
+    for k in range(n - 1, -1, -1):
+        o = ops[k]
+        bl[k] = o["d"] + o["lat"] + max([bl[s] for s in succ[k]] + [0.0])
+    tfirst = {}
+    for t, lst in enumerate(tiles):
+        if lst:
+            tfirst[lst[0]] = t
+    tleft = [len(x) for x in tiles]
+    bank = [None] * 8
+    bfree = [(0.0, None)] * 8
+    left = [len(o["deps"]) for o in ops]
+    ready = [k for k in range(n) if left[k] == 0]
+    fin = [0.0] * n
+    free = {}
+    order = []
+    rt = [0.0] * n
+    pri = [PW * (bl[k] - SKEW * ops[k]["c"] + BONUS.get(kind(ops[k]), 0.0)) for k in range(n)]
+    free["n"] = -1.0
+    while ready:
+        best = None
+        for k in ready:
+            o = ops[k]
+            st = max(rt[k], free.get(o["e"], 0.0))
+            if best is not None and st - pri[k] > best[0][0]:
+                continue
+            b = -1
+            if k in tfirst:
+                cand = [(bfree[i][0], i) for i in range(8) if bank[i] is None]
+                if not cand:
+                    continue
+                f, b = min(cand)
+                st = max(st, f + SEML if f > 0 else 0.0)
+            key = (st - pri[k], k)
+            if best is None or key < best[0]:
+                best = (key, k, st, b)
+        if best is None:
+            raise ValueError("no free PSUM bank")
+        _, k, st, b = best
+        o = ops[k]
+        ready.remove(k)
+        if b >= 0:
+            t = tfirst[k]
+            bankof[t] = b
+            bank[b] = t
+            if bfree[b][1] is not None:
+                o["deps"].add(bfree[b][1])
+        if o["e"] != "n":
+            free[o["e"]] = st + o["d"]
+        fin[k] = st + o["d"] + o["lat"]
+        o["st"] = st
+        order.append(k)
+        for t in o["ps"]:
+            tleft[t] -= 1
+            if tleft[t] == 0:
+                bb = bankof[t]
+                bank[bb] = None
+                bfree[bb] = (fin[k], k)
+        for s in succ[k]:
+            left[s] -= 1
+            x = fin[k] + (SEML if ops[s]["e"] != o["e"] else 0.05)
+            if x > rt[s]:
+                rt[s] = x
+            if left[s] == 0:
+                ready.append(s)
+    return order
+
+
+def emit(g, T, ENG, CSEM, ops, order, nlocal):
+    count = {"v": 0, "s": 0, "p": 0, "g": 0}
+    known = {e: {} for e in ENG}
+    done = {}
+    waited = {}
+    for k in order:
+        o = ops[k]
+        e = o["e"]
+        if e == "n":
+            done[k] = (o["sem"], o["inc"], {})
+            continue
+        q = ENG[e]
+        need = {}
+        imp = dict(known[e])
+        for d in o["deps"]:
+            if done[d] is None or d in o["soft"]:
+                continue
+            if e == "p" and ops[d]["e"] == "p":
+                continue
+            s, v, _i = done[d]
+            if known[e].get(s, 0) < v and need.get(s, (0, 0))[0] < v:
+                need[s] = (v, d)
+        for s in list(need):
+            v, d = need[s]
+            for s2 in need:
+                if s2 != s and done[need[s2][1]][2].get(s, 0) >= v:
+                    del need[s]
+                    break
+        for s in need:
+            v, d = need[s]
+            q.wait_ge(T.sem[s], v)
+            waited[s] = max(waited.get(s, 0), v)
+            for a, b in done[d][2].items():
+                if known[e].get(a, 0) < b:
+                    known[e][a] = b
+            known[e][s] = max(known[e].get(s, 0), v)
+        inst = o["f"]()
+        if o["sem"] == "-":
+            done[k] = None
+            continue
+        if o["sem"] is None:
+            count[e] += 1
+            s, v = CSEM[e], count[e]
+            inst.then_inc(T.sem[s], 1)
+        else:
+            s, v = o["sem"], o["inc"]
+            inst.then_inc(T.sem[s], v)
+        done[k] = (s, v, dict(known[e]))
+    total = {CSEM[e]: count[e] for e in count if count[e]}
+    total["lsem"] = nlocal
+    for k in order:
+        o = ops[k]
+        if o["sem"] not in (None, "-"):
+            total[o["sem"]] = o["inc"]
+    for s in total:
+        if waited.get(s, 0) < total[s]:
+            g.wait_ge(T.sem[s], total[s])

@@ -2,19 +2,21 @@ from concourse.bass import DstId, RemoteDMATransfer
 from concourse.mybir import dt, AluOpType, AxisListType, ActivationFunctionType
 
 W, L, S, N = 2048, 256, 8, 8
-NCH = 4
-LC = L // NCH
-CW = 16 * LC
-ALPHA = 60.0
-MID = 1023.5
-BIGP = 8192.0
+H = 128
+SB = 4
+SW = 16 * H // SB
+HW = 16 * H
+SH = 65536.0
+MAGIC = 1.5 * 2.0 ** 39
+BIG = 4096.0
 AL = AluOpType
 AF = ActivationFunctionType
 
-U_ = ["L0a", "L0b", "L0i", "LEa", "LEb", "LEi", "L1_0", "L1_1", "ndo", "ndi", "nd2"] + ["%s_%d" % (n, t) for n in ("L2", "L3", "L4", "LF") for t in (0, 1)]
-H_ = ["e0b", "d0i", "wd", "mh"] + ["%s_%d" % (n, t) for n in ("h1", "m1", "g1", "h2", "h3", "h4", "hF", "m2", "m3", "m4") for t in (0, 1)]
-F_ = ["d0f", "dS_0", "dS_1", "mq", "q", "ga", "yd0", "yd1", "yef", "ndf", "ndg"] + ["ln%d_%d" % (k, t) for k in (2, 3, 4) for t in (0, 1)]
-B_ = ["x0", "xi", "r1a", "r1b", "r1i", "any"] + ["%s_%d" % (n, t) for n in ("r2", "r3", "r4", "bs", "sq", "ch", "go") for t in (0, 1)]
+R2 = (0, 1)
+U_ = ["L0a", "L0b", "L0i", "L1a", "L1i", "L1b"] + ["%s_%d" % (n, t) for n in ("L2", "L3", "L4", "LF") for t in R2]
+H_ = ["wd", "mh", "ndo", "ndi", "nd2"] + ["%s_%d" % (n, t) for n in ("h0", "h1", "h2", "h3", "h4", "hF", "m1", "m2", "m3", "m4") for t in R2]
+F_ = ["yd0", "yd1", "yef", "dT", "ut"] + ["zc%d" % k for k in (1, 2, 3, 4)]
+B_ = ["x0", "xi", "f1a", "f1_0", "f1_1", "any", "bs", "sq", "ch"] + ["%s_%d" % (n, t) for n in ("f2", "f3", "f4") for t in R2] + ["tt%d" % k for k in (1, 2, 3, 4)]
 I_ = ["qi", "ni"]
 POOLS = {"PU": (U_, "uint16"), "PH": (H_, "float16"), "PF": (F_, "float32"), "PB": (B_, "bfloat16"), "PI": (I_, "int32")}
 SLOT = {}
@@ -24,39 +26,38 @@ for _p in POOLS:
     SCRATCH[_p] = ("sbuf", [128, 256 * len(_names)], _dt)
     for _k, _n in enumerate(_names):
         SLOT[_n] = (_p, 256 * _k)
-SCRATCH.update({
-    "dgs": ("sbuf", [128, W], "int32"), "dgf": ("sbuf", [128, W], "float32"), "xs": ("sbuf", [128, W], "bfloat16"),
-    "dcod": ("sbuf", [128, W], "bfloat16"), "xs2": ("sbuf", [128, W], "bfloat16"), "code2": ("sbuf", [128, W], "bfloat16"),
-    "xr0": ("sbuf", [128, 16 * L], "bfloat16"), "xr1": ("sbuf", [128, 16 * L], "bfloat16"), "xrn": ("sbuf", [128, 16 * L], "bfloat16"),
-    "zb": ("sbuf", [128, 32 * L], "bfloat16"), "ab": ("sbuf", [128, 32 * L], "bfloat16"), "gb": ("sbuf", [128, 32 * L], "bfloat16"),
-    "gh": ("sbuf", [128, 16 * L], "float16"),
-    "selb": ("sbuf", [128, 2048], "bfloat16"), "seln": ("sbuf", [128, 2048], "bfloat16"), "edb": ("sbuf", [128, 2048], "bfloat16"), "edh": ("sbuf", [128, 2048], "float16"),
-    "onb": ("sbuf", [128, 256], "bfloat16"), "onf": ("sbuf", [128, 256], "float32"), "on16": ("sbuf", [128, 128], "float32"),
-    "idb": ("sbuf", [128, 128], "bfloat16"), "idh": ("sbuf", [128, 128], "float16"), "idn": ("sbuf", [128, 128], "float16"), "idq": ("sbuf", [128, 128], "float16"), "idm": ("sbuf", [128, 128], "float16"),
-    "id37": ("sbuf", [128, 128], "float16"), "idp": ("sbuf", [128, 128], "bfloat16"), "idnb": ("sbuf", [128, 128], "bfloat16"), "idf": ("sbuf", [128, 128], "float32"),
-    "blk0": ("sbuf", [128, 128], "bfloat16"), "blk": ("sbuf", [128, 128], "bfloat16"),
-    "dupf": ("sbuf", [128, 256], "float32"), "dupb": ("sbuf", [128, 256], "bfloat16"), "iop": ("sbuf", [128, 256], "float32"),
-    "prow": ("sbuf", [128, 256], "bfloat16"), "rst": ("sbuf", [128, 256], "float32"),
-    "pm": ("sbuf", [128, 512], "float32"), "eq": ("sbuf", [128, 256], "bfloat16"),
-    "iq": ("sbuf", [128, 128], "float32"), "thi": ("sbuf", [128, 4], "int32"), "tii": ("sbuf", [128, 4], "int32"), "sgi": ("sbuf", [128, 4], "int32"),
-    "tif": ("sbuf", [128, 4], "float32"), "sgf": ("sbuf", [128, 4], "float32"),
-    "gq": ("sbuf", [128, 512], "float32"), "gj": ("sbuf", [128, 128], "bfloat16"),
-    "pk": ("sbuf", [128, 256], "bfloat16"), "pk2": ("sbuf", [128, 256], "bfloat16"),
-    "pt": ("sbuf", [128, 8], "float32"), "pt2": ("sbuf", [128, 8], "float32"),
-    "asum": ("sbuf", [128, 8], "float32"), "acol": ("sbuf", [128, 8], "float32"),
-})
+for _n, _w, _dt in (
+        ("dgs", W, "int32"), ("xs", W, "bfloat16"), ("xq", W, "bfloat16"), ("xq2", W, "bfloat16"),
+        ("P0", W, "float32"), ("P1", W, "float32"), ("P2", W, "float32"),
+        ("xr0", 16 * L, "bfloat16"), ("xr1", 16 * L, "bfloat16"), ("xrn", 16 * L, "bfloat16"),
+        ("zf", 32 * L, "float32"), ("gf", 16 * L, "float32"), ("zb", 32 * L, "bfloat16"), ("ab", 32 * L, "bfloat16"),
+        ("gh", 16 * L, "float16"), ("yb", 16 * L, "bfloat16"), ("ed", 2048, "bfloat16"), ("edh", 2048, "float16"),
+        ("onb", 256, "bfloat16"), ("onf", 256, "float32"), ("onh", 128, "float16"), ("ngb", 128, "bfloat16"),
+        ("idb", 128, "bfloat16"), ("idh", 128, "float16"), ("idn", 128, "float16"), ("idq", 128, "float16"), ("id37", 128, "float16"),
+        ("idp", 128, "bfloat16"), ("idnb", 128, "bfloat16"), ("idf", 128, "float32"), ("ids", 128, "bfloat16"),
+        ("blk0", 128, "bfloat16"), ("blk", 128, "bfloat16"),
+        ("dupf", 256, "float32"), ("dupb", 256, "bfloat16"), ("iop", 256, "float32"), ("prow", 256, "bfloat16"), ("rst", 256, "float32"),
+        ("pm", 512, "float32"), ("eq", 256, "bfloat16"), ("iq", 128, "float32"),
+        ("thi", 4, "int32"), ("tii", 4, "int32"), ("sgi", 4, "int32"), ("tif", 4, "float32"), ("sgf", 4, "float32"), ("thc", 4, "float32"),
+        ("gq", 512, "float32"), ("gj", 128, "bfloat16"), ("pk", 256, "bfloat16"), ("pk2", 256, "bfloat16"),
+        ("thd", 128, "float16"), ("thd2", 128, "float16"), ("asum", 8, "float32"), ("acol", 8, "float32")):
+    SCRATCH[_n] = ("sbuf", [128, _w], _dt)
 for _k in range(8):
     SCRATCH["bank%d" % _k] = ("psum", [128, 512], "float32")
-SEMAPHORES = ["cv", "cs", "cp", "cg", "lsem", "ltab", "rx", "rtab", "rpk", "rpt", "rnh", "rn2"] + ["re%d" % c for c in range(NCH)] + ["rr%d" % c for c in range(NCH)] + ["ld%d" % k for k in range(10)]
+SEMAPHORES = ["cv", "cs", "cp", "cg", "lsem", "ltab", "rx", "rxq", "rtab", "rpk", "rnh", "rn2", "re0", "re1", "rr0", "rr1"] + ["ld%d" % k for k in range(10)]
 
-CY = 0.83e-3 * 1.2
-RELU = {(1, 0), (1, 2), (2, 3), (3, 3)}
-SG1 = ((1, 2), (0, 1))
-RS = ()
-CHS = True
-EDV, XR0, XRN, XR1 = "ssvsssssssvsssvs", "ssv", "v", "vs"
+G0V = ((0, 0), (1, 0))
+G1V = (1,)
+VIA = tuple((t, 4, h, 0) for t in R2 for h in R2)
+TS = ()
+XR0, XRN, XR1 = "s", "g", "g"
+ABW = {1: 2, 2: 2, 3: 2, 4: 1, 5: 1}
+
+CY = 0.83e-3 * 1.1
+PC = 0.42e-3 * 1.1
 GC = 1.5
 HOP = 2.5
+LAT = {"x": 4.0, "d0": 6.0, "d1": 8.0, "small": 8.5, "first": 2.0, "xq": 9.0, "tab": 18.0}
 
 
 def rank_program(g, core, T, topo):
@@ -70,7 +71,7 @@ def rank_program(g, core, T, topo):
     ENG = {"v": g.vector, "s": g.scalar, "p": g.tensor, "g": g, "y": g.sync}
     CSEM = {"v": "cv", "s": "cs", "p": "cp", "g": "cg"}
 
-    def add(eng, dur, fn, r=(), w=(), ps=(), sem=None, inc=1, lat=0.0, extra=(), boost=0.0):
+    def add(eng, dur, fn, r=(), w=(), ps=(), sem=None, inc=1, lat=0.0, extra=()):
         k = len(ops)
         deps = set(extra)
         keys_w = list(w) + [("ps", t) for t in ps]
@@ -108,108 +109,91 @@ def rank_program(g, core, T, topo):
     def ps(t):
         return T["bank%d" % bankof[t]]
 
-    def rng(c):
-        if c is None:
-            return 0, L
-        if c < 0:
-            h = -1 - c
-            return 128 * h, 128 * h + 128
-        return LC * c, LC * c + LC
+    def PS(t, a, b):
+        return (lambda: ps(t)[:, a:b],)
 
-    def A(name, c=None):
+    def R(x):
+        return x[0]() if isinstance(x, tuple) else x
+
+    def A(name, h=None, a=0, b=H):
         p, o = SLOT[name]
-        a, b = rng(c)
-        return T[p][:, o + a:o + b]
+        if h is None:
+            return T[p][:, o:o + L]
+        return T[p][:, o + H * h + a:o + H * h + b]
 
-    def K(name, c=None):
-        a, b = rng(c)
-        return [(name, k) for k in range(a // LC, b // LC)]
-
-    def nn(c):
-        a, b = rng(c)
-        return b - a
+    def K(name, h=None, s=None):
+        return [(name, a, b) for a in (R2 if h is None else (h,)) for b in (R2 if s is None else (2 * s // SB,))]
 
     def vt(n, f):
         return 0.04 + max(64, n * f) * CY
 
     def vcopy(out, in_, n, f, r, w, p=()):
-        return add("v", vt(n, f), lambda: g.vector.tensor_copy(R(out), R(in_)), r, w, p)
-
-    def R(x):
-        return x[0]() if isinstance(x, tuple) else x
+        return add("v", vt(n, f), lambda: g.vector.tensor_copy(out, R(in_)), r, w, p)
 
     def vts(out, in0, s1, s2, o0, o1, n, f, r, w, p=()):
         def em():
-            i0 = R(in0)
             if o1 is None:
-                return g.vector.tensor_scalar(out, i0, s1, None, o0)
-            return g.vector.tensor_scalar(out, i0, s1, s2, o0, o1)
+                return g.vector.tensor_scalar(out, R(in0), s1, None, o0)
+            return g.vector.tensor_scalar(out, R(in0), s1, s2, o0, o1)
         return add("v", vt(n, f), em, r, w, p)
 
     def vtt(out, in0, in1, op, n, f, r, w, p=()):
         return add("v", vt(n, f), lambda: g.vector.tensor_tensor(out, R(in0), R(in1), op), r, w, p)
 
+    def vset(out, val, n, f, w):
+        return add("v", vt(n, f), lambda: g.vector.memset(out, val), (), w)
+
     def sact(out, in_, func, n, r, w, p=(), bias=0.0, scale=1.0, acc=None):
         def em():
-            i0 = R(in_)
             if acc is not None:
-                return g.scalar.activation(out, i0, func, bias=bias, scale=scale, accum_out=acc)
-            return g.scalar.activation(out, i0, func, bias=bias, scale=scale)
-        return add("s", 0.08 + n * CY, em, r, w, p)
+                return g.scalar.activation(out, R(in_), func, bias=bias, scale=scale, accum_out=acc)
+            return g.scalar.activation(out, R(in_), func, bias=bias, scale=scale)
+        return add("s", 0.06 + n * CY, em, r, w, p)
 
     def mm(lst, cyc, r, p):
         def em():
             out = None
-            for (a, b, lhs, rhs, st, sp) in lst:
-                out = g.tensor.matmul(ps(p)[:, a:b], lhs, rhs, st, sp)
+            for (c, lhs, rhs, st, sp) in lst:
+                out = g.tensor.matmul(ps(p)[:, c], lhs, rhs, st, sp)
             return out
-        return add("p", 0.03 + cyc * 0.6e-3, em, r, (), (p,))
+        return add("p", 0.03 + cyc * PC, em, r, (), (p,))
 
-    def load(eng, buf, src, sem, lat):
-        q = g.sync if eng == "y" else g.scalar
-        return add(eng, 0.1, lambda: q.dma_start(buf, src), (), [(sem, "ld")], (), sem, 16, lat)
+    C = slice
 
-    load("y", T.dgs[:, 0:W // 2], T.dg[:, 0:W // 2], "ld1", 4.5)
-    load("y", T.dgs[:, W // 2:W], T.dg[:, W // 2:W], "ld8", 7.0)
-    load("y", T.xs[:, :], T.xv[:, :], "ld0", 9.0)
-    load("y", T.thi[:, 0:1], T.th[:, :], "ld4", 9.5)
-    load("y", T.tii[:, 0:3], T.ti[:, :], "ld2", 9.5)
-    load("y", T.sgi[:, 0:3], T.sg[:, :], "ld3", 9.5)
+    def load(buf, src, sem, lat):
+        k = add("y", 0.1, lambda: g.sync.dma_start(buf, src), (), [(sem, "ld")], (), sem, 16, lat)
+        ops[k]["up"] = 100.0 - k
+
+    load(T.xs[:, :], T.xv[:, :], "ld0", LAT["x"])
+    load(T.dgs[:, 0:W // 2], T.dg[:, 0:W // 2], "ld1", LAT["d0"])
+    load(T.dgs[:, W // 2:W], T.dg[:, W // 2:W], "ld8", LAT["d1"])
+    load(T.thi[:, 0:1], T.th[:, :], "ld4", LAT["small"])
+    load(T.tii[:, 0:3], T.ti[:, :], "ld2", LAT["small"])
+    load(T.sgi[:, 0:3], T.sg[:, :], "ld3", LAT["small"])
     KX, KDG = ("ld0", "ld"), [("ld1", "ld"), ("ld8", "ld")]
 
-    add("v", vt(256, 0.5), lambda: g.vector.memset(T.onb[:, :], 1.0), (), ["onb"])
-    add("v", vt(256, 1), lambda: g.vector.memset(T.onf[:, :], 1.0), (), ["onf"])
-    add("v", vt(2048, 0.5), lambda: g.vector.memset(T.edb[:, :], 0.0), (), ["edb0"])
-    add("v", vt(2048, 0.5), lambda: g.vector.memset(T.selb[:, :], 0.0), (), ["selb0"])
-    add("g", 0.4, lambda: g.affine_select(T.idb[:, :], T.onb[:, 0:128], [[-1, 128]], AL.is_equal, 0.0, 0, 1), ["onb"], ["idb"])
-    add("g", 0.4, lambda: g.affine_select(T.blk0[:, :], T.onb[:, 0:128], [[-16, 8], [0, 16]], AL.is_ge, 0.0, 0, 1), ["onb"], ["blk0"])
-    add("g", 0.4, lambda: g.affine_select(T.blk[:, :], T.blk0[:, :], [[16, 8], [0, 16]], AL.is_ge, 0.0, 15, -1), ["blk0"], ["blk"])
-    add("g", 0.4, lambda: g.iota(T.iq[:, :], [[0, 8], [1, 16]], 0, 0, allow_small_or_imprecise_dtypes=True), (), ["iq"])
-    add("g", 0.6, lambda: g.affine_select(T.dupf[:, :], T.onf[:, :], [[-16, 8], [0, 2], [-1, 16]], AL.is_equal, 0.0, 0, 1), ["onf"], ["dupf"])
-    add("g", 0.6, lambda: g.iota(T.iop[:, :], [[0, 8], [0, 2], [1, 16]], 0, 0, allow_small_or_imprecise_dtypes=True), (), ["iop"])
-    for p in range(16):
-        def cp(p=p):
-            if EDV[p] == "v":
-                return g.vector.tensor_copy(T.edb[:, p * 128 + p:(p + 1) * 128:16], T.idb[:, p:128:16])
-            return g.scalar.activation(T.edb[:, p * 128 + p:(p + 1) * 128:16], T.idb[:, p:128:16], AF.Copy)
-        add(EDV[p], vt(8, 1), cp, ["idb", "edb0"], [("edb", p)])
-    KED = [("edb", p) for p in range(16)]
-    vcopy(T.edh[:, :], T.edb[:, :], 2048, 0.5, KED, ["edh"])
-    for p in range(16):
-        def cp2(p=p):
-            return g.scalar.activation(T.selb[:, p * 128 + p:(p + 1) * 128:16], T.blk[:, 0:128:16], AF.Copy)
-        add("s", 0.08 + 8 * CY, cp2, ["blk", "selb0"], [("selb", p)])
-    KSEL = [("selb", p) for p in range(16)]
-    if RELU:
-        vts(T.seln[:, :], T.selb[:, :], -1.0, None, AL.mult, None, 2048, 0.5, KSEL, ["seln"])
-    vcopy(T.idh[:, :], T.idb[:, :], 128, 0.5, ["idb"], ["idh"])
-    vts(T.idn[:, :], T.idb[:, :], -1.0, None, AL.mult, None, 128, 0.5, ["idb"], ["idn"])
-    vts(T.id37[:, :], T.idb[:, :], 37.0, None, AL.mult, None, 128, 0.5, ["idb"], ["id37"])
-    vts(T.idp[:, :], T.idb[:, :], BIGP / 2, None, AL.mult, None, 128, 0.5, ["idb"], ["idp"])
-    vts(T.idq[:, :], T.idb[:, :], 0.5, None, AL.mult, None, 128, 0.5, ["idb"], ["idq"])
-    vts(T.idm[:, :], T.idb[:, :], -0.5, None, AL.mult, None, 128, 0.5, ["idb"], ["idm"])
+    def gsel(out, in_, pat, op, base, cm, n, r, w):
+        return add("g", 0.17 + 2 * n * CY, lambda: g.affine_select(out, in_, pat, op, 0.0, base, cm), r, w)
 
-    def xrep(buf, src, rk, engs):
+    vset(T.onb[:, :], 1.0, 256, 0.5, ["onb"])
+    vset(T.ed[:, :], 1.0, 2048, 0.5, ["ed"])
+    vset(T.onf[:, :], 1.0, 256, 1, ["onf"])
+    vset(T.ngb[:, :], -1.0, 128, 0.5, ["ngb"])
+    gsel(T.idb[:, :], T.onb[:, 0:128], [[-1, 128]], AL.is_equal, 0, 1, 128, ["onb"], ["idb"])
+    gsel(T.blk0[:, :], T.onb[:, 0:128], [[-16, 8], [0, 16]], AL.is_ge, 0, 1, 128, ["onb"], ["blk0"])
+    gsel(T.blk[:, :], T.blk0[:, :], [[16, 8], [0, 16]], AL.is_ge, 15, -1, 128, ["blk0"], ["blk"])
+    add("g", 0.4, lambda: g.iota(T.iq[:, :], [[0, 8], [1, 16]], 0, 0, allow_small_or_imprecise_dtypes=True), (), ["iq"])
+    gsel(T.dupf[:, :], T.onf[:, :], [[-16, 8], [0, 2], [-1, 16]], AL.is_equal, 0, 1, 256, ["onf"], ["dupf"])
+    add("g", 0.6, lambda: g.iota(T.iop[:, :], [[0, 8], [0, 2], [1, 16]], 0, 0, allow_small_or_imprecise_dtypes=True), (), ["iop"])
+    for q in range(0, 16, 4):
+        gsel(T.ed[:, 128 * q:128 * q + 512], T.ed[:, 128 * q:128 * q + 512], [[-256, 4], [-16, 8], [255, 16]], AL.is_equal, -256 * q, 1, 512, ["ed"], [("ed", q)])
+    KED = [("ed", q) for q in range(0, 16, 4)]
+    for name, val in (("ids", SH), ("idf", 1.0), ("idh", 1.0), ("idnb", -1.0), ("idn", -1.0), ("idp", BIG), ("idq", 0.5), ("id37", 37.0)):
+        vts(T[name][:, :], T.idb[:, :], val, None, AL.mult, None, 128, 0.5, ["idb"], [name])
+    vcopy(T.edh[:, :], T.ed[:, :], 2048, 0.5, KED, ["edh"])
+    vcopy(T.onh[:, :], T.onb[:, 0:128], 128, 0.5, ["onb"], ["onh"])
+
+    def xrep(buf, src, rk, engs, scale=1.0):
         keys = []
         for p in range(16):
             e = engs[p % len(engs)]
@@ -217,211 +201,229 @@ def rank_program(g, core, T, topo):
             key = (buf, p)
             keys.append(key)
             if e == "v":
-                vcopy(o, src, 256, 0.5, rk, [key])
+                vts(o, src, scale, None, AL.mult, None, 256, 0.5, rk, [key])
+            elif e == "s":
+                sact(o, src, AF.Copy, 256, rk, [key], scale=scale)
             else:
-                sact(o, src, AF.Copy, 256, rk, [key])
+                gsel(o, src, [[0, L]], AL.is_ge, 0, 0, 256, rk, [key])
         return keys
 
-    xr0k = xrep("xr0", T.xs[:, 0:W:S], [KX], XR0)
-    vcopy(A("x0"), T.xs[:, 0:W:S], 256, 0.5, [KX], K("x0"))
-    for h in (0, 1):
-        vcopy(A("L0a", -1 - h), T.dgs[:, h * W // 2:(h + 1) * W // 2:S], 128, 1, [KDG[h]], K("L0a", -1 - h))
-
-    vcopy(T.tif[:, 0:3], T.tii[:, 0:3], 3, 1, [("ld2", "ld")], ["tif"])
-    vcopy(T.sgf[:, 0:3], T.sgi[:, 0:3], 3, 1, [("ld3", "ld")], ["sgf"])
-    for j, (a, b) in enumerate(((-1.0, 0.5), (-1.0, 0.5 + BIGP / 2), (1.0, 0.0), (1.0, -BIGP / 2))):
-        vts(T.pt[:, j:j + 1], T.thi[:, 0:1], a, b, AL.mult, AL.add, 1, 1, [("ld4", "ld")], ["ptk"])
-    PTK = ["ptk"]
+    sact(A("x0"), T.xs[:, 0:W:S], AF.Copy, L, [KX], K("x0"), scale=SH)
+    for h in R2:
+        sact(T.xq[:, h * W // 2:(h + 1) * W // 2], T.xs[:, h * W // 2:(h + 1) * W // 2], AF.Copy, W // 2, [KX], [("xq", h)], scale=SH)
+    KXQ = [("xq", h) for h in R2]
+    xr0k = xrep("xr0", A("x0"), K("x0"), XR0)
+    for h in R2:
+        vcopy(A("L0a", h), T.dgs[:, h * W // 2:(h + 1) * W // 2:S], H, 1, [KDG[h]], K("L0a", h))
+    for j in range(4):
+        c = C(512 * j, 512 * j + 512)
+        p = tile()
+        mm([(C(0, 512), T.ids[:, :], T.xs[:, c], True, True)], 512, [KX, "ids"], p)
+        vtt(T.P0[:, c], T.dgs[:, c], PS(p, 0, 512), AL.add, 512, 1, [KDG[j // 2]], [("P0", j)], (p,))
+    KP0 = [("P0", j) for j in range(4)]
+    vts(T.thc[:, 0:1], T.thi[:, 0:1], -1.0, 2048.0, AL.mult, AL.add, 1, 1, [("ld4", "ld")], ["thc"])
+    vts(T.thd[:, :], T.idh[:, :], T.thc[:, 0:1], None, AL.mult, None, 128, 0.5, ["idh", "thc"], ["thd"])
 
     def dest(r):
         return cores[r % N]
 
-    def send(dsts, names_in, names_out, sem, dur, rd, after=(), lsem="lsem"):
-        trs, tot = [], 0
-        pieces = len(names_in)
-        for k in range(pieces):
-            d = dsts[k]
-            rid, pid = topo.addr(d, core)
-            es = topo.engines(core, d)
-            n = 1
-            while 2 * n * pieces <= min(len(es), 8):
-                n *= 2
-            m = sum(1 << e for e in es[k * n:(k + 1) * n])
-            trs.append((DstId(rid=rid, pnc=pid), m, names_in[k], names_out[k], sem[k]))
-            tot += n
-        if lsem == "lsem":
-            cnt["l"] += tot
-
-        def em():
-            return g.remote_dma_fused([RemoteDMATransfer(dst_ids=[a], dma_engine_mask=m, remote_sem=T.sem[s_], src=i, dst=o)
-                                       for (a, m, i, o, s_) in trs], local_sem=T.sem[lsem])
-        return add("g", dur, em, rd, (), (), "-", 0, 0.0, after)
-
     cnt = {"l": 0}
 
-    def recv(sem, val, lat, after, keys):
-        return add("n", 0.0, None, (), keys, (), sem, val, lat, [after])
+    def send(d, names_in, names_out, sem, rd, after=(), lsem="lsem", dur=0.7):
+        pieces = len(names_in)
+        rid, pid = topo.addr(d, core)
+        es = topo.engines(core, d)
+        n = 1
+        while 2 * n * pieces <= min(len(es), 8):
+            n *= 2
+        masks = [sum(1 << e for e in es[k * n:(k + 1) * n]) for k in range(pieces)]
+        if lsem == "lsem":
+            cnt["l"] += n * pieces
 
-    s1 = dest(rank + 1)
-    k = send([s1, s1], [A("x0"), A("L0a")], [A("xi"), A("L0i")], ["rx", "rx"], 1.5, K("x0") + K("L0a"))
-    recv("rx", 8, HOP, k, K("xi") + K("L0i"))
+        def em():
+            return g.remote_dma_fused([RemoteDMATransfer(dst_ids=[DstId(rid=rid, pnc=pid)], dma_engine_mask=masks[k], remote_sem=T.sem[sem], src=names_in[k], dst=names_out[k])
+                                       for k in range(pieces)], local_sem=T.sem[lsem])
+        return add("g", dur, em, rd, (), (), "-", 0, 0.0, after), n * pieces
+
+    def recv(sem, sent, lat, keys):
+        return add("n", 0.0, None, (), keys, (), sem, sent[1], lat, [sent[0]])
+
+    s1, h2 = dest(rank + 1), dest(rank - 2)
+    k = send(s1, [A("x0")], [A("xi")], "rx", K("x0"))
+    recv("rx", k, HOP + LAT["first"], K("xi"))
 
     par = {}
+    GT_ = 0.06 + SW * GC * CY
 
-    def bufpair(buf, c):
-        n = par.get((buf, c), 0)
-        par[(buf, c)] = n + 1
-        o = (n % 2) * 16 * L + c * CW
-        return o, (buf, n % 2, c)
+    def room(buf, h, two=True):
+        n = par.get((buf, h), 0)
+        par[(buf, h)] = n + 1
+        n = n % 2 if two else 0
+        return n * 16 * L + h * HW, [(buf, n, h, s) for s in range(SB)]
 
-    GT_ = 0.06 + CW * GC * CY
+    def lanes(lst, h, s):
+        return A(lst, h, s * H // SB, (s + 1) * H // SB)
 
-    def diag(src, key, ed, kd, p, off=0, o0=0):
-        mm([(off, off + LC, ed[:, q * 128:(q + 1) * 128], src[:, o0 + q:o0 + CW:16], q == 0, q == 15) for q in range(16)], CW, [key] + kd, p)
+    def raw(eng, win, kw, lst, h):
+        buf = "gf" if eng == "s" else "gh"
+        o, keys = room(buf, h, False)
+        for s in range(SB):
+            out = T[buf][:, o + s * SW:o + (s + 1) * SW]
+            if eng == "s":
+                add("s", GT_, lambda out=out, s=s: g.scalar.activation(out, win[:, :].indirect(lanes(lst, h, s)), AF.Copy), kw + K(lst, h, s), [keys[s]])
+            else:
+                add("v", GT_, lambda out=out, s=s: g.vector.tensor_copy(out, win[:, :].indirect(lanes(lst, h, s))), kw + K(lst, h, s), [keys[s]])
+        return buf, o, keys
 
-    def view(X, kx, lst, kl, xr, kxr, c, st):
-        zo, zk = bufpair("zb", c)
-        add("v", GT_, lambda: g.vector.tensor_tensor(T.zb[:, zo:zo + CW], X[:, :].indirect(lst), xr[:, c * CW:(c + 1) * CW], AL.subtract),
-            [kx] + kl + kxr, [zk])
-        ao, ak = bufpair("ab", c)
-        if (st, c) in RELU:
-            vts(T.ab[:, ao:ao + CW], T.zb[:, zo:zo + CW], 0.0, 2.0, AL.max, AL.mult, CW, 0.5, [zk], [ak])
+    def view(t, k, win, kw, lst, h, xr, kxr, packed):
+        buf = "zf" if packed else "zb"
+        o, keys = room(buf, h)
+        ao, ak = room("ab", h)
+        yo, yk = room("yb", h, False)
+        bias = -1024.0 / SH if packed else 0.0
+        todo = []
+        for s in range(SB):
+            x = xr[:, h * HW + s * SW:h * HW + (s + 1) * SW]
+            if (t, k, h, s) in VIA:
+                y = T.yb[:, yo + s * SW:yo + (s + 1) * SW]
+                add("s", GT_, lambda y=y, s=s: g.scalar.activation(y, win[:, :].indirect(lanes(lst, h, s)), AF.Copy), kw + K(lst, h, s), [yk[s]])
+                p = tile()
+                mm([(C(0, SW), T.idb[:, :], y, True, False), (C(0, SW), T.idnb[:, :], x, False, True)], 2 * SW, [yk[s], "idb", "idnb"] + kxr, p)
+                sact(T.ab[:, ao + s * SW:ao + (s + 1) * SW], PS(p, 0, SW), AF.Abs, SW, (), [ak[s]], (p,), scale=1.0 / SH)
+                continue
+            out = T[buf][:, o + s * SW:o + (s + 1) * SW]
+            add("v", GT_, lambda out=out, s=s, x=x: g.vector.tensor_tensor(out, win[:, :].indirect(lanes(lst, h, s)), x, AL.subtract),
+                kw + K(lst, h, s) + kxr, [keys[s]])
+            todo.append(s)
+            if len(todo) == ABW[k] or s == SB - 1 or (t, k, h, s + 1) in VIA:
+                a, b = todo[0] * SW, (s + 1) * SW
+                sact(T.ab[:, ao + a:ao + b], T[buf][:, o + a:o + b], AF.Abs, b - a, [keys[x_] for x_ in todo], [ak[x_] for x_ in todo], bias=bias, scale=1.0 / SH)
+                todo = []
+        return (buf, o, keys, yo, yk), (ao, ak)
+
+    def own_rows(p, u, src, o, ed, rd, last=True):
+        o += u * HW // 2
+        mm([(C(64 * u, 64 * u + 64), ed[:, q * 128:(q + 1) * 128], src[:, o + q:o + HW // 2:16], q == 0, last and q == 15) for q in range(16)], 1024, rd, p)
+
+    def follow(t, k, src, h, Lk, hk):
+        buf, o, keys = src[:3]
+        if buf == "gh":
+            for u in R2:
+                p = tile()
+                s = u * SB // 2
+                own_rows(p, u, T.gh, o, T.edh, keys[s:s + SB // 2] + ["edh"])
+                vcopy(A(Lk, h, 64 * u, 64 * u + 64), PS(p, 64 * u, 64 * u + 64), 64, 1, (), K(Lk, h, s), (p,))
         else:
-            sact(T.ab[:, ao:ao + CW], T.zb[:, zo:zo + CW], AF.Abs, CW, [zk], [ak])
-        return zo, zk, ao, ak
-
-    def dist(v4, st, c, p, off, pen=None):
-        zo, zk, ao, ak = v4
-        two = (st, c) in RELU
-        if two:
-            mm([(off, off + LC, T.seln[:, q * 128:(q + 1) * 128], T.zb[:, zo + q:zo + CW:16], q == 0, False) for q in range(16)], CW, [zk, "seln"], p)
-        mm([(off, off + LC, T.selb[:, q * 128:(q + 1) * 128], T.ab[:, ao + q:ao + CW:16], q == 0 and not two, q == 15 and pen is None) for q in range(16)],
-           CW, [ak] + KSEL, p)
-        if pen is not None:
-            mm([(off, off + LC, T.idp[:, :], pen[0], False, True)], LC, pen[1] + ["idp"], p)
-
-    def rest(k, c, rk, q, th, kth):
-        j = 1 if (k - 1) in RS else 0
-        if k in RS:
-            sact(A(rk, c), F(lambda: ps(q)[:, 0:LC]), AF.Sign, LC, [kth], K(rk, c), (q,), bias=th[:, j:j + 1])
-        else:
-            vts(A(rk, c), F(lambda: ps(q)[:, 0:LC]), th[:, 2 + j:3 + j], 2.0, AL.is_ge, AL.mult, LC, 1, [kth], K(rk, c), (q,))
-
-    def home(t, c, L0, L1, r1, xr, kxr, kdg):
-        p = tile()
-        if c in SG1[t]:
-            go, gk = bufpair("gb", c)
-            add("s", GT_, lambda: g.scalar.activation(T.gb[:, go:go + CW], T.dcod[:, :].indirect(A(L0, c)), AF.Copy), ["code"] + K(L0, c), [gk])
-            diag(T.gb, gk, T.edb, KED, p, 0, go)
-            lk = "ln2_%d" % t
-            sact(A(lk, c), F(lambda: ps(p)[:, 0:LC]), AF.Ln, LC, (), K(lk, c), (p,))
-            vts(A(L1, c), A(lk, c), ALPHA, MID + 0.25, AL.mult, AL.add, LC, 1, K(lk, c), K(L1, c))
-        else:
-            add("v", GT_, lambda: g.vector.tensor_copy(T.gh[:, c * CW:(c + 1) * CW], T.dgs[:, :].indirect(A(L0, c))), kdg + K(L0, c), [("gh", c)])
-            diag(T.gh, ("gh", c), T.edh, ["edh"], p, 0, c * CW)
-            vcopy(A(L1, c), F(lambda: ps(p)[:, 0:LC]), LC, 1, (), K(L1, c), (p,))
-        yield
-        q = tile()
-        dist(view(T.xs, KX, A(L1, c), K(L1, c), xr, kxr, c, 1), 1, c, q, 0)
-        rest(1, c, r1, q, T.pt, "ptk")
-        yield
-
-    def walk(t, c, L1, r1, e0, tb, xr, kxr):
-        X, kx, code, kc, th, kth = tb["X"], tb["kx"], tb["code"], tb["kc"], tb["th"], tb["kth"]
-        h1 = "h1_%d" % t
-        m1 = "m1_%d" % t
-        vcopy(A(h1, c), A(L1, c), LC, 0.5, K(L1, c), K(h1, c))
-        lst, hp, rp, ms = L1, h1, r1, [m1]
-        for k in (2, 3, 4):
-            Lk, hk, lk, rk, mk = ["%s%d_%d" % (n, k, t) for n in ("L", "h", "ln", "r", "m")]
-            go, gk = bufpair("gb", c)
-
-            def gat(go=go, lst=lst):
-                return g.scalar.activation(T.gb[:, go:go + CW], code[:, :].indirect(A(lst, c)), AF.Copy)
-            add("s", GT_, gat, [kc] + K(lst, c), [gk])
             p = tile()
-            diag(T.gb, gk, T.edb, KED, p, 0, go)
-            sact(A(lk, c), F(lambda p=p: ps(p)[:, 0:LC]), AF.Ln, LC, (), K(lk, c), (p,))
-            vts(A(Lk, c), A(lk, c), ALPHA, MID + 0.25, AL.mult, AL.add, LC, 1, K(lk, c), K(Lk, c))
-            vcopy(A(hk, c), A(Lk, c), LC, 0.5, K(Lk, c), K(hk, c))
-            q = tile()
-            mm([(LC, 2 * LC, T.idh[:, :], A(hp, c), True, False), (LC, 2 * LC, T.idn[:, :], A(hk, c), False, True)], 2 * LC,
-               K(hp, c) + K(hk, c) + ["idh", "idn"], q)
-            if k == 2:
-                mm([(2 * LC, 3 * LC, T.idh[:, :], A(e0, c), True, False), (2 * LC, 3 * LC, T.idn[:, :], A(h1, c), False, True)], 2 * LC,
-                   K(e0, c) + K(h1, c) + ["idh", "idn"], q)
-                vtt(A(m1, c), A(r1, c), F(lambda q=q: ps(q)[:, 2 * LC:3 * LC]), AL.mult, LC, 1, K(r1, c), K(m1, c), (q,))
-            dist(view(X, kx, A(Lk, c), K(Lk, c), xr, kxr, c, k), k, c, q, 0, (A(rp, c), K(rp, c)))
-            rest(k, c, rk, q, th, kth)
-            vtt(A(mk, c), A(rk, c), F(lambda q=q: ps(q)[:, LC:2 * LC]), AL.mult, LC, 1, K(rk, c), K(mk, c), (q,))
-            lst, hp, rp = Lk, hk, rk
-            ms.append(mk)
+            for q0 in range(0, 16, 4):
+                mm([(C(q, 128, 16), T[buf][:, o + q:o + HW:16], T.idf[:, q:128:16], True, True) for q in range(q0, q0 + 4)], 1024, keys + ["idf"], p)
+            zc, tt = "zc%d" % k, "tt%d" % k
+            sact(A(zc, h), PS(p, 0, H), AF.Copy, H, (), K(zc, h), (p,))
+            p2 = tile()
+            mm([(C(0, H), A(zc, h), T.idf[:, :], True, False)], 512, K(zc, h) + ["idf"], p2)
+            if (t, k) in TS:
+                sact(A("ut", h), A(zc, h), AF.Identity, H, K(zc, h), K("ut", h), bias=MAGIC)
+                sact(A(tt, h), A("ut", h), AF.Identity, H, K("ut", h), K(tt, h), bias=-MAGIC)
+            else:
+                vts(A(tt, h), A(zc, h), MAGIC, MAGIC, AL.add, AL.subtract, H, 1, K(zc, h), K(tt, h))
+            mm([(C(0, H), A(tt, h), T.idnb[:, :], False, True)], 128, K(tt, h) + ["idnb"], p2)
+            vcopy(A(Lk, h), PS(p2, 0, H), H, 1, (), K(Lk, h), (p2,))
+        if hk:
+            vcopy(A(hk, h), A(Lk, h), H, 0.5, K(Lk, h), K(hk, h))
+
+    def sums(ab, cols, step, first, last):
+        return [(C(q, cols, 16), T.ab[:, ab[0] + q:ab[0] + HW:16], T.blk[:, 0:128:step], first, last and (first or q == 15)) for q in range(16)]
+
+    def change(t, k, h, q):
+        a, b = "h%d_%d" % (k - 1, t), "h%d_%d" % (k, t)
+        return [(C(H, 2 * H), A(a, h), T.idh[:, :], True, False), (C(H, 2 * H), A(b, h), T.idn[:, :], False, True)], K(a, h) + K(b, h) + ["idh", "idn"]
+
+    def rest(t, k, h, ab, thd, kth, fk, here=True):
+        q = tile()
+        lst, rd = change(t, k, h, q) if here else ([], [])
+        lst = lst + [(C(0, H), T.onh[:, :], thd, True, False)]
+        rd = rd + ["onh", kth, ab[1][0]]
+        mm(lst, 128 * len(lst), rd, q)
+        lst, rd = sums(ab, H, 16, False, k == 1), ab[1] + ["blk"]
+        if k > 1:
+            fp = "f%d_%d" % (k - 1, t)
+            lst, rd = lst + [(C(0, H), T.idp[:, :], A(fp, h), False, True)], rd + K(fp, h) + ["idp"]
+        mm(lst, 1024 + 128, rd, q)
+        sact(A(fk, h), PS(q, 0, H), AF.Sign, H, (), K(fk, h), (q,), bias=0.5 - 2048.0 + (BIG if k > 1 else 0.0))
+        if here:
+            mk = "m%d_%d" % (k, t)
+            vtt(A(mk, h), A(fk, h), PS(q, H, 2 * H), AL.mult, H, 1, K(fk, h), K(mk, h), (q,))
+
+    def first(t, h, L0, L1, h1):
+        src = raw("v", T.dgs, KDG, L0, h) if (t, h) in G0V else raw("s", T.P0, KP0, L0, h)
+        follow(t, 1, src, h, L1, h1)
+
+    def walk(t, h, tb, xr, kxr, qt, ut):
+        P, kp, X, kx, thd, kth = tb["P"], tb["kp"], tb["X"], tb["kx"], tb["thd"], tb["kth"]
+        for k in (2, 3):
+            z, ab = view(t, k, P, kp, "L%d_%d" % (k, t), h, xr, kxr, True)
+            follow(t, k + 1, z, h, "L%d_%d" % (k + 1, t), "h%d_%d" % (k + 1, t))
+            rest(t, k, h, ab, thd, kth, "f%d_%d" % (k, t))
             yield
+        z, ab = view(t, 4, X, kx, "L4_%d" % t, h, xr, kxr, False)
+        rest(t, 4, h, ab, thd, kth, "f4_%d" % t)
         LF, hF = "LF_%d" % t, "hF_%d" % t
         p = tile()
-        hs = [e0, h1] + ["h%d_%d" % (k, t) for k in (2, 3, 4)]
-        seq = [(T.idh, hp)] + [(T.idq, x) for x in ms]
-        for k in RS:
-            seq += [(T.idq, hs[k - 1]), (T.idm, hs[k])]
-        mm([(0, LC, w[:, :], A(x, c), i == 0, i == len(seq) - 1) for i, (w, x) in enumerate(seq)], len(seq) * LC,
-           sum([K(x, c) for w, x in seq], []) + ["idq", "idh", "idm"], p)
-        vcopy(A(LF, c), F(lambda: ps(p)[:, 0:LC]), LC, 1, (), K(LF, c), (p,))
-        zo, zk, ao, ak = v4 = view(X, kx, A(LF, c), K(LF, c), xr, kxr, c, 5)
-        vcopy(A(hF, c), A(LF, c), LC, 0.5, K(LF, c), K(hF, c))
-        p2 = tile()
-        diag(T.zb, zk, T.edb, KED, p2, LC, zo)
-        bs, sq, ch, dS = "bs_%d" % t, "sq_%d" % t, "ch_%d" % t, "dS_%d" % t
-        sact(A(bs, c), F(lambda: ps(p2)[:, LC:2 * LC]), AF.Sign, LC, (), K(bs, c), (p2,), bias=-0.5)
-        p3 = tile()
-        dist(v4, 5, c, p3, 0)
-        sact(A(dS, c), F(lambda: ps(p3)[:, 0:LC]), AF.Copy, LC, (), K(dS, c), (p3,))
-        p4 = tile()
-        mm([(0, LC, tb["GT"], A(bs, c), True, True)], LC, K(bs, c) + [tb["kgt"]], p4)
-        sact(A(sq, c), F(lambda: ps(p4)[:, 0:LC]), AF.Square, LC, (), K(sq, c), (p4,))
-        p5 = tile()
-        mm([(0, LC, tb["aG"], A(sq, c), True, True), (LC, 2 * LC, T.blk[:, :], A(sq, c), True, True)], 2 * LC, K(sq, c) + [tb["kag"], "blk"], p5)
-        if CHS:
-            sact(A(ch, c), F(lambda: ps(p5)[:, 0:LC]), AF.Sign, LC, [tb["knt"]], K(ch, c), (p5,), bias=tb["nt"][:, 4:5])
-        else:
-            vts(A(ch, c), F(lambda: ps(p5)[:, 0:LC]), tb["nt"][:, 5:6], None, AL.is_gt, None, LC, 1, [tb["knt"]], K(ch, c), (p5,))
-        sact(A("any", c), F(lambda: ps(p5)[:, LC:2 * LC]), AF.Sign, LC, (), K("any", c) + [("asum", t, c)], (p5,), bias=-16.0,
-             acc=T.asum[:, 4 * t + c:4 * t + c + 1])
+        ms = ["m%d_%d" % (k, t) for k in (1, 2, 3, 4)]
+        ends = ["h0_%d" % t, "h4_%d" % t]
+        mm([(C(0, H), T.idq[:, :], A(x, h), x == ends[0], False) for x in ends] + [(C(0, H), A(x, h), T.idq[:, :], False, x == ms[-1]) for x in ms],
+           6 * 128, sum([K(x, h) for x in ms + ends], []) + ["idq"], p)
+        vcopy(A(LF, h), PS(p, 0, H), H, 1, (), K(LF, h), (p,))
+        if t == 1:
+            sact(A("yef", h), PS(p, 0, H), AF.Copy, H, (), K("yef", h), (p,))
+        vcopy(A(hF, h), A(LF, h), H, 0.5, K(LF, h), K(hF, h))
         yield
-
-    def keep(t, h, D0h):
-        c = -1 - h
-        dS, ch, hF, go = "dS_%d" % t, "ch_%d" % t, "hF_%d" % t, "go_%d" % t
+        (buf, o, keys, yo, yk), ab = view(t, 5, X, kx, LF, h, xr, kxr, False)
+        p2 = tile()
+        for u in R2:
+            s = u * SB // 2
+            if (t, 5, h, s) in VIA:
+                own_rows(p2, u, T.yb, yo, T.ed, yk[s:s + SB // 2] + KED, False)
+                a = H * h + 64 * u
+                mm([(C(64 * u, 64 * u + 64), T.idnb[:, :], tb["x"](a, a + 64), False, True)], 64, tb["kxl"] + ["idnb"], p2)
+            else:
+                own_rows(p2, u, T.zb, o, T.ed, keys[s:s + SB // 2] + KED)
+        sact(A("bs", h), PS(p2, 0, H), AF.Sign, H, (), K("bs", h), (p2,), bias=-0.5)
+        p4 = tile()
+        mm([(C(0, H), tb["GT"], A("bs", h), True, True)], H, K("bs", h) + [tb["kgt"]], p4)
+        sact(A("sq", h), PS(p4, 0, H), AF.Square, H, (), K("sq", h), (p4,))
+        p5 = tile()
+        mm([(C(0, H), tb["aG"], T.ngb[:, :], True, False), (C(0, H), tb["aG"], A("sq", h), False, True), (C(H, H + 8), A("sq", h), T.blk[:, 0:128:16], True, True)],
+           2 * H + 64, K("sq", h) + [tb["kag"], "blk", "ngb"], p5)
+        sact(A("ch", h), PS(p5, 0, H), AF.Sign, H, (), K("ch", h), (p5,))
+        sact(A("any", h, 0, 8), PS(p5, H, H + 8), AF.Sign, 8, (), K("any", h) + [("asum", h)], (p5,), bias=-16.0, acc=T.asum[:, h:h + 1])
+        p3 = tile()
+        mm(sums(ab, H, 16, True, True), 1024, ab[1] + ["blk"], p3)
+        sact(A("dT", h), PS(p3, 0, H), AF.Copy, H, (), K("dT", h), (p3,))
+        mm([(C(H * h, H * h + H), T.id37[:, :], A(hF, h), True, False), (C(H * h, H * h + H), A("dT", h), T.idf[:, :], False, True)],
+           640, K(hF, h) + K("dT", h) + ["id37", "idf"], qt)
         p = tile()
-        mm([(0, 256, A(dS, c), T.dupf[:, :], True, False), (0, 256, T.onb[:, 0:128], T.prow[:, :], False, False)],
-           1024 + 256, K(dS, c) + ["dupf", "onb", "prow"], p)
-        mm([(0, 256, A(ch, c), T.dupb[:, :], False, True)], 256, K(ch, c) + ["dupb"], p)
+        mm([(C(0, 256), T.onb[:, 0:128], T.prow[:, :], True, False)] + sums(ab, 256, 8, False, False), 256 + 1024, ab[1] + ["blk", "onb", "prow"], p)
+        mm([(C(0, 256), A("ch", h), T.dupb[:, :], False, True)], 256, K("ch", h) + ["dupb"], p)
         add("v", vt(256, 1), lambda: g.vector.tensor_tensor_scan(T.pm[:, 256 * h:256 * h + 256], T.rst[:, :], ps(p)[:, 0:256], 0.0, AL.mult, AL.min),
             ["rst"], [("pm", h)], (p,))
         for x in range(8):
-            vtt(T.eq[:, 128 * h + 16 * x:128 * h + 16 * x + 16], T.pm[:, 256 * h + 32 * x + 16:256 * h + 32 * x + 32],
-                F(lambda x=x: ps(p)[:, 32 * x + 16:32 * x + 32]), AL.is_equal, 16, 1, [("pm", h)], [("eq", h, x)], (p,))
-        q = tile()
-        mm([(0, 128, T.id37[:, :], A(hF, c), True, False), (0, 128, T.idf[:, :], A(dS, c), False, True)],
-           640, K(hF, c) + K(dS, c) + ["id37", "idf"], q)
-        u = tile()
-        mm([(0, 128, T.idb[:, :], A(ch, c), True, False)], 128, K(ch, c) + ["idb"], u)
-        mm([(0, 128, T.eq[:, 128 * h:128 * h + 128], T.idnb[:, :], False, True)], 128, [("eq", h, x) for x in range(8)] + ["idnb"], u)
-        return q, u
+            vtt(T.eq[:, H * h + 16 * x:H * h + 16 * x + 16], T.pm[:, 256 * h + 32 * x + 16:256 * h + 32 * x + 32],
+                PS(p, 32 * x + 16, 32 * x + 32), AL.is_equal, 16, 1, [("pm", h)], [("eq", h, x)], (p,))
+        mm([(C(H * h, H * h + H), T.idb[:, :], A("ch", h), True, False), (C(H * h, H * h + H), T.eq[:, H * h:H * h + H], T.idnb[:, :], False, True)],
+           256, K("ch", h) + ["idb", "idnb"] + [("eq", h, x) for x in range(8)], ut)
+        yield
 
-    def finish(t, out, D0f, D0h, wt):
+    def finish(t, out, qt, ut):
+        D0 = "h0_%d" % t
         p = tile()
-        mm([(0, 1, T.on16[:, :], T.asum[:, 4 * t + c:4 * t + c + 1], c == 0, c == NCH - 1) for c in range(NCH)], 4 * 4 * 64,
-           [("asum", t, c) for c in range(NCH)] + ["on16"], p)
-        vcopy(T.acol[:, t:t + 1], F(lambda: ps(p)[:, 0:1]), 1, 1, (), [("acol", t)], (p,))
-        for c in (-1, -2):
-            q, u = wt[-1 - c]
-            vts(A("qi", c), F(lambda q=q: ps(q)[:, 0:128]), T.acol[:, t:t + 1], None, AL.add, None, 128, 1, [("acol", t)], K("qi", c), (q,))
-            vts(A("ni", c), A("qi", c), W - 1, None, AL.bitwise_and, None, 128, 1, K("qi", c), K("ni", c))
-            vtt(A("wd", c), A("ni", c), A(D0f, c), AL.subtract, 128, 2, K("ni", c) + K(D0f, c), K("wd", c))
-            vtt(A("mh", c), A("wd", c), F(lambda u=u: ps(u)[:, 0:128]), AL.mult, 128, 1, K("wd", c), K("mh", c), (u,))
-            v = tile()
-            mm([(0, 128, T.idh[:, :], A(D0h, c), True, False), (0, 128, T.idh[:, :], A("mh", c), False, True)], 256, K(D0h, c) + K("mh", c) + ["idh"], v)
-            vcopy(A(out, c), F(lambda v=v: ps(v)[:, 0:128]), 128, 1, (), K(out, c), (v,))
+        mm([(C(0, 1), T.onf[:, 0:128], T.asum[:, h:h + 1], h == 0, h == 1) for h in R2], 512, [("asum", h) for h in R2] + ["onf"], p)
+        sact(T.acol[:, 0:1], PS(p, 0, 1), AF.Copy, 1, (), ["acol"], (p,))
+        vts(A("qi"), PS(qt, 0, L), T.acol[:, 0:1], None, AL.add, None, L, 1, ["acol"], K("qi"), (qt,))
+        vts(A("ni"), A("qi"), W - 1, None, AL.bitwise_and, None, L, 1, K("qi"), K("ni"))
+        vtt(A("wd"), A("ni"), A(D0), AL.subtract, L, 2, K("ni") + K(D0), K("wd"))
+        vtt(A("mh"), A("wd"), PS(ut, 0, L), AL.mult, L, 1, K("wd"), K("mh"), (ut,))
+        vtt(A(out), A("mh"), A(D0), AL.add, L, 1 + t, K("mh") + K(D0), K(out))
 
     def run(gens):
         gens = list(enumerate(gens))
@@ -437,102 +439,116 @@ def rank_program(g, core, T, topo):
             gens = nxt
         cur[0] = 0
 
-    for h in (0, 1):
-        a, b = h * W // 2, (h + 1) * W // 2
-        vcopy(T.dgf[:, a:b], T.dgs[:, a:b], W // 2, 1, [KDG[h]], [("dgf", h)])
-        sact(T.dcod[:, a:b], T.dgf[:, a:b], AF.Exp, W // 2, [("dgf", h)], ["code"], bias=-MID / ALPHA, scale=1.0 / ALPHA)
+    def home0(h):
+        first(0, h, "L0a", "L1a", None)
+        k = send(s1, [A("L1a", h), A("L0a", h)], [A("L1i", h), A("L0i", h)], "re%d" % h, K("L1a", h) + K("L0a", h))
+        recv("re%d" % h, k, HOP, K("L1i", h) + K("L0i", h))
+        sent.append(k[0])
+        yield
+        z, ab = view(0, 1, T.xq, KXQ, "L1a", h, T.xr0, xr0k, False)
+        rest(0, 1, h, ab, T.thd[:, :], "thd", "f1a", False)
+        yield
 
-    run(home(0, c, "L0a", "LEa", "r1a", T.xr0, xr0k, KDG) for c in range(NCH))
-    for c in range(NCH):
-        last = send([s1], [A("LEa", c)], [A("LEi", c)], ["re%d" % c], 1.0, K("LEa", c))
-        recv("re%d" % c, 8, HOP, last, K("LEi", c))
-    for c in range(NCH):
-        last = send([s1], [A("r1a", c)], [A("r1i", c)], ["rr%d" % c], 1.0, K("r1a", c))
-        recv("rr%d" % c, 8, HOP, last, K("r1i", c))
+    sent = []
+    run(home0(h) for h in R2)
+    k = send(h2, [T.xq[:, :]], [T.xq2[:, :]], "rxq", KXQ, sent)
+    recv("rxq", k, LAT["xq"], ["xq2"])
+    for h in R2:
+        k = send(s1, [A("f1a", h)], [A("f1_0", h)], "rr%d" % h, K("f1a", h), (k[0],))
+        recv("rr%d" % h, k, HOP, K("f1_0", h))
 
-    for k in range(3):
-        vts(T.gq[:, 128 * k:128 * k + 128], T.iq[:, :], T.tif[:, k:k + 1], T.sgf[:, k:k + 1], AL.is_equal, AL.mult, 128, 1, ["iq", "tif", "sgf"], [("gq", k)])
+    vcopy(T.tif[:, 0:3], T.tii[:, 0:3], 3, 1, [("ld2", "ld")], ["tif"])
+    vcopy(T.sgf[:, 0:3], T.sgi[:, 0:3], 3, 1, [("ld3", "ld")], ["sgf"])
+    for j in range(3):
+        vts(T.gq[:, 128 * j:128 * j + 128], T.iq[:, :], T.tif[:, j:j + 1], T.sgf[:, j:j + 1], AL.is_equal, AL.mult, 128, 1, ["iq", "tif", "sgf"], [("gq", j)])
     vtt(T.gq[:, 384:512], T.gq[:, 0:128], T.gq[:, 128:256], AL.add, 128, 2, [("gq", 0), ("gq", 1)], [("gq", 3)])
     vtt(T.gq[:, 0:128], T.gq[:, 384:512], T.gq[:, 256:384], AL.add, 128, 2, [("gq", 3), ("gq", 2)], [("gq", 0)])
     vtt(T.gj[:, :], T.gq[:, 0:128], T.blk[:, :], AL.mult, 128, 2, [("gq", 0), "blk"], ["gj"])
     sact(T.pk[:, 128:256], T.gj[:, :], AF.Abs, 128, ["gj"], ["pkA"])
     p0 = tile()
-    mm([(0, 128, T.gj[:, :], T.idb[:, :], True, True), (128, 129, T.pk[:, 128:256], T.onb[:, 0:1], True, True)], 192, ["gj", "idb", "pkA", "onb"], p0)
-    sact(T.pk[:, 0:128], F(lambda: ps(p0)[:, 0:128]), AF.Copy, 128, (), ["pkG"], (p0,))
-    vts(T.pt[:, 4:5], F(lambda: ps(p0)[:, 128:129]), -1.0, None, AL.mult, None, 1, 1, (), ["ptn"], (p0,))
-    vcopy(T.pt[:, 5:6], F(lambda: ps(p0)[:, 128:129]), 1, 1, (), ["ptn"], (p0,))
+    mm([(C(0, 128), T.gj[:, :], T.idb[:, :], True, True)], 128, ["gj", "idb"], p0)
+    sact(T.pk[:, 0:128], PS(p0, 0, 128), AF.Copy, 128, (), ["pkG"], (p0,))
     xrnk = xrep("xrn", A("xi"), K("xi"), XRN)
-    vcopy(A("d0i"), A("L0i"), L, 0.5, K("L0i"), K("d0i"))
-    vcopy(A("d0f"), A("L0i"), L, 1, K("L0i"), K("d0f"))
 
-    h2 = dest(rank - 2)
-    k = send([h2, h2], [T.xs[:, :], T.dcod[:, :]], [T.xs2[:, :], T.code2[:, :]], ["rtab", "rtab"], 1.0, [KX, "code"], (last,), "ltab")
-    add("n", 0.0, None, ["code"], (), (), "ltab", 8, 25.0, [k])
-    recv("rtab", 8, 25.0, k, ["xs2", "code2"])
-    k = send([h2], [T.pk[:, :]], [T.pk2[:, :]], ["rpk"], 1.0, ["pkA", "pkG"], (k,))
-    recv("rpk", 8, 25.0, k, ["pk2"])
-    k = send([h2], [T.pt[:, 0:6]], [T.pt2[:, 0:6]], ["rpt"], 1.0, PTK + ["ptn"], (k,))
-    recv("rpt", 8, 25.0, k, ["pt2"])
+    k = send(h2, [T.P0[:, :]], [T.P2[:, :]], "rtab", KP0, (k[0],), "ltab")
+    add("n", 0.0, None, KP0, (), (), "ltab", k[1], LAT["tab"], [k[0]])
+    recv("rtab", k, LAT["tab"], ["P2"])
+    k = send(h2, [T.pk[:, 0:128], T.pk[:, 128:256], T.thd[:, :]], [T.pk2[:, 0:128], T.pk2[:, 128:256], T.thd2[:, :]], "rpk", ["pkA", "pkG", "thd"], (k[0],))
+    recv("rpk", k, LAT["tab"], ["pk2"])
 
-    vcopy(T.idf[:, :], T.idb[:, :], 128, 1, ["idb"], ["idf"])
-    vts(T.dupb[:, :], T.dupf[:, :], -BIGP, None, AL.mult, None, 256, 1, ["dupf"], ["dupb"])
+    vts(T.dupb[:, :], T.dupf[:, :], -2 * BIG, None, AL.mult, None, 256, 1, ["dupf"], ["dupb"])
     vts(T.prow[:, :], T.iop[:, :], 1.0 / 4096, 1.0 / 8192, AL.mult, AL.add, 256, 1, ["iop"], ["prow"])
-    add("v", vt(256, 1), lambda: g.vector.memset(T.rst[:, :], 1.0), (), ["rst"])
-    add("v", vt(8, 1), lambda: g.vector.memset(T.rst[:, 0:256:32], 0.0), (), ["rst"])
-    vts(T.idnb[:, :], T.idb[:, :], -1.0, None, AL.mult, None, 128, 0.5, ["idb"], ["idnb"])
-    add("v", vt(128, 1), lambda: g.vector.memset(T.on16[:, :], 1.0 / 16), (), ["on16"])
+    vset(T.rst[:, :], 1.0, 256, 1, ["rst"])
+    vset(T.rst[:, 0:256:32], 0.0, 8, 1, ["rst"])
 
-    tb = {"X": T.xs, "kx": KX, "code": T.dcod, "kc": "code", "th": T.pt, "kth": "ptk", "nt": T.pt, "knt": "ptn",
+    def away0(h):
+        vcopy(A("h0_0", h), A("L0i", h), H, 0.5, K("L0i", h), K("h0_0", h))
+        vcopy(A("h1_0", h), A("L1i", h), H, 0.5, K("L1i", h), K("h1_0", h))
+        follow(0, 2, raw("v", T.dgs, KDG, "L1i", h) if h in G1V else raw("s", T.P0, KP0, "L1i", h), h, "L2_0", "h2_0")
+        q = tile()
+        lst, rd = change(0, 1, h, q)
+        mm(lst, 256, rd + K("f1_0", h), q)
+        vtt(A("m1_0", h), A("f1_0", h), PS(q, H, 2 * H), AL.mult, H, 1, K("f1_0", h), K("m1_0", h), (q,))
+        yield
+        yield from walk(0, h, tb, T.xrn, xrnk, qt, ut)
+
+    tb = {"P": T.P0, "kp": KP0, "X": T.xq, "kx": KXQ, "thd": T.thd[:, :], "kth": "thd", "x": lambda a, b: A("xi")[:, a:b], "kxl": K("xi"),
           "GT": T.pk[:, 0:128], "kgt": "pkG", "aG": T.pk[:, 128:256], "kag": "pkA"}
-    run(walk(0, c, "LEi", "r1i", "d0i", tb, T.xrn, xrnk) for c in range(NCH))
-    wt = [keep(0, h, "d0i") for h in (0, 1)]
-    finish(0, "ndo", "d0f", "d0i", wt)
-    d1, d2 = dest(rank - 1), dest(rank - 3)
-    k = send([d1], [A("ndo")], [A("ndi")], ["rnh"], 1.0, K("ndo"))
-    recv("rnh", 8, HOP, k, K("ndi"))
-    k = send([d2], [A("ndo")], [A("nd2")], ["rn2"], 1.0, K("ndo"), (k,))
-    recv("rn2", 8, HOP, k, K("nd2"))
+    qt, ut = tile(), tile()
+    run(away0(h) for h in R2)
+    finish(0, "ndo", qt, ut)
+    k = send(dest(rank - 1), [A("ndo")], [A("ndi")], "rnh", K("ndo"))
+    recv("rnh", k, HOP, K("ndi"))
+    k = send(dest(rank - 3), [A("ndo")], [A("nd2")], "rn2", K("ndo"), (k[0],))
+    recv("rn2", k, HOP, K("nd2"))
 
-    vcopy(A("L0b"), T.dgs[:, 1:W:S], 256, 1, KDG, K("L0b"))
-    vcopy(A("e0b"), A("L0b"), 256, 0.5, K("L0b"), K("e0b"))
-    xr1k = xrep("xr1", T.xs[:, 1:W:S], [KX], XR1)
-    if SG1[1]:
-        vcopy(A("ndg"), A("ndi"), 256, 1, K("ndi"), K("ndg"))
-        sact(T.dcod[:, 0:W:S], A("ndg"), AF.Exp, 256, K("ndg"), ["code"], bias=-MID / ALPHA, scale=1.0 / ALPHA)
-    vcopy(T.dgs[:, 0:W:S], A("ndi"), 256, 1, K("ndi"), KDG)
-    run(home(1, c, "L0b", "LEb", "r1b", T.xr1, xr1k, KDG) for c in range(NCH))
-    vcopy(A("ndf"), A("nd2"), 256, 1, K("nd2"), K("ndf"))
-    sact(T.code2[:, 0:W:S], A("ndf"), AF.Exp, 256, K("ndf"), ["code2"], bias=-MID / ALPHA, scale=1.0 / ALPHA)
-    vcopy(A("yd0"), A("ndi"), 256, 1, K("ndi"), K("yd0"))
+    vcopy(A("L0b"), T.dgs[:, 1:W:S], L, 1, KDG, K("L0b"))
+    vcopy(A("h0_1"), A("L0b"), L, 0.5, K("L0b"), K("h0_1"))
+    xr1k = xrep("xr1", T.xq[:, 1:W:S], KXQ + K("L2_0"), XR1)
+    for j in range(4):
+        c = C(512 * j, 512 * j + 512)
+        p = tile()
+        mm([(C(0, 512), T.idnb[:, :], T.xq2[:, c], True, False), (C(0, 512), T.idb[:, :], T.xq[:, c], False, True)],
+           2 * 512, ["xq2", "idb", "idnb"] + KXQ + K("wd"), p)
+        vtt(T.P1[:, c], T.P2[:, c], PS(p, 0, 512), AL.add, 512, 1, ["P2"] + K("ndo"), [("P1", j)], (p,))
+    KP1 = [("P1", j) for j in range(4)]
+    vcopy(T.dgs[:, 0:W:S], A("ndi"), L, 1, K("ndi"), KDG)
+    p = tile()
+    mm([(C(0, L), T.idb[:, :], T.xq[:, 0:W:S], True, False), (C(0, L), T.idh[:, :], A("ndi"), False, True), (C(L, 2 * L), T.idh[:, :], A("ndi"), True, True)],
+       3 * L, K("ndi") + KXQ + ["idb", "idh"], p)
+    sact(T.P0[:, 0:W:S], PS(p, 0, L), AF.Copy, L, (), KP0, (p,))
+    sact(A("yd0"), PS(p, L, 2 * L), AF.Copy, L, (), K("yd0"), (p,))
     add("y", 0.1, lambda: g.sync.dma_start(T.yd[:, 0:L], A("yd0")), K("yd0"), (), (), "ld5", 16, 2.0)
-    vcopy(A("d0f"), A("L0b"), L, 1, K("L0b"), K("d0f"))
-    tb = {"X": T.xs2, "kx": "xs2", "code": T.code2, "kc": "code2", "th": T.pt2, "kth": "pt2", "nt": T.pt2, "knt": "pt2",
+    p = tile()
+    mm([(C(0, L), T.idb[:, :], T.xq[:, 0:W:S], True, False), (C(0, L), T.idh[:, :], A("nd2"), False, True),
+        (C(L, 2 * L), T.idb[:, :], T.xq2[:, 0:W:S], True, False), (C(L, 2 * L), T.idh[:, :], A("nd2"), False, True)],
+       4 * L, K("nd2") + KXQ + ["xq2", "idb", "idh"], p)
+    sact(T.P1[:, 0:W:S], PS(p, 0, L), AF.Copy, L, (), KP1, (p,))
+    sact(T.P2[:, 0:W:S], PS(p, L, 2 * L), AF.Copy, L, (), ["P2"], (p,))
+
+    def home1(h):
+        first(1, h, "L0b", "L1b", "h1_1")
+        yield
+        z, ab = view(1, 1, T.P1, KP1, "L1b", h, T.xr1, xr1k, True)
+        follow(1, 2, z, h, "L2_1", "h2_1")
+        rest(1, 1, h, ab, T.thd[:, :], "thd", "f1_1")
+        yield
+        yield from walk(1, h, tb, T.xr1, xr1k, qt, ut)
+
+    tb = {"P": T.P2, "kp": ["P2"], "X": T.xq2, "kx": ["xq2"], "thd": T.thd2[:, :], "kth": "pk2", "x": lambda a, b: T.xq[:, S * a + 1:S * b:S], "kxl": KXQ,
           "GT": T.pk2[:, 0:128], "kgt": "pk2", "aG": T.pk2[:, 128:256], "kag": "pk2"}
-    run(walk(1, c, "LEb", "r1b", "e0b", tb, T.xr1, xr1k) for c in range(NCH))
-    vcopy(A("yef"), A("LF_1"), L, 1, K("LF_1"), K("yef"))
+    qt, ut = tile(), tile()
+    run(home1(h) for h in R2)
     add("y", 0.1, lambda: g.sync.dma_start(T.ye[:, :], A("yef")), K("yef"), (), (), "ld6", 16, 2.0)
-    wt = [keep(1, h, "e0b") for h in (0, 1)]
-    finish(1, "yd1", "d0f", "e0b", wt)
+    finish(1, "yd1", qt, ut)
     add("y", 0.1, lambda: g.sync.dma_start(T.yd[:, L:2 * L], A("yd1")), K("yd1"), (), (), "ld7", 16, 2.0)
 
     order = schedule(ops, tiles, bankof)
     emit(g, T, ENG, CSEM, ops, order, cnt["l"])
 
 
-def F(fn):
-    return (fn,)
-
-
-PW = 0.01
-SKEW = 1.4
-BONUS = {}
-
-
-def kind(o):
-    n = o["n"]
-    return "%s%d %s" % (o["e"], o["c"], n[0] if isinstance(n, tuple) else n)
-
-
+PW = 0.02
+SKEW = 0.0
 SEML = 0.1
 
 
@@ -559,7 +575,7 @@ def schedule(ops, tiles, bankof):
     free = {}
     order = []
     rt = [0.0] * n
-    pri = [PW * (bl[k] - SKEW * ops[k]["c"] + BONUS.get(kind(ops[k]), 0.0)) for k in range(n)]
+    pri = [PW * (bl[k] - SKEW * ops[k]["c"]) + ops[k].get("up", 0.0) for k in range(n)]
     free["n"] = -1.0
     while ready:
         best = None
@@ -592,7 +608,6 @@ def schedule(ops, tiles, bankof):
         if o["e"] != "n":
             free[o["e"]] = st + o["d"]
         fin[k] = st + o["d"] + o["lat"]
-        o["st"] = st
         order.append(k)
         for t in o["ps"]:
             tleft[t] -= 1
@@ -623,7 +638,6 @@ def emit(g, T, ENG, CSEM, ops, order, nlocal):
             continue
         q = ENG[e]
         need = {}
-        imp = dict(known[e])
         for d in o["deps"]:
             if done[d] is None or d in o["soft"]:
                 continue

@@ -7,6 +7,7 @@ SB = 4
 SW = 16 * H // SB
 HW = 16 * H
 SH = 65536.0
+MID = 1024.0
 MAGIC = 1.5 * 2.0 ** 39
 BIG = 4096.0
 AL = AluOpType
@@ -14,9 +15,9 @@ AF = ActivationFunctionType
 
 R2 = (0, 1)
 U_ = ["L0a", "L0b", "L0i", "L1a", "L1i", "L1b"] + ["%s_%d" % (n, t) for n in ("L2", "L3", "L4", "LF") for t in R2]
-H_ = ["wd", "mh", "ndo", "ndi", "nd2"] + ["%s_%d" % (n, t) for n in ("h0", "h1", "h2", "h3", "h4", "hF", "m1", "m2", "m3", "m4") for t in R2]
-F_ = ["yd0", "yd1", "yef", "dT", "ut"] + ["zc%d" % k for k in (1, 2, 3, 4)]
-B_ = ["x0", "xi", "f1a", "f1_0", "f1_1", "any", "bs", "sq", "ch"] + ["%s_%d" % (n, t) for n in ("f2", "f3", "f4") for t in R2] + ["tt%d" % k for k in (1, 2, 3, 4)]
+H_ = ["wd", "mh", "ndo", "ndi", "nd2", "hA"] + ["%s_%d" % (n, t) for n in ("h0", "h1", "h2", "h3", "h4", "m1", "m2", "m3", "m4") for t in R2]
+F_ = ["yd0", "yd1", "yef", "ut"]
+B_ = ["x0", "xi", "xz0", "xzn", "xz1", "f1a", "f1_0", "f1_1", "any", "bt", "bs", "sq", "ch", "tt"] + ["%s_%d" % (n, t) for n in ("f2", "f3", "f4") for t in R2]
 I_ = ["qi", "ni"]
 POOLS = {"PU": (U_, "uint16"), "PH": (H_, "float16"), "PF": (F_, "float32"), "PB": (B_, "bfloat16"), "PI": (I_, "int32")}
 SLOT = {}
@@ -31,16 +32,16 @@ for _n, _w, _dt in (
         ("P0", W, "float32"), ("P1", W, "float32"), ("P2", W, "float32"),
         ("xr0", 16 * L, "bfloat16"), ("xr1", 16 * L, "bfloat16"), ("xrn", 16 * L, "bfloat16"),
         ("zf", 32 * L, "float32"), ("gf", 16 * L, "float32"), ("zb", 32 * L, "bfloat16"), ("ab", 32 * L, "bfloat16"),
-        ("gh", 16 * L, "float16"), ("yb", 16 * L, "bfloat16"), ("ed", 2048, "bfloat16"), ("edh", 2048, "float16"),
-        ("onb", 256, "bfloat16"), ("onf", 256, "float32"), ("onh", 128, "float16"), ("ngb", 128, "bfloat16"),
-        ("idb", 128, "bfloat16"), ("idh", 128, "float16"), ("idn", 128, "float16"), ("idq", 128, "float16"), ("id37", 128, "float16"),
-        ("idp", 128, "bfloat16"), ("idnb", 128, "bfloat16"), ("idf", 128, "float32"), ("ids", 128, "bfloat16"),
-        ("blk0", 128, "bfloat16"), ("blk", 128, "bfloat16"),
-        ("dupf", 256, "float32"), ("dupb", 256, "bfloat16"), ("iop", 256, "float32"), ("prow", 256, "bfloat16"), ("rst", 256, "float32"),
+        ("gh", 16 * L, "float16"), ("ed", 2048, "bfloat16"), ("edh", 2048, "float16"),
+        ("onb", 128, "bfloat16"), ("onf", 128, "float32"), ("onh", 128, "float16"), ("ngb", 128, "bfloat16"), ("cb", 512, "bfloat16"),
+        ("idb", 128, "bfloat16"), ("idh", 128, "float16"), ("idn", 128, "float16"), ("idq", 128, "float16"), ("id18", 128, "float16"),
+        ("idp", 128, "bfloat16"), ("idnb", 128, "bfloat16"), ("sel", 256, "float32"), ("ids", 128, "bfloat16"),
+        ("blk0", 128, "bfloat16"), ("blk", 128, "bfloat16"), ("blkn", 256, "bfloat16"), ("blk2", 256, "bfloat16"),
+        ("idm", 128, "bfloat16"), ("prow", 256, "bfloat16"), ("rst", 128, "float32"),
         ("pm", 512, "float32"), ("eq", 256, "bfloat16"), ("iq", 128, "float32"),
         ("thi", 4, "int32"), ("tii", 4, "int32"), ("sgi", 4, "int32"), ("tif", 4, "float32"), ("sgf", 4, "float32"), ("thc", 4, "float32"),
         ("gq", 512, "float32"), ("gj", 128, "bfloat16"), ("pk", 256, "bfloat16"), ("pk2", 256, "bfloat16"),
-        ("thd", 128, "float16"), ("thd2", 128, "float16"), ("asum", 8, "float32"), ("acol", 8, "float32")):
+        ("thd", 256, "float16"), ("thd2", 256, "float16"), ("asum", 8, "float32"), ("acol", 8, "float32")):
     SCRATCH[_n] = ("sbuf", [128, _w], _dt)
 for _k in range(8):
     SCRATCH["bank%d" % _k] = ("psum", [128, 512], "float32")
@@ -48,16 +49,20 @@ SEMAPHORES = ["cv", "cs", "cp", "cg", "lsem", "ltab", "rx", "rxq", "rtab", "rpk"
 
 G0V = ((0, 0), (1, 0))
 G1V = (1,)
-VIA = tuple((t, 4, h, 0) for t in R2 for h in R2)
+SWAP = tuple((t, k, h) for t in R2 for k in range(1, 6) for h in R2)
+XQ2 = ("ch", 1)
+BT = ()
+ANEW = ()
+LEAD = 0.0
 TS = ()
-XR0, XRN, XR1 = "s", "g", "g"
-ABW = {1: 2, 2: 2, 3: 2, 4: 1, 5: 1}
+XR0, XRN, XR1 = "ssv", "g", "g"
+ABW = {1: 2, 2: 2, 3: 2, 4: 2, 5: 2}
 
 CY = 0.83e-3 * 1.1
 PC = 0.42e-3 * 1.1
 GC = 1.5
 HOP = 2.5
-LAT = {"x": 4.0, "d0": 6.0, "d1": 8.0, "small": 8.5, "first": 2.0, "xq": 9.0, "tab": 18.0}
+LAT = {"x": 4.2, "d0": 6.2, "d1": 8.2, "small": 2.5, "first": 2.0, "flags": 4.0, "xq": 10.0, "tab": 18.0}
 
 
 def rank_program(g, core, T, topo):
@@ -97,10 +102,13 @@ def rank_program(g, core, T, topo):
         for x in r:
             own.setdefault(("r", x), []).append(k)
         soft = set(d for d in deps if ops[d]["e"] == eng and d not in hard and ps)
-        ops.append({"e": eng, "d": dur, "f": fn, "deps": deps, "ps": list(ps), "sem": sem, "inc": inc, "lat": lat, "c": cur[0], "soft": soft, "n": keys_w[0] if keys_w else "-"})
+        ops.append({"e": eng, "d": dur, "f": fn, "deps": deps, "ps": list(ps), "sem": sem, "inc": inc, "lat": lat, "c": cur[0], "soft": soft, "up": 0.0})
         for t in ps:
             tiles[t].append(k)
         return k
+
+    def early(k):
+        ops[k]["up"] = 1000.0 - 20.0 * k
 
     def tile():
         tiles.append([])
@@ -137,6 +145,9 @@ def rank_program(g, core, T, topo):
             return g.vector.tensor_scalar(out, R(in0), s1, s2, o0, o1)
         return add("v", vt(n, f), em, r, w, p)
 
+    def vmul(out, in0, val, n, r, w, f=0.5):
+        return vts(out, in0, val, None, AL.mult, None, n, f, r, w)
+
     def vtt(out, in0, in1, op, n, f, r, w, p=()):
         return add("v", vt(n, f), lambda: g.vector.tensor_tensor(out, R(in0), R(in1), op), r, w, p)
 
@@ -158,42 +169,76 @@ def rank_program(g, core, T, topo):
             return out
         return add("p", 0.03 + cyc * PC, em, r, (), (p,))
 
+    def group(lst):
+        return [x + (i == 0, i == len(lst) - 1) for i, x in enumerate(lst)]
+
+    def more(lst, last=False):
+        return [x + (False, last and i == len(lst) - 1) for i, x in enumerate(lst)]
+
     C = slice
 
-    def load(buf, src, sem, lat):
-        k = add("y", 0.1, lambda: g.sync.dma_start(buf, src), (), [(sem, "ld")], (), sem, 16, lat)
-        ops[k]["up"] = 100.0 - k
+    def load(eng, buf, src, sem, lat):
+        early(add(eng, 0.1, lambda: ENG[eng].dma_start(buf, src), (), [(sem, "ld")], (), sem, 16, lat))
 
-    load(T.xs[:, :], T.xv[:, :], "ld0", LAT["x"])
-    load(T.dgs[:, 0:W // 2], T.dg[:, 0:W // 2], "ld1", LAT["d0"])
-    load(T.dgs[:, W // 2:W], T.dg[:, W // 2:W], "ld8", LAT["d1"])
-    load(T.thi[:, 0:1], T.th[:, :], "ld4", LAT["small"])
-    load(T.tii[:, 0:3], T.ti[:, :], "ld2", LAT["small"])
-    load(T.sgi[:, 0:3], T.sg[:, :], "ld3", LAT["small"])
+    load("y", T.thi[:, 0:1], T.th[:, :], "ld4", LAT["small"])
+    load("y", T.xs[:, :], T.xv[:, :], "ld0", LAT["x"])
+    load("y", T.dgs[:, 0:W // 2], T.dg[:, 0:W // 2], "ld1", LAT["d0"])
+    load("y", T.dgs[:, W // 2:W], T.dg[:, W // 2:W], "ld8", LAT["d1"])
+    load("s", T.tii[:, 0:3], T.ti[:, :], "ld2", LAT["small"])
+    load("s", T.sgi[:, 0:3], T.sg[:, :], "ld3", LAT["x"])
     KX, KDG = ("ld0", "ld"), [("ld1", "ld"), ("ld8", "ld")]
 
     def gsel(out, in_, pat, op, base, cm, n, r, w):
         return add("g", 0.17 + 2 * n * CY, lambda: g.affine_select(out, in_, pat, op, 0.0, base, cm), r, w)
 
-    vset(T.onb[:, :], 1.0, 256, 0.5, ["onb"])
+    def giota(out, pat, n, w):
+        return add("g", 0.13 + 2 * n * CY, lambda: g.iota(out, pat, 0, 0, allow_small_or_imprecise_dtypes=True), (), w)
+
+    early(vset(T.onb[:, :], 1.0, 128, 0.5, ["onb"]))
+    early(giota(T.iq[:, :], [[0, 8], [1, 16]], 128, ["iq"]))
+    early(gsel(T.idb[:, :], T.onb[:, :], [[-1, 128]], AL.is_equal, 0, 1, 128, ["onb"], ["idb"]))
+    early(gsel(T.blk0[:, :], T.onb[:, :], [[-16, 8], [0, 16]], AL.is_ge, 0, 1, 128, ["onb"], ["blk0"]))
+    early(gsel(T.blk[:, :], T.blk0[:, :], [[16, 8], [0, 16]], AL.is_ge, 15, -1, 128, ["blk0"], ["blk"]))
     vset(T.ed[:, :], 1.0, 2048, 0.5, ["ed"])
-    vset(T.onf[:, :], 1.0, 256, 1, ["onf"])
+    vset(T.onf[:, :], 1.0, 128, 1, ["onf"])
     vset(T.ngb[:, :], -1.0, 128, 0.5, ["ngb"])
-    gsel(T.idb[:, :], T.onb[:, 0:128], [[-1, 128]], AL.is_equal, 0, 1, 128, ["onb"], ["idb"])
-    gsel(T.blk0[:, :], T.onb[:, 0:128], [[-16, 8], [0, 16]], AL.is_ge, 0, 1, 128, ["onb"], ["blk0"])
-    gsel(T.blk[:, :], T.blk0[:, :], [[16, 8], [0, 16]], AL.is_ge, 15, -1, 128, ["blk0"], ["blk"])
-    add("g", 0.4, lambda: g.iota(T.iq[:, :], [[0, 8], [1, 16]], 0, 0, allow_small_or_imprecise_dtypes=True), (), ["iq"])
-    gsel(T.dupf[:, :], T.onf[:, :], [[-16, 8], [0, 2], [-1, 16]], AL.is_equal, 0, 1, 256, ["onf"], ["dupf"])
-    add("g", 0.6, lambda: g.iota(T.iop[:, :], [[0, 8], [0, 2], [1, 16]], 0, 0, allow_small_or_imprecise_dtypes=True), (), ["iop"])
+    vset(T.cb[:, :], -MID / 128, 512, 0.5, ["cb"])
+    for z in ("xz0", "xzn", "xz1"):
+        vset(A(z), 0.0, L, 0.5, K(z))
     for q in range(0, 16, 4):
         gsel(T.ed[:, 128 * q:128 * q + 512], T.ed[:, 128 * q:128 * q + 512], [[-256, 4], [-16, 8], [255, 16]], AL.is_equal, -256 * q, 1, 512, ["ed"], [("ed", q)])
-    KED = [("ed", q) for q in range(0, 16, 4)]
-    for name, val in (("ids", SH), ("idf", 1.0), ("idh", 1.0), ("idnb", -1.0), ("idn", -1.0), ("idp", BIG), ("idq", 0.5), ("id37", 37.0)):
-        vts(T[name][:, :], T.idb[:, :], val, None, AL.mult, None, 128, 0.5, ["idb"], [name])
-    vcopy(T.edh[:, :], T.ed[:, :], 2048, 0.5, KED, ["edh"])
-    vcopy(T.onh[:, :], T.onb[:, 0:128], 128, 0.5, ["onb"], ["onh"])
+        vcopy(T.edh[:, 128 * q:128 * q + 512], T.ed[:, 128 * q:128 * q + 512], 512, 0.5, [("ed", q)], [("edh", q)])
+    KED, KEH = [[(n, q) for q in range(0, 16, 4)] for n in ("ed", "edh")]
+    for name, val in (("ids", SH), ("idh", 1.0), ("idnb", -1.0), ("idn", -1.0), ("idp", BIG), ("idm", -2 * BIG), ("idq", 0.5), ("id18", 18.5)):
+        vmul(T[name][:, :], T.idb[:, :], val, 128, ["idb"], [name])
+    vmul(T.sel[:, 0:128], T.idb[:, :], 1.0, 128, ["idb"], ["idf"], 1)
+    vmul(T.sel[:, 128:256], T.blk[:, :], -1.0 / SH, 128, ["blk"], ["sel"], 1)
+    for name, val in (("blkn", -1.0 / SH), ("blk2", 2.0 / SH)):
+        vmul(T[name][:, 0:128], T.blk[:, :], val, 128, ["blk"], [name])
+        vmul(T[name][:, 128:256], T.blk[:, :], val, 128, ["blk"], [name])
+    vmul(T.onh[:, :], T.onb[:, 0:128], 1.0, 128, ["onb"], ["onh"])
+    vset(T.prow[:, 128:256], 0.0, 128, 0.5, ["prow"])
+    vts(T.prow[:, 0:128], T.iq[:, :], 1.0 / 4096, 1.0 / 8192, AL.mult, AL.add, 128, 1, ["iq"], ["prow"])
+    vset(T.rst[:, :], 1.0, 128, 1, ["rst"])
+    vset(T.rst[:, 0:128:16], 0.0, 8, 1, ["rst"])
+    for x in ("thd", "thd2"):
+        vmul(T[x][:, 0:128], T.onb[:, 0:128], MID / 128, 128, ["onb"], [x + "m"])
+    vts(T.thc[:, 0:1], T.thi[:, 0:1], -1.0, 2048.0, AL.mult, AL.add, 1, 1, [("ld4", "ld")], ["thc"])
+    vmul(T.thd[:, 128:256], T.idh[:, :], T.thc[:, 0:1], 128, ["idh", "thc"], ["thd"])
 
-    def xrep(buf, src, rk, engs, scale=1.0):
+    vcopy(T.tif[:, 0:3], T.tii[:, 0:3], 3, 1, [("ld2", "ld")], ["tif"])
+    vcopy(T.sgf[:, 0:3], T.sgi[:, 0:3], 3, 1, [("ld3", "ld")], ["sgf"])
+    for j in range(3):
+        vts(T.gq[:, 128 * j:128 * j + 128], T.iq[:, :], T.tif[:, j:j + 1], T.sgf[:, j:j + 1], AL.is_equal, AL.mult, 128, 1, ["iq", "tif", "sgf"], [("gq", j)])
+    vtt(T.gq[:, 384:512], T.gq[:, 0:128], T.gq[:, 128:256], AL.add, 128, 2, [("gq", 0), ("gq", 1)], [("gq", 3)])
+    vtt(T.gq[:, 0:128], T.gq[:, 384:512], T.gq[:, 256:384], AL.add, 128, 2, [("gq", 3), ("gq", 2)], [("gq", 0)])
+    vtt(T.gj[:, :], T.gq[:, 0:128], T.blk[:, :], AL.mult, 128, 2, [("gq", 0), "blk"], ["gj"])
+    sact(T.pk[:, 128:256], T.gj[:, :], AF.Abs, 128, ["gj"], ["pkA"])
+    p0 = tile()
+    mm(group([(C(0, 128), T.gj[:, :], T.idb[:, :])]), 128, ["gj", "idb"], p0)
+    sact(T.pk[:, 0:128], PS(p0, 0, 128), AF.Copy, 128, (), ["pkG"], (p0,))
+
+    def lane_views(buf, z, col, rk, engs, steps):
         keys = []
         for p in range(16):
             e = engs[p % len(engs)]
@@ -201,28 +246,29 @@ def rank_program(g, core, T, topo):
             key = (buf, p)
             keys.append(key)
             if e == "v":
-                vts(o, src, scale, None, AL.mult, None, 256, 0.5, rk, [key])
+                vcopy(o, col(0, L), L, 0.5, rk, [key])
             elif e == "s":
-                sact(o, src, AF.Copy, 256, rk, [key], scale=scale)
+                sact(o, col(0, L), AF.Copy, L, rk, [key])
             else:
-                gsel(o, src, [[0, L]], AL.is_ge, 0, 0, 256, rk, [key])
-        return keys
+                gsel(o, col(0, L), [[0, L]], AL.is_ge, 0, 0, L, rk, [key])
+        for h in R2:
+            if any(x + (h,) in SWAP for x in steps):
+                gsel(A(z, h, 64, H), col(H * h + 64, H * h + H), [[0, 64]], AL.is_ge, 0, 0, 64, rk, K(z, h))
+        return {"xr": T[buf], "kxr": keys, "z": z}
 
     sact(A("x0"), T.xs[:, 0:W:S], AF.Copy, L, [KX], K("x0"), scale=SH)
     for h in R2:
         sact(T.xq[:, h * W // 2:(h + 1) * W // 2], T.xs[:, h * W // 2:(h + 1) * W // 2], AF.Copy, W // 2, [KX], [("xq", h)], scale=SH)
     KXQ = [("xq", h) for h in R2]
-    xr0k = xrep("xr0", A("x0"), K("x0"), XR0)
+    X0 = lane_views("xr0", "xz0", lambda a, b: A("x0")[:, a:b], K("x0"), XR0, [(0, 1)])
     for h in R2:
         vcopy(A("L0a", h), T.dgs[:, h * W // 2:(h + 1) * W // 2:S], H, 1, [KDG[h]], K("L0a", h))
     for j in range(4):
         c = C(512 * j, 512 * j + 512)
         p = tile()
-        mm([(C(0, 512), T.ids[:, :], T.xs[:, c], True, True)], 512, [KX, "ids"], p)
+        mm(group([(C(0, 512), T.onb[:, 0:128], T.cb[:, :]), (C(0, 512), T.ids[:, :], T.xs[:, c])]), 1024, [KX, "ids", "onb", "cb"], p)
         vtt(T.P0[:, c], T.dgs[:, c], PS(p, 0, 512), AL.add, 512, 1, [KDG[j // 2]], [("P0", j)], (p,))
     KP0 = [("P0", j) for j in range(4)]
-    vts(T.thc[:, 0:1], T.thi[:, 0:1], -1.0, 2048.0, AL.mult, AL.add, 1, 1, [("ld4", "ld")], ["thc"])
-    vts(T.thd[:, :], T.idh[:, :], T.thc[:, 0:1], None, AL.mult, None, 128, 0.5, ["idh", "thc"], ["thd"])
 
     def dest(r):
         return cores[r % N]
@@ -253,6 +299,7 @@ def rank_program(g, core, T, topo):
     recv("rx", k, HOP + LAT["first"], K("xi"))
 
     par = {}
+    turned = set()
     GT_ = 0.06 + SW * GC * CY
 
     def room(buf, h, two=True):
@@ -261,169 +308,202 @@ def rank_program(g, core, T, topo):
         n = n % 2 if two else 0
         return n * 16 * L + h * HW, [(buf, n, h, s) for s in range(SB)]
 
-    def lanes(lst, h, s):
-        return A(lst, h, s * H // SB, (s + 1) * H // SB)
-
-    def raw(eng, win, kw, lst, h):
-        buf = "gf" if eng == "s" else "gh"
-        o, keys = room(buf, h, False)
-        for s in range(SB):
-            out = T[buf][:, o + s * SW:o + (s + 1) * SW]
-            if eng == "s":
-                add("s", GT_, lambda out=out, s=s: g.scalar.activation(out, win[:, :].indirect(lanes(lst, h, s)), AF.Copy), kw + K(lst, h, s), [keys[s]])
-            else:
-                add("v", GT_, lambda out=out, s=s: g.vector.tensor_copy(out, win[:, :].indirect(lanes(lst, h, s))), kw + K(lst, h, s), [keys[s]])
-        return buf, o, keys
-
-    def view(t, k, win, kw, lst, h, xr, kxr, packed):
-        buf = "zf" if packed else "zb"
-        o, keys = room(buf, h)
-        ao, ak = room("ab", h)
-        yo, yk = room("yb", h, False)
-        bias = -1024.0 / SH if packed else 0.0
-        todo = []
-        for s in range(SB):
-            x = xr[:, h * HW + s * SW:h * HW + (s + 1) * SW]
-            if (t, k, h, s) in VIA:
-                y = T.yb[:, yo + s * SW:yo + (s + 1) * SW]
-                add("s", GT_, lambda y=y, s=s: g.scalar.activation(y, win[:, :].indirect(lanes(lst, h, s)), AF.Copy), kw + K(lst, h, s), [yk[s]])
-                p = tile()
-                mm([(C(0, SW), T.idb[:, :], y, True, False), (C(0, SW), T.idnb[:, :], x, False, True)], 2 * SW, [yk[s], "idb", "idnb"] + kxr, p)
-                sact(T.ab[:, ao + s * SW:ao + (s + 1) * SW], PS(p, 0, SW), AF.Abs, SW, (), [ak[s]], (p,), scale=1.0 / SH)
-                continue
-            out = T[buf][:, o + s * SW:o + (s + 1) * SW]
-            add("v", GT_, lambda out=out, s=s, x=x: g.vector.tensor_tensor(out, win[:, :].indirect(lanes(lst, h, s)), x, AL.subtract),
-                kw + K(lst, h, s) + kxr, [keys[s]])
-            todo.append(s)
-            if len(todo) == ABW[k] or s == SB - 1 or (t, k, h, s + 1) in VIA:
-                a, b = todo[0] * SW, (s + 1) * SW
-                sact(T.ab[:, ao + a:ao + b], T[buf][:, o + a:o + b], AF.Abs, b - a, [keys[x_] for x_ in todo], [ak[x_] for x_ in todo], bias=bias, scale=1.0 / SH)
-                todo = []
-        return (buf, o, keys, yo, yk), (ao, ak)
+    def gather(eng, out, win, lst, h, s, rd, key, x=None):
+        src = win[:, :].indirect(A(lst, h, s * H // SB, (s + 1) * H // SB))
+        if eng == "s":
+            return add("s", GT_, lambda: g.scalar.activation(out, src, AF.Copy), rd + K(lst, h, s), [key])
+        if x is None:
+            return add("v", GT_, lambda: g.vector.tensor_copy(out, src), rd + K(lst, h, s), [key])
+        return add("v", GT_, lambda: g.vector.tensor_tensor(out, src, x, AL.subtract), rd + K(lst, h, s), [key])
 
     def own_rows(p, u, src, o, ed, rd, last=True):
         o += u * HW // 2
         mm([(C(64 * u, 64 * u + 64), ed[:, q * 128:(q + 1) * 128], src[:, o + q:o + HW // 2:16], q == 0, last and q == 15) for q in range(16)], 1024, rd, p)
 
-    def follow(t, k, src, h, Lk, hk):
-        buf, o, keys = src[:3]
-        if buf == "gh":
+    def own_packed(p, buf, o, keys, cols, last):
+        for q0 in range(0, 16, 4):
+            mm(more([(C(q, cols, 16), T[buf][:, o + q:o + HW:16], T.sel[:, q:cols:16]) for q in range(q0, q0 + 4)], last and q0 == 12), 1024, keys + ["idf", "sel"], p)
+
+    def unpack(t, k, p, h, Lk, hk):
+        if (t, k) in TS:
+            sact(A("ut", h), PS(p, 0, H), AF.Identity, H, (), K("ut", h), (p,), bias=MAGIC)
+            sact(A("tt", h), A("ut", h), AF.Identity, H, K("ut", h), K("tt", h), bias=-MAGIC)
+        else:
+            vts(A("tt", h), PS(p, 0, H), MAGIC, MAGIC, AL.add, AL.subtract, H, 1, (), K("tt", h), (p,))
+        vtt(A(hk, h), PS(p, 0, H), A("tt", h), AL.subtract, H, 1, K("tt", h), K(hk, h), (p,))
+        turned.add((hk, h))
+        p2 = tile()
+        mm(group([(C(0, H), A(hk, h), T.idh[:, :])]), 128, K(hk, h) + ["idh"], p2)
+        vcopy(A(Lk, h), PS(p2, 0, H), H, 1, (), K(Lk, h), (p2,))
+
+    def column(t, k, eng, lst, h, Lk, hk):
+        if eng == "v":
+            o, keys = room("gh", h, False)
+            for s in range(SB):
+                gather("v", T.gh[:, o + s * SW:o + (s + 1) * SW], T.dgs, lst, h, s, KDG, keys[s])
             for u in R2:
                 p = tile()
                 s = u * SB // 2
-                own_rows(p, u, T.gh, o, T.edh, keys[s:s + SB // 2] + ["edh"])
+                own_rows(p, u, T.gh, o, T.edh, keys[s:s + SB // 2] + KEH)
                 vcopy(A(Lk, h, 64 * u, 64 * u + 64), PS(p, 64 * u, 64 * u + 64), 64, 1, (), K(Lk, h, s), (p,))
+            if hk != "hA":
+                vcopy(A(hk, h), A(Lk, h), H, 0.5, K(Lk, h), K(hk, h))
         else:
+            o, keys = room("gf", h, False)
+            for s in range(SB):
+                gather("s", T.gf[:, o + s * SW:o + (s + 1) * SW], T.P0, lst, h, s, KP0, keys[s])
             p = tile()
-            for q0 in range(0, 16, 4):
-                mm([(C(q, 128, 16), T[buf][:, o + q:o + HW:16], T.idf[:, q:128:16], True, True) for q in range(q0, q0 + 4)], 1024, keys + ["idf"], p)
-            zc, tt = "zc%d" % k, "tt%d" % k
-            sact(A(zc, h), PS(p, 0, H), AF.Copy, H, (), K(zc, h), (p,))
-            p2 = tile()
-            mm([(C(0, H), A(zc, h), T.idf[:, :], True, False)], 512, K(zc, h) + ["idf"], p2)
-            if (t, k) in TS:
-                sact(A("ut", h), A(zc, h), AF.Identity, H, K(zc, h), K("ut", h), bias=MAGIC)
-                sact(A(tt, h), A("ut", h), AF.Identity, H, K("ut", h), K(tt, h), bias=-MAGIC)
-            else:
-                vts(A(tt, h), A(zc, h), MAGIC, MAGIC, AL.add, AL.subtract, H, 1, K(zc, h), K(tt, h))
-            mm([(C(0, H), A(tt, h), T.idnb[:, :], False, True)], 128, K(tt, h) + ["idnb"], p2)
-            vcopy(A(Lk, h), PS(p2, 0, H), H, 1, (), K(Lk, h), (p2,))
-        if hk:
-            vcopy(A(hk, h), A(Lk, h), H, 0.5, K(Lk, h), K(hk, h))
+            mm([(C(0, H), T.onh[:, :], T.thd[:, 0:H], True, False)], 128, ["onh", "thdm", keys[0]], p)
+            own_packed(p, "gf", o, keys, H, True)
+            unpack(t, k, p, h, Lk, hk)
 
-    def sums(ab, cols, step, first, last):
-        return [(C(q, cols, 16), T.ab[:, ab[0] + q:ab[0] + HW:16], T.blk[:, 0:128:step], first, last and (first or q == 15)) for q in range(16)]
+    def view(t, k, win, kw, lst, h, X, packed):
+        buf = "zf" if packed else "zb"
+        o, keys = room(buf, h)
+        ao, ak = room("ab", h)
+        swap = (t, k, h) in SWAP
+        todo = []
+        for s in range(SB):
+            x = X["xr"][:, h * HW + s * SW:h * HW + (s + 1) * SW]
+            out = T[buf][:, o + s * SW:o + (s + 1) * SW]
+            if swap and s >= SB // 2:
+                gather("s", out, win, lst, h, s, kw, keys[s])
+                if (h, s) not in X or (t, k) in ANEW:
+                    X[h, s] = tile()
+                    mm(group([(C(0, SW), T.idb[:, :], x)]), SW, ["idb"] + X["kxr"] + K(lst, h, s), X[h, s])
+                p = X[h, s]
+                vtt(T.ab[:, ao + s * SW:ao + (s + 1) * SW], out, PS(p, 0, SW), AL.max, SW, 1, [keys[s]], [ak[s]], (p,))
+                continue
+            gather("v", out, win, lst, h, s, kw + X["kxr"], keys[s], x)
+            todo.append(s)
+            if len(todo) == ABW[k]:
+                a, b = todo[0] * SW, (s + 1) * SW
+                half = not (swap or packed)
+                sact(T.ab[:, ao + a:ao + b], T[buf][:, o + a:o + b], AF.Abs if half else AF.Relu, b - a, [keys[i] for i in todo], [ak[i] for i in todo],
+                     scale=0.5 if half else 1.0)
+                todo = []
+        return {"buf": buf, "o": o, "keys": keys, "ao": ao, "ak": ak, "swap": swap, "packed": packed, "z": X["z"], "h": h}
 
-    def change(t, k, h, q):
+    def sums(buf, o, sel, a, b):
+        return [(C(a + q, b, 16), T[buf][:, o + q:o + HW:16], sel[:, 0:b - a:16]) for q in range(16)]
+
+    def less(v, a, b):
+        lst, rd = [], []
+        if v["swap"]:
+            lst, rd = [(C(a, b), A(v["z"], v["h"]), T.blkn[:, 0:b - a])], K(v["z"], v["h"]) + ["blkn"]
+            if not v["packed"]:
+                lst, rd = lst + sums("zb", v["o"], T.blkn, a, b), rd + v["keys"]
+        return lst, rd
+
+    def turn(c, name, h, ident):
+        return (c, ident, A(name, h)) if (name, h) in turned else (c, A(name, h), ident)
+
+    def back(c, name, h, ident):
+        return (c, A(name, h), ident) if (name, h) in turned else (c, ident, A(name, h))
+
+    def change(t, k, h):
         a, b = "h%d_%d" % (k - 1, t), "h%d_%d" % (k, t)
-        return [(C(H, 2 * H), A(a, h), T.idh[:, :], True, False), (C(H, 2 * H), A(b, h), T.idn[:, :], False, True)], K(a, h) + K(b, h) + ["idh", "idn"]
+        c = C(2 * H, 3 * H)
+        return group([turn(c, a, h, T.idh[:, :]), turn(c, b, h, T.idn[:, :])]), K(a, h) + K(b, h) + ["idh", "idn"]
 
-    def rest(t, k, h, ab, thd, kth, fk, here=True):
+    def flagged(t, k, h, fk, q):
+        mk = "m%d_%d" % (k, t)
+        vtt(A(mk, h), A(fk, h), PS(q, 2 * H, 3 * H), AL.mult, H, 1, K(fk, h), K(mk, h), (q,))
+        turned.add((mk, h))
+
+    def step(t, k, h, win, kw, lst, X, thd, kth, fk, packed, here=True):
+        v = view(t, k, win, kw, lst, h, X, packed)
         q = tile()
-        lst, rd = change(t, k, h, q) if here else ([], [])
-        lst = lst + [(C(0, H), T.onh[:, :], thd, True, False)]
-        rd = rd + ["onh", kth, ab[1][0]]
-        mm(lst, 128 * len(lst), rd, q)
-        lst, rd = sums(ab, H, 16, False, k == 1), ab[1] + ["blk"]
+        a = 0 if packed else H
+        pre, rd = change(t, k, h) if here else ([], [])
+        mm(pre + [(C(a, 2 * H), T.onh[:, :], thd[:, a:2 * H], True, False)], 512, rd + ["onh", v["keys"][0]] + kth, q)
+        lst, rd = less(v, H, 2 * H)
+        if lst:
+            mm(more(lst), 64 + 64 * len(lst), rd, q)
+        if packed:
+            own_packed(q, "zf", v["o"], v["keys"], 2 * H, False)
+        lst, rd = sums("ab", v["ao"], T.blk2, H, 2 * H), v["ak"] + ["blk2"]
         if k > 1:
             fp = "f%d_%d" % (k - 1, t)
-            lst, rd = lst + [(C(0, H), T.idp[:, :], A(fp, h), False, True)], rd + K(fp, h) + ["idp"]
-        mm(lst, 1024 + 128, rd, q)
-        sact(A(fk, h), PS(q, 0, H), AF.Sign, H, (), K(fk, h), (q,), bias=0.5 - 2048.0 + (BIG if k > 1 else 0.0))
+            lst, rd = lst + [(C(H, 2 * H), T.idp[:, :], A(fp, h))], rd + K(fp, h) + ["idp"]
+        mm(more(lst, True), 1024 + 128, rd, q)
+        if packed:
+            unpack(t, k + 1, q, h, "L%d_%d" % (k + 1, t), "h%d_%d" % (k + 1, t))
+        sact(A(fk, h), PS(q, H, 2 * H), AF.Sign, H, (), K(fk, h), (q,), bias=0.5 - 2048.0 + (BIG if k > 1 else 0.0))
         if here:
-            mk = "m%d_%d" % (k, t)
-            vtt(A(mk, h), A(fk, h), PS(q, H, 2 * H), AL.mult, H, 1, K(fk, h), K(mk, h), (q,))
+            flagged(t, k, h, fk, q)
 
-    def first(t, h, L0, L1, h1):
-        src = raw("v", T.dgs, KDG, L0, h) if (t, h) in G0V else raw("s", T.P0, KP0, L0, h)
-        follow(t, 1, src, h, L1, h1)
-
-    def walk(t, h, tb, xr, kxr, qt, ut):
-        P, kp, X, kx, thd, kth = tb["P"], tb["kp"], tb["X"], tb["kx"], tb["thd"], tb["kth"]
-        for k in (2, 3):
-            z, ab = view(t, k, P, kp, "L%d_%d" % (k, t), h, xr, kxr, True)
-            follow(t, k + 1, z, h, "L%d_%d" % (k + 1, t), "h%d_%d" % (k + 1, t))
-            rest(t, k, h, ab, thd, kth, "f%d_%d" % (k, t))
-            yield
-        z, ab = view(t, 4, X, kx, "L4_%d" % t, h, xr, kxr, False)
-        rest(t, 4, h, ab, thd, kth, "f4_%d" % t)
-        LF, hF = "LF_%d" % t, "hF_%d" % t
+    def walk(t, h, tb, X, kq, ut):
+        for k in (2, 3, 4):
+            win, kw = (tb["P"], tb["kp"]) if k < 4 else (tb["X"], tb["kx"])
+            step(t, k, h, win, kw, "L%d_%d" % (k, t), X, tb["thd"], tb["kth"], "f%d_%d" % (k, t), k < 4)
+            if k < 4:
+                yield
+        LF = "LF_%d" % t
+        terms = ["h0_%d" % t, "h4_%d" % t] + ["m%d_%d" % (k, t) for k in (1, 2, 3, 4)]
+        kt = sum([K(x, h) for x in terms], [])
         p = tile()
-        ms = ["m%d_%d" % (k, t) for k in (1, 2, 3, 4)]
-        ends = ["h0_%d" % t, "h4_%d" % t]
-        mm([(C(0, H), T.idq[:, :], A(x, h), x == ends[0], False) for x in ends] + [(C(0, H), A(x, h), T.idq[:, :], False, x == ms[-1]) for x in ms],
-           6 * 128, sum([K(x, h) for x in ms + ends], []) + ["idq"], p)
+        mm(group([back(C(0, H), x, h, T.idq[:, :]) for x in terms]), 6 * 128, kt + ["idq"], p)
         vcopy(A(LF, h), PS(p, 0, H), H, 1, (), K(LF, h), (p,))
         if t == 1:
             sact(A("yef", h), PS(p, 0, H), AF.Copy, H, (), K("yef", h), (p,))
-        vcopy(A(hF, h), A(LF, h), H, 0.5, K(LF, h), K(hF, h))
         yield
-        (buf, o, keys, yo, yk), ab = view(t, 5, X, kx, LF, h, xr, kxr, False)
+        v = view(t, 5, tb["X"], tb["kx"], LF, h, X, False)
+        cur[0] = -LEAD if h == 0 else cur[0]
         p2 = tile()
-        for u in R2:
-            s = u * SB // 2
-            if (t, 5, h, s) in VIA:
-                own_rows(p2, u, T.yb, yo, T.ed, yk[s:s + SB // 2] + KED, False)
-                a = H * h + 64 * u
-                mm([(C(64 * u, 64 * u + 64), T.idnb[:, :], tb["x"](a, a + 64), False, True)], 64, tb["kxl"] + ["idnb"], p2)
-            else:
-                own_rows(p2, u, T.zb, o, T.ed, keys[s:s + SB // 2] + KED)
+        if (t, h) in BT:
+            p1 = tile()
+            mm(group([(C(0, H), A(v["z"], h), T.idnb[:, :])] + [(C(q, H, 16), T.ab[:, v["ao"] + q:v["ao"] + HW:16], T.idb[:, q:H:16]) for q in range(16)]),
+               1024 + 128, v["ak"] + K(v["z"], h) + ["idb", "idnb"], p1)
+            sact(A("bt", h), PS(p1, 0, H), AF.Sign, H, (), K("bt", h), (p1,), bias=-0.5)
+            mm(group([(C(0, H), A("bt", h), T.idb[:, :])]), H, K("bt", h) + ["idb"], p2)
+        else:
+            for u in R2:
+                s = u * SB // 2
+                y = v["swap"] and u == 1
+                own_rows(p2, u, T.zb, v["o"], T.ed, v["keys"][s:s + SB // 2] + KED, not y)
+                if y:
+                    mm(more([(C(64, H), T.idnb[:, :], A(v["z"], h, 64, H))], True), 64, K(v["z"], h) + ["idnb"], p2)
         sact(A("bs", h), PS(p2, 0, H), AF.Sign, H, (), K("bs", h), (p2,), bias=-0.5)
         p4 = tile()
-        mm([(C(0, H), tb["GT"], A("bs", h), True, True)], H, K("bs", h) + [tb["kgt"]], p4)
+        mm(group([(C(0, H), tb["GT"], A("bs", h))]), H, K("bs", h) + [tb["kgt"]], p4)
         sact(A("sq", h), PS(p4, 0, H), AF.Square, H, (), K("sq", h), (p4,))
         p5 = tile()
-        mm([(C(0, H), tb["aG"], T.ngb[:, :], True, False), (C(0, H), tb["aG"], A("sq", h), False, True), (C(H, H + 8), A("sq", h), T.blk[:, 0:128:16], True, True)],
+        mm(group([(C(0, H), tb["aG"], T.ngb[:, :]), (C(0, H), tb["aG"], A("sq", h))]) + group([(C(H, H + 8), A("sq", h), T.blk[:, 0:128:16])]),
            2 * H + 64, K("sq", h) + [tb["kag"], "blk", "ngb"], p5)
         sact(A("ch", h), PS(p5, 0, H), AF.Sign, H, (), K("ch", h), (p5,))
         sact(A("any", h, 0, 8), PS(p5, H, H + 8), AF.Sign, 8, (), K("any", h) + [("asum", h)], (p5,), bias=-16.0, acc=T.asum[:, h:h + 1])
-        p3 = tile()
-        mm(sums(ab, H, 16, True, True), 1024, ab[1] + ["blk"], p3)
-        sact(A("dT", h), PS(p3, 0, H), AF.Copy, H, (), K("dT", h), (p3,))
-        mm([(C(H * h, H * h + H), T.id37[:, :], A(hF, h), True, False), (C(H * h, H * h + H), A("dT", h), T.idf[:, :], False, True)],
-           640, K(hF, h) + K("dT", h) + ["id37", "idf"], qt)
-        p = tile()
-        mm([(C(0, 256), T.onb[:, 0:128], T.prow[:, :], True, False)] + sums(ab, 256, 8, False, False), 256 + 1024, ab[1] + ["blk", "onb", "prow"], p)
-        mm([(C(0, 256), A("ch", h), T.dupb[:, :], False, True)], 256, K("ch", h) + ["dupb"], p)
-        add("v", vt(256, 1), lambda: g.vector.tensor_tensor_scan(T.pm[:, 256 * h:256 * h + 256], T.rst[:, :], ps(p)[:, 0:256], 0.0, AL.mult, AL.min),
-            ["rst"], [("pm", h)], (p,))
-        for x in range(8):
-            vtt(T.eq[:, H * h + 16 * x:H * h + 16 * x + 16], T.pm[:, 256 * h + 32 * x + 16:256 * h + 32 * x + 32],
-                PS(p, 32 * x + 16, 32 * x + 32), AL.is_equal, 16, 1, [("pm", h)], [("eq", h, x)], (p,))
-        mm([(C(H * h, H * h + H), T.idb[:, :], A("ch", h), True, False), (C(H * h, H * h + H), T.eq[:, H * h:H * h + H], T.idnb[:, :], False, True)],
-           256, K("ch", h) + ["idb", "idnb"] + [("eq", h, x) for x in range(8)], ut)
+        p = kq[h] = tile()
+        c = C(H * h, H * h + H)
+        lst, rd = less(v, 0, 2 * H)
+        mm([(C(0, 2 * H), T.onb[:, :], T.prow[:, :], True, False)] + more([turn(C(H, 2 * H), x, h, T.id18[:, :]) for x in terms]),
+           8 * 128, kt + ["onb", "prow", "id18", v["keys"][0]], p)
+        if lst:
+            mm(more(lst), 256 + 64 * len(lst), rd, p)
+        mm(more(sums("ab", v["ao"], T.blk2, 0, 2 * H)), 1024, v["ak"] + ["blk2"], p)
+        mm(more([(C(0, H), A("ch", h), T.idm[:, :])], True), H, K("ch", h) + ["idm"], p)
+        a, b = T.pm[:, 2 * H * h:2 * H * h + H], C(2 * H * h + H - 1, 2 * H * h - 1 if h else None, -1)
+        add("v", vt(H, 1), lambda: g.vector.tensor_tensor_scan(a, T.rst[:, :], ps(p)[:, 0:H], 0.0, AL.mult, AL.min), ["rst"], [("pm", h)], (p,))
+        add("v", vt(H, 1), lambda: g.vector.tensor_tensor_scan(T.pm[:, 2 * H * h + 2 * H - 1:2 * H * h + H - 1:-1], T.rst[:, :], T.pm[:, b], 0.0, AL.mult, AL.min),
+            ["rst", ("pm", h)], [("pn", h)])
+        vtt(T.eq[:, c], T.pm[:, 2 * H * h + H:2 * H * h + 2 * H], PS(p, 0, H), AL.is_equal, H, 1, [("pn", h)], [("eq", h)], (p,))
+        mm(group([turn(C(L + H * h, L + H * h + H), terms[0], h, T.idh[:, :])]) + group([(c, A("ch", h), T.idb[:, :]), (c, T.idnb[:, :], T.eq[:, c])]), 384,
+           K("ch", h) + K(terms[0], h) + ["idb", "idnb", "idh", ("eq", h)], ut)
         yield
 
-    def finish(t, out, qt, ut):
+    def finish(t, out, kq, ut):
         D0 = "h0_%d" % t
         p = tile()
-        mm([(C(0, 1), T.onf[:, 0:128], T.asum[:, h:h + 1], h == 0, h == 1) for h in R2], 512, [("asum", h) for h in R2] + ["onf"], p)
+        mm(group([(C(0, 1), T.onf[:, 0:128], T.asum[:, h:h + 1]) for h in R2]), 512, [("asum", h) for h in R2] + ["onf"], p)
         sact(T.acol[:, 0:1], PS(p, 0, 1), AF.Copy, 1, (), ["acol"], (p,))
-        vts(A("qi"), PS(qt, 0, L), T.acol[:, 0:1], None, AL.add, None, L, 1, ["acol"], K("qi"), (qt,))
+        for h in R2:
+            vts(A("qi", h), PS(kq[h], H, 2 * H), T.acol[:, 0:1], None, AL.add, None, H, 1, ["acol"], K("qi", h), (kq[h],))
         vts(A("ni"), A("qi"), W - 1, None, AL.bitwise_and, None, L, 1, K("qi"), K("ni"))
-        vtt(A("wd"), A("ni"), A(D0), AL.subtract, L, 2, K("ni") + K(D0), K("wd"))
+        vtt(A("wd"), A("ni"), PS(ut, L, 2 * L), AL.subtract, L, 1, K("ni"), K("wd"), (ut,))
         vtt(A("mh"), A("wd"), PS(ut, 0, L), AL.mult, L, 1, K("wd"), K("mh"), (ut,))
-        vtt(A(out), A("mh"), A(D0), AL.add, L, 1 + t, K("mh") + K(D0), K(out))
+        p = tile()
+        mm(sum([group([(C(H * h, H * h + H), T.idh[:, :], A(D0, h)), (C(H * h, H * h + H), A("mh", h), T.idh[:, :])]) for h in R2], []), 512, K(D0) + K("mh") + ["idh"], p)
+        vcopy(A(out), PS(p, 0, L), L, 1, (), K(out), (p,))
 
     def run(gens):
         gens = list(enumerate(gens))
@@ -440,61 +520,45 @@ def rank_program(g, core, T, topo):
         cur[0] = 0
 
     def home0(h):
-        first(0, h, "L0a", "L1a", None)
+        column(0, 1, "v" if (0, h) in G0V else "s", "L0a", h, "L1a", "hA")
         k = send(s1, [A("L1a", h), A("L0a", h)], [A("L1i", h), A("L0i", h)], "re%d" % h, K("L1a", h) + K("L0a", h))
         recv("re%d" % h, k, HOP, K("L1i", h) + K("L0i", h))
         sent.append(k[0])
         yield
-        z, ab = view(0, 1, T.xq, KXQ, "L1a", h, T.xr0, xr0k, False)
-        rest(0, 1, h, ab, T.thd[:, :], "thd", "f1a", False)
+        step(0, 1, h, T.xq, KXQ, "L1a", X0, T.thd, ["thd"], "f1a", False, False)
         yield
 
     sent = []
     run(home0(h) for h in R2)
-    k = send(h2, [T.xq[:, :]], [T.xq2[:, :]], "rxq", KXQ, sent)
-    recv("rxq", k, LAT["xq"], ["xq2"])
     for h in R2:
-        k = send(s1, [A("f1a", h)], [A("f1_0", h)], "rr%d" % h, K("f1a", h), (k[0],))
-        recv("rr%d" % h, k, HOP, K("f1_0", h))
+        k = send(s1, [A("f1a", h)], [A("f1_0", h)], "rr%d" % h, K("f1a", h), sent)
+        recv("rr%d" % h, k, LAT["flags"], K("f1_0", h))
+        sent.append(k[0])
+    k = ka = send(h2, [T.P0[:, 0:W // 2]], [T.P2[:, 0:W // 2]], "rxq", KP0, sent, "ltab")
+    recv("rxq", k, LAT["xq"], [("P2", 0)])
+    XN = lane_views("xrn", "xzn", lambda a, b: A("xi")[:, a:b], K("xi"), XRN, [(0, k_) for k_ in range(2, 6)])
 
-    vcopy(T.tif[:, 0:3], T.tii[:, 0:3], 3, 1, [("ld2", "ld")], ["tif"])
-    vcopy(T.sgf[:, 0:3], T.sgi[:, 0:3], 3, 1, [("ld3", "ld")], ["sgf"])
-    for j in range(3):
-        vts(T.gq[:, 128 * j:128 * j + 128], T.iq[:, :], T.tif[:, j:j + 1], T.sgf[:, j:j + 1], AL.is_equal, AL.mult, 128, 1, ["iq", "tif", "sgf"], [("gq", j)])
-    vtt(T.gq[:, 384:512], T.gq[:, 0:128], T.gq[:, 128:256], AL.add, 128, 2, [("gq", 0), ("gq", 1)], [("gq", 3)])
-    vtt(T.gq[:, 0:128], T.gq[:, 384:512], T.gq[:, 256:384], AL.add, 128, 2, [("gq", 3), ("gq", 2)], [("gq", 0)])
-    vtt(T.gj[:, :], T.gq[:, 0:128], T.blk[:, :], AL.mult, 128, 2, [("gq", 0), "blk"], ["gj"])
-    sact(T.pk[:, 128:256], T.gj[:, :], AF.Abs, 128, ["gj"], ["pkA"])
-    p0 = tile()
-    mm([(C(0, 128), T.gj[:, :], T.idb[:, :], True, True)], 128, ["gj", "idb"], p0)
-    sact(T.pk[:, 0:128], PS(p0, 0, 128), AF.Copy, 128, (), ["pkG"], (p0,))
-    xrnk = xrep("xrn", A("xi"), K("xi"), XRN)
-
-    k = send(h2, [T.P0[:, :]], [T.P2[:, :]], "rtab", KP0, (k[0],), "ltab")
-    add("n", 0.0, None, KP0, (), (), "ltab", k[1], LAT["tab"], [k[0]])
-    recv("rtab", k, LAT["tab"], ["P2"])
-    k = send(h2, [T.pk[:, 0:128], T.pk[:, 128:256], T.thd[:, :]], [T.pk2[:, 0:128], T.pk2[:, 128:256], T.thd2[:, :]], "rpk", ["pkA", "pkG", "thd"], (k[0],))
+    k = send(h2, [T.P0[:, W // 2:W]], [T.P2[:, W // 2:W]], "rtab", KP0, (k[0],), "ltab")
+    add("n", 0.0, None, KP0, (), (), "ltab", ka[1] + k[1], LAT["tab"], [k[0]])
+    recv("rtab", k, LAT["tab"], [("P2", 1)])
+    KP2 = [("P2", h) for h in R2]
+    k = send(h2, [T.pk[:, 0:128], T.pk[:, 128:256], T.thd[:, 128:256]], [T.pk2[:, 0:128], T.pk2[:, 128:256], T.thd2[:, 128:256]], "rpk", ["pkA", "pkG", "thd"], (k[0],))
     recv("rpk", k, LAT["tab"], ["pk2"])
-
-    vts(T.dupb[:, :], T.dupf[:, :], -2 * BIG, None, AL.mult, None, 256, 1, ["dupf"], ["dupb"])
-    vts(T.prow[:, :], T.iop[:, :], 1.0 / 4096, 1.0 / 8192, AL.mult, AL.add, 256, 1, ["iop"], ["prow"])
-    vset(T.rst[:, :], 1.0, 256, 1, ["rst"])
-    vset(T.rst[:, 0:256:32], 0.0, 8, 1, ["rst"])
 
     def away0(h):
         vcopy(A("h0_0", h), A("L0i", h), H, 0.5, K("L0i", h), K("h0_0", h))
         vcopy(A("h1_0", h), A("L1i", h), H, 0.5, K("L1i", h), K("h1_0", h))
-        follow(0, 2, raw("v", T.dgs, KDG, "L1i", h) if h in G1V else raw("s", T.P0, KP0, "L1i", h), h, "L2_0", "h2_0")
+        column(0, 2, "v" if h in G1V else "s", "L1i", h, "L2_0", "h2_0")
         q = tile()
-        lst, rd = change(0, 1, h, q)
+        lst, rd = change(0, 1, h)
         mm(lst, 256, rd + K("f1_0", h), q)
-        vtt(A("m1_0", h), A("f1_0", h), PS(q, H, 2 * H), AL.mult, H, 1, K("f1_0", h), K("m1_0", h), (q,))
+        flagged(0, 1, h, "f1_0", q)
         yield
-        yield from walk(0, h, tb, T.xrn, xrnk, qt, ut)
+        yield from walk(0, h, tb, XN, qt, ut)
 
-    tb = {"P": T.P0, "kp": KP0, "X": T.xq, "kx": KXQ, "thd": T.thd[:, :], "kth": "thd", "x": lambda a, b: A("xi")[:, a:b], "kxl": K("xi"),
+    tb = {"P": T.P0, "kp": KP0, "X": T.xq, "kx": KXQ, "thd": T.thd, "kth": ["thd", "thdm"],
           "GT": T.pk[:, 0:128], "kgt": "pkG", "aG": T.pk[:, 128:256], "kag": "pkA"}
-    qt, ut = tile(), tile()
+    qt, ut = {}, tile()
     run(away0(h) for h in R2)
     finish(0, "ndo", qt, ut)
     k = send(dest(rank - 1), [A("ndo")], [A("ndi")], "rnh", K("ndo"))
@@ -504,40 +568,40 @@ def rank_program(g, core, T, topo):
 
     vcopy(A("L0b"), T.dgs[:, 1:W:S], L, 1, KDG, K("L0b"))
     vcopy(A("h0_1"), A("L0b"), L, 0.5, K("L0b"), K("h0_1"))
-    xr1k = xrep("xr1", T.xq[:, 1:W:S], KXQ + K("L2_0"), XR1)
+    X1 = lane_views("xr1", "xz1", lambda a, b: T.xq[:, S * a + 1:S * b:S], KXQ + K("L2_0"), XR1, [(1, k_) for k_ in range(1, 6)])
     for j in range(4):
         c = C(512 * j, 512 * j + 512)
+        sact(T.P1[:, c], T.P2[:, c], AF.Identity, 512, [KP2[j // 2]] + K(*XQ2), [("P1", j)], bias=MAGIC)
+        sact(T.xq2[:, c], T.P1[:, c], AF.Identity, 512, [("P1", j)], [("xq2", j)], bias=-MAGIC)
         p = tile()
-        mm([(C(0, 512), T.idnb[:, :], T.xq2[:, c], True, False), (C(0, 512), T.idb[:, :], T.xq[:, c], False, True)],
-           2 * 512, ["xq2", "idb", "idnb"] + KXQ + K("wd"), p)
-        vtt(T.P1[:, c], T.P2[:, c], PS(p, 0, 512), AL.add, 512, 1, ["P2"] + K("ndo"), [("P1", j)], (p,))
-    KP1 = [("P1", j) for j in range(4)]
+        mm(group([(C(0, 512), T.idnb[:, :], T.xq2[:, c]), (C(0, 512), T.idb[:, :], T.xq[:, c])]), 2 * 512, [("xq2", j), "idb", "idnb"] + KXQ + K("wd"), p)
+        vtt(T.P1[:, c], T.P2[:, c], PS(p, 0, 512), AL.add, 512, 1, [KP2[j // 2]] + K("ndo"), [("P1", j)], (p,))
+    KP1, KXQ2 = [[(n, j) for j in range(4)] for n in ("P1", "xq2")]
+
+    def packed(c, xq, nd):
+        return group([(c, T.onb[:, 0:128], T.cb[:, 0:L]), (c, T.idb[:, :], xq[:, 0:W:S]), (c, T.idh[:, :], A(nd))])
+
     vcopy(T.dgs[:, 0:W:S], A("ndi"), L, 1, K("ndi"), KDG)
     p = tile()
-    mm([(C(0, L), T.idb[:, :], T.xq[:, 0:W:S], True, False), (C(0, L), T.idh[:, :], A("ndi"), False, True), (C(L, 2 * L), T.idh[:, :], A("ndi"), True, True)],
-       3 * L, K("ndi") + KXQ + ["idb", "idh"], p)
+    mm(packed(C(0, L), T.xq, "ndi") + group([(C(L, 2 * L), T.idh[:, :], A("ndi"))]), 4 * L, K("ndi") + KXQ + ["idb", "idh", "onb", "cb"], p)
     sact(T.P0[:, 0:W:S], PS(p, 0, L), AF.Copy, L, (), KP0, (p,))
     sact(A("yd0"), PS(p, L, 2 * L), AF.Copy, L, (), K("yd0"), (p,))
     add("y", 0.1, lambda: g.sync.dma_start(T.yd[:, 0:L], A("yd0")), K("yd0"), (), (), "ld5", 16, 2.0)
     p = tile()
-    mm([(C(0, L), T.idb[:, :], T.xq[:, 0:W:S], True, False), (C(0, L), T.idh[:, :], A("nd2"), False, True),
-        (C(L, 2 * L), T.idb[:, :], T.xq2[:, 0:W:S], True, False), (C(L, 2 * L), T.idh[:, :], A("nd2"), False, True)],
-       4 * L, K("nd2") + KXQ + ["xq2", "idb", "idh"], p)
+    mm(packed(C(0, L), T.xq, "nd2") + packed(C(L, 2 * L), T.xq2, "nd2"), 6 * L, K("nd2") + KXQ + KXQ2 + ["idb", "idh", "onb", "cb"], p)
     sact(T.P1[:, 0:W:S], PS(p, 0, L), AF.Copy, L, (), KP1, (p,))
-    sact(T.P2[:, 0:W:S], PS(p, L, 2 * L), AF.Copy, L, (), ["P2"], (p,))
+    sact(T.P2[:, 0:W:S], PS(p, L, 2 * L), AF.Copy, L, (), KP2, (p,))
 
     def home1(h):
-        first(1, h, "L0b", "L1b", "h1_1")
+        column(1, 1, "v" if (1, h) in G0V else "s", "L0b", h, "L1b", "h1_1")
         yield
-        z, ab = view(1, 1, T.P1, KP1, "L1b", h, T.xr1, xr1k, True)
-        follow(1, 2, z, h, "L2_1", "h2_1")
-        rest(1, 1, h, ab, T.thd[:, :], "thd", "f1_1")
+        step(1, 1, h, T.P1, KP1, "L1b", X1, T.thd, ["thd", "thdm"], "f1_1", True)
         yield
-        yield from walk(1, h, tb, T.xr1, xr1k, qt, ut)
+        yield from walk(1, h, tb, X1, qt, ut)
 
-    tb = {"P": T.P2, "kp": ["P2"], "X": T.xq2, "kx": ["xq2"], "thd": T.thd2[:, :], "kth": "pk2", "x": lambda a, b: T.xq[:, S * a + 1:S * b:S], "kxl": KXQ,
+    tb = {"P": T.P2, "kp": KP2, "X": T.xq2, "kx": KXQ2, "thd": T.thd2, "kth": ["pk2", "thd2m"],
           "GT": T.pk2[:, 0:128], "kgt": "pk2", "aG": T.pk2[:, 128:256], "kag": "pk2"}
-    qt, ut = tile(), tile()
+    qt, ut = {}, tile()
     run(home1(h) for h in R2)
     add("y", 0.1, lambda: g.sync.dma_start(T.ye[:, :], A("yef")), K("yef"), (), (), "ld6", 16, 2.0)
     finish(1, "yd1", qt, ut)
@@ -548,7 +612,7 @@ def rank_program(g, core, T, topo):
 
 
 PW = 0.02
-SKEW = 0.0
+SKEW = 2.0
 SEML = 0.1
 
 
@@ -575,7 +639,7 @@ def schedule(ops, tiles, bankof):
     free = {}
     order = []
     rt = [0.0] * n
-    pri = [PW * (bl[k] - SKEW * ops[k]["c"]) + ops[k].get("up", 0.0) for k in range(n)]
+    pri = [PW * (bl[k] - SKEW * ops[k]["c"]) + ops[k]["up"] for k in range(n)]
     free["n"] = -1.0
     while ready:
         best = None

@@ -30,7 +30,7 @@ for _p in POOLS:
 for _n, _w, _dt in (
         ("dgs", W, "int32"), ("xs", W, "bfloat16"), ("xq", W, "bfloat16"), ("xq2", W, "bfloat16"),
         ("P0", W, "float32"), ("P1", W, "float32"), ("P2", W, "float32"),
-        ("xr0", 16 * L, "bfloat16"), ("xr1", 16 * L, "bfloat16"), ("xrn", 16 * L, "bfloat16"),
+        ("xr0", HW, "bfloat16"), ("xr1", HW, "bfloat16"), ("xrn", HW, "bfloat16"),
         ("zf", 32 * L, "float32"), ("gf", 16 * L, "float32"), ("zb", 32 * L, "bfloat16"), ("ab", 32 * L, "bfloat16"),
         ("gh", 16 * L, "float16"), ("ed", 2048, "bfloat16"), ("edh", 2048, "float16"),
         ("onb", 128, "bfloat16"), ("onf", 128, "float32"), ("onh", 128, "float16"), ("ngb", 128, "bfloat16"), ("cb", 512, "bfloat16"),
@@ -48,21 +48,23 @@ for _k in range(8):
 SEMAPHORES = ["cv", "cs", "cp", "cg", "lsem", "ltab", "rx", "rxq", "rtab", "rpk", "rnh", "rn2", "re0", "re1", "rr0", "rr1"] + ["ld%d" % k for k in range(10)]
 
 G0V = ((0, 0), (1, 0))
-G1V = (1,)
-SWAP = tuple((t, k, h) for t in R2 for k in range(1, 6) for h in R2)
+G1V = (0,)
+SPLIT = "s"
+X1W = ("qi", 0)
+PUP = 0.3
+XNW = ("L1i", 0)
+XQE = "ss"
 XQ2 = ("ch", 1)
 BT = ()
-ANEW = ()
 LEAD = 0.0
 TS = ()
-XR0, XRN, XR1 = "ssv", "g", "g"
-ABW = {1: 2, 2: 2, 3: 2, 4: 2, 5: 2}
+XR0, XRN, XR1 = "s", "g", "g"
 
 CY = 0.83e-3 * 1.1
 PC = 0.42e-3 * 1.1
 GC = 1.5
 HOP = 2.5
-LAT = {"x": 4.2, "d0": 6.2, "d1": 8.2, "small": 2.5, "first": 2.0, "flags": 4.0, "xq": 10.0, "tab": 18.0}
+LAT = {"x": 3.2, "d0": 5.2, "d1": 7.2, "x1": 8.2, "small": 2.5, "first": 2.0, "flags": 4.0, "xq": 10.0, "tab": 18.0}
 
 
 def rank_program(g, core, T, topo):
@@ -132,6 +134,9 @@ def rank_program(g, core, T, topo):
     def K(name, h=None, s=None):
         return [(name, a, b) for a in (R2 if h is None else (h,)) for b in (R2 if s is None else (2 * s // SB,))]
 
+    def lane(h, u):
+        return 64 * h + H * u
+
     def vt(n, f):
         return 0.04 + max(64, n * f) * CY
 
@@ -181,15 +186,46 @@ def rank_program(g, core, T, topo):
         early(add(eng, 0.1, lambda: ENG[eng].dma_start(buf, src), (), [(sem, "ld")], (), sem, 16, lat))
 
     load("y", T.thi[:, 0:1], T.th[:, :], "ld4", LAT["small"])
-    load("y", T.xs[:, :], T.xv[:, :], "ld0", LAT["x"])
+    load("y", T.xs[:, 0:W // 2], T.xv[:, 0:W // 2], "ld0", LAT["x"])
     load("y", T.dgs[:, 0:W // 2], T.dg[:, 0:W // 2], "ld1", LAT["d0"])
     load("y", T.dgs[:, W // 2:W], T.dg[:, W // 2:W], "ld8", LAT["d1"])
+    load("y", T.xs[:, W // 2:W], T.xv[:, W // 2:W], "ld9", LAT["x1"])
     load("s", T.tii[:, 0:3], T.ti[:, :], "ld2", LAT["small"])
     load("s", T.sgi[:, 0:3], T.sg[:, :], "ld3", LAT["x"])
-    KX, KDG = ("ld0", "ld"), [("ld1", "ld"), ("ld8", "ld")]
+    KX, KDG = [("ld0", "ld"), ("ld9", "ld")], [("ld1", "ld"), ("ld8", "ld")]
 
-    def gsel(out, in_, pat, op, base, cm, n, r, w):
-        return add("g", 0.17 + 2 * n * CY, lambda: g.affine_select(out, in_, pat, op, 0.0, base, cm), r, w)
+    def dest(r):
+        return cores[r % N]
+
+    cnt = {"l": 0}
+
+    def send(d, names_in, names_out, sem, rd, after=(), lsem="lsem", dur=0.7):
+        pieces = len(names_in)
+        rid, pid = topo.addr(d, core)
+        es = topo.engines(core, d)
+        n = 1
+        while 2 * n * pieces <= min(len(es), 8):
+            n *= 2
+        masks = [sum(1 << e for e in es[k * n:(k + 1) * n]) for k in range(pieces)]
+        if lsem == "lsem":
+            cnt["l"] += n * pieces
+
+        def em():
+            return g.remote_dma_fused([RemoteDMATransfer(dst_ids=[DstId(rid=rid, pnc=pid)], dma_engine_mask=masks[k], remote_sem=T.sem[sem], src=names_in[k], dst=names_out[k])
+                                       for k in range(pieces)], local_sem=T.sem[lsem])
+        return add("g", dur, em, rd, (), (), "-", 0, 0.0, after), n * pieces
+
+    def recv(sem, sent, lat, keys):
+        return add("n", 0.0, None, (), keys, (), sem, sent[1], lat, [sent[0]])
+
+    s1, h2 = dest(rank + 1), dest(rank - 2)
+    for h in R2:
+        sact(A("x0", h), T.xs[:, h * W // 2:(h + 1) * W // 2:S], AF.Copy, H, [KX[h]], K("x0", h), scale=SH)
+    kx0 = send(s1, [A("x0", 0)], [A("xi", 0)], "rx", K("x0", 0))
+    recv("rx", kx0, HOP + LAT["first"], K("xi", 0))
+
+    def gsel(out, in_, pat, op, base, cm, n, r, w, after=()):
+        return add("g", 0.17 + 2 * n * CY, lambda: g.affine_select(out, in_, pat, op, 0.0, base, cm), r, w, extra=after)
 
     def giota(out, pat, n, w):
         return add("g", 0.13 + 2 * n * CY, lambda: g.iota(out, pat, 0, 0, allow_small_or_imprecise_dtypes=True), (), w)
@@ -206,7 +242,8 @@ def rank_program(g, core, T, topo):
     for z in ("xz0", "xzn", "xz1"):
         vset(A(z), 0.0, L, 0.5, K(z))
     for q in range(0, 16, 4):
-        gsel(T.ed[:, 128 * q:128 * q + 512], T.ed[:, 128 * q:128 * q + 512], [[-256, 4], [-16, 8], [255, 16]], AL.is_equal, -256 * q, 1, 512, ["ed"], [("ed", q)])
+        gsel(T.ed[:, 128 * q:128 * q + 512], T.ed[:, 128 * q:128 * q + 512], [[-256, 4], [-16, 8], [255, 16]], AL.is_equal, -256 * q, 1, 512, ["ed"], [("ed", q)],
+             kx0[:1] if q >= 8 else ())
         vcopy(T.edh[:, 128 * q:128 * q + 512], T.ed[:, 128 * q:128 * q + 512], 512, 0.5, [("ed", q)], [("edh", q)])
     KED, KEH = [[(n, q) for q in range(0, 16, 4)] for n in ("ed", "edh")]
     for name, val in (("ids", SH), ("idh", 1.0), ("idnb", -1.0), ("idn", -1.0), ("idp", BIG), ("idm", -2 * BIG), ("idq", 0.5), ("id18", 18.5)):
@@ -238,69 +275,44 @@ def rank_program(g, core, T, topo):
     mm(group([(C(0, 128), T.gj[:, :], T.idb[:, :])]), 128, ["gj", "idb"], p0)
     sact(T.pk[:, 0:128], PS(p0, 0, 128), AF.Copy, 128, (), ["pkG"], (p0,))
 
-    def lane_views(buf, z, col, rk, engs, steps):
-        keys = []
-        for p in range(16):
-            e = engs[p % len(engs)]
-            o = T[buf][:, p:16 * L:16]
-            key = (buf, p)
-            keys.append(key)
-            if e == "v":
-                vcopy(o, col(0, L), L, 0.5, rk, [key])
-            elif e == "s":
-                sact(o, col(0, L), AF.Copy, L, rk, [key])
-            else:
-                gsel(o, col(0, L), [[0, L]], AL.is_ge, 0, 0, L, rk, [key])
-        for h in R2:
-            if any(x + (h,) in SWAP for x in steps):
-                gsel(A(z, h, 64, H), col(H * h + 64, H * h + H), [[0, 64]], AL.is_ge, 0, 0, 64, rk, K(z, h))
-        return {"xr": T[buf], "kxr": keys, "z": z}
+    def copy(e, out, in_, n, r, w, after=()):
+        if e == "v":
+            vcopy(out, in_, n, 0.5, r, w)
+        elif e == "s":
+            sact(out, in_, AF.Copy, n, r, w)
+        else:
+            gsel(out, in_, [[0, n]], AL.is_ge, 0, 0, n, r, w, after)
 
-    sact(A("x0"), T.xs[:, 0:W:S], AF.Copy, L, [KX], K("x0"), scale=SH)
+    def lane_views(buf, z, col, rk, engs, when, after=()):
+        for p in range(16):
+            copy(engs[p % len(engs)], T[buf][:, p:HW:16], col(0, H), H, rk[0], [(buf, p)], after)
+        for h in R2:
+            copy(engs[0], A(z, h, 64, H), col(lane(h, 1), lane(h, 1) + 64), 64, rk[1], K(z, h), after)
+        return {"xr": T[buf], "kxr": [(buf, p) for p in range(16)], "z": z, "col": col, "kc": rk[1] + when}
+
+    def voters(name, t):
+        for h in R2:
+            for u in R2:
+                vcopy(A(name, h, 64 * u, 64 * u + 64), T.dgs[:, S * lane(h, u) + t:S * (lane(h, u) + 64):S], 64, 1, [KDG[u]], K(name, h, 2 * u))
+
     for h in R2:
-        sact(T.xq[:, h * W // 2:(h + 1) * W // 2], T.xs[:, h * W // 2:(h + 1) * W // 2], AF.Copy, W // 2, [KX], [("xq", h)], scale=SH)
+        c = C(h * W // 2, (h + 1) * W // 2)
+        if XQE[h] == "s":
+            sact(T.xq[:, c], T.xs[:, c], AF.Copy, W // 2, [KX[h]], [("xq", h)], scale=SH)
+        else:
+            vmul(T.xq[:, c], T.xs[:, c], SH, W // 2, [KX[h]], [("xq", h)])
     KXQ = [("xq", h) for h in R2]
-    X0 = lane_views("xr0", "xz0", lambda a, b: A("x0")[:, a:b], K("x0"), XR0, [(0, 1)])
-    for h in R2:
-        vcopy(A("L0a", h), T.dgs[:, h * W // 2:(h + 1) * W // 2:S], H, 1, [KDG[h]], K("L0a", h))
+    X0 = lane_views("xr0", "xz0", lambda a, b: A("x0")[:, a:b], [K("x0", h) for h in R2], XR0, [])
+    voters("L0a", 0)
     for j in range(4):
         c = C(512 * j, 512 * j + 512)
         p = tile()
-        mm(group([(C(0, 512), T.onb[:, 0:128], T.cb[:, :]), (C(0, 512), T.ids[:, :], T.xs[:, c])]), 1024, [KX, "ids", "onb", "cb"], p)
+        mm(group([(C(0, 512), T.onb[:, 0:128], T.cb[:, :]), (C(0, 512), T.ids[:, :], T.xs[:, c])]), 1024, [KX[j // 2], KDG[j // 2], "ids", "onb", "cb"], p)
         vtt(T.P0[:, c], T.dgs[:, c], PS(p, 0, 512), AL.add, 512, 1, [KDG[j // 2]], [("P0", j)], (p,))
     KP0 = [("P0", j) for j in range(4)]
 
-    def dest(r):
-        return cores[r % N]
-
-    cnt = {"l": 0}
-
-    def send(d, names_in, names_out, sem, rd, after=(), lsem="lsem", dur=0.7):
-        pieces = len(names_in)
-        rid, pid = topo.addr(d, core)
-        es = topo.engines(core, d)
-        n = 1
-        while 2 * n * pieces <= min(len(es), 8):
-            n *= 2
-        masks = [sum(1 << e for e in es[k * n:(k + 1) * n]) for k in range(pieces)]
-        if lsem == "lsem":
-            cnt["l"] += n * pieces
-
-        def em():
-            return g.remote_dma_fused([RemoteDMATransfer(dst_ids=[DstId(rid=rid, pnc=pid)], dma_engine_mask=masks[k], remote_sem=T.sem[sem], src=names_in[k], dst=names_out[k])
-                                       for k in range(pieces)], local_sem=T.sem[lsem])
-        return add("g", dur, em, rd, (), (), "-", 0, 0.0, after), n * pieces
-
-    def recv(sem, sent, lat, keys):
-        return add("n", 0.0, None, (), keys, (), sem, sent[1], lat, [sent[0]])
-
-    s1, h2 = dest(rank + 1), dest(rank - 2)
-    k = send(s1, [A("x0")], [A("xi")], "rx", K("x0"))
-    recv("rx", k, HOP + LAT["first"], K("xi"))
-
     par = {}
     turned = set()
-    GT_ = 0.06 + SW * GC * CY
 
     def room(buf, h, two=True):
         n = par.get((buf, h), 0)
@@ -308,13 +320,17 @@ def rank_program(g, core, T, topo):
         n = n % 2 if two else 0
         return n * 16 * L + h * HW, [(buf, n, h, s) for s in range(SB)]
 
-    def gather(eng, out, win, lst, h, s, rd, key, x=None):
-        src = win[:, :].indirect(A(lst, h, s * H // SB, (s + 1) * H // SB))
-        if eng == "s":
-            return add("s", GT_, lambda: g.scalar.activation(out, src, AF.Copy), rd + K(lst, h, s), [key])
-        if x is None:
-            return add("v", GT_, lambda: g.vector.tensor_copy(out, src), rd + K(lst, h, s), [key])
-        return add("v", GT_, lambda: g.vector.tensor_tensor(out, src, x, AL.subtract), rd + K(lst, h, s), [key])
+    def gather(eng, buf, o, keys, win, lst, h, u, rd, xr=None):
+        n = 1 if eng in SPLIT else 2
+        for s in range(2 * u, 2 * u + 2, n):
+            def em(s=s):
+                out, src = T[buf][:, o + s * SW:o + (s + n) * SW], win[:, :].indirect(A(lst, h, s * H // SB, (s + n) * H // SB))
+                if eng == "s":
+                    return g.scalar.activation(out, src, AF.Copy)
+                if xr is None:
+                    return g.vector.tensor_copy(out, src)
+                return g.vector.tensor_tensor(out, src, xr[:, (2 * h + s) * SW:(2 * h + s + n) * SW], AL.subtract)
+            ops[add(eng, 0.06 + n * SW * GC * CY, em, rd + K(lst, h, s), keys[s:s + n])]["n"] = n * SW
 
     def own_rows(p, u, src, o, ed, rd, last=True):
         o += u * HW // 2
@@ -339,8 +355,8 @@ def rank_program(g, core, T, topo):
     def column(t, k, eng, lst, h, Lk, hk):
         if eng == "v":
             o, keys = room("gh", h, False)
-            for s in range(SB):
-                gather("v", T.gh[:, o + s * SW:o + (s + 1) * SW], T.dgs, lst, h, s, KDG, keys[s])
+            for u in R2:
+                gather("v", "gh", o, keys, T.dgs, lst, h, u, KDG)
             for u in R2:
                 p = tile()
                 s = u * SB // 2
@@ -350,8 +366,8 @@ def rank_program(g, core, T, topo):
                 vcopy(A(hk, h), A(Lk, h), H, 0.5, K(Lk, h), K(hk, h))
         else:
             o, keys = room("gf", h, False)
-            for s in range(SB):
-                gather("s", T.gf[:, o + s * SW:o + (s + 1) * SW], T.P0, lst, h, s, KP0, keys[s])
+            for u in R2:
+                gather("s", "gf", o, keys, T.P0, lst, h, u, KP0)
             p = tile()
             mm([(C(0, H), T.onh[:, :], T.thd[:, 0:H], True, False)], 128, ["onh", "thdm", keys[0]], p)
             own_packed(p, "gf", o, keys, H, True)
@@ -361,38 +377,24 @@ def rank_program(g, core, T, topo):
         buf = "zf" if packed else "zb"
         o, keys = room(buf, h)
         ao, ak = room("ab", h)
-        swap = (t, k, h) in SWAP
-        todo = []
-        for s in range(SB):
-            x = X["xr"][:, h * HW + s * SW:h * HW + (s + 1) * SW]
-            out = T[buf][:, o + s * SW:o + (s + 1) * SW]
-            if swap and s >= SB // 2:
-                gather("s", out, win, lst, h, s, kw, keys[s])
-                if (h, s) not in X or (t, k) in ANEW:
-                    X[h, s] = tile()
-                    mm(group([(C(0, SW), T.idb[:, :], x)]), SW, ["idb"] + X["kxr"] + K(lst, h, s), X[h, s])
-                p = X[h, s]
-                vtt(T.ab[:, ao + s * SW:ao + (s + 1) * SW], out, PS(p, 0, SW), AL.max, SW, 1, [keys[s]], [ak[s]], (p,))
-                continue
-            gather("v", out, win, lst, h, s, kw + X["kxr"], keys[s], x)
-            todo.append(s)
-            if len(todo) == ABW[k]:
-                a, b = todo[0] * SW, (s + 1) * SW
-                half = not (swap or packed)
-                sact(T.ab[:, ao + a:ao + b], T[buf][:, o + a:o + b], AF.Abs if half else AF.Relu, b - a, [keys[i] for i in todo], [ak[i] for i in todo],
-                     scale=0.5 if half else 1.0)
-                todo = []
-        return {"buf": buf, "o": o, "keys": keys, "ao": ao, "ak": ak, "swap": swap, "packed": packed, "z": X["z"], "h": h}
+        gather("v", buf, o, keys, win, lst, h, 0, kw + X["kxr"], X["xr"])
+        gather("s", buf, o, keys, win, lst, h, 1, kw)
+        sact(T.ab[:, ao:ao + 2 * SW], T[buf][:, o:o + 2 * SW], AF.Relu, 2 * SW, keys[0:2], ak[0:2])
+        for s in (2, 3):
+            if (h, s) not in X:
+                X[h, s] = tile()
+                a = lane(h, 1) + 32 * (s - 2)
+                mm([(C(q, SW, 16), T.idb[:, :], X["col"](a, a + 32), True, True) for q in range(16)], 1024, ["idb"] + X["kc"], X[h, s])
+            vtt(T.ab[:, ao + s * SW:ao + (s + 1) * SW], T[buf][:, o + s * SW:o + (s + 1) * SW], PS(X[h, s], 0, SW), AL.max, SW, 1, [keys[s]], [ak[s]], (X[h, s],))
+        return {"buf": buf, "o": o, "keys": keys, "ao": ao, "ak": ak, "packed": packed, "z": X["z"], "h": h}
 
     def sums(buf, o, sel, a, b):
         return [(C(a + q, b, 16), T[buf][:, o + q:o + HW:16], sel[:, 0:b - a:16]) for q in range(16)]
 
     def less(v, a, b):
-        lst, rd = [], []
-        if v["swap"]:
-            lst, rd = [(C(a, b), A(v["z"], v["h"]), T.blkn[:, 0:b - a])], K(v["z"], v["h"]) + ["blkn"]
-            if not v["packed"]:
-                lst, rd = lst + sums("zb", v["o"], T.blkn, a, b), rd + v["keys"]
+        lst, rd = [(C(a, b), A(v["z"], v["h"]), T.blkn[:, 0:b - a])], K(v["z"], v["h"]) + ["blkn"]
+        if not v["packed"]:
+            lst, rd = lst + sums("zb", v["o"], T.blkn, a, b), rd + v["keys"]
         return lst, rd
 
     def turn(c, name, h, ident):
@@ -446,7 +448,8 @@ def rank_program(g, core, T, topo):
         mm(group([back(C(0, H), x, h, T.idq[:, :]) for x in terms]), 6 * 128, kt + ["idq"], p)
         vcopy(A(LF, h), PS(p, 0, H), H, 1, (), K(LF, h), (p,))
         if t == 1:
-            sact(A("yef", h), PS(p, 0, H), AF.Copy, H, (), K("yef", h), (p,))
+            for u in R2:
+                sact(A("yef")[:, lane(h, u):lane(h, u) + 64], PS(p, 64 * u, 64 * u + 64), AF.Copy, 64, (), K("yef", h, 2 * u), (p,))
         yield
         v = view(t, 5, tb["X"], tb["kx"], LF, h, X, False)
         cur[0] = -LEAD if h == 0 else cur[0]
@@ -460,7 +463,7 @@ def rank_program(g, core, T, topo):
         else:
             for u in R2:
                 s = u * SB // 2
-                y = v["swap"] and u == 1
+                y = u == 1
                 own_rows(p2, u, T.zb, v["o"], T.ed, v["keys"][s:s + SB // 2] + KED, not y)
                 if y:
                     mm(more([(C(64, H), T.idnb[:, :], A(v["z"], h, 64, H))], True), 64, K(v["z"], h) + ["idnb"], p2)
@@ -502,7 +505,8 @@ def rank_program(g, core, T, topo):
         vtt(A("wd"), A("ni"), PS(ut, L, 2 * L), AL.subtract, L, 1, K("ni"), K("wd"), (ut,))
         vtt(A("mh"), A("wd"), PS(ut, 0, L), AL.mult, L, 1, K("wd"), K("mh"), (ut,))
         p = tile()
-        mm(sum([group([(C(H * h, H * h + H), T.idh[:, :], A(D0, h)), (C(H * h, H * h + H), A("mh", h), T.idh[:, :])]) for h in R2], []), 512, K(D0) + K("mh") + ["idh"], p)
+        mm(sum([group([(C(lane(h, u), lane(h, u) + 64), T.idh[:, :], A(D0, h, 64 * u, 64 * u + 64)), (C(lane(h, u), lane(h, u) + 64), A("mh", h), T.idh[:, 64 * u:64 * u + 64])])
+                for h in R2 for u in R2], []), 512, K(D0) + K("mh") + ["idh"], p)
         vcopy(A(out), PS(p, 0, L), L, 1, (), K(out), (p,))
 
     def run(gens):
@@ -521,8 +525,9 @@ def rank_program(g, core, T, topo):
 
     def home0(h):
         column(0, 1, "v" if (0, h) in G0V else "s", "L0a", h, "L1a", "hA")
-        k = send(s1, [A("L1a", h), A("L0a", h)], [A("L1i", h), A("L0i", h)], "re%d" % h, K("L1a", h) + K("L0a", h))
-        recv("re%d" % h, k, HOP, K("L1i", h) + K("L0i", h))
+        out, to = [("L1a", h), ("L0a", h)] + [("x0", 1)] * (1 - h), [("L1i", h), ("L0i", h)] + [("xi", 1)] * (1 - h)
+        k = send(s1, [A(*x) for x in out], [A(*x) for x in to], "re%d" % h, sum([K(*x) for x in out], []))
+        recv("re%d" % h, k, HOP, sum([K(*x) for x in to], []))
         sent.append(k[0])
         yield
         step(0, 1, h, T.xq, KXQ, "L1a", X0, T.thd, ["thd"], "f1a", False, False)
@@ -536,7 +541,7 @@ def rank_program(g, core, T, topo):
         sent.append(k[0])
     k = ka = send(h2, [T.P0[:, 0:W // 2]], [T.P2[:, 0:W // 2]], "rxq", KP0, sent, "ltab")
     recv("rxq", k, LAT["xq"], [("P2", 0)])
-    XN = lane_views("xrn", "xzn", lambda a, b: A("xi")[:, a:b], K("xi"), XRN, [(0, k_) for k_ in range(2, 6)])
+    XN = lane_views("xrn", "xzn", lambda a, b: A("xi")[:, a:b], [K("xi", h) for h in R2], XRN, K(*XNW), sent[:1])
 
     k = send(h2, [T.P0[:, W // 2:W]], [T.P2[:, W // 2:W]], "rtab", KP0, (k[0],), "ltab")
     add("n", 0.0, None, KP0, (), (), "ltab", ka[1] + k[1], LAT["tab"], [k[0]])
@@ -544,6 +549,7 @@ def rank_program(g, core, T, topo):
     KP2 = [("P2", h) for h in R2]
     k = send(h2, [T.pk[:, 0:128], T.pk[:, 128:256], T.thd[:, 128:256]], [T.pk2[:, 0:128], T.pk2[:, 128:256], T.thd2[:, 128:256]], "rpk", ["pkA", "pkG", "thd"], (k[0],))
     recv("rpk", k, LAT["tab"], ["pk2"])
+    ktab = k[0]
 
     def away0(h):
         vcopy(A("h0_0", h), A("L0i", h), H, 0.5, K("L0i", h), K("h0_0", h))
@@ -566,9 +572,9 @@ def rank_program(g, core, T, topo):
     k = send(dest(rank - 3), [A("ndo")], [A("nd2")], "rn2", K("ndo"), (k[0],))
     recv("rn2", k, HOP, K("nd2"))
 
-    vcopy(A("L0b"), T.dgs[:, 1:W:S], L, 1, KDG, K("L0b"))
+    voters("L0b", 1)
     vcopy(A("h0_1"), A("L0b"), L, 0.5, K("L0b"), K("h0_1"))
-    X1 = lane_views("xr1", "xz1", lambda a, b: T.xq[:, S * a + 1:S * b:S], KXQ + K("L2_0"), XR1, [(1, k_) for k_ in range(1, 6)])
+    X1 = lane_views("xr1", "xz1", lambda a, b: T.xq[:, S * a + 1:S * b:S], [KXQ, KXQ], XR1, K(*X1W), (ktab,))
     for j in range(4):
         c = C(512 * j, 512 * j + 512)
         sact(T.P1[:, c], T.P2[:, c], AF.Identity, 512, [KP2[j // 2]] + K(*XQ2), [("P1", j)], bias=MAGIC)
@@ -589,7 +595,7 @@ def rank_program(g, core, T, topo):
     add("y", 0.1, lambda: g.sync.dma_start(T.yd[:, 0:L], A("yd0")), K("yd0"), (), (), "ld5", 16, 2.0)
     p = tile()
     mm(packed(C(0, L), T.xq, "nd2") + packed(C(L, 2 * L), T.xq2, "nd2"), 6 * L, K("nd2") + KXQ + KXQ2 + ["idb", "idh", "onb", "cb"], p)
-    sact(T.P1[:, 0:W:S], PS(p, 0, L), AF.Copy, L, (), KP1, (p,))
+    ops[-1]["up"] = ops[sact(T.P1[:, 0:W:S], PS(p, 0, L), AF.Copy, L, (), KP1, (p,))]["up"] = PUP
     sact(T.P2[:, 0:W:S], PS(p, L, 2 * L), AF.Copy, L, (), KP2, (p,))
 
     def home1(h):
@@ -612,7 +618,9 @@ def rank_program(g, core, T, topo):
 
 
 PW = 0.02
-SKEW = 2.0
+TURNS, SKEWS, WEIGHTS = 4, (2.0, 3.0), tuple((a, b) for a in (0.3, 0.5, 1.0) for b in (0.2, 0.25, 0.3))
+CASES = ((1.15, 1.0), (1.3, 1.4), (1.5, 1.0), (1.9, 1.2))
+MADE = {}
 SEML = 0.1
 
 
@@ -626,6 +634,62 @@ def schedule(ops, tiles, bankof):
     for k in range(n - 1, -1, -1):
         o = ops[k]
         bl[k] = o["d"] + o["lat"] + max([bl[s] for s in succ[k]] + [0.0])
+    key = (tuple(bl), tuple(o["e"] for o in ops), TURNS, WEIGHTS, SKEWS, SEML)
+    if key not in MADE:
+        tries = []
+        for skew in SKEWS:
+            first = forwards(ops, tiles, succ, [PW * (bl[k] - skew * ops[k]["c"]) + ops[k]["up"] for k in range(n)])
+            for ahead, back in WEIGHTS:
+                last = first
+                for turn in range(TURNS):
+                    if last is None:
+                        break
+                    tries.append(last)
+                    far = backwards(ops, succ, last[0], back)
+                    last = forwards(ops, tiles, succ, [ahead * far[k] + ops[k]["up"] for k in range(n)])
+        MADE[key] = min(tries, key=lambda x: sum(replay(ops, x[1], x[3], gc, hop) / gc ** 0.5 for gc, hop in CASES))
+    fin, order, banks, more = MADE[key]
+    bankof.update(banks)
+    for k, d in more:
+        ops[k]["deps"].add(d)
+    return order
+
+
+def replay(ops, order, more, gc, hop):
+    fin, free, more = {}, {}, dict(more)
+    for k in order:
+        o = ops[k]
+        st = max([free.get(o["e"], 0.0)] + [fin[d] + (SEML if ops[d]["e"] != o["e"] else 0.05) for d in o["deps"]] + [fin[more[k]] + SEML if k in more else 0.0])
+        d = o["d"] + o.get("n", 0) * CY * (gc - GC)
+        if o["e"] != "n":
+            free[o["e"]] = st + d
+        fin[k] = st + d + o["lat"] * hop
+    return max(fin.values())
+
+
+def backwards(ops, succ, fin, back):
+    n = len(ops)
+    left = [len(x) for x in succ]
+    ready = [k for k in range(n) if left[k] == 0]
+    rt, bl, free = [0.0] * n, [0.0] * n, {}
+    while ready:
+        k = min(ready, key=lambda k: max(rt[k] + ops[k]["lat"], free.get(ops[k]["e"], 0.0)) - back * fin[k])
+        o = ops[k]
+        ready.remove(k)
+        bl[k] = max(rt[k] + o["lat"], free.get(o["e"], 0.0)) + o["d"]
+        if o["e"] != "n":
+            free[o["e"]] = bl[k]
+        for d in o["deps"]:
+            left[d] -= 1
+            rt[d] = max(rt[d], bl[k] + (SEML if ops[d]["e"] != o["e"] else 0.05))
+            if left[d] == 0:
+                ready.append(d)
+    return bl
+
+
+def forwards(ops, tiles, succ, pri):
+    n = len(ops)
+    bankof, more = {}, []
     tfirst = {}
     for t, lst in enumerate(tiles):
         if lst:
@@ -639,7 +703,6 @@ def schedule(ops, tiles, bankof):
     free = {}
     order = []
     rt = [0.0] * n
-    pri = [PW * (bl[k] - SKEW * ops[k]["c"]) + ops[k]["up"] for k in range(n)]
     free["n"] = -1.0
     while ready:
         best = None
@@ -659,7 +722,7 @@ def schedule(ops, tiles, bankof):
             if best is None or key < best[0]:
                 best = (key, k, st, b)
         if best is None:
-            raise ValueError("no free PSUM bank")
+            return None
         _, k, st, b = best
         o = ops[k]
         ready.remove(k)
@@ -668,7 +731,7 @@ def schedule(ops, tiles, bankof):
             bankof[t] = b
             bank[b] = t
             if bfree[b][1] is not None:
-                o["deps"].add(bfree[b][1])
+                more.append((k, bfree[b][1]))
         if o["e"] != "n":
             free[o["e"]] = st + o["d"]
         fin[k] = st + o["d"] + o["lat"]
@@ -686,7 +749,7 @@ def schedule(ops, tiles, bankof):
                 rt[s] = x
             if left[s] == 0:
                 ready.append(s)
-    return order
+    return fin, order, bankof, more
 
 
 def emit(g, T, ENG, CSEM, ops, order, nlocal):

@@ -15,9 +15,9 @@ AF = ActivationFunctionType
 
 R2 = (0, 1)
 U_ = ["L0a", "L0b", "L0i", "L1a", "L1i", "L1b"] + ["%s_%d" % (n, t) for n in ("L2", "L3", "L4", "LF") for t in R2]
-H_ = ["wd", "mh", "ndo", "ndi", "nd2", "hA"] + ["%s_%d" % (n, t) for n in ("h0", "h1", "h2", "h3", "h4", "m1", "m2", "m3", "m4") for t in R2]
-F_ = ["yd0", "yd1", "yef", "ut"]
-B_ = ["x0", "xi", "xz0", "xzn", "xz1", "f1a", "f1_0", "f1_1", "any", "bt", "bs", "sq", "ch", "tt"] + ["%s_%d" % (n, t) for n in ("f2", "f3", "f4") for t in R2]
+H_ = ["wd", "mh", "ndo", "ndi", "nd2", "hE", "dh"] + ["%s_%d" % (n, t) for n in ("h0", "h1", "h2", "h3", "h4", "m1", "m2", "m3", "m4") for t in R2]
+F_ = ["yd0", "yd1", "yef"]
+B_ = ["x0", "xi", "xz0", "xzn", "xz1", "f1a", "f1_0", "f1_1", "bs", "sq", "tt", "eq"] + ["%s_%d" % (n, t) for n in ("f2", "f3", "f4") for t in R2]
 I_ = ["qi", "ni"]
 POOLS = {"PU": (U_, "uint16"), "PH": (H_, "float16"), "PF": (F_, "float32"), "PB": (B_, "bfloat16"), "PI": (I_, "int32")}
 SLOT = {}
@@ -28,43 +28,38 @@ for _p in POOLS:
     for _k, _n in enumerate(_names):
         SLOT[_n] = (_p, 256 * _k)
 for _n, _w, _dt in (
-        ("dgs", W, "int32"), ("xs", W, "bfloat16"), ("xq", W, "bfloat16"), ("xq2", W, "bfloat16"),
+        ("dgs", W, "int32"), ("xs", W, "bfloat16"), ("xs2", W, "bfloat16"), ("dh0", W, "float16"), ("dh2", W, "float16"),
         ("P0", W, "float32"), ("P1", W, "float32"), ("P2", W, "float32"),
         ("xr0", HW, "bfloat16"), ("xr1", HW, "bfloat16"), ("xrn", HW, "bfloat16"),
-        ("zf", 32 * L, "float32"), ("gf", 16 * L, "float32"), ("zb", 32 * L, "bfloat16"), ("ab", 32 * L, "bfloat16"),
-        ("gh", 16 * L, "float16"), ("ed", 2048, "bfloat16"), ("edh", 2048, "float16"),
-        ("onb", 128, "bfloat16"), ("onf", 128, "float32"), ("onh", 128, "float16"), ("ngb", 128, "bfloat16"), ("cb", 512, "bfloat16"),
-        ("idb", 128, "bfloat16"), ("idh", 128, "float16"), ("idn", 128, "float16"), ("idq", 128, "float16"), ("id18", 128, "float16"),
-        ("idp", 128, "bfloat16"), ("idnb", 128, "bfloat16"), ("sel", 256, "float32"), ("ids", 128, "bfloat16"),
-        ("blk0", 128, "bfloat16"), ("blk", 128, "bfloat16"), ("blkn", 256, "bfloat16"), ("blk2", 256, "bfloat16"),
-        ("idm", 128, "bfloat16"), ("prow", 256, "bfloat16"), ("rst", 128, "float32"),
-        ("pm", 512, "float32"), ("eq", 256, "bfloat16"), ("iq", 128, "float32"),
+        ("zf", 32 * L, "float32"), ("zb", 32 * L, "bfloat16"), ("ab", 32 * L, "bfloat16"),
+        ("gh", 16 * L, "float16"), ("ed", 2048, "bfloat16"), ("onb", 512, "bfloat16"), ("ngb", 128, "bfloat16"),
+        ("idb", 128, "bfloat16"), ("idq", 128, "bfloat16"), ("id37", 128, "bfloat16"),
+        ("idp", 128, "bfloat16"), ("idn", 128, "bfloat16"), ("sel", 256, "float32"), ("ids", 128, "bfloat16"),
+        ("blk0", 128, "bfloat16"), ("blk", 128, "bfloat16"), ("bkn", 256, "bfloat16"), ("bk2", 256, "bfloat16"),
+        ("prow", 128, "bfloat16"), ("rst", 128, "float32"), ("pm", 512, "float32"), ("iq", 128, "float32"), ("chb", 288, "bfloat16"),
         ("thi", 4, "int32"), ("tii", 4, "int32"), ("sgi", 4, "int32"), ("tif", 4, "float32"), ("sgf", 4, "float32"), ("thc", 4, "float32"),
-        ("gq", 512, "float32"), ("gj", 128, "bfloat16"), ("pk", 256, "bfloat16"), ("pk2", 256, "bfloat16"),
+        ("gq", 512, "bfloat16"), ("gj", 128, "bfloat16"), ("pk", 272, "bfloat16"), ("pk2", 272, "bfloat16"),
         ("thd", 256, "float16"), ("thd2", 256, "float16"), ("asum", 8, "float32"), ("acol", 8, "float32")):
     SCRATCH[_n] = ("sbuf", [128, _w], _dt)
-for _k in range(8):
-    SCRATCH["bank%d" % _k] = ("psum", [128, 512], "float32")
-SEMAPHORES = ["cv", "cs", "cp", "cg", "lsem", "ltab", "rx", "rxq", "rtab", "rpk", "rnh", "rn2", "re0", "re1", "rr0", "rr1"] + ["ld%d" % k for k in range(10)]
+for _k in range(4):
+    SCRATCH["pair%d" % _k] = ("psum", [128, 1024], "float32")
+SEMAPHORES = ["cv", "cs", "cp", "cg", "lsem", "rx", "rdh", "rxs", "rpk", "rnh", "rn2", "re0", "re1", "rr0", "rr1"] + ["ld%d" % k for k in range(10)]
 
-G0V = ((0, 0), (1, 0))
-G1V = (0,)
-SPLIT = "s"
+CV = {(0, 1): "vvss", (0, 2): "vvss", (1, 1): "vvss"}
+RV = ((0, 5, 1), (1, 5, 1))
+QL = {"list": "s", "col": "vs", "colh": "v", "vote": "vvss", "h0": "v", "LF": "v", "hE": "s", "ye": "s", "qi": "s", "patch": "v",
+      "dh0": "vs", "P0": "vsvs", "P1": "vsvs", "P2": "svsv", "xr0": "sv", "xrn": "g", "xr1": "g", "const": "s"}
 X1W = ("qi", 0)
-PUP = 0.3
 XNW = ("L1i", 0)
-XQE = "ss"
-XQ2 = ("ch", 1)
-BT = ()
-LEAD = 0.0
-TS = ()
-XR0, XRN, XR1 = "s", "g", "g"
+PW1 = ("ch", 1)
+PUP = 0.3
+CUT = 8
 
-CY = 0.83e-3 * 1.1
-PC = 0.42e-3 * 1.1
+CY = 0.83e-3
+PC = 0.42e-3
 GC = 1.5
 HOP = 2.5
-LAT = {"x": 3.2, "d0": 5.2, "d1": 7.2, "x1": 8.2, "small": 2.5, "first": 2.0, "flags": 4.0, "xq": 10.0, "tab": 18.0}
+LAT = {"x": 3.2, "d0": 5.2, "d1": 7.2, "x1": 8.2, "small": 2.5, "first": 2.0, "flags": 4.0, "dh": 10.0, "tab": 18.0}
 
 
 def rank_program(g, core, T, topo):
@@ -72,7 +67,7 @@ def rank_program(g, core, T, topo):
     if rank is None:
         return
     cores = T.cores
-    ops, lastw, readers, tiles, own = [], {}, {}, [], {}
+    ops, lastw, readers, tiles, wide, own = [], {}, {}, [], [], {}
     bankof = {}
     cur = [0]
     ENG = {"v": g.vector, "s": g.scalar, "p": g.tensor, "g": g, "y": g.sync}
@@ -112,15 +107,17 @@ def rank_program(g, core, T, topo):
     def early(k):
         ops[k]["up"] = 1000.0 - 20.0 * k
 
-    def tile():
+    def tile(banks=1):
         tiles.append([])
+        wide.append(banks)
         return len(tiles) - 1
 
-    def ps(t):
-        return T["bank%d" % bankof[t]]
+    def ps(t, c):
+        o = 512 * (bankof[t] % 2)
+        return T["pair%d" % (bankof[t] // 2)][:, o + c.start:o + c.stop:c.step]
 
     def PS(t, a, b):
-        return (lambda: ps(t)[:, a:b],)
+        return (lambda: ps(t, slice(a, b)),)
 
     def R(x):
         return x[0]() if isinstance(x, tuple) else x
@@ -150,11 +147,8 @@ def rank_program(g, core, T, topo):
             return g.vector.tensor_scalar(out, R(in0), s1, s2, o0, o1)
         return add("v", vt(n, f), em, r, w, p)
 
-    def vmul(out, in0, val, n, r, w, f=0.5):
-        return vts(out, in0, val, None, AL.mult, None, n, f, r, w)
-
     def vtt(out, in0, in1, op, n, f, r, w, p=()):
-        return add("v", vt(n, f), lambda: g.vector.tensor_tensor(out, R(in0), R(in1), op), r, w, p)
+        return add("v", vt(n, f), lambda: g.vector.tensor_tensor(R(out), R(in0), R(in1), op), r, w, p)
 
     def vset(out, val, n, f, w):
         return add("v", vt(n, f), lambda: g.vector.memset(out, val), (), w)
@@ -166,11 +160,23 @@ def rank_program(g, core, T, topo):
             return g.scalar.activation(out, R(in_), func, bias=bias, scale=scale)
         return add("s", 0.06 + n * CY, em, r, w, p)
 
+    def gsel(out, in_, pat, op, base, cm, n, r, w, after=()):
+        return add("g", 0.17 + 2 * n * CY, lambda: g.affine_select(out, in_, pat, op, 0.0, base, cm), r, w, extra=after)
+
+    def move(e, out, in_, n, r, w, p=(), f=1, scale=1.0, bias=0.0, after=()):
+        if e == "g":
+            return gsel(out, in_, [[0, n]], AL.is_ge, 0, 0, n, r, w, after)
+        if e == "s":
+            return sact(out, in_, AF.Identity if bias else AF.Copy, n, r, w, p, bias, scale)
+        if bias or not isinstance(scale, float) or scale != 1.0:
+            return vts(out, in_, scale, bias, AL.mult, AL.add, n, f, r, w, p)
+        return vcopy(out, in_, n, f, r, w, p)
+
     def mm(lst, cyc, r, p):
         def em():
             out = None
             for (c, lhs, rhs, st, sp) in lst:
-                out = g.tensor.matmul(ps(p)[:, c], lhs, rhs, st, sp)
+                out = g.tensor.matmul(ps(p, c), lhs, rhs, st, sp)
             return out
         return add("p", 0.03 + cyc * PC, em, r, (), (p,))
 
@@ -181,6 +187,7 @@ def rank_program(g, core, T, topo):
         return [x + (False, last and i == len(lst) - 1) for i, x in enumerate(lst)]
 
     C = slice
+    ONE = T.onb[:, 0:128]
 
     def load(eng, buf, src, sem, lat):
         early(add(eng, 0.1, lambda: ENG[eng].dma_start(buf, src), (), [(sem, "ld")], (), sem, 16, lat))
@@ -199,7 +206,7 @@ def rank_program(g, core, T, topo):
 
     cnt = {"l": 0}
 
-    def send(d, names_in, names_out, sem, rd, after=(), lsem="lsem", dur=0.7):
+    def send(d, names_in, names_out, sem, rd, after=(), dur=0.7):
         pieces = len(names_in)
         rid, pid = topo.addr(d, core)
         es = topo.engines(core, d)
@@ -207,12 +214,11 @@ def rank_program(g, core, T, topo):
         while 2 * n * pieces <= min(len(es), 8):
             n *= 2
         masks = [sum(1 << e for e in es[k * n:(k + 1) * n]) for k in range(pieces)]
-        if lsem == "lsem":
-            cnt["l"] += n * pieces
+        cnt["l"] += n * pieces
 
         def em():
             return g.remote_dma_fused([RemoteDMATransfer(dst_ids=[DstId(rid=rid, pnc=pid)], dma_engine_mask=masks[k], remote_sem=T.sem[sem], src=names_in[k], dst=names_out[k])
-                                       for k in range(pieces)], local_sem=T.sem[lsem])
+                                       for k in range(pieces)], local_sem=T.sem.lsem)
         return add("g", dur, em, rd, (), (), "-", 0, 0.0, after), n * pieces
 
     def recv(sem, sent, lat, keys):
@@ -220,48 +226,40 @@ def rank_program(g, core, T, topo):
 
     s1, h2 = dest(rank + 1), dest(rank - 2)
     for h in R2:
-        sact(A("x0", h), T.xs[:, h * W // 2:(h + 1) * W // 2:S], AF.Copy, H, [KX[h]], K("x0", h), scale=SH)
+        sact(A("x0", h), T.xs[:, h * W // 2:(h + 1) * W // 2:S], AF.Copy, H, [KX[h]], K("x0", h))
     kx0 = send(s1, [A("x0", 0)], [A("xi", 0)], "rx", K("x0", 0))
     recv("rx", kx0, HOP + LAT["first"], K("xi", 0))
 
-    def gsel(out, in_, pat, op, base, cm, n, r, w, after=()):
-        return add("g", 0.17 + 2 * n * CY, lambda: g.affine_select(out, in_, pat, op, 0.0, base, cm), r, w, extra=after)
-
-    def giota(out, pat, n, w):
-        return add("g", 0.13 + 2 * n * CY, lambda: g.iota(out, pat, 0, 0, allow_small_or_imprecise_dtypes=True), (), w)
-
-    early(vset(T.onb[:, :], 1.0, 128, 0.5, ["onb"]))
-    early(giota(T.iq[:, :], [[0, 8], [1, 16]], 128, ["iq"]))
-    early(gsel(T.idb[:, :], T.onb[:, :], [[-1, 128]], AL.is_equal, 0, 1, 128, ["onb"], ["idb"]))
-    early(gsel(T.blk0[:, :], T.onb[:, :], [[-16, 8], [0, 16]], AL.is_ge, 0, 1, 128, ["onb"], ["blk0"]))
+    early(vset(T.onb[:, :], 1.0, 512, 0.5, ["onb"]))
+    early(add("g", 0.13 + 256 * CY, lambda: g.iota(T.iq[:, :], [[0, 8], [1, 16]], 0, 0, allow_small_or_imprecise_dtypes=True), (), ["iq"]))
+    early(gsel(T.idb[:, :], ONE, [[-1, 128]], AL.is_equal, 0, 1, 128, ["onb"], ["idb"]))
+    early(gsel(T.blk0[:, :], ONE, [[-16, 8], [0, 16]], AL.is_ge, 0, 1, 128, ["onb"], ["blk0"]))
     early(gsel(T.blk[:, :], T.blk0[:, :], [[16, 8], [0, 16]], AL.is_ge, 15, -1, 128, ["blk0"], ["blk"]))
-    vset(T.ed[:, :], 1.0, 2048, 0.5, ["ed"])
-    vset(T.onf[:, :], 1.0, 128, 1, ["onf"])
+    first = len(ops)
     vset(T.ngb[:, :], -1.0, 128, 0.5, ["ngb"])
-    vset(T.cb[:, :], -MID / 128, 512, 0.5, ["cb"])
     for z in ("xz0", "xzn", "xz1"):
         vset(A(z), 0.0, L, 0.5, K(z))
     for q in range(0, 16, 4):
-        gsel(T.ed[:, 128 * q:128 * q + 512], T.ed[:, 128 * q:128 * q + 512], [[-256, 4], [-16, 8], [255, 16]], AL.is_equal, -256 * q, 1, 512, ["ed"], [("ed", q)],
+        gsel(T.ed[:, 128 * q:128 * q + 512], T.onb[:, :], [[-256, 4], [-16, 8], [255, 16]], AL.is_equal, -256 * q, 1, 512, ["onb"], [("ed", q)],
              kx0[:1] if q >= 8 else ())
-        vcopy(T.edh[:, 128 * q:128 * q + 512], T.ed[:, 128 * q:128 * q + 512], 512, 0.5, [("ed", q)], [("edh", q)])
-    KED, KEH = [[(n, q) for q in range(0, 16, 4)] for n in ("ed", "edh")]
-    for name, val in (("ids", SH), ("idh", 1.0), ("idnb", -1.0), ("idn", -1.0), ("idp", BIG), ("idm", -2 * BIG), ("idq", 0.5), ("id18", 18.5)):
-        vmul(T[name][:, :], T.idb[:, :], val, 128, ["idb"], [name])
-    vmul(T.sel[:, 0:128], T.idb[:, :], 1.0, 128, ["idb"], ["idf"], 1)
-    vmul(T.sel[:, 128:256], T.blk[:, :], -1.0 / SH, 128, ["blk"], ["sel"], 1)
-    for name, val in (("blkn", -1.0 / SH), ("blk2", 2.0 / SH)):
-        vmul(T[name][:, 0:128], T.blk[:, :], val, 128, ["blk"], [name])
-        vmul(T[name][:, 128:256], T.blk[:, :], val, 128, ["blk"], [name])
-    vmul(T.onh[:, :], T.onb[:, 0:128], 1.0, 128, ["onb"], ["onh"])
-    vset(T.prow[:, 128:256], 0.0, 128, 0.5, ["prow"])
-    vts(T.prow[:, 0:128], T.iq[:, :], 1.0 / 4096, 1.0 / 8192, AL.mult, AL.add, 128, 1, ["iq"], ["prow"])
+    KED = [("ed", q) for q in range(0, 16, 4)]
+    for name, val in (("ids", SH), ("idn", -1.0), ("idp", BIG), ("idq", 0.5), ("id37", 37.0)):
+        move(QL["const"], T[name][:, :], T.idb[:, :], 128, ["idb"], [name], f=0.5, scale=val)
+    move(QL["const"], T.sel[:, 0:128], T.idb[:, :], 128, ["idb"], ["idf"], scale=SH)
+    move(QL["const"], T.sel[:, 128:256], T.blk[:, :], 128, ["blk"], ["sel"], scale=-1.0)
+    for name, val in (("bkn", -1.0), ("bk2", 2.0)):
+        move("v", T[name][:, 0:128], T.blk[:, :], 128, ["blk"], [name], f=0.5, scale=val / 8192)
+        move("v", T[name][:, 128:256], T.blk[:, :], 128, ["blk"], [name], f=0.5, scale=val)
+    BN, B2 = T.bkn[:, 128:256], T.bk2[:, 128:256]
+    for x in ("pk", "pk2"):
+        vcopy(T[x][:, 256:264], T.blk[:, 0:128:16], 8, 0.5, ["blk"], [x + "B"])
+    move("v", T.prow[:, :], T.iq[:, :], 128, ["iq"], ["prow"], scale=2.0 ** -25, bias=2.0 ** -26)
     vset(T.rst[:, :], 1.0, 128, 1, ["rst"])
     vset(T.rst[:, 0:128:16], 0.0, 8, 1, ["rst"])
     for x in ("thd", "thd2"):
-        vmul(T[x][:, 0:128], T.onb[:, 0:128], MID / 128, 128, ["onb"], [x + "m"])
-    vts(T.thc[:, 0:1], T.thi[:, 0:1], -1.0, 2048.0, AL.mult, AL.add, 1, 1, [("ld4", "ld")], ["thc"])
-    vmul(T.thd[:, 128:256], T.idh[:, :], T.thc[:, 0:1], 128, ["idh", "thc"], ["thd"])
+        move("v", T[x][:, 0:128], ONE, 128, ["onb"], [x + "m"], f=0.5, scale=MID / 128)
+    move("v", T.thc[:, 0:1], T.thi[:, 0:1], 1, [("ld4", "ld")], ["thc"], scale=-1.0, bias=2048.0)
+    vts(T.thd[:, 128:256], T.idb[:, :], T.thc[:, 0:1], None, AL.mult, None, 128, 0.5, ["idb", "thc"], ["thd"])
 
     vcopy(T.tif[:, 0:3], T.tii[:, 0:3], 3, 1, [("ld2", "ld")], ["tif"])
     vcopy(T.sgf[:, 0:3], T.sgi[:, 0:3], 3, 1, [("ld3", "ld")], ["sgf"])
@@ -274,42 +272,40 @@ def rank_program(g, core, T, topo):
     p0 = tile()
     mm(group([(C(0, 128), T.gj[:, :], T.idb[:, :])]), 128, ["gj", "idb"], p0)
     sact(T.pk[:, 0:128], PS(p0, 0, 128), AF.Copy, 128, (), ["pkG"], (p0,))
+    for o in ops[first:]:
+        o["up"] = CUP if o["e"] in "vs" else 0.0
 
-    def copy(e, out, in_, n, r, w, after=()):
-        if e == "v":
-            vcopy(out, in_, n, 0.5, r, w)
-        elif e == "s":
-            sact(out, in_, AF.Copy, n, r, w)
-        else:
-            gsel(out, in_, [[0, n]], AL.is_ge, 0, 0, n, r, w, after)
-
-    def lane_views(buf, z, col, rk, engs, when, after=()):
+    def lane_views(buf, z, col, rk, when, after=()):
+        e = QL[buf]
         for p in range(16):
-            copy(engs[p % len(engs)], T[buf][:, p:HW:16], col(0, H), H, rk[0], [(buf, p)], after)
+            move(e[p % len(e)], T[buf][:, p:HW:16], col(0, H), H, rk[0], [(buf, p)], f=0.5, after=after)
         for h in R2:
-            copy(engs[0], A(z, h, 64, H), col(lane(h, 1), lane(h, 1) + 64), 64, rk[1], K(z, h), after)
+            move(e[0], A(z, h, 64, H), col(lane(h, 1), lane(h, 1) + 64), 64, rk[1], K(z, h), f=0.5, after=after)
         return {"xr": T[buf], "kxr": [(buf, p) for p in range(16)], "z": z, "col": col, "kc": rk[1] + when}
 
     def voters(name, t):
         for h in R2:
             for u in R2:
-                vcopy(A(name, h, 64 * u, 64 * u + 64), T.dgs[:, S * lane(h, u) + t:S * (lane(h, u) + 64):S], 64, 1, [KDG[u]], K(name, h, 2 * u))
+                move(QL["vote"][2 * t + u], A(name, h, 64 * u, 64 * u + 64), T.dgs[:, S * lane(h, u) + t:S * (lane(h, u) + 64):S], 64, [KDG[u]], K(name, h, 2 * u))
 
+    def pack(e, out, x, d, n, rd, w, o=0, p=None):
+        p = tile() if p is None else p
+        mm(group([(C(o, o + n), T.ids[:, :], x), (C(o, o + n), T.idb[:, :], d)]), 2 * n, rd + ["ids", "idb"], p)
+        return move(e, out, PS(p, o, o + n), n, (), w, (p,), scale=1.0 / SH, bias=-MID / SH)
+
+    def table(name, x, kx, d, kd, when=()):
+        for j in range(4):
+            c = C(512 * j, 512 * j + 512)
+            pack(QL[name][j], T[name][:, c], x[:, c], d[:, c], 512, [kx[j // 2], kd[j // 2]] + list(when), [(name, j)])
+        return [(name, j) for j in range(4)]
+
+    X0 = lane_views("xr0", "xz0", lambda a, b: A("x0")[:, a:b], [K("x0", h) for h in R2], [])
+    voters("L0a", 0)
     for h in R2:
         c = C(h * W // 2, (h + 1) * W // 2)
-        if XQE[h] == "s":
-            sact(T.xq[:, c], T.xs[:, c], AF.Copy, W // 2, [KX[h]], [("xq", h)], scale=SH)
-        else:
-            vmul(T.xq[:, c], T.xs[:, c], SH, W // 2, [KX[h]], [("xq", h)])
-    KXQ = [("xq", h) for h in R2]
-    X0 = lane_views("xr0", "xz0", lambda a, b: A("x0")[:, a:b], [K("x0", h) for h in R2], XR0, [])
-    voters("L0a", 0)
-    for j in range(4):
-        c = C(512 * j, 512 * j + 512)
-        p = tile()
-        mm(group([(C(0, 512), T.onb[:, 0:128], T.cb[:, :]), (C(0, 512), T.ids[:, :], T.xs[:, c])]), 1024, [KX[j // 2], KDG[j // 2], "ids", "onb", "cb"], p)
-        vtt(T.P0[:, c], T.dgs[:, c], PS(p, 0, 512), AL.add, 512, 1, [KDG[j // 2]], [("P0", j)], (p,))
-    KP0 = [("P0", j) for j in range(4)]
+        move(QL["dh0"][h], T.dh0[:, c], T.dgs[:, c], W // 2, [KDG[h]], [("dh0", h)])
+    KDH = [("dh0", h) for h in R2]
+    KP0 = table("P0", T.xs, KX, T.dh0, KDH)
 
     par = {}
     turned = set()
@@ -320,82 +316,56 @@ def rank_program(g, core, T, topo):
         n = n % 2 if two else 0
         return n * 16 * L + h * HW, [(buf, n, h, s) for s in range(SB)]
 
-    def gather(eng, buf, o, keys, win, lst, h, u, rd, xr=None):
-        n = 1 if eng in SPLIT else 2
-        for s in range(2 * u, 2 * u + 2, n):
-            def em(s=s):
-                out, src = T[buf][:, o + s * SW:o + (s + n) * SW], win[:, :].indirect(A(lst, h, s * H // SB, (s + n) * H // SB))
-                if eng == "s":
-                    return g.scalar.activation(out, src, AF.Copy)
-                if xr is None:
-                    return g.vector.tensor_copy(out, src)
-                return g.vector.tensor_tensor(out, src, xr[:, (2 * h + s) * SW:(2 * h + s + n) * SW], AL.subtract)
-            ops[add(eng, 0.06 + n * SW * GC * CY, em, rd + K(lst, h, s), keys[s:s + n])]["n"] = n * SW
+    def gather(eng, buf, o, keys, win, lst, h, s, n, rd, xr=None):
+        def em():
+            out, src = T[buf][:, o + s * SW:o + (s + n) * SW], win[:, :].indirect(A(lst, h, s * H // SB, (s + n) * H // SB))
+            if eng == "s":
+                return g.scalar.activation(out, src, AF.Copy)
+            if xr is None:
+                return g.vector.tensor_copy(out, src)
+            return g.vector.tensor_tensor(out, src, xr[:, (2 * h + s) * SW:(2 * h + s + n) * SW], AL.subtract)
+        ops[add(eng, 0.06 + n * SW * GC * CY, em, rd + K(lst, h, s), keys[s:s + n])]["n"] = n * SW
 
-    def own_rows(p, u, src, o, ed, rd, last=True):
+    def own_rows(p, u, src, o, rd, last=True):
         o += u * HW // 2
-        mm([(C(64 * u, 64 * u + 64), ed[:, q * 128:(q + 1) * 128], src[:, o + q:o + HW // 2:16], q == 0, last and q == 15) for q in range(16)], 1024, rd, p)
+        mm([(C(64 * u, 64 * u + 64), T.ed[:, q * 128:(q + 1) * 128], src[:, o + q:o + HW // 2:16], q == 0, last and q == 15) for q in range(16)], 1024, rd + KED, p)
 
-    def own_packed(p, buf, o, keys, cols, last):
-        for q0 in range(0, 16, 4):
-            mm(more([(C(q, cols, 16), T[buf][:, o + q:o + HW:16], T.sel[:, q:cols:16]) for q in range(q0, q0 + 4)], last and q0 == 12), 1024, keys + ["idf", "sel"], p)
-
-    def unpack(t, k, p, h, Lk, hk):
-        if (t, k) in TS:
-            sact(A("ut", h), PS(p, 0, H), AF.Identity, H, (), K("ut", h), (p,), bias=MAGIC)
-            sact(A("tt", h), A("ut", h), AF.Identity, H, K("ut", h), K("tt", h), bias=-MAGIC)
-        else:
-            vts(A("tt", h), PS(p, 0, H), MAGIC, MAGIC, AL.add, AL.subtract, H, 1, (), K("tt", h), (p,))
-        vtt(A(hk, h), PS(p, 0, H), A("tt", h), AL.subtract, H, 1, K("tt", h), K(hk, h), (p,))
-        turned.add((hk, h))
-        p2 = tile()
-        mm(group([(C(0, H), A(hk, h), T.idh[:, :])]), 128, K(hk, h) + ["idh"], p2)
-        vcopy(A(Lk, h), PS(p2, 0, H), H, 1, (), K(Lk, h), (p2,))
-
-    def column(t, k, eng, lst, h, Lk, hk):
-        if eng == "v":
-            o, keys = room("gh", h, False)
-            for u in R2:
-                gather("v", "gh", o, keys, T.dgs, lst, h, u, KDG)
-            for u in R2:
-                p = tile()
-                s = u * SB // 2
-                own_rows(p, u, T.gh, o, T.edh, keys[s:s + SB // 2] + KEH)
-                vcopy(A(Lk, h, 64 * u, 64 * u + 64), PS(p, 64 * u, 64 * u + 64), 64, 1, (), K(Lk, h, s), (p,))
-            if hk != "hA":
-                vcopy(A(hk, h), A(Lk, h), H, 0.5, K(Lk, h), K(hk, h))
-        else:
-            o, keys = room("gf", h, False)
-            for u in R2:
-                gather("s", "gf", o, keys, T.P0, lst, h, u, KP0)
+    def column(t, k, lst, h, Lk, hk):
+        o, keys = room("gh", h, False)
+        e = CV[t, k]
+        for s in (0, 2):
+            if e[s] == e[s + 1]:
+                gather(e[s], "gh", o, keys, T.dgs, lst, h, s, 2, KDG)
+            else:
+                for x in (s, s + 1):
+                    gather(e[x], "gh", o, keys, T.dgs, lst, h, x, 1, KDG)
+        for u in R2:
             p = tile()
-            mm([(C(0, H), T.onh[:, :], T.thd[:, 0:H], True, False)], 128, ["onh", "thdm", keys[0]], p)
-            own_packed(p, "gf", o, keys, H, True)
-            unpack(t, k, p, h, Lk, hk)
+            own_rows(p, u, T.gh, o, keys[2 * u:2 * u + 2])
+            move(QL["col"][u], A(Lk, h, 64 * u, 64 * u + 64), PS(p, 64 * u, 64 * u + 64), 64, (), K(Lk, h, 2 * u), (p,))
+        if hk:
+            move(QL["colh"], A(hk, h), A(Lk, h), H, K(Lk, h), K(hk, h), f=0.5)
 
     def view(t, k, win, kw, lst, h, X, packed):
         buf = "zf" if packed else "zb"
         o, keys = room(buf, h)
         ao, ak = room("ab", h)
-        gather("v", buf, o, keys, win, lst, h, 0, kw + X["kxr"], X["xr"])
-        gather("s", buf, o, keys, win, lst, h, 1, kw)
-        sact(T.ab[:, ao:ao + 2 * SW], T[buf][:, o:o + 2 * SW], AF.Relu, 2 * SW, keys[0:2], ak[0:2])
-        for s in (2, 3):
-            if (h, s) not in X:
-                X[h, s] = tile()
-                a = lane(h, 1) + 32 * (s - 2)
-                mm([(C(q, SW, 16), T.idb[:, :], X["col"](a, a + 32), True, True) for q in range(16)], 1024, ["idb"] + X["kc"], X[h, s])
-            vtt(T.ab[:, ao + s * SW:ao + (s + 1) * SW], T[buf][:, o + s * SW:o + (s + 1) * SW], PS(X[h, s], 0, SW), AL.max, SW, 1, [keys[s]], [ak[s]], (X[h, s],))
-        return {"buf": buf, "o": o, "keys": keys, "ao": ao, "ak": ak, "packed": packed, "z": X["z"], "h": h}
+        gather("v", buf, o, keys, win, lst, h, 0, 2, kw + X["kxr"], X["xr"])
+        gather("s", buf, o, keys, win, lst, h, 2, 2, kw)
+        if (t, k, h) in RV:
+            vts(T.ab[:, ao:ao + 2 * SW], T[buf][:, o:o + 2 * SW], 0.0, None, AL.max, None, 2 * SW, 0.5, keys[0:2], ak[0:2])
+        else:
+            sact(T.ab[:, ao:ao + 2 * SW], T[buf][:, o:o + 2 * SW], AF.Relu, 2 * SW, keys[0:2], ak[0:2])
+        if h not in X:
+            X[h] = tile(2)
+            for s in R2:
+                a = lane(h, 1) + 32 * s
+                mm([(C(SW * s + q, SW * s + SW, 16), T.idb[:, :], X["col"](a, a + 32), True, True) for q in range(16)], 1024, ["idb"] + X["kc"], X[h])
+        vtt(T.ab[:, ao + 2 * SW:ao + 4 * SW], T[buf][:, o + 2 * SW:o + 4 * SW], PS(X[h], 0, 2 * SW), AL.max, 2 * SW, 1, keys[2:4], ak[2:4], (X[h],))
+        return {"o": o, "keys": keys, "ao": ao, "ak": ak, "z": X["z"]}
 
     def sums(buf, o, sel, a, b):
         return [(C(a + q, b, 16), T[buf][:, o + q:o + HW:16], sel[:, 0:b - a:16]) for q in range(16)]
-
-    def less(v, a, b):
-        lst, rd = [(C(a, b), A(v["z"], v["h"]), T.blkn[:, 0:b - a])], K(v["z"], v["h"]) + ["blkn"]
-        if not v["packed"]:
-            lst, rd = lst + sums("zb", v["o"], T.blkn, a, b), rd + v["keys"]
-        return lst, rd
 
     def turn(c, name, h, ident):
         return (c, ident, A(name, h)) if (name, h) in turned else (c, A(name, h), ident)
@@ -406,7 +376,7 @@ def rank_program(g, core, T, topo):
     def change(t, k, h):
         a, b = "h%d_%d" % (k - 1, t), "h%d_%d" % (k, t)
         c = C(2 * H, 3 * H)
-        return group([turn(c, a, h, T.idh[:, :]), turn(c, b, h, T.idn[:, :])]), K(a, h) + K(b, h) + ["idh", "idn"]
+        return group([turn(c, a, h, T.idb[:, :]), turn(c, b, h, T.idn[:, :])]), K(a, h) + K(b, h) + ["idb", "idn"]
 
     def flagged(t, k, h, fk, q):
         mk = "m%d_%d" % (k, t)
@@ -418,24 +388,31 @@ def rank_program(g, core, T, topo):
         q = tile()
         a = 0 if packed else H
         pre, rd = change(t, k, h) if here else ([], [])
-        mm(pre + [(C(a, 2 * H), T.onh[:, :], thd[:, a:2 * H], True, False)], 512, rd + ["onh", v["keys"][0]] + kth, q)
-        lst, rd = less(v, H, 2 * H)
-        if lst:
-            mm(more(lst), 64 + 64 * len(lst), rd, q)
+        mm(pre + [(C(a, 2 * H), ONE, thd[:, a:2 * H], True, False), (C(H, 2 * H), A(v["z"], h), BN, False, False)], 128 * len(pre) + 3 * H - a,
+           rd + ["onb", "bkn", v["keys"][0]] + kth + K(v["z"], h), q)
         if packed:
-            own_packed(q, "zf", v["o"], v["keys"], 2 * H, False)
-        lst, rd = sums("ab", v["ao"], T.blk2, H, 2 * H), v["ak"] + ["blk2"]
+            for q0 in range(0, 16, 4):
+                mm(more([(C(x, 2 * H, 16), T.zf[:, v["o"] + x:v["o"] + HW:16], T.sel[:, x:2 * H:16]) for x in range(q0, q0 + 4)]), 1024, v["keys"] + ["idf", "sel"], q)
+        else:
+            mm(more(sums("zb", v["o"], BN, H, 2 * H)), 1024, v["keys"], q)
+        lst, rd = sums("ab", v["ao"], B2, H, 2 * H), v["ak"] + ["bk2"]
         if k > 1:
             fp = "f%d_%d" % (k - 1, t)
             lst, rd = lst + [(C(H, 2 * H), T.idp[:, :], A(fp, h))], rd + K(fp, h) + ["idp"]
         mm(more(lst, True), 1024 + 128, rd, q)
         if packed:
-            unpack(t, k + 1, q, h, "L%d_%d" % (k + 1, t), "h%d_%d" % (k + 1, t))
+            hk, Lk = "h%d_%d" % (k + 1, t), "L%d_%d" % (k + 1, t)
+            vts(A("tt", h), PS(q, 0, H), MAGIC, MAGIC, AL.add, AL.subtract, H, 1, (), K("tt", h), (q,))
+            vtt(A(hk, h), PS(q, 0, H), A("tt", h), AL.subtract, H, 1, K("tt", h), K(hk, h), (q,))
+            turned.add((hk, h))
+            p = tile()
+            mm(group([(C(0, H), A(hk, h), T.idb[:, :])]), 128, K(hk, h) + ["idb"], p)
+            move(QL["list"], A(Lk, h), PS(p, 0, H), H, (), K(Lk, h), (p,))
         sact(A(fk, h), PS(q, H, 2 * H), AF.Sign, H, (), K(fk, h), (q,), bias=0.5 - 2048.0 + (BIG if k > 1 else 0.0))
         if here:
             flagged(t, k, h, fk, q)
 
-    def walk(t, h, tb, X, kq, ut):
+    def walk(t, h, tb, X, ut):
         for k in (2, 3, 4):
             win, kw = (tb["P"], tb["kp"]) if k < 4 else (tb["X"], tb["kx"])
             step(t, k, h, win, kw, "L%d_%d" % (k, t), X, tb["thd"], tb["kth"], "f%d_%d" % (k, t), k < 4)
@@ -445,69 +422,69 @@ def rank_program(g, core, T, topo):
         terms = ["h0_%d" % t, "h4_%d" % t] + ["m%d_%d" % (k, t) for k in (1, 2, 3, 4)]
         kt = sum([K(x, h) for x in terms], [])
         p = tile()
-        mm(group([back(C(0, H), x, h, T.idq[:, :]) for x in terms]), 6 * 128, kt + ["idq"], p)
-        vcopy(A(LF, h), PS(p, 0, H), H, 1, (), K(LF, h), (p,))
+        lst = group([back(C(0, H), x, h, T.idq[:, :]) for x in terms])
+        mm(lst[:5], 5 * 128, kt[:10] + ["idq"], p)
+        mm(lst[5:], 128, kt[10:], p)
+        move(QL["LF"], A(LF, h), PS(p, 0, H), H, (), K(LF, h), (p,))
+        move(QL["hE"], A("hE", h), PS(p, 0, H), H, (), K("hE", h), (p,))
         if t == 1:
             for u in R2:
-                sact(A("yef")[:, lane(h, u):lane(h, u) + 64], PS(p, 64 * u, 64 * u + 64), AF.Copy, 64, (), K("yef", h, 2 * u), (p,))
+                move(QL["ye"], A("yef")[:, lane(h, u):lane(h, u) + 64], A("hE", h, 64 * u, 64 * u + 64), 64, K("hE", h), K("yef", h, 2 * u))
         yield
-        v = view(t, 5, tb["X"], tb["kx"], LF, h, X, False)
-        cur[0] = -LEAD if h == 0 else cur[0]
-        p2 = tile()
-        if (t, h) in BT:
-            p1 = tile()
-            mm(group([(C(0, H), A(v["z"], h), T.idnb[:, :])] + [(C(q, H, 16), T.ab[:, v["ao"] + q:v["ao"] + HW:16], T.idb[:, q:H:16]) for q in range(16)]),
-               1024 + 128, v["ak"] + K(v["z"], h) + ["idb", "idnb"], p1)
-            sact(A("bt", h), PS(p1, 0, H), AF.Sign, H, (), K("bt", h), (p1,), bias=-0.5)
-            mm(group([(C(0, H), A("bt", h), T.idb[:, :])]), H, K("bt", h) + ["idb"], p2)
-        else:
-            for u in R2:
-                s = u * SB // 2
-                y = u == 1
-                own_rows(p2, u, T.zb, v["o"], T.ed, v["keys"][s:s + SB // 2] + KED, not y)
-                if y:
-                    mm(more([(C(64, H), T.idnb[:, :], A(v["z"], h, 64, H))], True), 64, K(v["z"], h) + ["idnb"], p2)
-        sact(A("bs", h), PS(p2, 0, H), AF.Sign, H, (), K("bs", h), (p2,), bias=-0.5)
-        p4 = tile()
-        mm(group([(C(0, H), tb["GT"], A("bs", h))]), H, K("bs", h) + [tb["kgt"]], p4)
-        sact(A("sq", h), PS(p4, 0, H), AF.Square, H, (), K("sq", h), (p4,))
-        p5 = tile()
-        mm(group([(C(0, H), tb["aG"], T.ngb[:, :]), (C(0, H), tb["aG"], A("sq", h))]) + group([(C(H, H + 8), A("sq", h), T.blk[:, 0:128:16])]),
-           2 * H + 64, K("sq", h) + [tb["kag"], "blk", "ngb"], p5)
-        sact(A("ch", h), PS(p5, 0, H), AF.Sign, H, (), K("ch", h), (p5,))
-        sact(A("any", h, 0, 8), PS(p5, H, H + 8), AF.Sign, 8, (), K("any", h) + [("asum", h)], (p5,), bias=-16.0, acc=T.asum[:, h:h + 1])
-        p = kq[h] = tile()
-        c = C(H * h, H * h + H)
-        lst, rd = less(v, 0, 2 * H)
-        mm([(C(0, 2 * H), T.onb[:, :], T.prow[:, :], True, False)] + more([turn(C(H, 2 * H), x, h, T.id18[:, :]) for x in terms]),
-           8 * 128, kt + ["onb", "prow", "id18", v["keys"][0]], p)
-        if lst:
-            mm(more(lst), 256 + 64 * len(lst), rd, p)
-        mm(more(sums("ab", v["ao"], T.blk2, 0, 2 * H)), 1024, v["ak"] + ["blk2"], p)
-        mm(more([(C(0, H), A("ch", h), T.idm[:, :])], True), H, K("ch", h) + ["idm"], p)
-        a, b = T.pm[:, 2 * H * h:2 * H * h + H], C(2 * H * h + H - 1, 2 * H * h - 1 if h else None, -1)
-        add("v", vt(H, 1), lambda: g.vector.tensor_tensor_scan(a, T.rst[:, :], ps(p)[:, 0:H], 0.0, AL.mult, AL.min), ["rst"], [("pm", h)], (p,))
-        add("v", vt(H, 1), lambda: g.vector.tensor_tensor_scan(T.pm[:, 2 * H * h + 2 * H - 1:2 * H * h + H - 1:-1], T.rst[:, :], T.pm[:, b], 0.0, AL.mult, AL.min),
-            ["rst", ("pm", h)], [("pn", h)])
-        vtt(T.eq[:, c], T.pm[:, 2 * H * h + H:2 * H * h + 2 * H], PS(p, 0, H), AL.is_equal, H, 1, [("pn", h)], [("eq", h)], (p,))
-        mm(group([turn(C(L + H * h, L + H * h + H), terms[0], h, T.idh[:, :])]) + group([(c, A("ch", h), T.idb[:, :]), (c, T.idnb[:, :], T.eq[:, c])]), 384,
-           K("ch", h) + K(terms[0], h) + ["idb", "idnb", "idh", ("eq", h)], ut)
+        ballot(t, h, tb, X, ut)
         yield
 
-    def finish(t, out, kq, ut):
+    def ballot(t, h, tb, X, ut):
+        v = view(t, 5, tb["X"], tb["kx"], "LF_%d" % t, h, X, False)
+        qt, gt, at = ut
         D0 = "h0_%d" % t
+        lanes = [C(lane(h, u), lane(h, u) + 64) for u in R2]
+        part = [C(64 * u, 64 * u + 64) for u in R2]
         p = tile()
-        mm(group([(C(0, 1), T.onf[:, 0:128], T.asum[:, h:h + 1]) for h in R2]), 512, [("asum", h) for h in R2] + ["onf"], p)
-        sact(T.acol[:, 0:1], PS(p, 0, 1), AF.Copy, 1, (), ["acol"], (p,))
-        for h in R2:
-            vts(A("qi", h), PS(kq[h], H, 2 * H), T.acol[:, 0:1], None, AL.add, None, H, 1, ["acol"], K("qi", h), (kq[h],))
+        for u in R2:
+            own_rows(p, u, T.zb, v["o"], v["keys"][2 * u:2 * u + 2], u == 0)
+        mm(more([(C(64, H), T.idn[:, :], A(v["z"], h, 64, H))], True), 64, K(v["z"], h) + ["idn"], p)
+        sact(A("bs", h), PS(p, 0, H), AF.Sign, H, (), K("bs", h), (p,), bias=-0.5)
+        mm(group([(C(H, 2 * H), tb["GT"], A("bs", h))]), H, K("bs", h) + [tb["kgt"]], p)
+        sact(A("sq", h), PS(p, H, 2 * H), AF.Square, H, (), K("sq", h), (p,))
+        c = C(2 * H, 3 * H + 8)
+        mm(group([(c, T.ngb[:, :], tb["aG"]), (c, A("sq", h), tb["aG"])]), 2 * H + 16, K("sq", h) + tb["kag"] + ["ngb"], p)
+        o = 144 * h
+        ch = T.chb[:, o:o + H]
+        sact(T.chb[:, o:o + H + 8], PS(p, 2 * H, 3 * H + 8), AF.Sign, H + 8, (), K("ch", h), (p,))
+        mm([(C(0, 8), ONE, T.chb[:, o + H:o + H + 8], h == 0, h == 1)], 64, K("ch", h) + ["onb"], at)
+        p = tile()
+        mm([(C(0, 2 * H), A(v["z"], h), T.bkn[:, :], True, False), (C(0, H), ONE, T.prow[:, :], False, False)], 3 * H,
+           K(v["z"], h) + ["onb", "prow", "bkn", v["keys"][0]], p)
+        for buf, off, sel, rd in (("zb", v["o"], T.bkn, v["keys"]), ("ab", v["ao"], T.bk2, v["ak"] + ["bk2"])):
+            lst = more(sums(buf, off, sel, 0, 2 * H), buf == "ab")
+            for q in range(0, 16, CUT):
+                mm(lst[q:q + CUT], 64 * CUT, rd, p)
+        sact(A("dh", h), PS(p, H, 2 * H), AF.Identity, H, (), K("dh", h), (p,), bias=-2040.0)
+        mm(sum([group([(lanes[u], T.id37[:, :], A("hE", h)[:, part[u]]), (lanes[u], A("dh", h), T.idb[:, part[u]])]) for u in R2], []), 256,
+           K("hE", h) + K("dh", h) + ["id37", "idb"], qt)
+        mm(sum([group([(C(L + lane(h, u), L + lane(h, u) + 64), T.idb[:, :], A(D0, h)[:, part[u]])]) for u in R2], []), 128, K(D0, h) + ["idb"], qt)
+        key = PS(p, 0, H)
+        vtt(key, key, ch, AL.subtract, H, 1, K("ch", h), [("key", h)], (p,))
+        a, b = T.pm[:, 2 * H * h:2 * H * h + H], C(2 * H * h + H - 1, 2 * H * h - 1 if h else None, -1)
+        add("v", vt(H, 1), lambda: g.vector.tensor_tensor_scan(a, T.rst[:, :], R(key), 0.0, AL.mult, AL.min), ["rst", ("key", h)], [("pm", h)], (p,))
+        add("v", vt(H, 1), lambda: g.vector.tensor_tensor_scan(T.pm[:, 2 * H * h + 2 * H - 1:2 * H * h + H - 1:-1], T.rst[:, :], T.pm[:, b], 0.0, AL.mult, AL.min),
+            ["rst", ("pm", h)], [("pn", h)])
+        vtt(A("eq", h), T.pm[:, 2 * H * h + H:2 * H * h + 2 * H], key, AL.is_equal, H, 1, [("pn", h), ("key", h)], K("eq", h), (p,))
+        mm(sum([group([(lanes[u], ch, T.idb[:, part[u]]), (lanes[u], A("eq", h), T.idn[:, part[u]])]) for u in R2], []), 256,
+           K("ch", h) + K("eq", h) + ["idb", "idn"], gt)
+
+    def finish(out, ut):
+        qt, gt, at = ut
+        sact(T.asum[:, 0:8], PS(at, 0, 8), AF.Identity, 8, (), ["acol"], (at,), bias=2040.0 / 8, acc=T.acol[:, 0:1])
+        if QL["qi"] == "s":
+            sact(A("qi"), PS(qt, 0, L), AF.Identity, L, ["acol"], K("qi"), (qt,), bias=T.acol[:, 0:1])
+        else:
+            vts(A("qi"), PS(qt, 0, L), T.acol[:, 0:1], None, AL.add, None, L, 1, ["acol"], K("qi"), (qt,))
         vts(A("ni"), A("qi"), W - 1, None, AL.bitwise_and, None, L, 1, K("qi"), K("ni"))
-        vtt(A("wd"), A("ni"), PS(ut, L, 2 * L), AL.subtract, L, 1, K("ni"), K("wd"), (ut,))
-        vtt(A("mh"), A("wd"), PS(ut, 0, L), AL.mult, L, 1, K("wd"), K("mh"), (ut,))
-        p = tile()
-        mm(sum([group([(C(lane(h, u), lane(h, u) + 64), T.idh[:, :], A(D0, h, 64 * u, 64 * u + 64)), (C(lane(h, u), lane(h, u) + 64), A("mh", h), T.idh[:, 64 * u:64 * u + 64])])
-                for h in R2 for u in R2], []), 512, K(D0) + K("mh") + ["idh"], p)
-        vcopy(A(out), PS(p, 0, L), L, 1, (), K(out), (p,))
+        vtt(A("wd"), A("ni"), PS(qt, L, 2 * L), AL.subtract, L, 1, K("ni"), K("wd"), (qt,))
+        vtt(A("mh"), A("wd"), PS(gt, 0, L), AL.mult, L, 1, K("wd"), K("mh"), (gt,))
+        vtt(A(out), A("mh"), PS(qt, L, 2 * L), AL.add, L, 1, K("mh"), K(out), (qt,))
 
     def run(gens):
         gens = list(enumerate(gens))
@@ -524,13 +501,13 @@ def rank_program(g, core, T, topo):
         cur[0] = 0
 
     def home0(h):
-        column(0, 1, "v" if (0, h) in G0V else "s", "L0a", h, "L1a", "hA")
+        column(0, 1, "L0a", h, "L1a", None)
         out, to = [("L1a", h), ("L0a", h)] + [("x0", 1)] * (1 - h), [("L1i", h), ("L0i", h)] + [("xi", 1)] * (1 - h)
         k = send(s1, [A(*x) for x in out], [A(*x) for x in to], "re%d" % h, sum([K(*x) for x in out], []))
         recv("re%d" % h, k, HOP, sum([K(*x) for x in to], []))
         sent.append(k[0])
         yield
-        step(0, 1, h, T.xq, KXQ, "L1a", X0, T.thd, ["thd"], "f1a", False, False)
+        step(0, 1, h, T.xs, KX, "L1a", X0, T.thd, ["thd"], "f1a", False, False)
         yield
 
     sent = []
@@ -539,155 +516,220 @@ def rank_program(g, core, T, topo):
         k = send(s1, [A("f1a", h)], [A("f1_0", h)], "rr%d" % h, K("f1a", h), sent)
         recv("rr%d" % h, k, LAT["flags"], K("f1_0", h))
         sent.append(k[0])
-    k = ka = send(h2, [T.P0[:, 0:W // 2]], [T.P2[:, 0:W // 2]], "rxq", KP0, sent, "ltab")
-    recv("rxq", k, LAT["xq"], [("P2", 0)])
-    XN = lane_views("xrn", "xzn", lambda a, b: A("xi")[:, a:b], [K("xi", h) for h in R2], XRN, K(*XNW), sent[:1])
-
-    k = send(h2, [T.P0[:, W // 2:W]], [T.P2[:, W // 2:W]], "rtab", KP0, (k[0],), "ltab")
-    add("n", 0.0, None, KP0, (), (), "ltab", ka[1] + k[1], LAT["tab"], [k[0]])
-    recv("rtab", k, LAT["tab"], [("P2", 1)])
-    KP2 = [("P2", h) for h in R2]
+    k = send(h2, [T.dh0[:, :]], [T.dh2[:, :]], "rdh", KDH, sent)
+    recv("rdh", k, LAT["dh"], ["dh2"])
+    XN = lane_views("xrn", "xzn", lambda a, b: A("xi")[:, a:b], [K("xi", h) for h in R2], K(*XNW), sent[:1])
+    k = send(h2, [T.xs[:, :]], [T.xs2[:, :]], "rxs", KX, (k[0],))
+    recv("rxs", k, LAT["tab"], ["xs2"])
     k = send(h2, [T.pk[:, 0:128], T.pk[:, 128:256], T.thd[:, 128:256]], [T.pk2[:, 0:128], T.pk2[:, 128:256], T.thd2[:, 128:256]], "rpk", ["pkA", "pkG", "thd"], (k[0],))
     recv("rpk", k, LAT["tab"], ["pk2"])
     ktab = k[0]
 
     def away0(h):
-        vcopy(A("h0_0", h), A("L0i", h), H, 0.5, K("L0i", h), K("h0_0", h))
-        vcopy(A("h1_0", h), A("L1i", h), H, 0.5, K("L1i", h), K("h1_0", h))
-        column(0, 2, "v" if h in G1V else "s", "L1i", h, "L2_0", "h2_0")
+        for x in "01":
+            move(QL["h0"], A("h%s_0" % x, h), A("L%si" % x, h), H, K("L%si" % x, h), K("h%s_0" % x, h), f=0.5)
+        column(0, 2, "L1i", h, "L2_0", "h2_0")
         q = tile()
         lst, rd = change(0, 1, h)
         mm(lst, 256, rd + K("f1_0", h), q)
         flagged(0, 1, h, "f1_0", q)
         yield
-        yield from walk(0, h, tb, XN, qt, ut)
+        yield from walk(0, h, tb, XN, ut)
 
-    tb = {"P": T.P0, "kp": KP0, "X": T.xq, "kx": KXQ, "thd": T.thd, "kth": ["thd", "thdm"],
-          "GT": T.pk[:, 0:128], "kgt": "pkG", "aG": T.pk[:, 128:256], "kag": "pkA"}
-    qt, ut = {}, tile()
+    tb = {"P": T.P0, "kp": KP0, "X": T.xs, "kx": KX, "thd": T.thd, "kth": ["thd", "thdm"],
+          "GT": T.pk[:, 0:128], "kgt": "pkG", "aG": T.pk[:, 128:264], "kag": ["pkA", "pkB"]}
+    ut = (tile(), tile(), tile())
     run(away0(h) for h in R2)
-    finish(0, "ndo", qt, ut)
+    finish("ndo", ut)
     k = send(dest(rank - 1), [A("ndo")], [A("ndi")], "rnh", K("ndo"))
     recv("rnh", k, HOP, K("ndi"))
     k = send(dest(rank - 3), [A("ndo")], [A("nd2")], "rn2", K("ndo"), (k[0],))
     recv("rn2", k, HOP, K("nd2"))
 
     voters("L0b", 1)
-    vcopy(A("h0_1"), A("L0b"), L, 0.5, K("L0b"), K("h0_1"))
-    X1 = lane_views("xr1", "xz1", lambda a, b: T.xq[:, S * a + 1:S * b:S], [KXQ, KXQ], XR1, K(*X1W), (ktab,))
-    for j in range(4):
-        c = C(512 * j, 512 * j + 512)
-        sact(T.P1[:, c], T.P2[:, c], AF.Identity, 512, [KP2[j // 2]] + K(*XQ2), [("P1", j)], bias=MAGIC)
-        sact(T.xq2[:, c], T.P1[:, c], AF.Identity, 512, [("P1", j)], [("xq2", j)], bias=-MAGIC)
-        p = tile()
-        mm(group([(C(0, 512), T.idnb[:, :], T.xq2[:, c]), (C(0, 512), T.idb[:, :], T.xq[:, c])]), 2 * 512, [("xq2", j), "idb", "idnb"] + KXQ + K("wd"), p)
-        vtt(T.P1[:, c], T.P2[:, c], PS(p, 0, 512), AL.add, 512, 1, [KP2[j // 2]] + K("ndo"), [("P1", j)], (p,))
-    KP1, KXQ2 = [[(n, j) for j in range(4)] for n in ("P1", "xq2")]
+    move(QL["h0"], A("h0_1"), A("L0b"), L, K("L0b"), K("h0_1"), f=0.5)
+    X1 = lane_views("xr1", "xz1", lambda a, b: T.xs[:, S * a + 1:S * b:S], [KX, KX], K(*X1W), (ktab,))
+    KP1 = table("P1", T.xs, KX, T.dh2, ["dh2"] * 2, K(*PW1))
+    KP2 = table("P2", T.xs2, ["xs2"] * 2, T.dh2, ["dh2"] * 2, K(*PW1))
 
-    def packed(c, xq, nd):
-        return group([(c, T.onb[:, 0:128], T.cb[:, 0:L]), (c, T.idb[:, :], xq[:, 0:W:S]), (c, T.idh[:, :], A(nd))])
-
-    vcopy(T.dgs[:, 0:W:S], A("ndi"), L, 1, K("ndi"), KDG)
-    p = tile()
-    mm(packed(C(0, L), T.xq, "ndi") + group([(C(L, 2 * L), T.idh[:, :], A("ndi"))]), 4 * L, K("ndi") + KXQ + ["idb", "idh", "onb", "cb"], p)
-    sact(T.P0[:, 0:W:S], PS(p, 0, L), AF.Copy, L, (), KP0, (p,))
-    sact(A("yd0"), PS(p, L, 2 * L), AF.Copy, L, (), K("yd0"), (p,))
+    move(QL["patch"], T.dgs[:, 0:W:S], A("ndi"), L, K("ndi"), KDG)
+    sact(A("yd0"), A("ndi"), AF.Copy, L, K("ndi"), K("yd0"))
     add("y", 0.1, lambda: g.sync.dma_start(T.yd[:, 0:L], A("yd0")), K("yd0"), (), (), "ld5", 16, 2.0)
-    p = tile()
-    mm(packed(C(0, L), T.xq, "nd2") + packed(C(L, 2 * L), T.xq2, "nd2"), 6 * L, K("nd2") + KXQ + KXQ2 + ["idb", "idh", "onb", "cb"], p)
-    ops[-1]["up"] = ops[sact(T.P1[:, 0:W:S], PS(p, 0, L), AF.Copy, L, (), KP1, (p,))]["up"] = PUP
-    sact(T.P2[:, 0:W:S], PS(p, L, 2 * L), AF.Copy, L, (), KP2, (p,))
+    k = pack("s", T.P1[:, 0:W:S], T.xs[:, 0:W:S], A("nd2"), L, K("nd2") + KX, KP1)
+    ops[k]["up"] = ops[k - 1]["up"] = PUP
+    pack("s", T.P2[:, 0:W:S], T.xs2[:, 0:W:S], A("nd2"), L, K("nd2") + ["xs2"], KP2)
 
     def home1(h):
-        column(1, 1, "v" if (1, h) in G0V else "s", "L0b", h, "L1b", "h1_1")
+        column(1, 1, "L0b", h, "L1b", "h1_1")
         yield
         step(1, 1, h, T.P1, KP1, "L1b", X1, T.thd, ["thd", "thdm"], "f1_1", True)
         yield
-        yield from walk(1, h, tb, X1, qt, ut)
+        yield from walk(1, h, tb, X1, ut)
 
-    tb = {"P": T.P2, "kp": KP2, "X": T.xq2, "kx": KXQ2, "thd": T.thd2, "kth": ["pk2", "thd2m"],
-          "GT": T.pk2[:, 0:128], "kgt": "pk2", "aG": T.pk2[:, 128:256], "kag": "pk2"}
-    qt, ut = {}, tile()
+    tb = {"P": T.P2, "kp": KP2, "X": T.xs2, "kx": ["xs2"], "thd": T.thd2, "kth": ["pk2", "thd2m"],
+          "GT": T.pk2[:, 0:128], "kgt": "pk2", "aG": T.pk2[:, 128:264], "kag": ["pk2", "pk2B"]}
+    ut = (tile(), tile(), tile())
     run(home1(h) for h in R2)
     add("y", 0.1, lambda: g.sync.dma_start(T.ye[:, :], A("yef")), K("yef"), (), (), "ld6", 16, 2.0)
-    finish(1, "yd1", qt, ut)
+    finish("yd1", ut)
     add("y", 0.1, lambda: g.sync.dma_start(T.yd[:, L:2 * L], A("yd1")), K("yd1"), (), (), "ld7", 16, 2.0)
 
-    order = schedule(ops, tiles, bankof)
+    order = schedule(ops, tiles, wide, bankof)
     emit(g, T, ENG, CSEM, ops, order, cnt["l"])
 
 
+CUP = 3.0
 PW = 0.02
-TURNS, SKEWS, WEIGHTS = 4, (2.0, 3.0), tuple((a, b) for a in (0.3, 0.5, 1.0) for b in (0.2, 0.25, 0.3))
-CASES = ((1.15, 1.0), (1.3, 1.4), (1.5, 1.0), (1.9, 1.2))
+TURNS, SKEWS, WEIGHTS = 3, (2.0, 3.0), tuple((a, b) for a in (0.3, 0.5, 1.0) for b in (0.2, 0.3))
+CASES = ((1.5, 1.0, 0.9), (1.15, 1.05, 0.8), (1.9, 1.4, 1.2), (1.2, 1.35, 1.0), (1.9, 1.1, 1.1), (1.4, 1.1, 1.4))
+SHAKES, SWAPS = 600, 3000
+SEML, SEMQ = 0.08, 0.04
 MADE = {}
-SEML = 0.1
 
 
-def schedule(ops, tiles, bankof):
+def times(ops, case):
+    gc, f, hop = case
+    return ([(o["d"] - o.get("n", 0) * GC * CY) * (f if o["e"] in "vspg" else 1.0) + o.get("n", 0) * gc * CY for o in ops], [o["lat"] * hop for o in ops])
+
+
+def draw(seed):
+    return (seed * 1103515245 + 12345) % 2 ** 31
+
+
+def schedule(ops, tiles, wide, bankof):
     n = len(ops)
-    succ = [[] for _ in range(n)]
-    for k in range(n):
-        for d in ops[k]["deps"]:
-            succ[d].append(k)
-    bl = [0.0] * n
-    for k in range(n - 1, -1, -1):
-        o = ops[k]
-        bl[k] = o["d"] + o["lat"] + max([bl[s] for s in succ[k]] + [0.0])
-    key = (tuple(bl), tuple(o["e"] for o in ops), TURNS, WEIGHTS, SKEWS, SEML)
+    key = (tuple(o["d"] for o in ops), tuple(o["e"] for o in ops))
     if key not in MADE:
-        tries = []
-        for skew in SKEWS:
-            first = forwards(ops, tiles, succ, [PW * (bl[k] - skew * ops[k]["c"]) + ops[k]["up"] for k in range(n)])
-            for ahead, back in WEIGHTS:
-                last = first
-                for turn in range(TURNS):
-                    if last is None:
-                        break
-                    tries.append(last)
-                    far = backwards(ops, succ, last[0], back)
-                    last = forwards(ops, tiles, succ, [ahead * far[k] + ops[k]["up"] for k in range(n)])
-        MADE[key] = min(tries, key=lambda x: sum(replay(ops, x[1], x[3], gc, hop) / gc ** 0.5 for gc, hop in CASES))
-    fin, order, banks, more = MADE[key]
+        eng = [o["e"] for o in ops]
+        pre = [[(d, SEML if eng[d] != eng[k] else 0.0 if eng[k] == "p" or d in ops[k]["soft"] else SEMQ) for d in sorted(ops[k]["deps"])] for k in range(n)]
+        succ = [[] for _ in range(n)]
+        for k in range(n):
+            for d, gap in pre[k]:
+                succ[d].append((k, gap))
+        cases = [times(ops, c) for c in CASES]
+        up = [o["up"] for o in ops]
+
+        def linked(more):
+            out = list(pre)
+            for k, d in more:
+                out[k] = out[k] + [(d, SEML if eng[d] != eng[k] else 0.0)]
+            return out
+
+        def worth(order, pre):
+            return sum(max(replay(eng, pre, order, c)[0]) / (b[0] * b[1]) ** 0.5 for c, b in zip(cases, CASES))
+
+        def fore(c, pri):
+            last = forwards(ops, eng, c, tiles, wide, pre, succ, pri)
+            return None if last is None else (worth(last[1], linked(last[3])), last, c, pri)
+
+        best = None
+        for c in cases[:2]:
+            bl = [0.0] * n
+            for k in range(n - 1, -1, -1):
+                bl[k] = c[0][k] + c[1][k] + max([bl[s] for s, gap in succ[k]] + [0.0])
+            for skew in SKEWS:
+                first = fore(c, [PW * (bl[k] - skew * ops[k]["c"]) + up[k] for k in range(n)])
+                for ahead, back in WEIGHTS:
+                    last = first
+                    for turn in range(TURNS):
+                        if last is None:
+                            break
+                        far = backwards(eng, c, pre, succ, last[1][0], back)
+                        last = fore(c, [ahead * far[k] + up[k] for k in range(n)])
+                        if last is not None and (best is None or last[0] < best[0]):
+                            best = last
+        seed = 1
+        for turn in range(SHAKES):
+            pri = list(best[3])
+            for x in range(12):
+                seed = draw(seed)
+                pri[(seed >> 8) % n] += ((seed >> 3) % 32 - 15.5) / 24.0
+            last = fore(best[2], pri)
+            if last is not None and last[0] <= best[0]:
+                best = last
+        fin, order, banks, more = best[1]
+        MADE[key] = (polish(eng, linked(more), order, cases, worth), banks, more)
+    order, banks, more = MADE[key]
     bankof.update(banks)
     for k, d in more:
         ops[k]["deps"].add(d)
     return order
 
 
-def replay(ops, order, more, gc, hop):
-    fin, free, more = {}, {}, dict(more)
+def replay(eng, pre, order, case):
+    dur, lat = case
+    fin, why, free, last = [0.0] * len(eng), [None] * len(eng), {}, {}
     for k in order:
-        o = ops[k]
-        st = max([free.get(o["e"], 0.0)] + [fin[d] + (SEML if ops[d]["e"] != o["e"] else 0.05) for d in o["deps"]] + [fin[more[k]] + SEML if k in more else 0.0])
-        d = o["d"] + o.get("n", 0) * CY * (gc - GC)
-        if o["e"] != "n":
-            free[o["e"]] = st + d
-        fin[k] = st + d + o["lat"] * hop
-    return max(fin.values())
+        e = eng[k]
+        st, w = free.get(e, 0.0), (last.get(e), True)
+        for d, gap in pre[k]:
+            if fin[d] + gap > st:
+                st, w = fin[d] + gap, (d, False)
+        if e != "n":
+            free[e], last[e] = st + dur[k], k
+        fin[k], why[k] = st + dur[k] + lat[k], w
+    return fin, why
 
 
-def backwards(ops, succ, fin, back):
-    n = len(ops)
+def polish(eng, pre, order, cases, worth):
+    n = len(eng)
+    cur, seed, pairs = worth(order, pre), 7, []
+    deps = [set(d for d, gap in x) for x in pre]
+    for turn in range(SWAPS):
+        if not pairs:
+            for c in cases:
+                fin, why = replay(eng, pre, order, c)
+                k = fin.index(max(fin))
+                while why[k][0] is not None:
+                    if why[k][1]:
+                        pairs.append((why[k][0], k))
+                    k = why[k][0]
+        seed = draw(seed)
+        u, v = pairs[(seed >> 8) % len(pairs)]
+        a, b = order.index(u), order.index(v)
+        for x in range((seed >> 4) % 3):
+            y = a - 1
+            while y >= 0 and eng[order[y]] != eng[v]:
+                y -= 1
+            a = y if y >= 0 else a
+        need, engs, ahead = set(deps[v]), set(), []
+        for k in order[a:b][::-1]:
+            if k in need or eng[k] in engs:
+                ahead.append(k)
+                need |= deps[k]
+                if eng[k] != "n":
+                    engs.add(eng[k])
+        if eng[v] in engs:
+            continue
+        new = order[:a] + ahead[::-1] + [v] + [k for k in order[a:b] if k not in ahead] + order[b + 1:]
+        w = worth(new, pre)
+        if w <= cur:
+            order, cur, pairs = new, w, []
+    return order
+
+
+def backwards(eng, case, pre, succ, fin, back):
+    dur, lat = case
+    n = len(eng)
     left = [len(x) for x in succ]
     ready = [k for k in range(n) if left[k] == 0]
     rt, bl, free = [0.0] * n, [0.0] * n, {}
     while ready:
-        k = min(ready, key=lambda k: max(rt[k] + ops[k]["lat"], free.get(ops[k]["e"], 0.0)) - back * fin[k])
-        o = ops[k]
+        k = min(ready, key=lambda k: max(rt[k] + lat[k], free.get(eng[k], 0.0)) - back * fin[k])
         ready.remove(k)
-        bl[k] = max(rt[k] + o["lat"], free.get(o["e"], 0.0)) + o["d"]
-        if o["e"] != "n":
-            free[o["e"]] = bl[k]
-        for d in o["deps"]:
+        bl[k] = max(rt[k] + lat[k], free.get(eng[k], 0.0)) + dur[k]
+        if eng[k] != "n":
+            free[eng[k]] = bl[k]
+        for d, gap in pre[k]:
             left[d] -= 1
-            rt[d] = max(rt[d], bl[k] + (SEML if ops[d]["e"] != o["e"] else 0.05))
+            rt[d] = max(rt[d], bl[k] + gap)
             if left[d] == 0:
                 ready.append(d)
     return bl
 
 
-def forwards(ops, tiles, succ, pri):
+def forwards(ops, eng, case, tiles, wide, pre, succ, pri):
+    dur, lat = case
     n = len(ops)
     bankof, more = {}, []
     tfirst = {}
@@ -697,56 +739,59 @@ def forwards(ops, tiles, succ, pri):
     tleft = [len(x) for x in tiles]
     bank = [None] * 8
     bfree = [(0.0, None)] * 8
-    left = [len(o["deps"]) for o in ops]
+    left = [len(x) for x in pre]
     ready = [k for k in range(n) if left[k] == 0]
     fin = [0.0] * n
-    free = {}
+    free = {e: 0.0 for e in "vspgy"}
     order = []
     rt = [0.0] * n
     free["n"] = -1.0
     while ready:
-        best = None
+        best, low = None, 1e9
         for k in ready:
-            o = ops[k]
-            st = max(rt[k], free.get(o["e"], 0.0))
-            if best is not None and st - pri[k] > best[0][0]:
+            st = free[eng[k]]
+            if rt[k] > st:
+                st = rt[k]
+            if st - pri[k] >= low:
                 continue
             b = -1
             if k in tfirst:
-                cand = [(bfree[i][0], i) for i in range(8) if bank[i] is None]
+                if wide[tfirst[k]] == 2:
+                    cand = [(max(bfree[i][0], bfree[i + 1][0]), 0, i) for i in (0, 2, 4, 6) if bank[i] is None and bank[i + 1] is None]
+                else:
+                    cand = [(max(bfree[i][0] + SEML, st), bank[i ^ 1] is None, i) for i in range(7, -1, -1) if bank[i] is None]
                 if not cand:
                     continue
-                f, b = min(cand)
-                st = max(st, f + SEML if f > 0 else 0.0)
-            key = (st - pri[k], k)
-            if best is None or key < best[0]:
-                best = (key, k, st, b)
+                f, x, b = min(cand)
+                st = max(st, f)
+                if st - pri[k] >= low:
+                    continue
+            best, low = (k, st, b), st - pri[k]
         if best is None:
             return None
-        _, k, st, b = best
-        o = ops[k]
+        k, st, b = best
         ready.remove(k)
         if b >= 0:
             t = tfirst[k]
             bankof[t] = b
-            bank[b] = t
-            if bfree[b][1] is not None:
-                more.append((k, bfree[b][1]))
-        if o["e"] != "n":
-            free[o["e"]] = st + o["d"]
-        fin[k] = st + o["d"] + o["lat"]
+            for i in range(b, b + wide[t]):
+                bank[i] = t
+                if bfree[i][1] is not None:
+                    more.append((k, bfree[i][1]))
+        if eng[k] != "n":
+            free[eng[k]] = st + dur[k]
+        fin[k] = st + dur[k] + lat[k]
         order.append(k)
-        for t in o["ps"]:
+        for t in ops[k]["ps"]:
             tleft[t] -= 1
             if tleft[t] == 0:
-                bb = bankof[t]
-                bank[bb] = None
-                bfree[bb] = (fin[k], k)
-        for s in succ[k]:
+                for i in range(bankof[t], bankof[t] + wide[t]):
+                    bank[i] = None
+                    bfree[i] = (fin[k], k)
+        for s, gap in succ[k]:
             left[s] -= 1
-            x = fin[k] + (SEML if ops[s]["e"] != o["e"] else 0.05)
-            if x > rt[s]:
-                rt[s] = x
+            if fin[k] + gap > rt[s]:
+                rt[s] = fin[k] + gap
             if left[s] == 0:
                 ready.append(s)
     return fin, order, bankof, more

@@ -9,15 +9,17 @@ HW = 16 * H
 SH = 65536.0
 MID = 1024.0
 MAGIC = 1.5 * 2.0 ** 39
+WHOLE = 1.5 * 2.0 ** 23
+DM = 2040.0
 BIG = 4096.0
 AL = AluOpType
 AF = ActivationFunctionType
 
 R2 = (0, 1)
-U_ = ["L0a", "L0b", "L0i", "L1a", "L1i", "L1b"] + ["%s_%d" % (n, t) for n in ("L2", "L3", "L4", "LF") for t in R2]
-H_ = ["wd", "mh", "ndo", "ndi", "nd2", "hE", "dh"] + ["%s_%d" % (n, t) for n in ("h0", "h1", "h2", "h3", "h4", "m1", "m2", "m3", "m4") for t in R2]
+U_ = ["L0a", "L1a", "L0i", "L1i", "L0b", "L1b"] + ["%s_%d" % (n, t) for n in ("L2", "L3", "L4") for t in R2]
+H_ = ["wd", "ndo", "ndi", "nd2", "d3", "pn", "dh"] + ["%s_%d" % (n, t) for n in ("h0", "h1", "h2", "h3", "h4", "m1", "m2", "m3") for t in R2]
 F_ = ["yd0", "yd1", "yef"]
-B_ = ["x0", "xi", "xz0", "xzn", "xz1", "f1a", "f1_0", "f1_1", "bs", "sq", "tt", "eq"] + ["%s_%d" % (n, t) for n in ("f2", "f3", "f4") for t in R2]
+B_ = ["x0", "xi", "xz0", "xzn", "xz1", "f1a", "f1_0", "f1_1", "bs", "sq", "tt", "eq", "ub", "pz"] + ["%s_%d" % (n, t) for n in ("f2", "f3") for t in R2]
 I_ = ["qi", "ni"]
 POOLS = {"PU": (U_, "uint16"), "PH": (H_, "float16"), "PF": (F_, "float32"), "PB": (B_, "bfloat16"), "PI": (I_, "int32")}
 SLOT = {}
@@ -26,45 +28,64 @@ for _p in POOLS:
     _names, _dt = POOLS[_p]
     SCRATCH[_p] = ("sbuf", [128, 256 * len(_names)], _dt)
     for _k, _n in enumerate(_names):
-        SLOT[_n] = (_p, 256 * _k)
+        SLOT[_n] = (_p, 256 * _k, H)
+for _k, _n in enumerate(("L0a", "L1a", "L0i", "L1i")):
+    SLOT[_n] = ("PU", 512 * (_k // 2) + H * (_k % 2), 2 * H)
 for _n, _w, _dt in (
-        ("dgs", W, "int32"), ("xs", W, "bfloat16"), ("xs2", W, "bfloat16"), ("dh0", W, "float16"), ("dh2", W, "float16"),
+        ("dgs", W, "int32"), ("xs", W + 272, "bfloat16"), ("xs2", W + 272, "bfloat16"), ("dh0", W + 256, "float16"), ("dh2", W + 256, "float16"),
         ("P0", W, "float32"), ("P1", W, "float32"), ("P2", W, "float32"),
         ("xr0", HW, "bfloat16"), ("xr1", HW, "bfloat16"), ("xrn", HW, "bfloat16"),
         ("zf", 32 * L, "float32"), ("zb", 32 * L, "bfloat16"), ("ab", 32 * L, "bfloat16"),
-        ("gh", 16 * L, "float16"), ("ed", 2048, "bfloat16"), ("onb", 512, "bfloat16"), ("ngb", 128, "bfloat16"),
-        ("idb", 128, "bfloat16"), ("idq", 128, "bfloat16"), ("id37", 128, "bfloat16"),
-        ("idp", 128, "bfloat16"), ("idn", 128, "bfloat16"), ("sel", 256, "float32"), ("ids", 128, "bfloat16"),
-        ("blk0", 128, "bfloat16"), ("blk", 128, "bfloat16"), ("bkn", 256, "bfloat16"), ("bk2", 256, "bfloat16"),
+        ("gh", 16 * L, "float16"), ("ed", 2048, "bfloat16"), ("onb", 128, "bfloat16"), ("ngb", 128, "bfloat16"),
+        ("idb", 128, "bfloat16"), ("idq", 128, "bfloat16"), ("id37", 128, "bfloat16"), ("idp", 128, "bfloat16"), ("idn", 128, "bfloat16"),
+        ("ids", 128, "bfloat16"), ("idk", 128, "bfloat16"), ("idr", 128, "bfloat16"), ("idt", 128, "bfloat16"), ("idm", 128, "bfloat16"), ("mid", 64, "bfloat16"), ("sel", 384, "float32"),
+        ("blk0", 128, "bfloat16"), ("blk", 128, "bfloat16"), ("xsel", 384, "bfloat16"), ("zsel", 384, "bfloat16"), ("bk2", 256, "bfloat16"),
         ("prow", 128, "bfloat16"), ("rst", 128, "float32"), ("pm", 512, "float32"), ("iq", 128, "float32"), ("chb", 288, "bfloat16"),
-        ("thi", 4, "int32"), ("tii", 4, "int32"), ("sgi", 4, "int32"), ("tif", 4, "float32"), ("sgf", 4, "float32"), ("thc", 4, "float32"),
-        ("gq", 512, "bfloat16"), ("gj", 128, "bfloat16"), ("pk", 272, "bfloat16"), ("pk2", 272, "bfloat16"),
-        ("thd", 256, "float16"), ("thd2", 256, "float16"), ("asum", 8, "float32"), ("acol", 8, "float32")):
+        ("thi", 128, "int32"), ("tii", 768, "int32"), ("tib", 768, "bfloat16"), ("gq", 512, "bfloat16"), ("gj", 128, "bfloat16"),
+        ("asum", 8, "float32"), ("acol", 8, "float32")):
     SCRATCH[_n] = ("sbuf", [128, _w], _dt)
 for _k in range(4):
     SCRATCH["pair%d" % _k] = ("psum", [128, 1024], "float32")
-SEMAPHORES = ["cv", "cs", "cp", "cg", "lsem", "rx", "rdh", "rxs", "rpk", "rnh", "rn2", "re0", "re1", "rr0", "rr1"] + ["ld%d" % k for k in range(10)]
+SEMAPHORES = ["cv", "cs", "cp", "cg", "lsem", "rx", "ry", "rh", "rd0", "rd1", "rx0", "rx1", "rnh", "rn2", "re0", "re1", "rr0", "rr1"] + ["ld%d" % k for k in range(10)]
 
-CV = {(0, 1): "vvss", (0, 2): "vvss", (1, 1): "vvss"}
-RV = ((0, 5, 1), (1, 5, 1))
-QL = {"list": "s", "col": "vs", "colh": "v", "vote": "vvss", "h0": "v", "LF": "v", "hE": "s", "ye": "s", "qi": "s", "patch": "v",
-      "dh0": "vs", "P0": "vsvs", "P1": "vsvs", "P2": "svsv", "xr0": "sv", "xrn": "g", "xr1": "g", "const": "s"}
-X1W = ("qi", 0)
+QL = {"list": "s", "col": "vs", "colh": "v", "vote": "vvss", "h0": "v", "L4": "s", "ye": "s", "patch": "v",
+      "dh0": "gs", "yd0": "g", "P0": "vsvs", "P1": "vsvs", "P2": "svsv", "xr0": "sv", "xrn": "g", "xr1": "g", "const": "s"}
+CARRY = {(0, 1): (), (0, 2): (), (0, 3): (1, 2), (1, 1): (), (1, 2): (1,), (1, 3): (2,)}
+X1W = ("ub", 1)
 XNW = ("L1i", 0)
-PW1 = ("ch", 1)
+PW1, PW2 = ("ub", 1), ("ch", 1)
 PUP = 0.3
-CUT = 8
 
 CY = 0.83e-3
 PC = 0.42e-3
 GC = 1.5
-HOP = 2.5
-LAT = {"x": 3.2, "d0": 5.2, "d1": 7.2, "x1": 8.2, "small": 2.5, "first": 2.0, "flags": 4.0, "dh": 10.0, "tab": 18.0}
+HOP = 1.8
+WIRE = 256 / 45e3
+LAT = {"x": 3.2, "d0": 5.2, "d1": 7.2, "x1": 8.2, "small": 2.5, "first": 2.0, "hand": 7.0}
+XCUT = (0, 1152, W + 256)
+
+
+def helper(T, topo, rank):
+    c, d = T.cores[rank], T.cores[(rank - 2) % N]
+    return [x for x in topo.cores_of(c) if x not in T.cores and topo.die(x) == topo.die(c) and topo.may_write(x, d)][0]
+
+
+def hand_on(g, core, T, topo, rank):
+    c, d = T.cores[rank], T.cores[(rank - 2) % N]
+    rid, pid = topo.addr(d, core)
+    es = topo.engines(core, d)[0:8]
+    g.wait_ge(T.sem.rh, len(topo.engines(c, core)[-8:]))
+    for j in R2:
+        g.remote_dma(T.xs2[:, XCUT[j]:XCUT[j + 1]], T.xs[:, XCUT[j]:XCUT[j + 1]], T.sem["rx%d" % j], T.sem.lsem, pid, rid, sum(1 << e for e in es))
+        g.wait_ge(T.sem.lsem, (j + 1) * len(es))
 
 
 def rank_program(g, core, T, topo):
     rank = T.rank_of(core)
     if rank is None:
+        for r in range(N):
+            if helper(T, topo, r) == core:
+                hand_on(g, core, T, topo, r)
         return
     cores = T.cores
     ops, lastw, readers, tiles, wide, own = [], {}, {}, [], [], {}
@@ -123,10 +144,10 @@ def rank_program(g, core, T, topo):
         return x[0]() if isinstance(x, tuple) else x
 
     def A(name, h=None, a=0, b=H):
-        p, o = SLOT[name]
+        p, o, far = SLOT[name]
         if h is None:
             return T[p][:, o:o + L]
-        return T[p][:, o + H * h + a:o + H * h + b]
+        return T[p][:, o + far * h + a:o + far * h + b]
 
     def K(name, h=None, s=None):
         return [(name, a, b) for a in (R2 if h is None else (h,)) for b in (R2 if s is None else (2 * s // SB,))]
@@ -144,7 +165,7 @@ def rank_program(g, core, T, topo):
         def em():
             if o1 is None:
                 return g.vector.tensor_scalar(out, R(in0), s1, None, o0)
-            return g.vector.tensor_scalar(out, R(in0), s1, s2, o0, o1)
+            return g.vector.tensor_scalar(out, R(in0), R(s1), R(s2), o0, o1)
         return add("v", vt(n, f), em, r, w, p)
 
     def vtt(out, in0, in1, op, n, f, r, w, p=()):
@@ -186,19 +207,23 @@ def rank_program(g, core, T, topo):
     def more(lst, last=False):
         return [x + (False, last and i == len(lst) - 1) for i, x in enumerate(lst)]
 
+    def opened(lst):
+        return [lst[0] + (True, False)] + more(lst[1:])
+
     C = slice
-    ONE = T.onb[:, 0:128]
+    ONE = T.onb[:, :]
+    PK, PK2, THD, THD2 = T.xs[:, W:W + 272], T.xs2[:, W:W + 272], T.dh0[:, W:W + 256], T.dh2[:, W:W + 256]
 
     def load(eng, buf, src, sem, lat):
         early(add(eng, 0.1, lambda: ENG[eng].dma_start(buf, src), (), [(sem, "ld")], (), sem, 16, lat))
 
-    load("y", T.thi[:, 0:1], T.th[:, :], "ld4", LAT["small"])
+    load("y", T.thi[0:1, :], T.th[:, :], "ld4", LAT["small"])
     load("y", T.xs[:, 0:W // 2], T.xv[:, 0:W // 2], "ld0", LAT["x"])
     load("y", T.dgs[:, 0:W // 2], T.dg[:, 0:W // 2], "ld1", LAT["d0"])
     load("y", T.dgs[:, W // 2:W], T.dg[:, W // 2:W], "ld8", LAT["d1"])
     load("y", T.xs[:, W // 2:W], T.xv[:, W // 2:W], "ld9", LAT["x1"])
-    load("s", T.tii[:, 0:3], T.ti[:, :], "ld2", LAT["small"])
-    load("s", T.sgi[:, 0:3], T.sg[:, :], "ld3", LAT["x"])
+    load("s", T.tii[0:1, 0:384], T.ti[:, :], "ld2", LAT["small"])
+    load("s", T.tii[0:1, 384:768], T.sg[:, :], "ld3", LAT["small"])
     KX, KDG = [("ld0", "ld"), ("ld9", "ld")], [("ld1", "ld"), ("ld8", "ld")]
 
     def dest(r):
@@ -206,72 +231,75 @@ def rank_program(g, core, T, topo):
 
     cnt = {"l": 0}
 
-    def send(d, names_in, names_out, sem, rd, after=(), dur=0.7):
-        pieces = len(names_in)
+    def send(d, src, dst, sem, rd, after=(), dur=0.7, part=C(0, 8)):
         rid, pid = topo.addr(d, core)
-        es = topo.engines(core, d)
-        n = 1
-        while 2 * n * pieces <= min(len(es), 8):
-            n *= 2
-        masks = [sum(1 << e for e in es[k * n:(k + 1) * n]) for k in range(pieces)]
-        cnt["l"] += n * pieces
+        es = topo.engines(core, d)[part]
+        cnt["l"] += len(es)
+        return add("g", dur, lambda: g.remote_dma(dst, src, T.sem[sem], T.sem.lsem, pid, rid, sum(1 << e for e in es)), rd, (), (), "-", 0, 0.0, after), len(es)
 
-        def em():
-            return g.remote_dma_fused([RemoteDMATransfer(dst_ids=[DstId(rid=rid, pnc=pid)], dma_engine_mask=masks[k], remote_sem=T.sem[sem], src=names_in[k], dst=names_out[k])
-                                       for k in range(pieces)], local_sem=T.sem.lsem)
-        return add("g", dur, em, rd, (), (), "-", 0, 0.0, after), n * pieces
-
-    def recv(sem, sent, lat, keys):
-        return add("n", 0.0, None, (), keys, (), sem, sent[1], lat, [sent[0]])
+    def recv(sem, sent, cols, keys, lat=0.0):
+        k = add("n", 0.0, None, (), (), (), "-", 0, lat, [sent[0]])
+        k = add("w", cols * WIRE, None, (), ["wire"], (), "-", 0, 0.0, [k])
+        return add("n", 0.0, None, (), keys, (), sem, sent[1], HOP, [k])
 
     s1, h2 = dest(rank + 1), dest(rank - 2)
     for h in R2:
         sact(A("x0", h), T.xs[:, h * W // 2:(h + 1) * W // 2:S], AF.Copy, H, [KX[h]], K("x0", h))
-    kx0 = send(s1, [A("x0", 0)], [A("xi", 0)], "rx", K("x0", 0))
-    recv("rx", kx0, HOP + LAT["first"], K("xi", 0))
+    kx0 = send(s1, A("x0", 0), A("xi", 0), "rx", K("x0", 0), dur=0.7 + LAT["first"])
+    recv("rx", kx0, H, K("xi", 0))
+    kx1 = send(s1, A("x0", 1), A("xi", 1), "ry", K("x0", 1), kx0[:1])
+    recv("ry", kx1, H, K("xi", 1))
 
-    early(vset(T.onb[:, :], 1.0, 512, 0.5, ["onb"]))
+    early(vset(ONE, 1.0, 128, 0.5, ["onb"]))
+    early(vset(T.ed[:, :], 0.0, 2048, 0.5, ["ed"]))
     early(add("g", 0.13 + 256 * CY, lambda: g.iota(T.iq[:, :], [[0, 8], [1, 16]], 0, 0, allow_small_or_imprecise_dtypes=True), (), ["iq"]))
     early(gsel(T.idb[:, :], ONE, [[-1, 128]], AL.is_equal, 0, 1, 128, ["onb"], ["idb"]))
     early(gsel(T.blk0[:, :], ONE, [[-16, 8], [0, 16]], AL.is_ge, 0, 1, 128, ["onb"], ["blk0"]))
     early(gsel(T.blk[:, :], T.blk0[:, :], [[16, 8], [0, 16]], AL.is_ge, 15, -1, 128, ["blk0"], ["blk"]))
     first = len(ops)
     vset(T.ngb[:, :], -1.0, 128, 0.5, ["ngb"])
+    vset(T.mid[:, :], MID / 128, 64, 0.5, ["mid"])
     for z in ("xz0", "xzn", "xz1"):
         vset(A(z), 0.0, L, 0.5, K(z))
-    for q in range(0, 16, 4):
-        gsel(T.ed[:, 128 * q:128 * q + 512], T.onb[:, :], [[-256, 4], [-16, 8], [255, 16]], AL.is_equal, -256 * q, 1, 512, ["onb"], [("ed", q)],
-             kx0[:1] if q >= 8 else ())
-    KED = [("ed", q) for q in range(0, 16, 4)]
-    for name, val in (("ids", SH), ("idn", -1.0), ("idp", BIG), ("idq", 0.5), ("id37", 37.0)):
+    for x in range(8):
+        vcopy(T.ed[:, 16 * x:16 * x + 129 * 15 + 1:129], T.idb[:, 16 * x:16 * x + 16], 16, 0.5, ["idb"], ["ed"])
+    for name, val in (("ids", SH), ("idn", -1.0), ("idp", BIG), ("idm", -BIG), ("idq", 0.5), ("idr", 0.25), ("idt", -0.5), ("id37", 37.0), ("idk", 1.0 / 8192)):
         move(QL["const"], T[name][:, :], T.idb[:, :], 128, ["idb"], [name], f=0.5, scale=val)
     move(QL["const"], T.sel[:, 0:128], T.idb[:, :], 128, ["idb"], ["idf"], scale=SH)
-    move(QL["const"], T.sel[:, 128:256], T.blk[:, :], 128, ["blk"], ["sel"], scale=-1.0)
-    for name, val in (("bkn", -1.0), ("bk2", 2.0)):
-        move("v", T[name][:, 0:128], T.blk[:, :], 128, ["blk"], [name], f=0.5, scale=val / 8192)
-        move("v", T[name][:, 128:256], T.blk[:, :], 128, ["blk"], [name], f=0.5, scale=val)
-    BN, B2 = T.bkn[:, 128:256], T.bk2[:, 128:256]
-    for x in ("pk", "pk2"):
-        vcopy(T[x][:, 256:264], T.blk[:, 0:128:16], 8, 0.5, ["blk"], [x + "B"])
-    move("v", T.prow[:, :], T.iq[:, :], 128, ["iq"], ["prow"], scale=2.0 ** -25, bias=2.0 ** -26)
+    for j in (1, 2):
+        c = C(128 * j, 128 * j + 128)
+        move(QL["const"], T.sel[:, c], T.blk[:, :], 128, ["blk"], ["sel"], scale=-1.0)
+        for x in ("xsel", "zsel"):
+            move("v", T[x][:, c], T.blk[:, :], 128, ["blk"], [x], f=0.5, scale=-1.0)
+        move("v", T.bk2[:, 128 * j - 128:128 * j], T.blk[:, :], 128, ["blk"], ["bk2"], f=0.5, scale=2.0)
+    for x, val in (("xsel", -SH), ("zsel", SH)):
+        move("v", T[x][:, 0:128], T.idb[:, :], 128, ["idb"], [x], f=0.5, scale=val)
+    BN = T.zsel[:, 128:256]
+    for x, y in (("pk", PK), ("pk2", PK2)):
+        vcopy(y[:, 256:264], T.blk[:, 0:128:16], 8, 0.5, ["blk"], [x + "B"])
+    move("v", T.prow[0:64, :], T.iq[0:64, :], 128, ["iq"], ["prow"], scale=2.0 ** -24, bias=2.0 ** -25)
+    vset(T.prow[64:128, :], DM / 8192 / 64, 128, 0.5, ["prow"])
     vset(T.rst[:, :], 1.0, 128, 1, ["rst"])
     vset(T.rst[:, 0:128:16], 0.0, 8, 1, ["rst"])
-    for x in ("thd", "thd2"):
-        move("v", T[x][:, 0:128], ONE, 128, ["onb"], [x + "m"], f=0.5, scale=MID / 128)
-    move("v", T.thc[:, 0:1], T.thi[:, 0:1], 1, [("ld4", "ld")], ["thc"], scale=-1.0, bias=2048.0)
-    vts(T.thd[:, 128:256], T.idb[:, :], T.thc[:, 0:1], None, AL.mult, None, 128, 0.5, ["idb", "thc"], ["thd"])
+    move("v", THD[:, 0:128], ONE, 128, ["onb"], ["thd"], f=0.5, scale=0.0)
+    move("v", THD[0:1, 0:128], T.thi[0:1, :], 128, [("ld4", "ld")], ["thd"], scale=-1.0, bias=2048.0)
+    for x, y in (("thd", THD), ("thd2", THD2)):
+        move("v", y[:, 128:256], ONE, 128, ["onb"], [x + "m"], f=0.5, scale=-DM / 128)
 
-    vcopy(T.tif[:, 0:3], T.tii[:, 0:3], 3, 1, [("ld2", "ld")], ["tif"])
-    vcopy(T.sgf[:, 0:3], T.sgi[:, 0:3], 3, 1, [("ld3", "ld")], ["sgf"])
+    p0 = tile()
+    for x in R2:
+        move("vs"[x], T.tib[0:1, 384 * x:384 * x + 384], T.tii[0:1, 384 * x:384 * x + 384], 384, [("ld%d" % (2 + x), "ld")], [("tib", x)])
+    mm([(C(3 * x + j, 3 * x + j + 1), T.tib[0:1, 384 * x + j:384 * x + 384:3], T.onb[0:1, 0:1], True, True) for x in R2 for j in range(3)], 6 * 64,
+       [("tib", 0), ("tib", 1), "onb"], p0)
     for j in range(3):
-        vts(T.gq[:, 128 * j:128 * j + 128], T.iq[:, :], T.tif[:, j:j + 1], T.sgf[:, j:j + 1], AL.is_equal, AL.mult, 128, 1, ["iq", "tif", "sgf"], [("gq", j)])
+        vts(T.gq[:, 128 * j:128 * j + 128], T.iq[:, :], PS(p0, j, j + 1), PS(p0, 3 + j, 4 + j), AL.is_equal, AL.mult, 128, 1, ["iq"], [("gq", j)], (p0,))
     vtt(T.gq[:, 384:512], T.gq[:, 0:128], T.gq[:, 128:256], AL.add, 128, 2, [("gq", 0), ("gq", 1)], [("gq", 3)])
     vtt(T.gq[:, 0:128], T.gq[:, 384:512], T.gq[:, 256:384], AL.add, 128, 2, [("gq", 3), ("gq", 2)], [("gq", 0)])
     vtt(T.gj[:, :], T.gq[:, 0:128], T.blk[:, :], AL.mult, 128, 2, [("gq", 0), "blk"], ["gj"])
-    sact(T.pk[:, 128:256], T.gj[:, :], AF.Abs, 128, ["gj"], ["pkA"])
+    sact(PK[:, 128:256], T.gj[:, :], AF.Abs, 128, ["gj"], ["pkA"])
     p0 = tile()
     mm(group([(C(0, 128), T.gj[:, :], T.idb[:, :])]), 128, ["gj", "idb"], p0)
-    sact(T.pk[:, 0:128], PS(p0, 0, 128), AF.Copy, 128, (), ["pkG"], (p0,))
+    sact(PK[:, 0:128], PS(p0, 0, 128), AF.Copy, 128, (), ["pkG"], (p0,))
     for o in ops[first:]:
         o["up"] = CUP if o["e"] in "vs" else 0.0
 
@@ -288,24 +316,27 @@ def rank_program(g, core, T, topo):
             for u in R2:
                 move(QL["vote"][2 * t + u], A(name, h, 64 * u, 64 * u + 64), T.dgs[:, S * lane(h, u) + t:S * (lane(h, u) + 64):S], 64, [KDG[u]], K(name, h, 2 * u))
 
-    def pack(e, out, x, d, n, rd, w, o=0, p=None):
-        p = tile() if p is None else p
-        mm(group([(C(o, o + n), T.ids[:, :], x), (C(o, o + n), T.idb[:, :], d)]), 2 * n, rd + ["ids", "idb"], p)
-        return move(e, out, PS(p, o, o + n), n, (), w, (p,), scale=1.0 / SH, bias=-MID / SH)
+    def pack(e, out, x, d, n, rd, w):
+        p = tile()
+        mm(group([(C(0, n), T.ids[:, :], x), (C(0, n), T.idb[:, :], d)]), 2 * n, rd + ["ids", "idb"], p)
+        return move(e, out, PS(p, 0, n), n, (), w, (p,), scale=1.0 / SH, bias=-MID / SH)
 
     def table(name, x, kx, d, kd, when=()):
         for j in range(4):
             c = C(512 * j, 512 * j + 512)
-            pack(QL[name][j], T[name][:, c], x[:, c], d[:, c], 512, [kx[j // 2], kd[j // 2]] + list(when), [(name, j)])
+            pack(QL[name][j], T[name][:, c], x[:, c], d[:, c], 512, kx(j) + [kd[j // 2]] + list(when), [(name, j)])
         return [(name, j) for j in range(4)]
 
+    first = len(ops)
     X0 = lane_views("xr0", "xz0", lambda a, b: A("x0")[:, a:b], [K("x0", h) for h in R2], [])
     voters("L0a", 0)
+    for o in ops[first:]:
+        o["up"] = CUP
     for h in R2:
         c = C(h * W // 2, (h + 1) * W // 2)
         move(QL["dh0"][h], T.dh0[:, c], T.dgs[:, c], W // 2, [KDG[h]], [("dh0", h)])
     KDH = [("dh0", h) for h in R2]
-    KP0 = table("P0", T.xs, KX, T.dh0, KDH)
+    KP0 = table("P0", T.xs, lambda j: KX[j // 2:j // 2 + 1], T.dh0, KDH)
 
     par = {}
     turned = set()
@@ -318,7 +349,7 @@ def rank_program(g, core, T, topo):
 
     def gather(eng, buf, o, keys, win, lst, h, s, n, rd, xr=None):
         def em():
-            out, src = T[buf][:, o + s * SW:o + (s + n) * SW], win[:, :].indirect(A(lst, h, s * H // SB, (s + n) * H // SB))
+            out, src = T[buf][:, o + s * SW:o + (s + n) * SW], win[:, 0:W].indirect(A(lst, h, s * H // SB, (s + n) * H // SB))
             if eng == "s":
                 return g.scalar.activation(out, src, AF.Copy)
             if xr is None:
@@ -326,36 +357,24 @@ def rank_program(g, core, T, topo):
             return g.vector.tensor_tensor(out, src, xr[:, (2 * h + s) * SW:(2 * h + s + n) * SW], AL.subtract)
         ops[add(eng, 0.06 + n * SW * GC * CY, em, rd + K(lst, h, s), keys[s:s + n])]["n"] = n * SW
 
-    def own_rows(p, u, src, o, rd, last=True):
-        o += u * HW // 2
-        mm([(C(64 * u, 64 * u + 64), T.ed[:, q * 128:(q + 1) * 128], src[:, o + q:o + HW // 2:16], q == 0, last and q == 15) for q in range(16)], 1024, rd + KED, p)
-
-    def column(t, k, lst, h, Lk, hk):
+    def column(lst, h, Lk, hk):
         o, keys = room("gh", h, False)
-        e = CV[t, k]
-        for s in (0, 2):
-            if e[s] == e[s + 1]:
-                gather(e[s], "gh", o, keys, T.dgs, lst, h, s, 2, KDG)
-            else:
-                for x in (s, s + 1):
-                    gather(e[x], "gh", o, keys, T.dgs, lst, h, x, 1, KDG)
         for u in R2:
-            p = tile()
-            own_rows(p, u, T.gh, o, keys[2 * u:2 * u + 2])
-            move(QL["col"][u], A(Lk, h, 64 * u, 64 * u + 64), PS(p, 64 * u, 64 * u + 64), 64, (), K(Lk, h, 2 * u), (p,))
+            gather("vs"[u], "gh", o, keys, T.dgs, lst, h, 2 * u, 2, KDG)
+        for u in R2:
+            p, a = tile(), o + u * HW // 2
+            mm(group([(C(0, 64), T.ed[:, q * 128:(q + 1) * 128], T.gh[:, a + q:a + HW // 2:16]) for q in range(16)]), 1024, keys[2 * u:2 * u + 2] + ["ed"], p)
+            move(QL["col"][u], A(Lk, h, 64 * u, 64 * u + 64), PS(p, 0, 64), 64, (), K(Lk, h, 2 * u), (p,))
         if hk:
-            move(QL["colh"], A(hk, h), A(Lk, h), H, K(Lk, h), K(hk, h), f=0.5)
+            move(QL["colh"], A(hk, h), A(Lk, h), H, K(Lk, h), K(hk, h), f=0.5, bias=-MID)
 
-    def view(t, k, win, kw, lst, h, X, packed):
+    def view(win, kw, lst, h, X, packed):
         buf = "zf" if packed else "zb"
         o, keys = room(buf, h)
         ao, ak = room("ab", h)
         gather("v", buf, o, keys, win, lst, h, 0, 2, kw + X["kxr"], X["xr"])
         gather("s", buf, o, keys, win, lst, h, 2, 2, kw)
-        if (t, k, h) in RV:
-            vts(T.ab[:, ao:ao + 2 * SW], T[buf][:, o:o + 2 * SW], 0.0, None, AL.max, None, 2 * SW, 0.5, keys[0:2], ak[0:2])
-        else:
-            sact(T.ab[:, ao:ao + 2 * SW], T[buf][:, o:o + 2 * SW], AF.Relu, 2 * SW, keys[0:2], ak[0:2])
+        sact(T.ab[:, ao:ao + 2 * SW], T[buf][:, o:o + 2 * SW], AF.Relu, 2 * SW, keys[0:2], ak[0:2])
         if h not in X:
             X[h] = tile(2)
             for s in R2:
@@ -365,7 +384,7 @@ def rank_program(g, core, T, topo):
         return {"o": o, "keys": keys, "ao": ao, "ak": ak, "z": X["z"]}
 
     def sums(buf, o, sel, a, b):
-        return [(C(a + q, b, 16), T[buf][:, o + q:o + HW:16], sel[:, 0:b - a:16]) for q in range(16)]
+        return [(C(a + q, b, 16), T[buf][:, o + q:o + HW:16], sel[:, q:b - a:16]) for q in range(16)]
 
     def turn(c, name, h, ident):
         return (c, ident, A(name, h)) if (name, h) in turned else (c, A(name, h), ident)
@@ -384,67 +403,111 @@ def rank_program(g, core, T, topo):
         turned.add((mk, h))
 
     def step(t, k, h, win, kw, lst, X, thd, kth, fk, packed, here=True):
-        v = view(t, k, win, kw, lst, h, X, packed)
+        v = view(win, kw, lst, h, X, packed)
         q = tile()
-        a = 0 if packed else H
-        pre, rd = change(t, k, h) if here else ([], [])
-        mm(pre + [(C(a, 2 * H), ONE, thd[:, a:2 * H], True, False), (C(H, 2 * H), A(v["z"], h), BN, False, False)], 128 * len(pre) + 3 * H - a,
-           rd + ["onb", "bkn", v["keys"][0]] + kth + K(v["z"], h), q)
+        b = 3 * H if k == 3 else 2 * H
+        rd = ["onb", "zsel"] + K(lst, h) + kth + K(v["z"], h)
+        if k == 3:
+            h2 = "h2_%d" % t
+            mm(opened([(C(0, b), A(v["z"], h), T.xsel[:, :]), (C(H, 2 * H), ONE, thd[:, 0:H]), turn(C(0, H), h2, h, T.idn[:, :])]), 5 * H,
+               rd + ["xsel", "idn"] + K(h2, h), q)
+        elif here:
+            pre, r2 = change(t, k, h)
+            mm(pre, 2 * H, r2 + K(lst, h), q)
+        fixed = [(C(H, 2 * H), ONE, thd[:, 0:H]), (C(H, 2 * H), A(v["z"], h), BN)]
         if packed:
+            lst = (more if k == 3 else opened)(sums("zf", v["o"], T.sel, 0, b))
             for q0 in range(0, 16, 4):
-                mm(more([(C(x, 2 * H, 16), T.zf[:, v["o"] + x:v["o"] + HW:16], T.sel[:, x:2 * H:16]) for x in range(q0, q0 + 4)]), 1024, v["keys"] + ["idf", "sel"], q)
+                mm(lst[q0:q0 + 4], 1024, v["keys"] + ["idf", "sel"], q)
+            if k < 3:
+                mm(more(fixed), 2 * H, rd, q)
         else:
+            mm(opened(fixed), 2 * H, rd, q)
             mm(more(sums("zb", v["o"], BN, H, 2 * H)), 1024, v["keys"], q)
-        lst, rd = sums("ab", v["ao"], B2, H, 2 * H), v["ak"] + ["bk2"]
-        if k > 1:
-            fp = "f%d_%d" % (k - 1, t)
+        lst, rd = sums("ab", v["ao"], T.bk2, H, b), v["ak"] + ["bk2"]
+        before = ["f%d_%d" % (x, t) for x in CARRY[t, k]]
+        for fp in before:
             lst, rd = lst + [(C(H, 2 * H), T.idp[:, :], A(fp, h))], rd + K(fp, h) + ["idp"]
-        mm(more(lst, True), 1024 + 128, rd, q)
+        mm(more(lst, True), 1024 + 128 * len(before), rd, q)
+        hk, Lk = "h%d_%d" % (k + 1, t), "L%d_%d" % (k + 1, t)
         if packed:
-            hk, Lk = "h%d_%d" % (k + 1, t), "L%d_%d" % (k + 1, t)
             vts(A("tt", h), PS(q, 0, H), MAGIC, MAGIC, AL.add, AL.subtract, H, 1, (), K("tt", h), (q,))
             vtt(A(hk, h), PS(q, 0, H), A("tt", h), AL.subtract, H, 1, K("tt", h), K(hk, h), (q,))
             turned.add((hk, h))
+        if packed and k < 3:
             p = tile()
             mm(group([(C(0, H), A(hk, h), T.idb[:, :])]), 128, K(hk, h) + ["idb"], p)
-            move(QL["list"], A(Lk, h), PS(p, 0, H), H, (), K(Lk, h), (p,))
-        sact(A(fk, h), PS(q, H, 2 * H), AF.Sign, H, (), K(fk, h), (q,), bias=0.5 - 2048.0 + (BIG if k > 1 else 0.0))
-        if here:
+            move(QL["list"], A(Lk, h), PS(p, 0, H), H, (), K(Lk, h), (p,), bias=MID)
+        sign = -1.0 if k == 3 else 1.0
+        sact(A(fk, h), PS(q, H, 2 * H), AF.Sign, H, (), K(fk, h), (q,), bias=sign * (0.5 - 2048.0 + BIG * len(before)), scale=sign)
+        if k == 3:
+            mk = "m3_%d" % t
+            vtt(A(mk, h), A(fk, h), A(hk, h), AL.mult, H, 1, K(fk, h) + K(hk, h), K(mk, h))
+            turned.add((mk, h))
+            vts(A("d3", h), PS(q, 2 * H, 3 * H), WHOLE, WHOLE + DM, AL.add, AL.subtract, H, 1, (), K("d3", h), (q,))
+        elif here:
             flagged(t, k, h, fk, q)
 
     def walk(t, h, tb, X, ut):
-        for k in (2, 3, 4):
-            win, kw = (tb["P"], tb["kp"]) if k < 4 else (tb["X"], tb["kx"])
-            step(t, k, h, win, kw, "L%d_%d" % (k, t), X, tb["thd"], tb["kth"], "f%d_%d" % (k, t), k < 4)
-            if k < 4:
+        for k in (2, 3):
+            step(t, k, h, tb["P"], tb["kp"], "L%d_%d" % (k, t), X, tb["thd"], tb["kth"], "f%d_%d" % (k, t), True)
+            if k < 3:
                 yield
-        LF = "LF_%d" % t
-        terms = ["h0_%d" % t, "h4_%d" % t] + ["m%d_%d" % (k, t) for k in (1, 2, 3, 4)]
-        kt = sum([K(x, h) for x in terms], [])
+        L4 = "L4_%d" % t
+        half, quarter = T.idq[:, :], T.idr[:, :]
+        terms = [("h0", half), ("h2", half), ("m1", half), ("m2", half)]
+        if t == 0:
+            q = tile()
+            c = C(2 * H, 3 * H)
+            ys = ["h1_0", "h2_0", "m2_0"]
+            mm(group([turn(c, "h0_0", h, T.idb[:, :])] + [turn(c, x, h, T.idt[:, :]) for x in ys]), 4 * H,
+               sum([K(x, h) for x in ys], K("h0_0", h) + K("f1_0", h)) + ["idb", "idt"], q)
+            flagged(0, 1, h, "f1_0", q)
+            terms = [("h0", half), ("h1", quarter), ("h2", quarter), ("m2", quarter), ("m1", half)]
+        terms = [("%s_%d" % (x, t), y) for x, y in terms + [("h4", half), ("m3", half)]]
+        kt = sum([K(x, h) for x, y in terms], [])
         p = tile()
-        lst = group([back(C(0, H), x, h, T.idq[:, :]) for x in terms])
-        mm(lst[:5], 5 * 128, kt[:10] + ["idq"], p)
-        mm(lst[5:], 128, kt[10:], p)
-        move(QL["LF"], A(LF, h), PS(p, 0, H), H, (), K(LF, h), (p,))
-        move(QL["hE"], A("hE", h), PS(p, 0, H), H, (), K("hE", h), (p,))
-        if t == 1:
-            for u in R2:
-                move(QL["ye"], A("yef")[:, lane(h, u):lane(h, u) + 64], A("hE", h, 64 * u, 64 * u + 64), 64, K("hE", h), K("yef", h, 2 * u))
+        lst = group([back(C(0, H), x, h, y) for x, y in terms])
+        mm(lst[:-1], (len(lst) - 1) * 128, kt[:-2] + ["idq", "idr"], p)
+        mm(lst[-1:], 128, kt[-2:], p)
+        move(QL["L4"], A(L4, h), PS(p, 0, H), H, (), K(L4, h), (p,), bias=MID)
         yield
-        ballot(t, h, tb, X, ut)
+        last(t, h, tb, X, terms, kt)
+        ballot(t, h, tb, ut)
         yield
 
-    def ballot(t, h, tb, X, ut):
-        v = view(t, 5, tb["X"], tb["kx"], "LF_%d" % t, h, X, False)
+    def last(t, h, tb, X, terms, kt):
+        v = view(tb["X"], tb["kx"], "L4_%d" % t, h, X, False)
+        q = tile()
+        h3, f3 = "h3_%d" % t, "f3_%d" % t
+        c = C(3 * H, 4 * H)
+        mm(group([turn(c, x, h, y) for x, y in terms] + [turn(c, h3, h, T.idn[:, :])]), (len(terms) + 1) * H, kt + K(h3, h) + ["idn"], q)
+        mm(opened([(C(0, 3 * H), A(v["z"], h), T.xsel[:, :]), (C(H, 3 * H), ONE, tb["thd"][:, :]), (C(0, H), T.idn[:, :], A("tt", h)),
+                   (C(H, 2 * H), T.idp[:, :], A(f3, h)), (C(2 * H, 3 * H), T.idn[:, :], A("d3", h))]),
+           8 * H, K(v["z"], h) + K("tt", h) + K(f3, h) + K("d3", h) + tb["kth"] + ["onb", "xsel", "idp"], q)
+        mm(more(sums("zb", v["o"], T.zsel, 0, 3 * H)), 1024, v["keys"] + ["zsel"], q)
+        mm(more(sums("ab", v["ao"], T.bk2, H, 3 * H), True), 1024, v["ak"] + ["bk2"], q)
+        vts(A("ub", h), PS(q, H, 2 * H), 2048.0 + BIG - 0.5, None, AL.is_lt, None, H, 1, (), K("ub", h), (q,))
+        vtt(A("pz", h), A("ub", h), PS(q, 0, H), AL.mult, H, 1, K("ub", h), K("pz", h), (q,))
+        pd = PS(q, 2 * H, 3 * H)
+        vtt(pd, A("ub", h), pd, AL.mult, H, 1, K("ub", h), [("pd", h)], (q,))
+        vtt(A("dh", h), A("d3", h), pd, AL.add, H, 1, K("d3", h) + [("pd", h)], K("dh", h), (q,))
+        vtt(A("pn", h), A("ub", h), PS(q, 3 * H, 4 * H), AL.mult, H, 1, K("ub", h), K("pn", h), (q,))
+
+    def ballot(t, h, tb, ut):
         qt, gt, at = ut
-        D0 = "h0_%d" % t
-        lanes = [C(lane(h, u), lane(h, u) + 64) for u in R2]
+        D0, h3 = "h0_%d" % t, "h3_%d" % t
         part = [C(64 * u, 64 * u + 64) for u in R2]
+
+        def lanes(o, u):
+            return C(o + lane(h, u), o + lane(h, u) + 64)
+
+        def rows(o, terms):
+            return [(lanes(o, u), x, ident[:, part[u]]) for u in R2 for x, ident in terms]
+
         p = tile()
-        for u in R2:
-            own_rows(p, u, T.zb, v["o"], v["keys"][2 * u:2 * u + 2], u == 0)
-        mm(more([(C(64, H), T.idn[:, :], A(v["z"], h, 64, H))], True), 64, K(v["z"], h) + ["idn"], p)
-        sact(A("bs", h), PS(p, 0, H), AF.Sign, H, (), K("bs", h), (p,), bias=-0.5)
+        mm(group([(C(0, H), A(x, h), T.idb[:, :]) for x in ("tt", "pz")]), 2 * H, K("tt", h) + K("pz", h) + ["idb"], p)
+        sact(A("bs", h), PS(p, 0, H), AF.Sign, H, (), K("bs", h), (p,), bias=-SH / 2)
         mm(group([(C(H, 2 * H), tb["GT"], A("bs", h))]), H, K("bs", h) + [tb["kgt"]], p)
         sact(A("sq", h), PS(p, H, 2 * H), AF.Square, H, (), K("sq", h), (p,))
         c = C(2 * H, 3 * H + 8)
@@ -453,38 +516,32 @@ def rank_program(g, core, T, topo):
         ch = T.chb[:, o:o + H]
         sact(T.chb[:, o:o + H + 8], PS(p, 2 * H, 3 * H + 8), AF.Sign, H + 8, (), K("ch", h), (p,))
         mm([(C(0, 8), ONE, T.chb[:, o + H:o + H + 8], h == 0, h == 1)], 64, K("ch", h) + ["onb"], at)
+        lst = rows(0, [(A(h3, h), T.id37), (A("pn", h), T.id37), (A("dh", h), T.idb)]) + rows(L, [(A(h3, h), T.idb), (A("pn", h), T.idb)] * t)
+        mm(group(lst), 64 * len(lst), K(h3, h) + K("pn", h) + K("dh", h) + ["id37", "idb"], qt)
+        if t == 1 and h == 1:
+            move(QL["ye"], A("yef"), PS(qt, L, 2 * L), L, (), K("yef"), (qt,), bias=MID)
         p = tile()
-        mm([(C(0, 2 * H), A(v["z"], h), T.bkn[:, :], True, False), (C(0, H), ONE, T.prow[:, :], False, False)], 3 * H,
-           K(v["z"], h) + ["onb", "prow", "bkn", v["keys"][0]], p)
-        for buf, off, sel, rd in (("zb", v["o"], T.bkn, v["keys"]), ("ab", v["ao"], T.bk2, v["ak"] + ["bk2"])):
-            lst = more(sums(buf, off, sel, 0, 2 * H), buf == "ab")
-            for q in range(0, 16, CUT):
-                mm(lst[q:q + CUT], 64 * CUT, rd, p)
-        sact(A("dh", h), PS(p, H, 2 * H), AF.Identity, H, (), K("dh", h), (p,), bias=-2040.0)
-        mm(sum([group([(lanes[u], T.id37[:, :], A("hE", h)[:, part[u]]), (lanes[u], A("dh", h), T.idb[:, part[u]])]) for u in R2], []), 256,
-           K("hE", h) + K("dh", h) + ["id37", "idb"], qt)
-        mm(sum([group([(C(L + lane(h, u), L + lane(h, u) + 64), T.idb[:, :], A(D0, h)[:, part[u]])]) for u in R2], []), 128, K(D0, h) + ["idb"], qt)
+        lst = group([(C(0, H), ONE, T.prow[:, :]), (C(0, H), T.idk[:, :], A("dh", h)), (C(0, H), T.idn[:, :], ch)])
+        mm(lst[:2], 2 * H, K("dh", h) + ["onb", "prow", "idk"], p)
+        mm(lst[2:], H, K("ch", h) + ["idn"], p)
         key = PS(p, 0, H)
-        vtt(key, key, ch, AL.subtract, H, 1, K("ch", h), [("key", h)], (p,))
         a, b = T.pm[:, 2 * H * h:2 * H * h + H], C(2 * H * h + H - 1, 2 * H * h - 1 if h else None, -1)
-        add("v", vt(H, 1), lambda: g.vector.tensor_tensor_scan(a, T.rst[:, :], R(key), 0.0, AL.mult, AL.min), ["rst", ("key", h)], [("pm", h)], (p,))
+        add("v", vt(H, 1), lambda: g.vector.tensor_tensor_scan(a, T.rst[:, :], R(key), 0.0, AL.mult, AL.min), ["rst"], [("pm", h)], (p,))
         add("v", vt(H, 1), lambda: g.vector.tensor_tensor_scan(T.pm[:, 2 * H * h + 2 * H - 1:2 * H * h + H - 1:-1], T.rst[:, :], T.pm[:, b], 0.0, AL.mult, AL.min),
-            ["rst", ("pm", h)], [("pn", h)])
-        vtt(A("eq", h), T.pm[:, 2 * H * h + H:2 * H * h + 2 * H], key, AL.is_equal, H, 1, [("pn", h), ("key", h)], K("eq", h), (p,))
-        mm(sum([group([(lanes[u], ch, T.idb[:, part[u]]), (lanes[u], A("eq", h), T.idn[:, part[u]])]) for u in R2], []), 256,
-           K("ch", h) + K("eq", h) + ["idb", "idn"], gt)
+            ["rst", ("pm", h)], [("pb", h)])
+        vtt(A("eq", h), T.pm[:, 2 * H * h + H:2 * H * h + 2 * H], key, AL.is_equal, H, 1, [("pb", h)], K("eq", h), (p,))
+        lst = rows(0, [(T.ngb[:, :], T.idp), (ch, T.idp)]) + rows(L, [(ch, T.idm)])
+        lst += [(lanes(L, u), x, y) for u in R2 for x, y in ((T.idb[:, :], A(D0, h)[:, part[u]]), (ONE, T.mid[:, :]))]
+        mm(opened(lst), 64 * len(lst), K("ch", h) + K(D0, h) + ["ngb", "idp", "idm", "idb", "onb", "mid"], gt)
+        mm(more(rows(0, [(A("eq", h), T.idm)]) + rows(L, [(A("eq", h), T.idp)]), True), 256, K("eq", h), gt)
 
     def finish(out, ut):
         qt, gt, at = ut
-        sact(T.asum[:, 0:8], PS(at, 0, 8), AF.Identity, 8, (), ["acol"], (at,), bias=2040.0 / 8, acc=T.acol[:, 0:1])
-        if QL["qi"] == "s":
-            sact(A("qi"), PS(qt, 0, L), AF.Identity, L, ["acol"], K("qi"), (qt,), bias=T.acol[:, 0:1])
-        else:
-            vts(A("qi"), PS(qt, 0, L), T.acol[:, 0:1], None, AL.add, None, L, 1, ["acol"], K("qi"), (qt,))
+        sact(T.asum[:, 0:8], PS(at, 0, 8), AF.Identity, 8, (), ["acol"], (at,), bias=(DM + 37 * MID) / 8, acc=T.acol[:, 0:1])
+        sact(A("qi"), PS(qt, 0, L), AF.Identity, L, ["acol"], K("qi"), (qt,), bias=T.acol[:, 0:1])
         vts(A("ni"), A("qi"), W - 1, None, AL.bitwise_and, None, L, 1, K("qi"), K("ni"))
-        vtt(A("wd"), A("ni"), PS(qt, L, 2 * L), AL.subtract, L, 1, K("ni"), K("wd"), (qt,))
-        vtt(A("mh"), A("wd"), PS(gt, 0, L), AL.mult, L, 1, K("wd"), K("mh"), (gt,))
-        vtt(A(out), A("mh"), PS(qt, L, 2 * L), AL.add, L, 1, K("mh"), K(out), (qt,))
+        vtt(A("wd"), A("ni"), PS(gt, 0, L), AL.add, L, 1, K("ni"), K("wd"), (gt,))
+        vtt(A(out), A("wd"), PS(gt, L, 2 * L), AL.max, L, 1, K("wd"), K(out), (gt,))
 
     def run(gens):
         gens = list(enumerate(gens))
@@ -501,73 +558,73 @@ def rank_program(g, core, T, topo):
         cur[0] = 0
 
     def home0(h):
-        column(0, 1, "L0a", h, "L1a", None)
-        out, to = [("L1a", h), ("L0a", h)] + [("x0", 1)] * (1 - h), [("L1i", h), ("L0i", h)] + [("xi", 1)] * (1 - h)
-        k = send(s1, [A(*x) for x in out], [A(*x) for x in to], "re%d" % h, sum([K(*x) for x in out], []))
-        recv("re%d" % h, k, HOP, sum([K(*x) for x in to], []))
+        column("L0a", h, "L1a", None)
+        k = send(s1, A("L0a", h, 0, 2 * H), A("L0i", h, 0, 2 * H), "re%d" % h, K("L0a", h) + K("L1a", h), sent[:2])
+        recv("re%d" % h, k, 2 * H, K("L0i", h) + K("L1i", h))
         sent.append(k[0])
         yield
-        step(0, 1, h, T.xs, KX, "L1a", X0, T.thd, ["thd"], "f1a", False, False)
+        step(0, 1, h, T.xs, KX, "L1a", X0, THD, ["thd"], "f1a", False, False)
         yield
 
-    sent = []
+    kh = send(helper(T, topo, rank), T.xs[:, 0:XCUT[2]], T.xs[:, 0:XCUT[2]], "rh", KX + ["pkA", "pkG"], kx0[:1], part=C(-8, None))
+    ops[kh[0]]["up"] = CUP
+    sent = [kh[0], kx1[0]]
     run(home0(h) for h in R2)
+    k = send(h2, T.dh0[:, 0:W // 2], T.dh2[:, 0:W // 2], "rd0", KDH[:1], sent, part=C(0, 8, 2))
+    recv("rd0", k, W // 2, [("dh2", 0)])
+    sent.append(k[0])
     for h in R2:
-        k = send(s1, [A("f1a", h)], [A("f1_0", h)], "rr%d" % h, K("f1a", h), sent)
-        recv("rr%d" % h, k, LAT["flags"], K("f1_0", h))
+        k = send(s1, A("f1a", h), A("f1_0", h), "rr%d" % h, K("f1a", h), sent, part=C(1, 8, 2))
+        recv("rr%d" % h, k, H, K("f1_0", h))
         sent.append(k[0])
-    k = send(h2, [T.dh0[:, :]], [T.dh2[:, :]], "rdh", KDH, sent)
-    recv("rdh", k, LAT["dh"], ["dh2"])
-    XN = lane_views("xrn", "xzn", lambda a, b: A("xi")[:, a:b], [K("xi", h) for h in R2], K(*XNW), sent[:1])
-    k = send(h2, [T.xs[:, :]], [T.xs2[:, :]], "rxs", KX, (k[0],))
-    recv("rxs", k, LAT["tab"], ["xs2"])
-    k = send(h2, [T.pk[:, 0:128], T.pk[:, 128:256], T.thd[:, 128:256]], [T.pk2[:, 0:128], T.pk2[:, 128:256], T.thd2[:, 128:256]], "rpk", ["pkA", "pkG", "thd"], (k[0],))
-    recv("rpk", k, LAT["tab"], ["pk2"])
+        if h == 0:
+            recv("rx0", kh, XCUT[1], [("xs2", 0)], LAT["hand"])
+    k = send(h2, T.dh0[:, W // 2:W + 128], T.dh2[:, W // 2:W + 128], "rd1", KDH[1:] + ["thd"], sent)
+    recv("rd1", k, W // 2 + 128, [("dh2", 1)])
+    recv("rx1", kh, XCUT[2] - XCUT[1], [("xs2", 1)])
     ktab = k[0]
+    XN = lane_views("xrn", "xzn", lambda a, b: A("xi")[:, a:b], [K("xi", h) for h in R2], K(*XNW))
+    KX2, KD2 = [("xs2", j) for j in R2], [("dh2", j) for j in R2]
 
     def away0(h):
         for x in "01":
-            move(QL["h0"], A("h%s_0" % x, h), A("L%si" % x, h), H, K("L%si" % x, h), K("h%s_0" % x, h), f=0.5)
-        column(0, 2, "L1i", h, "L2_0", "h2_0")
-        q = tile()
-        lst, rd = change(0, 1, h)
-        mm(lst, 256, rd + K("f1_0", h), q)
-        flagged(0, 1, h, "f1_0", q)
+            move(QL["h0"], A("h%s_0" % x, h), A("L%si" % x, h), H, K("L%si" % x, h), K("h%s_0" % x, h), f=0.5, bias=-MID)
+        column("L1i", h, "L2_0", "h2_0")
         yield
         yield from walk(0, h, tb, XN, ut)
 
-    tb = {"P": T.P0, "kp": KP0, "X": T.xs, "kx": KX, "thd": T.thd, "kth": ["thd", "thdm"],
-          "GT": T.pk[:, 0:128], "kgt": "pkG", "aG": T.pk[:, 128:264], "kag": ["pkA", "pkB"]}
+    tb = {"P": T.P0, "kp": KP0, "X": T.xs, "kx": KX, "thd": THD, "kth": ["thd", "thdm"],
+          "GT": PK[:, 0:128], "kgt": "pkG", "aG": PK[:, 128:264], "kag": ["pkA", "pkB"]}
     ut = (tile(), tile(), tile())
     run(away0(h) for h in R2)
     finish("ndo", ut)
-    k = send(dest(rank - 1), [A("ndo")], [A("ndi")], "rnh", K("ndo"))
-    recv("rnh", k, HOP, K("ndi"))
-    k = send(dest(rank - 3), [A("ndo")], [A("nd2")], "rn2", K("ndo"), (k[0],))
-    recv("rn2", k, HOP, K("nd2"))
+    k = send(dest(rank - 1), A("ndo"), A("ndi"), "rnh", K("ndo"))
+    recv("rnh", k, L, K("ndi"))
+    k = send(dest(rank - 3), A("ndo"), A("nd2"), "rn2", K("ndo"), (k[0],))
+    recv("rn2", k, L, K("nd2"))
 
     voters("L0b", 1)
-    move(QL["h0"], A("h0_1"), A("L0b"), L, K("L0b"), K("h0_1"), f=0.5)
+    move(QL["h0"], A("h0_1"), A("L0b"), L, K("L0b"), K("h0_1"), f=0.5, bias=-MID)
     X1 = lane_views("xr1", "xz1", lambda a, b: T.xs[:, S * a + 1:S * b:S], [KX, KX], K(*X1W), (ktab,))
-    KP1 = table("P1", T.xs, KX, T.dh2, ["dh2"] * 2, K(*PW1))
-    KP2 = table("P2", T.xs2, ["xs2"] * 2, T.dh2, ["dh2"] * 2, K(*PW1))
+    KP1 = table("P1", T.xs, lambda j: KX[j // 2:j // 2 + 1], T.dh2, KD2, K(*PW1))
+    KP2 = table("P2", T.xs2, lambda j: KX2[:j // 2 + 1], T.dh2, KD2, K(*PW2))
 
     move(QL["patch"], T.dgs[:, 0:W:S], A("ndi"), L, K("ndi"), KDG)
-    sact(A("yd0"), A("ndi"), AF.Copy, L, K("ndi"), K("yd0"))
+    move(QL["yd0"], A("yd0"), A("ndi"), L, K("ndi"), K("yd0"))
     add("y", 0.1, lambda: g.sync.dma_start(T.yd[:, 0:L], A("yd0")), K("yd0"), (), (), "ld5", 16, 2.0)
     k = pack("s", T.P1[:, 0:W:S], T.xs[:, 0:W:S], A("nd2"), L, K("nd2") + KX, KP1)
     ops[k]["up"] = ops[k - 1]["up"] = PUP
-    pack("s", T.P2[:, 0:W:S], T.xs2[:, 0:W:S], A("nd2"), L, K("nd2") + ["xs2"], KP2)
+    pack("s", T.P2[:, 0:W:S], T.xs2[:, 0:W:S], A("nd2"), L, K("nd2") + KX2, KP2)
 
     def home1(h):
-        column(1, 1, "L0b", h, "L1b", "h1_1")
+        column("L0b", h, "L1b", "h1_1")
         yield
-        step(1, 1, h, T.P1, KP1, "L1b", X1, T.thd, ["thd", "thdm"], "f1_1", True)
+        step(1, 1, h, T.P1, KP1, "L1b", X1, THD, ["thd"], "f1_1", True)
         yield
         yield from walk(1, h, tb, X1, ut)
 
-    tb = {"P": T.P2, "kp": KP2, "X": T.xs2, "kx": ["xs2"], "thd": T.thd2, "kth": ["pk2", "thd2m"],
-          "GT": T.pk2[:, 0:128], "kgt": "pk2", "aG": T.pk2[:, 128:264], "kag": ["pk2", "pk2B"]}
+    tb = {"P": T.P2, "kp": KP2, "X": T.xs2, "kx": KX2, "thd": THD2, "kth": [KD2[1], "thd2m"],
+          "GT": PK2[:, 0:128], "kgt": KX2[1], "aG": PK2[:, 128:264], "kag": [KX2[1], "pk2B"]}
     ut = (tile(), tile(), tile())
     run(home1(h) for h in R2)
     add("y", 0.1, lambda: g.sync.dma_start(T.ye[:, :], A("yef")), K("yef"), (), (), "ld6", 16, 2.0)
@@ -581,15 +638,16 @@ def rank_program(g, core, T, topo):
 CUP = 3.0
 PW = 0.02
 TURNS, SKEWS, WEIGHTS = 3, (2.0, 3.0), tuple((a, b) for a in (0.3, 0.5, 1.0) for b in (0.2, 0.3))
-CASES = ((1.5, 1.0, 0.9), (1.15, 1.05, 0.8), (1.9, 1.4, 1.2), (1.2, 1.35, 1.0), (1.9, 1.1, 1.1), (1.4, 1.1, 1.4))
-SHAKES, SWAPS = 600, 3000
+CASES = ((1.5, 1.0, 1.0, 1.0), (1.15, 1.05, 0.8, 1.2), (1.9, 1.4, 1.2, 1.0), (1.2, 1.35, 1.0, 0.7), (1.9, 1.1, 1.1, 1.5), (1.4, 1.1, 1.4, 1.3))
+SHAKES, SWAPS, WARM = 300, 16000, 0.2
 SEML, SEMQ = 0.08, 0.04
+LOADS = 7
 MADE = {}
 
 
 def times(ops, case):
-    gc, f, hop = case
-    return ([(o["d"] - o.get("n", 0) * GC * CY) * (f if o["e"] in "vspg" else 1.0) + o.get("n", 0) * gc * CY for o in ops], [o["lat"] * hop for o in ops])
+    gc, f, hop, wire = case
+    return ([(o["d"] - o.get("n", 0) * GC * CY) * (f if o["e"] in "vspg" else wire if o["e"] == "w" else 1.0) + o.get("n", 0) * gc * CY for o in ops], [o["lat"] * hop for o in ops])
 
 
 def draw(seed):
@@ -601,7 +659,7 @@ def schedule(ops, tiles, wide, bankof):
     key = (tuple(o["d"] for o in ops), tuple(o["e"] for o in ops))
     if key not in MADE:
         eng = [o["e"] for o in ops]
-        pre = [[(d, SEML if eng[d] != eng[k] else 0.0 if eng[k] == "p" or d in ops[k]["soft"] else SEMQ) for d in sorted(ops[k]["deps"])] for k in range(n)]
+        pre = [[(d, SEML if eng[d] != eng[k] else 0.0 if eng[k] in "pw" or d in ops[k]["soft"] else SEMQ) for d in sorted(ops[k]["deps"])] for k in range(n)]
         succ = [[] for _ in range(n)]
         for k in range(n):
             for d, gap in pre[k]:
@@ -609,18 +667,24 @@ def schedule(ops, tiles, wide, bankof):
         cases = [times(ops, c) for c in CASES]
         up = [o["up"] for o in ops]
 
-        def linked(more):
-            out = list(pre)
-            for k, d in more:
-                out[k] = out[k] + [(d, SEML if eng[d] != eng[k] else 0.0)]
-            return out
+        opens = {x[0]: t for t, x in enumerate(tiles) if x}
+        shuts = {x[-1]: [t for t, y in enumerate(tiles) if y and y[-1] == x[-1]] for x in tiles if x}
 
-        def worth(order, pre):
-            return sum(max(replay(eng, pre, order, c)[0]) / (b[0] * b[1]) ** 0.5 for c, b in zip(cases, CASES))
+        def worth(order):
+            tot, more, ways = 0.0, None, []
+            for c, b in zip(cases, CASES):
+                got = replay(eng, pre, order, c, more, opens, shuts, wide)
+                if got is None:
+                    return None
+                fin, why, more = got
+                tot += max(fin) / (b[0] * b[1]) ** 0.5
+                ways.append((fin, why))
+            return tot, more, ways
 
         def fore(c, pri):
             last = forwards(ops, eng, c, tiles, wide, pre, succ, pri)
-            return None if last is None else (worth(last[1], linked(last[3])), last, c, pri)
+            w = None if last is None else worth(last[1])
+            return None if w is None else (w[0], last, c, pri)
 
         best = None
         for c in cases[:2]:
@@ -647,65 +711,102 @@ def schedule(ops, tiles, wide, bankof):
             last = fore(best[2], pri)
             if last is not None and last[0] <= best[0]:
                 best = last
-        fin, order, banks, more = best[1]
-        MADE[key] = (polish(eng, linked(more), order, cases, worth), banks, more)
-    order, banks, more = MADE[key]
-    bankof.update(banks)
-    for k, d in more:
-        ops[k]["deps"].add(d)
+        order = polish(eng, pre, best[1][1], worth)
+        MADE[key] = (order, worth(order)[1])
+    order, more = MADE[key]
+    for k in more:
+        t, b, before = more[k]
+        bankof[t] = b
+        ops[k]["deps"].update(before)
     return order
 
 
-def replay(eng, pre, order, case):
+def replay(eng, pre, order, case, more, opens, shuts, wide):
     dur, lat = case
-    fin, why, free, last = [0.0] * len(eng), [None] * len(eng), {}, {}
+    fin, why, free, last = [0.0] * len(eng), [None] * len(eng), dict.fromkeys("vspgywn", 0.0), dict.fromkeys("vspgywn")
+    deal = more is None
+    if deal:
+        more, user, held = {}, [None] * 8, {}
+        at = [0.0] * 8
     for k in order:
         e = eng[k]
-        st, w = free.get(e, 0.0), (last.get(e), True)
+        st, w = free[e], None
         for d, gap in pre[k]:
             if fin[d] + gap > st:
-                st, w = fin[d] + gap, (d, False)
+                st, w = fin[d] + gap, d
+        if k in opens:
+            if deal:
+                t = opens[k]
+                if wide[t] == 2:
+                    cand = [(max(at[i], at[i + 1]), 0, i) for i in (0, 2, 4, 6) if at[i] is not None and at[i + 1] is not None]
+                else:
+                    cand = [(max(at[i] + SEML, st), at[i ^ 1] is not None, i) for i in range(7, -1, -1) if at[i] is not None]
+                if not cand:
+                    return None
+                b = min(cand)[2]
+                held[t] = range(b, b + wide[t])
+                more[k] = (t, b, [user[i] for i in held[t] if user[i] is not None])
+                for i in held[t]:
+                    at[i] = None
+            for d in more[k][2]:
+                if fin[d] + SEML > st and eng[d] != e:
+                    st, w = fin[d] + SEML, d
+        why[k] = (last[e], True) if w is None else (w, False)
         if e != "n":
             free[e], last[e] = st + dur[k], k
-        fin[k], why[k] = st + dur[k] + lat[k], w
-    return fin, why
+        fin[k] = st + dur[k] + lat[k]
+        if deal and k in shuts:
+            for t in shuts[k]:
+                for i in held[t]:
+                    at[i], user[i] = fin[k], k
+    return fin, why, more
 
 
-def polish(eng, pre, order, cases, worth):
-    n = len(eng)
-    cur, seed, pairs = worth(order, pre), 7, []
+def polish(eng, pre, order, worth):
+    got, seed, pairs = worth(order), 7, []
+    best = (got[0], order)
     deps = [set(d for d, gap in x) for x in pre]
+    after = [set() for x in pre]
+    for k, x in enumerate(deps):
+        for d in x:
+            after[d].add(k)
     for turn in range(SWAPS):
         if not pairs:
-            for c in cases:
-                fin, why = replay(eng, pre, order, c)
+            for fin, why in got[2]:
                 k = fin.index(max(fin))
                 while why[k][0] is not None:
-                    if why[k][1]:
+                    if why[k][1] and eng[k] not in "yw":
                         pairs.append((why[k][0], k))
                     k = why[k][0]
         seed = draw(seed)
         u, v = pairs[(seed >> 8) % len(pairs)]
-        a, b = order.index(u), order.index(v)
-        for x in range((seed >> 4) % 3):
+        way = 1 if (seed >> 7) % 2 else -1
+        lst, link = (order, deps) if way == 1 else (order[::-1], after)
+        if way == -1:
+            u, v = v, u
+        a, b = lst.index(u), lst.index(v)
+        for x in range((seed >> 4) % 4):
             y = a - 1
-            while y >= 0 and eng[order[y]] != eng[v]:
+            while y >= 0 and eng[lst[y]] != eng[v]:
                 y -= 1
             a = y if y >= 0 else a
-        need, engs, ahead = set(deps[v]), set(), []
-        for k in order[a:b][::-1]:
+        need, engs, ahead = set(link[v]), set(), []
+        for k in lst[a:b][::-1]:
             if k in need or eng[k] in engs:
                 ahead.append(k)
-                need |= deps[k]
+                need |= link[k]
                 if eng[k] != "n":
                     engs.add(eng[k])
-        if eng[v] in engs:
+        if eng[v] in engs or min(ahead + [u, v]) < LOADS:
             continue
-        new = order[:a] + ahead[::-1] + [v] + [k for k in order[a:b] if k not in ahead] + order[b + 1:]
-        w = worth(new, pre)
-        if w <= cur:
-            order, cur, pairs = new, w, []
-    return order
+        new = (lst[:a] + ahead[::-1] + [v] + [k for k in lst[a:b] if k not in ahead] + lst[b + 1:])[::way]
+        w = worth(new)
+        seed = draw(seed)
+        if w is not None and w[0] <= got[0] + WARM * (1.0 - turn / SWAPS) * ((seed >> 8) % 64) / 64.0:
+            order, got, pairs = new, w, []
+            if w[0] < best[0]:
+                best = (w[0], new)
+    return best[1]
 
 
 def backwards(eng, case, pre, succ, fin, back):
@@ -742,7 +843,7 @@ def forwards(ops, eng, case, tiles, wide, pre, succ, pri):
     left = [len(x) for x in pre]
     ready = [k for k in range(n) if left[k] == 0]
     fin = [0.0] * n
-    free = {e: 0.0 for e in "vspgy"}
+    free = {e: 0.0 for e in "vspgyw"}
     order = []
     rt = [0.0] * n
     free["n"] = -1.0
@@ -805,8 +906,8 @@ def emit(g, T, ENG, CSEM, ops, order, nlocal):
     for k in order:
         o = ops[k]
         e = o["e"]
-        if e == "n":
-            done[k] = (o["sem"], o["inc"], {})
+        if e in "nw":
+            done[k] = None if o["sem"] == "-" else (o["sem"], o["inc"], {})
             continue
         q = ENG[e]
         need = {}

from concourse.bass import DstId, RemoteDMATransfer
from concourse.mybir import dt, AluOpType, AxisListType, ActivationFunctionType

W, L, S, N = 2048, 256, 8, 8
H = 128
SB = 4
SW = 16 * H // SB
HW = 16 * H
SH = 65536.0
MID = 1024.0
MAGIC = 1.5 * 2.0 ** 39
WHOLE = 1.5 * 2.0 ** 23
DM = 2040.0
BIG = 4096.0
AL = AluOpType
AF = ActivationFunctionType

R2 = (0, 1)
U_ = ["L0a", "L1a", "L0i", "L1i", "L0b", "L1b"] + ["%s_%d" % (n, t) for n in ("L2", "L3", "L4") for t in R2]
H_ = ["wd", "ndo", "ndi", "nd2", "d3", "pn", "dh"] + ["%s_%d" % (n, t) for n in ("h0", "h1", "h2", "h3", "h4", "m1", "m2", "m3") for t in R2]
F_ = ["yd0", "yd1", "yef"]
B_ = ["x0", "xi", "xz0", "xzn", "xz1", "f1a", "f1_0", "f1_1", "bs", "sq", "tt", "eq", "ub", "pz"] + ["%s_%d" % (n, t) for n in ("f2", "f3") for t in R2]
I_ = ["qi", "ni"]
POOLS = {"PU": (U_, "uint16"), "PH": (H_, "float16"), "PF": (F_, "float32"), "PB": (B_, "bfloat16"), "PI": (I_, "int32")}
SLOT = {}
SCRATCH = {}
for _p in POOLS:
    _names, _dt = POOLS[_p]
    SCRATCH[_p] = ("sbuf", [128, 256 * len(_names)], _dt)
    for _k, _n in enumerate(_names):
        SLOT[_n] = (_p, 256 * _k, H)
for _k, _n in enumerate(("L0a", "L1a", "L0i", "L1i")):
    SLOT[_n] = ("PU", 512 * (_k // 2) + H * (_k % 2), 2 * H)
for _n, _w, _dt in (
        ("dgs", W, "int32"), ("xs", W + 272, "bfloat16"), ("xs2", W + 272, "bfloat16"), ("dh0", W + 256, "float16"), ("dh2", W + 256, "float16"),
        ("P0", W, "float32"), ("P1", W, "float32"), ("P2", W, "float32"),
        ("xr0", HW, "bfloat16"), ("xr1", HW, "bfloat16"), ("xrn", HW, "bfloat16"),
        ("zf", 32 * L, "float32"), ("zb", 32 * L, "bfloat16"), ("ab", 32 * L, "bfloat16"),
        ("gh", 16 * L, "float16"), ("ed", 2048, "bfloat16"), ("onb", 128, "bfloat16"), ("ngb", 128, "bfloat16"),
        ("idb", 128, "bfloat16"), ("idq", 128, "bfloat16"), ("id37", 128, "bfloat16"), ("idp", 128, "bfloat16"), ("idn", 128, "bfloat16"),
        ("ids", 128, "bfloat16"), ("idk", 128, "bfloat16"), ("idr", 128, "bfloat16"), ("idt", 128, "bfloat16"), ("idm", 128, "bfloat16"), ("mid", 64, "bfloat16"), ("sel", 384, "float32"),
        ("blk0", 128, "bfloat16"), ("blk", 128, "bfloat16"), ("xsel", 384, "bfloat16"), ("zsel", 384, "bfloat16"), ("bk2", 256, "bfloat16"),
        ("prow", 128, "bfloat16"), ("rst", 128, "float32"), ("pm", 512, "float32"), ("iq", 128, "float32"), ("chb", 288, "bfloat16"),
        ("thi", 128, "int32"), ("tii", 768, "int32"), ("tib", 768, "bfloat16"), ("gq", 512, "bfloat16"), ("gj", 128, "bfloat16"),
        ("asum", 8, "float32"), ("acol", 8, "float32")):
    SCRATCH[_n] = ("sbuf", [128, _w], _dt)
for _k in range(4):
    SCRATCH["pair%d" % _k] = ("psum", [128, 1024], "float32")
SEMAPHORES = ["cv", "cs", "cp", "cg", "lsem", "rx", "ry", "rh", "rd0", "rd1", "rx0", "rx1", "rnh", "rn2", "re0", "re1", "rr0", "rr1"] + ["ld%d" % k for k in range(10)]

QL = {"list": "s", "col": "vs", "colh": "v", "vote": "vvss", "h0": "v", "L4": "s", "ye": "s", "patch": "v",
      "dh0": "gs", "yd0": "g", "P0": "vsvs", "P1": "vsvs", "P2": "svsv", "xr0": "sv", "xrn": "g", "xr1": "g", "const": "s"}
CARRY = {(0, 1): (), (0, 2): (), (0, 3): (1, 2), (1, 1): (), (1, 2): (1,), (1, 3): (2,)}
X1W = ("ub", 1)
XNW = ("L1i", 0)
PW1, PW2 = ("ub", 1), ("ch", 1)
PUP = 0.3

CY = 0.83e-3
PC = 0.42e-3
GC = 1.5
HOP = 1.8
WIRE = 256 / 45e3
LAT = {"x": 3.2, "d0": 5.2, "d1": 7.2, "x1": 8.2, "small": 2.5, "first": 2.0, "hand": 7.0}
XCUT = (0, 1152, W + 256)


def helper(T, topo, rank):
    c, d = T.cores[rank], T.cores[(rank - 2) % N]
    return [x for x in topo.cores_of(c) if x not in T.cores and topo.die(x) == topo.die(c) and topo.may_write(x, d)][0]


def hand_on(g, core, T, topo, rank):
    c, d = T.cores[rank], T.cores[(rank - 2) % N]
    rid, pid = topo.addr(d, core)
    es = topo.engines(core, d)[0:8]
    g.wait_ge(T.sem.rh, len(topo.engines(c, core)[-8:]))
    for j in R2:
        g.remote_dma(T.xs2[:, XCUT[j]:XCUT[j + 1]], T.xs[:, XCUT[j]:XCUT[j + 1]], T.sem["rx%d" % j], T.sem.lsem, pid, rid, sum(1 << e for e in es))
        g.wait_ge(T.sem.lsem, (j + 1) * len(es))


def rank_program(g, core, T, topo):
    rank = T.rank_of(core)
    if rank is None:
        for r in range(N):
            if helper(T, topo, r) == core:
                hand_on(g, core, T, topo, r)
        return
    cores = T.cores
    ops, lastw, readers, tiles, wide, own = [], {}, {}, [], [], {}
    bankof = {}
    cur = [0]
    ENG = {"v": g.vector, "s": g.scalar, "p": g.tensor, "g": g, "y": g.sync}
    CSEM = {"v": "cv", "s": "cs", "p": "cp", "g": "cg"}

    def add(eng, dur, fn, r=(), w=(), ps=(), sem=None, inc=1, lat=0.0, extra=()):
        k = len(ops)
        deps = set(extra)
        keys_w = list(w) + [("ps", t) for t in ps]
        for x in r:
            if x in lastw:
                deps.add(lastw[x])
        for x in keys_w:
            if x in lastw:
                deps.add(lastw[x])
            deps.update(readers.get(x, ()))
        for x in r:
            readers.setdefault(x, []).append(k)
        for x in keys_w:
            lastw[x] = k
            readers[x] = []
        deps.discard(k)
        hard = set(extra)
        for x in list(r) + list(w):
            hard.update(own.get(("w", x), ()))
        for x in w:
            hard.update(own.get(("r", x), ()))
            own.setdefault(("w", x), []).append(k)
        for x in r:
            own.setdefault(("r", x), []).append(k)
        soft = set(d for d in deps if ops[d]["e"] == eng and d not in hard and ps)
        ops.append({"e": eng, "d": dur, "f": fn, "deps": deps, "ps": list(ps), "sem": sem, "inc": inc, "lat": lat, "c": cur[0], "soft": soft, "up": 0.0})
        for t in ps:
            tiles[t].append(k)
        return k

    def early(k):
        ops[k]["up"] = 1000.0 - 20.0 * k

    def tile(banks=1):
        tiles.append([])
        wide.append(banks)
        return len(tiles) - 1

    def ps(t, c):
        o = 512 * (bankof[t] % 2)
        return T["pair%d" % (bankof[t] // 2)][:, o + c.start:o + c.stop:c.step]

    def PS(t, a, b):
        return (lambda: ps(t, slice(a, b)),)

    def R(x):
        return x[0]() if isinstance(x, tuple) else x

    def A(name, h=None, a=0, b=H):
        p, o, far = SLOT[name]
        if h is None:
            return T[p][:, o:o + L]
        return T[p][:, o + far * h + a:o + far * h + b]

    def K(name, h=None, s=None):
        return [(name, a, b) for a in (R2 if h is None else (h,)) for b in (R2 if s is None else (2 * s // SB,))]

    def lane(h, u):
        return 64 * h + H * u

    def vt(n, f):
        return 0.04 + max(64, n * f) * CY

    def vcopy(out, in_, n, f, r, w, p=()):
        return add("v", vt(n, f), lambda: g.vector.tensor_copy(out, R(in_)), r, w, p)

    def vts(out, in0, s1, s2, o0, o1, n, f, r, w, p=()):
        def em():
            if o1 is None:
                return g.vector.tensor_scalar(out, R(in0), s1, None, o0)
            return g.vector.tensor_scalar(out, R(in0), R(s1), R(s2), o0, o1)
        return add("v", vt(n, f), em, r, w, p)

    def vtt(out, in0, in1, op, n, f, r, w, p=()):
        return add("v", vt(n, f), lambda: g.vector.tensor_tensor(R(out), R(in0), R(in1), op), r, w, p)

    def vset(out, val, n, f, w):
        return add("v", vt(n, f), lambda: g.vector.memset(out, val), (), w)

    def sact(out, in_, func, n, r, w, p=(), bias=0.0, scale=1.0, acc=None):
        def em():
            if acc is not None:
                return g.scalar.activation(out, R(in_), func, bias=bias, scale=scale, accum_out=acc)
            return g.scalar.activation(out, R(in_), func, bias=bias, scale=scale)
        return add("s", 0.06 + n * CY, em, r, w, p)

    def gsel(out, in_, pat, op, base, cm, n, r, w, after=()):
        return add("g", 0.17 + 2 * n * CY, lambda: g.affine_select(out, in_, pat, op, 0.0, base, cm), r, w, extra=after)

    def move(e, out, in_, n, r, w, p=(), f=1, scale=1.0, bias=0.0, after=()):
        if e == "g":
            return gsel(out, in_, [[0, n]], AL.is_ge, 0, 0, n, r, w, after)
        if e == "s":
            return sact(out, in_, AF.Identity if bias else AF.Copy, n, r, w, p, bias, scale)
        if bias or not isinstance(scale, float) or scale != 1.0:
            return vts(out, in_, scale, bias, AL.mult, AL.add, n, f, r, w, p)
        return vcopy(out, in_, n, f, r, w, p)

    def mm(lst, cyc, r, p):
        def em():
            out = None
            for (c, lhs, rhs, st, sp) in lst:
                out = g.tensor.matmul(ps(p, c), lhs, rhs, st, sp)
            return out
        return add("p", 0.03 + cyc * PC, em, r, (), (p,))

    def group(lst):
        return [x + (i == 0, i == len(lst) - 1) for i, x in enumerate(lst)]

    def more(lst, last=False):
        return [x + (False, last and i == len(lst) - 1) for i, x in enumerate(lst)]

    def opened(lst):
        return [lst[0] + (True, False)] + more(lst[1:])

    C = slice
    ONE = T.onb[:, :]
    PK, PK2, THD, THD2 = T.xs[:, W:W + 272], T.xs2[:, W:W + 272], T.dh0[:, W:W + 256], T.dh2[:, W:W + 256]

    def load(eng, buf, src, sem, lat):
        early(add(eng, 0.1, lambda: ENG[eng].dma_start(buf, src), (), [(sem, "ld")], (), sem, 16, lat))

    load("y", T.thi[0:1, :], T.th[:, :], "ld4", LAT["small"])
    load("y", T.xs[:, 0:W // 2], T.xv[:, 0:W // 2], "ld0", LAT["x"])
    load("y", T.dgs[:, 0:W // 2], T.dg[:, 0:W // 2], "ld1", LAT["d0"])
    load("y", T.dgs[:, W // 2:W], T.dg[:, W // 2:W], "ld8", LAT["d1"])
    load("y", T.xs[:, W // 2:W], T.xv[:, W // 2:W], "ld9", LAT["x1"])
    load("s", T.tii[0:1, 0:384], T.ti[:, :], "ld2", LAT["small"])
    load("s", T.tii[0:1, 384:768], T.sg[:, :], "ld3", LAT["small"])
    KX, KDG = [("ld0", "ld"), ("ld9", "ld")], [("ld1", "ld"), ("ld8", "ld")]

    def dest(r):
        return cores[r % N]

    cnt = {"l": 0}

    def send(d, src, dst, sem, rd, after=(), dur=0.7, part=C(0, 8)):
        rid, pid = topo.addr(d, core)
        es = topo.engines(core, d)[part]
        cnt["l"] += len(es)
        return add("g", dur, lambda: g.remote_dma(dst, src, T.sem[sem], T.sem.lsem, pid, rid, sum(1 << e for e in es)), rd, (), (), "-", 0, 0.0, after), len(es)

    def recv(sem, sent, cols, keys, lat=0.0):
        k = add("n", 0.0, None, (), (), (), "-", 0, lat, [sent[0]])
        k = add("w", cols * WIRE, None, (), ["wire"], (), "-", 0, 0.0, [k])
        return add("n", 0.0, None, (), keys, (), sem, sent[1], HOP, [k])

    s1, h2 = dest(rank + 1), dest(rank - 2)
    for h in R2:
        sact(A("x0", h), T.xs[:, h * W // 2:(h + 1) * W // 2:S], AF.Copy, H, [KX[h]], K("x0", h))
    kx0 = send(s1, A("x0", 0), A("xi", 0), "rx", K("x0", 0), dur=0.7 + LAT["first"])
    recv("rx", kx0, H, K("xi", 0))
    kx1 = send(s1, A("x0", 1), A("xi", 1), "ry", K("x0", 1), kx0[:1])
    recv("ry", kx1, H, K("xi", 1))

    early(vset(ONE, 1.0, 128, 0.5, ["onb"]))
    early(vset(T.ed[:, :], 0.0, 2048, 0.5, ["ed"]))
    early(add("g", 0.13 + 256 * CY, lambda: g.iota(T.iq[:, :], [[0, 8], [1, 16]], 0, 0, allow_small_or_imprecise_dtypes=True), (), ["iq"]))
    early(gsel(T.idb[:, :], ONE, [[-1, 128]], AL.is_equal, 0, 1, 128, ["onb"], ["idb"]))
    early(gsel(T.blk0[:, :], ONE, [[-16, 8], [0, 16]], AL.is_ge, 0, 1, 128, ["onb"], ["blk0"]))
    early(gsel(T.blk[:, :], T.blk0[:, :], [[16, 8], [0, 16]], AL.is_ge, 15, -1, 128, ["blk0"], ["blk"]))
    first = len(ops)
    vset(T.ngb[:, :], -1.0, 128, 0.5, ["ngb"])
    vset(T.mid[:, :], MID / 128, 64, 0.5, ["mid"])
    for z in ("xz0", "xzn", "xz1"):
        vset(A(z), 0.0, L, 0.5, K(z))
    for x in range(8):
        vcopy(T.ed[:, 16 * x:16 * x + 129 * 15 + 1:129], T.idb[:, 16 * x:16 * x + 16], 16, 0.5, ["idb"], ["ed"])
    for name, val in (("ids", SH), ("idn", -1.0), ("idp", BIG), ("idm", -BIG), ("idq", 0.5), ("idr", 0.25), ("idt", -0.5), ("id37", 37.0), ("idk", 1.0 / 8192)):
        move(QL["const"], T[name][:, :], T.idb[:, :], 128, ["idb"], [name], f=0.5, scale=val)
    move(QL["const"], T.sel[:, 0:128], T.idb[:, :], 128, ["idb"], ["idf"], scale=SH)
    for j in (1, 2):
        c = C(128 * j, 128 * j + 128)
        move(QL["const"], T.sel[:, c], T.blk[:, :], 128, ["blk"], ["sel"], scale=-1.0)
        for x in ("xsel", "zsel"):
            move("v", T[x][:, c], T.blk[:, :], 128, ["blk"], [x], f=0.5, scale=-1.0)
        move("v", T.bk2[:, 128 * j - 128:128 * j], T.blk[:, :], 128, ["blk"], ["bk2"], f=0.5, scale=2.0)
    for x, val in (("xsel", -SH), ("zsel", SH)):
        move("v", T[x][:, 0:128], T.idb[:, :], 128, ["idb"], [x], f=0.5, scale=val)
    BN = T.zsel[:, 128:256]
    for x, y in (("pk", PK), ("pk2", PK2)):
        vcopy(y[:, 256:264], T.blk[:, 0:128:16], 8, 0.5, ["blk"], [x + "B"])
    move("v", T.prow[0:64, :], T.iq[0:64, :], 128, ["iq"], ["prow"], scale=2.0 ** -24, bias=2.0 ** -25)
    vset(T.prow[64:128, :], DM / 8192 / 64, 128, 0.5, ["prow"])
    vset(T.rst[:, :], 1.0, 128, 1, ["rst"])
    vset(T.rst[:, 0:128:16], 0.0, 8, 1, ["rst"])
    move("v", THD[:, 0:128], ONE, 128, ["onb"], ["thd"], f=0.5, scale=0.0)
    move("v", THD[0:1, 0:128], T.thi[0:1, :], 128, [("ld4", "ld")], ["thd"], scale=-1.0, bias=2048.0)
    for x, y in (("thd", THD), ("thd2", THD2)):
        move("v", y[:, 128:256], ONE, 128, ["onb"], [x + "m"], f=0.5, scale=-DM / 128)

    p0 = tile()
    for x in R2:
        move("vs"[x], T.tib[0:1, 384 * x:384 * x + 384], T.tii[0:1, 384 * x:384 * x + 384], 384, [("ld%d" % (2 + x), "ld")], [("tib", x)])
    mm([(C(3 * x + j, 3 * x + j + 1), T.tib[0:1, 384 * x + j:384 * x + 384:3], T.onb[0:1, 0:1], True, True) for x in R2 for j in range(3)], 6 * 64,
       [("tib", 0), ("tib", 1), "onb"], p0)
    for j in range(3):
        vts(T.gq[:, 128 * j:128 * j + 128], T.iq[:, :], PS(p0, j, j + 1), PS(p0, 3 + j, 4 + j), AL.is_equal, AL.mult, 128, 1, ["iq"], [("gq", j)], (p0,))
    vtt(T.gq[:, 384:512], T.gq[:, 0:128], T.gq[:, 128:256], AL.add, 128, 2, [("gq", 0), ("gq", 1)], [("gq", 3)])
    vtt(T.gq[:, 0:128], T.gq[:, 384:512], T.gq[:, 256:384], AL.add, 128, 2, [("gq", 3), ("gq", 2)], [("gq", 0)])
    vtt(T.gj[:, :], T.gq[:, 0:128], T.blk[:, :], AL.mult, 128, 2, [("gq", 0), "blk"], ["gj"])
    sact(PK[:, 128:256], T.gj[:, :], AF.Abs, 128, ["gj"], ["pkA"])
    p0 = tile()
    mm(group([(C(0, 128), T.gj[:, :], T.idb[:, :])]), 128, ["gj", "idb"], p0)
    sact(PK[:, 0:128], PS(p0, 0, 128), AF.Copy, 128, (), ["pkG"], (p0,))
    for o in ops[first:]:
        o["up"] = CUP if o["e"] in "vs" else 0.0

    def lane_views(buf, z, col, rk, when, after=()):
        e = QL[buf]
        for p in range(16):
            move(e[p % len(e)], T[buf][:, p:HW:16], col(0, H), H, rk[0], [(buf, p)], f=0.5, after=after)
        for h in R2:
            move(e[0], A(z, h, 64, H), col(lane(h, 1), lane(h, 1) + 64), 64, rk[1], K(z, h), f=0.5, after=after)
        return {"xr": T[buf], "kxr": [(buf, p) for p in range(16)], "z": z, "col": col, "kc": rk[1] + when}

    def voters(name, t):
        for h in R2:
            for u in R2:
                move(QL["vote"][2 * t + u], A(name, h, 64 * u, 64 * u + 64), T.dgs[:, S * lane(h, u) + t:S * (lane(h, u) + 64):S], 64, [KDG[u]], K(name, h, 2 * u))

    def pack(e, out, x, d, n, rd, w):
        p = tile()
        mm(group([(C(0, n), T.ids[:, :], x), (C(0, n), T.idb[:, :], d)]), 2 * n, rd + ["ids", "idb"], p)
        return move(e, out, PS(p, 0, n), n, (), w, (p,), scale=1.0 / SH, bias=-MID / SH)

    def table(name, x, kx, d, kd, when=()):
        for j in range(4):
            c = C(512 * j, 512 * j + 512)
            pack(QL[name][j], T[name][:, c], x[:, c], d[:, c], 512, kx(j) + [kd[j // 2]] + list(when), [(name, j)])
        return [(name, j) for j in range(4)]

    first = len(ops)
    X0 = lane_views("xr0", "xz0", lambda a, b: A("x0")[:, a:b], [K("x0", h) for h in R2], [])
    voters("L0a", 0)
    for o in ops[first:]:
        o["up"] = CUP
    for h in R2:
        c = C(h * W // 2, (h + 1) * W // 2)
        move(QL["dh0"][h], T.dh0[:, c], T.dgs[:, c], W // 2, [KDG[h]], [("dh0", h)])
    KDH = [("dh0", h) for h in R2]
    KP0 = table("P0", T.xs, lambda j: KX[j // 2:j // 2 + 1], T.dh0, KDH)

    par = {}
    turned = set()

    def room(buf, h, two=True):
        n = par.get((buf, h), 0)
        par[(buf, h)] = n + 1
        n = n % 2 if two else 0
        return n * 16 * L + h * HW, [(buf, n, h, s) for s in range(SB)]

    def gather(eng, buf, o, keys, win, lst, h, s, n, rd, xr=None):
        def em():
            out, src = T[buf][:, o + s * SW:o + (s + n) * SW], win[:, 0:W].indirect(A(lst, h, s * H // SB, (s + n) * H // SB))
            if eng == "s":
                return g.scalar.activation(out, src, AF.Copy)
            if xr is None:
                return g.vector.tensor_copy(out, src)
            return g.vector.tensor_tensor(out, src, xr[:, (2 * h + s) * SW:(2 * h + s + n) * SW], AL.subtract)
        ops[add(eng, 0.06 + n * SW * GC * CY, em, rd + K(lst, h, s), keys[s:s + n])]["n"] = n * SW

    def column(lst, h, Lk, hk):
        o, keys = room("gh", h, False)
        for u in R2:
            gather("vs"[u], "gh", o, keys, T.dgs, lst, h, 2 * u, 2, KDG)
        for u in R2:
            p, a = tile(), o + u * HW // 2
            mm(group([(C(0, 64), T.ed[:, q * 128:(q + 1) * 128], T.gh[:, a + q:a + HW // 2:16]) for q in range(16)]), 1024, keys[2 * u:2 * u + 2] + ["ed"], p)
            move(QL["col"][u], A(Lk, h, 64 * u, 64 * u + 64), PS(p, 0, 64), 64, (), K(Lk, h, 2 * u), (p,))
        if hk:
            move(QL["colh"], A(hk, h), A(Lk, h), H, K(Lk, h), K(hk, h), f=0.5, bias=-MID)

    def view(win, kw, lst, h, X, packed):
        buf = "zf" if packed else "zb"
        o, keys = room(buf, h)
        ao, ak = room("ab", h)
        gather("v", buf, o, keys, win, lst, h, 0, 2, kw + X["kxr"], X["xr"])
        gather("s", buf, o, keys, win, lst, h, 2, 2, kw)
        sact(T.ab[:, ao:ao + 2 * SW], T[buf][:, o:o + 2 * SW], AF.Relu, 2 * SW, keys[0:2], ak[0:2])
        if h not in X:
            X[h] = tile(2)
            for s in R2:
                a = lane(h, 1) + 32 * s
                mm([(C(SW * s + q, SW * s + SW, 16), T.idb[:, :], X["col"](a, a + 32), True, True) for q in range(16)], 1024, ["idb"] + X["kc"], X[h])
        vtt(T.ab[:, ao + 2 * SW:ao + 4 * SW], T[buf][:, o + 2 * SW:o + 4 * SW], PS(X[h], 0, 2 * SW), AL.max, 2 * SW, 1, keys[2:4], ak[2:4], (X[h],))
        return {"o": o, "keys": keys, "ao": ao, "ak": ak, "z": X["z"]}

    def sums(buf, o, sel, a, b):
        return [(C(a + q, b, 16), T[buf][:, o + q:o + HW:16], sel[:, q:b - a:16]) for q in range(16)]

    def turn(c, name, h, ident):
        return (c, ident, A(name, h)) if (name, h) in turned else (c, A(name, h), ident)

    def back(c, name, h, ident):
        return (c, A(name, h), ident) if (name, h) in turned else (c, ident, A(name, h))

    def change(t, k, h):
        a, b = "h%d_%d" % (k - 1, t), "h%d_%d" % (k, t)
        c = C(2 * H, 3 * H)
        return group([turn(c, a, h, T.idb[:, :]), turn(c, b, h, T.idn[:, :])]), K(a, h) + K(b, h) + ["idb", "idn"]

    def flagged(t, k, h, fk, q):
        mk = "m%d_%d" % (k, t)
        vtt(A(mk, h), A(fk, h), PS(q, 2 * H, 3 * H), AL.mult, H, 1, K(fk, h), K(mk, h), (q,))
        turned.add((mk, h))

    def step(t, k, h, win, kw, lst, X, thd, kth, fk, packed, here=True):
        v = view(win, kw, lst, h, X, packed)
        q = tile()
        b = 3 * H if k == 3 else 2 * H
        rd = ["onb", "zsel"] + K(lst, h) + kth + K(v["z"], h)
        if k == 3:
            h2 = "h2_%d" % t
            mm(opened([(C(0, b), A(v["z"], h), T.xsel[:, :]), (C(H, 2 * H), ONE, thd[:, 0:H]), turn(C(0, H), h2, h, T.idn[:, :])]), 5 * H,
               rd + ["xsel", "idn"] + K(h2, h), q)
        elif here:
            pre, r2 = change(t, k, h)
            mm(pre, 2 * H, r2 + K(lst, h), q)
        fixed = [(C(H, 2 * H), ONE, thd[:, 0:H]), (C(H, 2 * H), A(v["z"], h), BN)]
        if packed:
            lst = (more if k == 3 else opened)(sums("zf", v["o"], T.sel, 0, b))
            for q0 in range(0, 16, 4):
                mm(lst[q0:q0 + 4], 1024, v["keys"] + ["idf", "sel"], q)
            if k < 3:
                mm(more(fixed), 2 * H, rd, q)
        else:
            mm(opened(fixed), 2 * H, rd, q)
            mm(more(sums("zb", v["o"], BN, H, 2 * H)), 1024, v["keys"], q)
        lst, rd = sums("ab", v["ao"], T.bk2, H, b), v["ak"] + ["bk2"]
        before = ["f%d_%d" % (x, t) for x in CARRY[t, k]]
        for fp in before:
            lst, rd = lst + [(C(H, 2 * H), T.idp[:, :], A(fp, h))], rd + K(fp, h) + ["idp"]
        mm(more(lst, True), 1024 + 128 * len(before), rd, q)
        hk, Lk = "h%d_%d" % (k + 1, t), "L%d_%d" % (k + 1, t)
        if packed:
            vts(A("tt", h), PS(q, 0, H), MAGIC, MAGIC, AL.add, AL.subtract, H, 1, (), K("tt", h), (q,))
            vtt(A(hk, h), PS(q, 0, H), A("tt", h), AL.subtract, H, 1, K("tt", h), K(hk, h), (q,))
            turned.add((hk, h))
        if packed and k < 3:
            p = tile()
            mm(group([(C(0, H), A(hk, h), T.idb[:, :])]), 128, K(hk, h) + ["idb"], p)
            move(QL["list"], A(Lk, h), PS(p, 0, H), H, (), K(Lk, h), (p,), bias=MID)
        sign = -1.0 if k == 3 else 1.0
        sact(A(fk, h), PS(q, H, 2 * H), AF.Sign, H, (), K(fk, h), (q,), bias=sign * (0.5 - 2048.0 + BIG * len(before)), scale=sign)
        if k == 3:
            mk = "m3_%d" % t
            vtt(A(mk, h), A(fk, h), A(hk, h), AL.mult, H, 1, K(fk, h) + K(hk, h), K(mk, h))
            turned.add((mk, h))
            vts(A("d3", h), PS(q, 2 * H, 3 * H), WHOLE, WHOLE + DM, AL.add, AL.subtract, H, 1, (), K("d3", h), (q,))
        elif here:
            flagged(t, k, h, fk, q)

    def walk(t, h, tb, X, ut):
        for k in (2, 3):
            step(t, k, h, tb["P"], tb["kp"], "L%d_%d" % (k, t), X, tb["thd"], tb["kth"], "f%d_%d" % (k, t), True)
            if k < 3:
                yield
        L4 = "L4_%d" % t
        half, quarter = T.idq[:, :], T.idr[:, :]
        terms = [("h0", half), ("h2", half), ("m1", half), ("m2", half)]
        if t == 0:
            q = tile()
            c = C(2 * H, 3 * H)
            ys = ["h1_0", "h2_0", "m2_0"]
            mm(group([turn(c, "h0_0", h, T.idb[:, :])] + [turn(c, x, h, T.idt[:, :]) for x in ys]), 4 * H,
               sum([K(x, h) for x in ys], K("h0_0", h) + K("f1_0", h)) + ["idb", "idt"], q)
            flagged(0, 1, h, "f1_0", q)
            terms = [("h0", half), ("h1", quarter), ("h2", quarter), ("m2", quarter), ("m1", half)]
        terms = [("%s_%d" % (x, t), y) for x, y in terms + [("h4", half), ("m3", half)]]
        kt = sum([K(x, h) for x, y in terms], [])
        p = tile()
        lst = group([back(C(0, H), x, h, y) for x, y in terms])
        mm(lst[:-1], (len(lst) - 1) * 128, kt[:-2] + ["idq", "idr"], p)
        mm(lst[-1:], 128, kt[-2:], p)
        move(QL["L4"], A(L4, h), PS(p, 0, H), H, (), K(L4, h), (p,), bias=MID)
        yield
        last(t, h, tb, X, terms, kt)
        ballot(t, h, tb, ut)
        yield

    def last(t, h, tb, X, terms, kt):
        v = view(tb["X"], tb["kx"], "L4_%d" % t, h, X, False)
        q = tile()
        h3, f3 = "h3_%d" % t, "f3_%d" % t
        c = C(3 * H, 4 * H)
        mm(group([turn(c, x, h, y) for x, y in terms] + [turn(c, h3, h, T.idn[:, :])]), (len(terms) + 1) * H, kt + K(h3, h) + ["idn"], q)
        mm(opened([(C(0, 3 * H), A(v["z"], h), T.xsel[:, :]), (C(H, 3 * H), ONE, tb["thd"][:, :]), (C(0, H), T.idn[:, :], A("tt", h)),
                   (C(H, 2 * H), T.idp[:, :], A(f3, h)), (C(2 * H, 3 * H), T.idn[:, :], A("d3", h))]),
           8 * H, K(v["z"], h) + K("tt", h) + K(f3, h) + K("d3", h) + tb["kth"] + ["onb", "xsel", "idp"], q)
        mm(more(sums("zb", v["o"], T.zsel, 0, 3 * H)), 1024, v["keys"] + ["zsel"], q)
        mm(more(sums("ab", v["ao"], T.bk2, H, 3 * H), True), 1024, v["ak"] + ["bk2"], q)
        vts(A("ub", h), PS(q, H, 2 * H), 2048.0 + BIG - 0.5, None, AL.is_lt, None, H, 1, (), K("ub", h), (q,))
        vtt(A("pz", h), A("ub", h), PS(q, 0, H), AL.mult, H, 1, K("ub", h), K("pz", h), (q,))
        pd = PS(q, 2 * H, 3 * H)
        vtt(pd, A("ub", h), pd, AL.mult, H, 1, K("ub", h), [("pd", h)], (q,))
        vtt(A("dh", h), A("d3", h), pd, AL.add, H, 1, K("d3", h) + [("pd", h)], K("dh", h), (q,))
        vtt(A("pn", h), A("ub", h), PS(q, 3 * H, 4 * H), AL.mult, H, 1, K("ub", h), K("pn", h), (q,))

    def ballot(t, h, tb, ut):
        qt, gt, at = ut
        D0, h3 = "h0_%d" % t, "h3_%d" % t
        part = [C(64 * u, 64 * u + 64) for u in R2]

        def lanes(o, u):
            return C(o + lane(h, u), o + lane(h, u) + 64)

        def rows(o, terms):
            return [(lanes(o, u), x, ident[:, part[u]]) for u in R2 for x, ident in terms]

        p = tile()
        mm(group([(C(0, H), A(x, h), T.idb[:, :]) for x in ("tt", "pz")]), 2 * H, K("tt", h) + K("pz", h) + ["idb"], p)
        sact(A("bs", h), PS(p, 0, H), AF.Sign, H, (), K("bs", h), (p,), bias=-SH / 2)
        mm(group([(C(H, 2 * H), tb["GT"], A("bs", h))]), H, K("bs", h) + [tb["kgt"]], p)
        sact(A("sq", h), PS(p, H, 2 * H), AF.Square, H, (), K("sq", h), (p,))
        c = C(2 * H, 3 * H + 8)
        mm(group([(c, T.ngb[:, :], tb["aG"]), (c, A("sq", h), tb["aG"])]), 2 * H + 16, K("sq", h) + tb["kag"] + ["ngb"], p)
        o = 144 * h
        ch = T.chb[:, o:o + H]
        sact(T.chb[:, o:o + H + 8], PS(p, 2 * H, 3 * H + 8), AF.Sign, H + 8, (), K("ch", h), (p,))
        mm([(C(0, 8), ONE, T.chb[:, o + H:o + H + 8], h == 0, h == 1)], 64, K("ch", h) + ["onb"], at)
        lst = rows(0, [(A(h3, h), T.id37), (A("pn", h), T.id37), (A("dh", h), T.idb)]) + rows(L, [(A(h3, h), T.idb), (A("pn", h), T.idb)] * t)
        mm(group(lst), 64 * len(lst), K(h3, h) + K("pn", h) + K("dh", h) + ["id37", "idb"], qt)
        if t == 1 and h == 1:
            move(QL["ye"], A("yef"), PS(qt, L, 2 * L), L, (), K("yef"), (qt,), bias=MID)
        p = tile()
        lst = group([(C(0, H), ONE, T.prow[:, :]), (C(0, H), T.idk[:, :], A("dh", h)), (C(0, H), T.idn[:, :], ch)])
        mm(lst[:2], 2 * H, K("dh", h) + ["onb", "prow", "idk"], p)
        mm(lst[2:], H, K("ch", h) + ["idn"], p)
        key = PS(p, 0, H)
        a, b = T.pm[:, 2 * H * h:2 * H * h + H], C(2 * H * h + H - 1, 2 * H * h - 1 if h else None, -1)
        add("v", vt(H, 1), lambda: g.vector.tensor_tensor_scan(a, T.rst[:, :], R(key), 0.0, AL.mult, AL.min), ["rst"], [("pm", h)], (p,))
        add("v", vt(H, 1), lambda: g.vector.tensor_tensor_scan(T.pm[:, 2 * H * h + 2 * H - 1:2 * H * h + H - 1:-1], T.rst[:, :], T.pm[:, b], 0.0, AL.mult, AL.min),
            ["rst", ("pm", h)], [("pb", h)])
        vtt(A("eq", h), T.pm[:, 2 * H * h + H:2 * H * h + 2 * H], key, AL.is_equal, H, 1, [("pb", h)], K("eq", h), (p,))
        lst = rows(0, [(T.ngb[:, :], T.idp), (ch, T.idp)]) + rows(L, [(ch, T.idm)])
        lst += [(lanes(L, u), x, y) for u in R2 for x, y in ((T.idb[:, :], A(D0, h)[:, part[u]]), (ONE, T.mid[:, :]))]
        mm(opened(lst), 64 * len(lst), K("ch", h) + K(D0, h) + ["ngb", "idp", "idm", "idb", "onb", "mid"], gt)
        mm(more(rows(0, [(A("eq", h), T.idm)]) + rows(L, [(A("eq", h), T.idp)]), True), 256, K("eq", h), gt)

    def finish(out, ut):
        qt, gt, at = ut
        sact(T.asum[:, 0:8], PS(at, 0, 8), AF.Identity, 8, (), ["acol"], (at,), bias=(DM + 37 * MID) / 8, acc=T.acol[:, 0:1])
        sact(A("qi"), PS(qt, 0, L), AF.Identity, L, ["acol"], K("qi"), (qt,), bias=T.acol[:, 0:1])
        vts(A("ni"), A("qi"), W - 1, None, AL.bitwise_and, None, L, 1, K("qi"), K("ni"))
        vtt(A("wd"), A("ni"), PS(gt, 0, L), AL.add, L, 1, K("ni"), K("wd"), (gt,))
        vtt(A(out), A("wd"), PS(gt, L, 2 * L), AL.max, L, 1, K("wd"), K(out), (gt,))

    def run(gens):
        gens = list(enumerate(gens))
        while gens:
            nxt = []
            for c, x in gens:
                cur[0] = c
                try:
                    next(x)
                    nxt.append((c, x))
                except StopIteration:
                    pass
            gens = nxt
        cur[0] = 0

    def home0(h):
        column("L0a", h, "L1a", None)
        k = send(s1, A("L0a", h, 0, 2 * H), A("L0i", h, 0, 2 * H), "re%d" % h, K("L0a", h) + K("L1a", h), sent[:2])
        recv("re%d" % h, k, 2 * H, K("L0i", h) + K("L1i", h))
        sent.append(k[0])
        yield
        step(0, 1, h, T.xs, KX, "L1a", X0, THD, ["thd"], "f1a", False, False)
        yield

    kh = send(helper(T, topo, rank), T.xs[:, 0:XCUT[2]], T.xs[:, 0:XCUT[2]], "rh", KX + ["pkA", "pkG"], kx0[:1], part=C(-8, None))
    ops[kh[0]]["up"] = CUP
    sent = [kh[0], kx1[0]]
    run(home0(h) for h in R2)
    k = send(h2, T.dh0[:, 0:W // 2], T.dh2[:, 0:W // 2], "rd0", KDH[:1], sent, part=C(0, 8, 2))
    recv("rd0", k, W // 2, [("dh2", 0)])
    sent.append(k[0])
    for h in R2:
        k = send(s1, A("f1a", h), A("f1_0", h), "rr%d" % h, K("f1a", h), sent, part=C(1, 8, 2))
        recv("rr%d" % h, k, H, K("f1_0", h))
        sent.append(k[0])
        if h == 0:
            recv("rx0", kh, XCUT[1], [("xs2", 0)], LAT["hand"])
    k = send(h2, T.dh0[:, W // 2:W + 128], T.dh2[:, W // 2:W + 128], "rd1", KDH[1:] + ["thd"], sent)
    recv("rd1", k, W // 2 + 128, [("dh2", 1)])
    recv("rx1", kh, XCUT[2] - XCUT[1], [("xs2", 1)])
    ktab = k[0]
    XN = lane_views("xrn", "xzn", lambda a, b: A("xi")[:, a:b], [K("xi", h) for h in R2], K(*XNW))
    KX2, KD2 = [("xs2", j) for j in R2], [("dh2", j) for j in R2]

    def away0(h):
        for x in "01":
            move(QL["h0"], A("h%s_0" % x, h), A("L%si" % x, h), H, K("L%si" % x, h), K("h%s_0" % x, h), f=0.5, bias=-MID)
        column("L1i", h, "L2_0", "h2_0")
        yield
        yield from walk(0, h, tb, XN, ut)

    tb = {"P": T.P0, "kp": KP0, "X": T.xs, "kx": KX, "thd": THD, "kth": ["thd", "thdm"],
          "GT": PK[:, 0:128], "kgt": "pkG", "aG": PK[:, 128:264], "kag": ["pkA", "pkB"]}
    ut = (tile(), tile(), tile())
    run(away0(h) for h in R2)
    finish("ndo", ut)
    k = send(dest(rank - 1), A("ndo"), A("ndi"), "rnh", K("ndo"))
    recv("rnh", k, L, K("ndi"))
    k = send(dest(rank - 3), A("ndo"), A("nd2"), "rn2", K("ndo"), (k[0],))
    recv("rn2", k, L, K("nd2"))

    voters("L0b", 1)
    move(QL["h0"], A("h0_1"), A("L0b"), L, K("L0b"), K("h0_1"), f=0.5, bias=-MID)
    X1 = lane_views("xr1", "xz1", lambda a, b: T.xs[:, S * a + 1:S * b:S], [KX, KX], K(*X1W), (ktab,))
    KP1 = table("P1", T.xs, lambda j: KX[j // 2:j // 2 + 1], T.dh2, KD2, K(*PW1))
    KP2 = table("P2", T.xs2, lambda j: KX2[:j // 2 + 1], T.dh2, KD2, K(*PW2))

    move(QL["patch"], T.dgs[:, 0:W:S], A("ndi"), L, K("ndi"), KDG)
    move(QL["yd0"], A("yd0"), A("ndi"), L, K("ndi"), K("yd0"))
    add("y", 0.1, lambda: g.sync.dma_start(T.yd[:, 0:L], A("yd0")), K("yd0"), (), (), "ld5", 16, 2.0)
    k = pack("s", T.P1[:, 0:W:S], T.xs[:, 0:W:S], A("nd2"), L, K("nd2") + KX, KP1)
    ops[k]["up"] = ops[k - 1]["up"] = PUP
    pack("s", T.P2[:, 0:W:S], T.xs2[:, 0:W:S], A("nd2"), L, K("nd2") + KX2, KP2)

    def home1(h):
        column("L0b", h, "L1b", "h1_1")
        yield
        step(1, 1, h, T.P1, KP1, "L1b", X1, THD, ["thd"], "f1_1", True)
        yield
        yield from walk(1, h, tb, X1, ut)

    tb = {"P": T.P2, "kp": KP2, "X": T.xs2, "kx": KX2, "thd": THD2, "kth": [KD2[1], "thd2m"],
          "GT": PK2[:, 0:128], "kgt": KX2[1], "aG": PK2[:, 128:264], "kag": [KX2[1], "pk2B"]}
    ut = (tile(), tile(), tile())
    run(home1(h) for h in R2)
    add("y", 0.1, lambda: g.sync.dma_start(T.ye[:, :], A("yef")), K("yef"), (), (), "ld6", 16, 2.0)
    finish("yd1", ut)
    add("y", 0.1, lambda: g.sync.dma_start(T.yd[:, L:2 * L], A("yd1")), K("yd1"), (), (), "ld7", 16, 2.0)

    order = schedule(ops, tiles, wide, bankof)
    emit(g, T, ENG, CSEM, ops, order, cnt["l"])


CUP = 3.0
PW = 0.02
TURNS, SKEWS, WEIGHTS = 3, (2.0, 3.0), tuple((a, b) for a in (0.3, 0.5, 1.0) for b in (0.2, 0.3))
CASES = ((1.5, 1.0, 1.0, 1.0), (1.15, 1.05, 0.8, 1.2), (1.9, 1.4, 1.2, 1.0), (1.2, 1.35, 1.0, 0.7), (1.9, 1.1, 1.1, 1.5), (1.4, 1.1, 1.4, 1.3))
SHAKES, SWAPS, WARM = 300, 16000, 0.2
SEML, SEMQ = 0.08, 0.04
LOADS = 7
MADE = {}


def times(ops, case):
    gc, f, hop, wire = case
    return ([(o["d"] - o.get("n", 0) * GC * CY) * (f if o["e"] in "vspg" else wire if o["e"] == "w" else 1.0) + o.get("n", 0) * gc * CY for o in ops], [o["lat"] * hop for o in ops])


def draw(seed):
    return (seed * 1103515245 + 12345) % 2 ** 31


def schedule(ops, tiles, wide, bankof):
    n = len(ops)
    key = (tuple(o["d"] for o in ops), tuple(o["e"] for o in ops))
    if key not in MADE:
        eng = [o["e"] for o in ops]
        pre = [[(d, SEML if eng[d] != eng[k] else 0.0 if eng[k] in "pw" or d in ops[k]["soft"] else SEMQ) for d in sorted(ops[k]["deps"])] for k in range(n)]
        succ = [[] for _ in range(n)]
        for k in range(n):
            for d, gap in pre[k]:
                succ[d].append((k, gap))
        cases = [times(ops, c) for c in CASES]
        up = [o["up"] for o in ops]

        opens = {x[0]: t for t, x in enumerate(tiles) if x}
        shuts = {x[-1]: [t for t, y in enumerate(tiles) if y and y[-1] == x[-1]] for x in tiles if x}

        def worth(order):
            tot, more, ways = 0.0, None, []
            for c, b in zip(cases, CASES):
                got = replay(eng, pre, order, c, more, opens, shuts, wide)
                if got is None:
                    return None
                fin, why, more = got
                tot += max(fin) / (b[0] * b[1]) ** 0.5
                ways.append((fin, why))
            return tot, more, ways

        def fore(c, pri):
            last = forwards(ops, eng, c, tiles, wide, pre, succ, pri)
            w = None if last is None else worth(last[1])
            return None if w is None else (w[0], last, c, pri)

        best = None
        for c in cases[:2]:
            bl = [0.0] * n
            for k in range(n - 1, -1, -1):
                bl[k] = c[0][k] + c[1][k] + max([bl[s] for s, gap in succ[k]] + [0.0])
            for skew in SKEWS:
                first = fore(c, [PW * (bl[k] - skew * ops[k]["c"]) + up[k] for k in range(n)])
                for ahead, back in WEIGHTS:
                    last = first
                    for turn in range(TURNS):
                        if last is None:
                            break
                        far = backwards(eng, c, pre, succ, last[1][0], back)
                        last = fore(c, [ahead * far[k] + up[k] for k in range(n)])
                        if last is not None and (best is None or last[0] < best[0]):
                            best = last
        seed = 1
        for turn in range(SHAKES):
            pri = list(best[3])
            for x in range(12):
                seed = draw(seed)
                pri[(seed >> 8) % n] += ((seed >> 3) % 32 - 15.5) / 24.0
            last = fore(best[2], pri)
            if last is not None and last[0] <= best[0]:
                best = last
        order = polish(eng, pre, best[1][1], worth)
        MADE[key] = (order, worth(order)[1])
    order, more = MADE[key]
    for k in more:
        t, b, before = more[k]
        bankof[t] = b
        ops[k]["deps"].update(before)
    return order


def replay(eng, pre, order, case, more, opens, shuts, wide):
    dur, lat = case
    fin, why, free, last = [0.0] * len(eng), [None] * len(eng), dict.fromkeys("vspgywn", 0.0), dict.fromkeys("vspgywn")
    deal = more is None
    if deal:
        more, user, held = {}, [None] * 8, {}
        at = [0.0] * 8
    for k in order:
        e = eng[k]
        st, w = free[e], None
        for d, gap in pre[k]:
            if fin[d] + gap > st:
                st, w = fin[d] + gap, d
        if k in opens:
            if deal:
                t = opens[k]
                if wide[t] == 2:
                    cand = [(max(at[i], at[i + 1]), 0, i) for i in (0, 2, 4, 6) if at[i] is not None and at[i + 1] is not None]
                else:
                    cand = [(max(at[i] + SEML, st), at[i ^ 1] is not None, i) for i in range(7, -1, -1) if at[i] is not None]
                if not cand:
                    return None
                b = min(cand)[2]
                held[t] = range(b, b + wide[t])
                more[k] = (t, b, [user[i] for i in held[t] if user[i] is not None])
                for i in held[t]:
                    at[i] = None
            for d in more[k][2]:
                if fin[d] + SEML > st and eng[d] != e:
                    st, w = fin[d] + SEML, d
        why[k] = (last[e], True) if w is None else (w, False)
        if e != "n":
            free[e], last[e] = st + dur[k], k
        fin[k] = st + dur[k] + lat[k]
        if deal and k in shuts:
            for t in shuts[k]:
                for i in held[t]:
                    at[i], user[i] = fin[k], k
    return fin, why, more


def polish(eng, pre, order, worth):
    got, seed, pairs = worth(order), 7, []
    best = (got[0], order)
    deps = [set(d for d, gap in x) for x in pre]
    after = [set() for x in pre]
    for k, x in enumerate(deps):
        for d in x:
            after[d].add(k)
    for turn in range(SWAPS):
        if not pairs:
            for fin, why in got[2]:
                k = fin.index(max(fin))
                while why[k][0] is not None:
                    if why[k][1] and eng[k] not in "yw":
                        pairs.append((why[k][0], k))
                    k = why[k][0]
        seed = draw(seed)
        u, v = pairs[(seed >> 8) % len(pairs)]
        way = 1 if (seed >> 7) % 2 else -1
        lst, link = (order, deps) if way == 1 else (order[::-1], after)
        if way == -1:
            u, v = v, u
        a, b = lst.index(u), lst.index(v)
        for x in range((seed >> 4) % 4):
            y = a - 1
            while y >= 0 and eng[lst[y]] != eng[v]:
                y -= 1
            a = y if y >= 0 else a
        need, engs, ahead = set(link[v]), set(), []
        for k in lst[a:b][::-1]:
            if k in need or eng[k] in engs:
                ahead.append(k)
                need |= link[k]
                if eng[k] != "n":
                    engs.add(eng[k])
        if eng[v] in engs or min(ahead + [u, v]) < LOADS:
            continue
        new = (lst[:a] + ahead[::-1] + [v] + [k for k in lst[a:b] if k not in ahead] + lst[b + 1:])[::way]
        w = worth(new)
        seed = draw(seed)
        if w is not None and w[0] <= got[0] + WARM * (1.0 - turn / SWAPS) * ((seed >> 8) % 64) / 64.0:
            order, got, pairs = new, w, []
            if w[0] < best[0]:
                best = (w[0], new)
    return best[1]


def backwards(eng, case, pre, succ, fin, back):
    dur, lat = case
    n = len(eng)
    left = [len(x) for x in succ]
    ready = [k for k in range(n) if left[k] == 0]
    rt, bl, free = [0.0] * n, [0.0] * n, {}
    while ready:
        k = min(ready, key=lambda k: max(rt[k] + lat[k], free.get(eng[k], 0.0)) - back * fin[k])
        ready.remove(k)
        bl[k] = max(rt[k] + lat[k], free.get(eng[k], 0.0)) + dur[k]
        if eng[k] != "n":
            free[eng[k]] = bl[k]
        for d, gap in pre[k]:
            left[d] -= 1
            rt[d] = max(rt[d], bl[k] + gap)
            if left[d] == 0:
                ready.append(d)
    return bl


def forwards(ops, eng, case, tiles, wide, pre, succ, pri):
    dur, lat = case
    n = len(ops)
    bankof, more = {}, []
    tfirst = {}
    for t, lst in enumerate(tiles):
        if lst:
            tfirst[lst[0]] = t
    tleft = [len(x) for x in tiles]
    bank = [None] * 8
    bfree = [(0.0, None)] * 8
    left = [len(x) for x in pre]
    ready = [k for k in range(n) if left[k] == 0]
    fin = [0.0] * n
    free = {e: 0.0 for e in "vspgyw"}
    order = []
    rt = [0.0] * n
    free["n"] = -1.0
    while ready:
        best, low = None, 1e9
        for k in ready:
            st = free[eng[k]]
            if rt[k] > st:
                st = rt[k]
            if st - pri[k] >= low:
                continue
            b = -1
            if k in tfirst:
                if wide[tfirst[k]] == 2:
                    cand = [(max(bfree[i][0], bfree[i + 1][0]), 0, i) for i in (0, 2, 4, 6) if bank[i] is None and bank[i + 1] is None]
                else:
                    cand = [(max(bfree[i][0] + SEML, st), bank[i ^ 1] is None, i) for i in range(7, -1, -1) if bank[i] is None]
                if not cand:
                    continue
                f, x, b = min(cand)
                st = max(st, f)
                if st - pri[k] >= low:
                    continue
            best, low = (k, st, b), st - pri[k]
        if best is None:
            return None
        k, st, b = best
        ready.remove(k)
        if b >= 0:
            t = tfirst[k]
            bankof[t] = b
            for i in range(b, b + wide[t]):
                bank[i] = t
                if bfree[i][1] is not None:
                    more.append((k, bfree[i][1]))
        if eng[k] != "n":
            free[eng[k]] = st + dur[k]
        fin[k] = st + dur[k] + lat[k]
        order.append(k)
        for t in ops[k]["ps"]:
            tleft[t] -= 1
            if tleft[t] == 0:
                for i in range(bankof[t], bankof[t] + wide[t]):
                    bank[i] = None
                    bfree[i] = (fin[k], k)
        for s, gap in succ[k]:
            left[s] -= 1
            if fin[k] + gap > rt[s]:
                rt[s] = fin[k] + gap
            if left[s] == 0:
                ready.append(s)
    return fin, order, bankof, more


def emit(g, T, ENG, CSEM, ops, order, nlocal):
    count = {"v": 0, "s": 0, "p": 0, "g": 0}
    known = {e: {} for e in ENG}
    done = {}
    waited = {}
    for k in order:
        o = ops[k]
        e = o["e"]
        if e in "nw":
            done[k] = None if o["sem"] == "-" else (o["sem"], o["inc"], {})
            continue
        q = ENG[e]
        need = {}
        for d in o["deps"]:
            if done[d] is None or d in o["soft"]:
                continue
            if e == "p" and ops[d]["e"] == "p":
                continue
            s, v, _i = done[d]
            if known[e].get(s, 0) < v and need.get(s, (0, 0))[0] < v:
                need[s] = (v, d)
        for s in list(need):
            v, d = need[s]
            for s2 in need:
                if s2 != s and done[need[s2][1]][2].get(s, 0) >= v:
                    del need[s]
                    break
        for s in need:
            v, d = need[s]
            q.wait_ge(T.sem[s], v)
            waited[s] = max(waited.get(s, 0), v)
            for a, b in done[d][2].items():
                if known[e].get(a, 0) < b:
                    known[e][a] = b
            known[e][s] = max(known[e].get(s, 0), v)
        inst = o["f"]()
        if o["sem"] == "-":
            done[k] = None
            continue
        if o["sem"] is None:
            count[e] += 1
            s, v = CSEM[e], count[e]
            inst.then_inc(T.sem[s], 1)
        else:
            s, v = o["sem"], o["inc"]
            inst.then_inc(T.sem[s], v)
        done[k] = (s, v, dict(known[e]))
    total = {CSEM[e]: count[e] for e in count if count[e]}
    total["lsem"] = nlocal
    for k in order:
        o = ops[k]
        if o["sem"] not in (None, "-"):
            total[o["sem"]] = o["inc"]
    for s in total:
        if waited.get(s, 0) < total[s]:
            g.wait_ge(T.sem[s], total[s])
